import numpy as np, ml_dtypes
CORES = [9,25,41,57]
N = 4
BF = ml_dtypes.bfloat16
def gentries(a):
    return np.ascontiguousarray(a.reshape(8, 16, -1).transpose(0, 2, 1)).reshape(8, -1)
def gtable(e):
    e = np.asarray(e); return np.ascontiguousarray(e.reshape(8, -1, 16).transpose(0, 2, 1)).reshape(128, -1).astype(np.int32)
F, S, T, LV, C, W = 1664, 256, 4, 3, 7, 3456
LN, SH = (1, 2, 4), (0, 1, 2)
def parts(rng):
    th = rng.integers(0, 4096, (N, 8, 16, F)); su = rng.integers(0, F, (N, 8, 16, F)); st = rng.integers(0, F, (N, 8, LV, S))
    h = F // 8; hot = np.argsort(rng.random((N, 8, F)), axis=-1)[..., :h]
    a = np.take_along_axis(hot, rng.integers(0, h, (N, 8, 16 * F)), 2).reshape(su.shape); su = np.where(rng.random(su.shape) < 0.5, a, su)
    a = np.take_along_axis(hot, rng.integers(0, h, (N, 8, LV * S)), 2).reshape(st.shape); st = np.where(rng.random(st.shape) < 0.75, a, st)
    near = np.take_along_axis(th, rng.integers(0, F, (N, 8, 1, S)), 3)[:, :, :, None, :] + rng.integers(-600, 601, (N, 8, 16, T, S))
    xs = np.where(rng.random((N, 8, 1, 1, S)) < 0.5, np.clip(near, 0, 4095), rng.integers(0, 4096, (N, 8, 16, T, S)))
    hv = (1 + rng.random((N, 8, 16, 16))) * np.exp2(rng.integers(-1, 1, (N, 8, 16, 16)))
    return th, su, st, xs, hv
def pack(th, su, st, xs, hv):
    return {"th": np.ascontiguousarray(th.reshape(N, 128, F)).astype(np.int32), "su": np.ascontiguousarray(su.reshape(N, 128, F)).astype(np.int32),
            "st": np.stack([gtable(a.reshape(8, -1)) for a in st]), "xs": np.ascontiguousarray(xs.reshape(N, 128, T * S)).astype(np.int32),
            "hv": np.ascontiguousarray(hv.reshape(N, 128, 16)).astype(np.float32).astype(BF)}
def setup_inputs(rng):
    return pack(*parts(rng))
def setup_inputs_corners(rng):
    th, su, st, xs, hv = parts(rng); v = np.arange(F)[None, :]; i = np.arange(16)[:, None]
    for q in range(N):
        for g in range(8):
            k = (g + q) % 4; o = su[q, g].copy()
            if k == 0: su[q, g] = np.where(rng.random((1, F)) < 0.5, v, o)
            if k == 1: su[q, g] = (v + i) % F
            if k == 2: su[q, g] = np.where(o % 3 == 0, 0, np.where(o % 3 == 1, F - 1, v))
            if k == 3: su[q, g] = np.where(i == rng.integers(0, 16, (1, F)), o, o[3:4])
    e = rng.random(st.shape); st = np.where(e < 0.15, 0, np.where(e < 0.3, F - 1, st)); st[..., S - 1] = F - 1; st[..., 0] = 0
    return pack(th, su, st, xs, hv)
def setup_inputs_crowd(rng):
    th, su, st, xs, hv = parts(rng)
    for q in range(N):
        for g in range(8):
            k = (g + q) % 4; n = S if k == 3 else 3; x0 = xs[q, g].copy()
            o = rng.permutation(F)[:LV * n].reshape(LV, n); y = rng.integers(0, 4096, (16, n))
            for l in range(LV):
                th[q, g][:, o[l]] = np.clip(y + rng.integers(-60, 61, (16, n)), 0, 4095)
                su[q, g][C::2, o[l]] = o[l]
                su[q, g][C + 1::2, o[l]] = o[l][rng.integers(0, n, (len(range(C + 1, 16, 2)), n))]
            lane = np.arange(S) if k == 3 else rng.integers(0, 3, S) if k == 2 else np.ones(S, np.int64)
            st[q, g] = o[:, lane]; xs[q, g] = np.clip(y[:, None, lane] + rng.integers(-100, 101, (16, T, S)), 0, 4095)
            if k == 1:
                z = 0 if (g >> 2) % 2 == q % 2 else S - 1
                st[q, g, :, z] = (o[:, 1] + 1 + rng.integers(0, F - 1, LV)) % F; xs[q, g, :, :, z] = x0[:, :, z]
    return pack(th, su, st, xs, hv)
def setup_inputs_ends(rng):
    kind = rng.integers(0, 4, (N, 8, 1, F)); mix = rng.integers(0, 2, (N, 8, 16, F)); i = np.arange(16)
    th = 4095 * np.where(kind == 0, 0, np.where(kind == 1, 1, mix))
    off = (rng.random((N, 8, 1, F)) < 0.25) & (i[:, None] == rng.integers(0, 16, (N, 8, 1, F))); th = np.where(off, np.abs(th - 1), th)
    th[..., [0, 1, 4]] = 0; th[..., [F - 1, F - 2, 2]] = 4095; th[:, :, 15, 1] = 1; th[:, :, 15, F - 2] = 4094
    e = rng.random((N, 8, 16, F)); su = np.where(e < 0.35, 0, np.where(e < 0.7, F - 1, rng.integers(0, F, e.shape)))
    su[..., F - 3] = np.where(i == 15, F - 2, np.where(i % 2 == 0, F - 1, 2)); su[..., 5] = np.where(i == 15, 1, np.where(i % 2 == 0, 4, 0))
    su[..., 3] = np.where(i % 2 == 0, F - 1, 2); su[..., 7] = np.where(i % 2 == 0, 4, 0)
    e = rng.random((N, 8, LV, S)); st = np.where(e < 0.35, 0, np.where(e < 0.7, F - 1, rng.integers(0, F, e.shape)))
    kind = rng.integers(0, 4, (N, 8, 1, T, S)); mix = rng.integers(0, 2, (N, 8, 16, T, S)); xs = 4095 * np.where(kind == 0, 0, np.where(kind == 1, 1, mix))
    for j, a, x in ((1, F - 3, 0), (2, 5, 4095), (3, 3, 0), (4, 7, 0)): st[..., S - j] = a; xs[..., S - j] = x
    hv = np.where(rng.random((N, 8, 16, 16)) < 0.5, 0.25, 2.0)
    return pack(th, su, st, xs, hv)
def setup_inputs_spread(rng):
    th, su, st, xs, hv = parts(rng)
    def uneven(n, shape, own):
        return np.minimum((n * np.power(rng.random(shape), np.exp2(rng.integers(-2, 3, own)))).astype(np.int64), n - 1)
    th = uneven(4096, th.shape, (N, 8, 1, F)); xs = uneven(4096, xs.shape, (N, 8, 1, T, S))
    su = uneven(F, su.shape, (N, 8, 1, F)); st = uneven(F, st.shape, (N, 8, LV, S))
    hv = (1 + rng.random((N, 8, 16, 16))) * np.exp2(rng.integers(-2, 1, (N, 8, 1, 16)))
    return pack(th, su, st, xs, hv)
def setup_inputs_ties(rng):
    th, su, st, xs, hv = parts(rng); m = F // 8
    for q in range(N):
        for g in range(8):
            base = rng.integers(0, 4093, (16, 8)); base[:, 0] = 0; base[:, 1] = 4092; pat = rng.integers(0, 4, (16, 8, 12))
            o = rng.permutation(F)[:8 * m].reshape(8, m); fam = rng.integers(0, 8, F); fam[o] = np.arange(8)[:, None]
            th[q, g] = base[:, fam] + pat[:, fam, rng.integers(0, 12, F)]
            su[q, g] = o[rng.integers(0, 8, F)[None, :], rng.integers(0, m, (16, F))]
            fs = rng.integers(0, 8, S); fs[0] = 0; fs[S - 1] = 1
            close = base[:, fs][:, None, :] + rng.integers(0, 4, (16, T, S))
            keep = (rng.random(S) < 0.6) | (fs < 2); xs[q, g] = np.where(keep[None, None, :], close, xs[q, g])
    st = rng.integers(0, F, st.shape)
    return pack(th, su, st, xs, hv)
def check_ranges(d):
    bad = []
    for k, lo, hi in (("th", 0, 4095), ("su", 0, F - 1), ("st", 0, F - 1), ("xs", 0, 4095), ("hv", 0.25, 2.0)):
        a = np.asarray(d[k]).astype(np.float64)
        if not (np.min(a) >= lo and np.max(a) <= hi): bad.append("range of " + k)
    return bad
def pick(A, ix):
    return np.stack([np.stack([np.take(A[q, g], ix[q, g], axis=1) for g in range(8)]) for q in range(N)])
def members(P, names):
    return pick(P, np.ascontiguousarray(names.transpose(0, 1, 3, 2)).reshape(N, 8, S * 16)).reshape(N, 8, 16, S, 16)
def reference(th, su, st, xs, hv):
    P = np.zeros((N, 8, 16, W), np.int64); P[..., :F] = th.reshape(N, 8, 16, F)
    U = np.zeros((N, 8, 16, W), np.int64); U[..., :F] = su.reshape(N, 8, 16, F)
    x = xs.astype(np.int64).reshape(N, 8, 16, T, S); first = np.stack([gentries(a) for a in st]).astype(np.int64).reshape(N, 8, LV, S)
    opener = [first[:, :, l] for l in range(LV)]; cand = [pick(U, a) for a in opener]
    X = [np.zeros((N, 8, 16, S), np.int64) for l in range(LV)]; kids = [np.ones((N, 8, 16, S)) for l in range(LV)]
    ym = []; m = 0
    for t in range(1, T + 1):
        for l in range(LV): X[l] = X[l] + x[:, :, :, t - 1]
        for l in range(LV):
            L = LN[l]
            if t % L != 0: continue
            D = np.abs(L * members(P, cand[l]) - X[l][..., None])
            M = np.add.reduce(np.exp(D * -(2.0 ** -(9 + SH[l]))), axis=-1) * 2.0 ** -4
            if l > 0: M = 0.5 * M + 0.5 * kids[l]
            ym.append(M)
            win = np.argmin(np.add.reduce(D, axis=2), axis=-1)
            b = np.take_along_axis(cand[l], win[:, :, None, :], 2)[:, :, 0]
            new = (3 * L * pick(P, b) + X[l]) >> (2 + SH[l])
            n0 = F + m * S
            for q in range(N):
                for g in range(8):
                    a, s = np.unique(opener[l][q, g], return_index=True)
                    U[q, g, m, a] = n0 + s
            col = pick(U, b)
            P[..., n0:n0 + S] = np.roll(new, l, axis=0); U[..., n0:n0 + S] = np.roll(col, l, axis=0)
            opener[l] = b; cand[l] = col; X[l] = np.zeros((N, 8, 16, S), np.int64); kids[l] = np.ones((N, 8, 16, S))
            if l + 1 < LV: kids[l + 1] = kids[l + 1] * M
            m += 1
    h = np.asarray(hv).astype(np.float64).reshape(N, 8, 16, 1, 16); yz = []
    for m in range(C):
        n0 = F + m * S
        D = np.abs(members(P, U[..., n0:n0 + S]) - P[..., n0:n0 + S][..., None])
        yz.append(np.add.reduce(h * np.exp(D * -(2.0 ** -9)), axis=-1) * 2.0 ** -4)
    return {"ym": np.concatenate(ym, axis=3).reshape(N, 128, C * S).astype(np.float32), "yz": np.concatenate(yz, axis=3).reshape(N, 128, C * S).astype(np.float32)}

def check_inputs(d):
    bad = list(check_ranges(d))
    if not bad:
        for name, y in reference(**d).items():
            for q in range(N):
                v = np.abs(np.asarray(y[q], np.float64)); s = np.sqrt(np.mean(v * v))
                if v.max() > 6 * s or s < 2.0 ** -4: bad.append('%s of rank %d is uneven or too small' % (name, q))
    return bad

@@ -1,0 +1,600 @@
+import math
+from concourse.mybir import AluOpType, ActivationFunctionType
+
+A = AluOpType
+AF = ActivationFunctionType
+F, S, W = 1664, 256, 3456
+LV = (0, 0, 1, 0, 0, 1, 2)
+TS = ((0,), (1,), (0, 1), (2,), (3,), (2, 3), (0, 1, 2, 3))
+BLIM = (1664, 1920, 1664, 2176, 2688, 2432, 1664)
+ALIM = (1664, 1664, 1664, 1920, 2176, 1664, 1664)
+KIDS = {2: (0, 1), 5: (3, 4), 6: (2, 5)}
+BIG = 3.0e7
+NG, ND = 4, 6
+CFG = dict(pe_sum=("R4", "R6", "E6"), gam=1.5, sca=3.5, cy=0.001, pc=0.0005, vf=0.06, sf=0.07, hop=0.12, slack=0.15, acc=3.6,
+           merge=16, alpha=1.0, v_add=(), on_s={}, by_max=(), gap=30.0, tol=0.2, wait=0.6, bias={})
+USES = ["E%d" % _k for _k in range(7)] + ["R%d" % _k for _k in range(7)]
+NAMES = sorted(["KE2", "KE5", "KE6", "c", "c0", "c1", "c2", "x"] + [_k + _u for _k in ("abs", "d", "exp", "out") for _u in USES + ["F3", "F4"]]
+               + [_k + _u for _k in ("half", "sum", "y") for _u in USES] + [_k + str(_m) for _k in ("b", "col", "el", "ext", "tg", "scE", "gE") for _m in range(7)]
+               + ["gR%d" % _m for _m in (2, 4, 5, 6)] + ["mxR%d" % _m for _m in range(2, 7)] + ["senda_%s%d" % (_k, _m) for _k in "cn" for _m in (2, 5, 6)])
+CFG.update(alpha=0, slack=0.05, pe_sum=("R4", "R6"), v_add=("E1", "E3", "E0", "E6"), gap=30, tol=0.02, wait=0.05, by_max=("R3", "R5"),
+           on_s={"E0": 6, "E2": 13, "E6": 1, "E1": 6, "R5": 7, "E5": 7, "R2": 4, "R4": 1, "E3": 1})
+URGENCY = """-180 88 -204 243 -28 165 155 101 -96 -229 -438 -25 -106 31 -242 -411 -253 14 -809 53 -33 225 -83 -123 221 41 -6 154 110 56 -295 216 205 193 177 465 136 68 -20 -4 -151 -106 -98 -598 -460 -212 -147 150 -366 -357 -299 -132 -723 108 -40 158 -69 -83 169 52 57 -71 112 -212 -220 39 -483 -150 -335 -360 146 -201 -474 -197 -88 -688 203 119 130 168 -96 286 196 -3 -31 -122 53 -485 -39 -264 -278 -242 -35 -754 323 407 -219 196 -90 400 -164 -116 -167 -156 -72 -344 -377 -53 -459 -493 -578 85 -820 -28 317 -198 288 285 59 196 -19 -118 -73 -232 -160 -127 -436 -5 76 172 -135 -100 -226 -168 -53 -170 120 -102 -15 277 135 147 -44 -24 82 -32 -193 -116 -161 -4 -71 -106 -122 -317 158 -773 120 70 32 159 87 82 51 324 -162 -1 -9 33 -198 95 -93 112 1 71 289 -260 -254 -302"""
+CFG["bias"] = dict(zip(NAMES, [int(_a) for _a in URGENCY.split()]))
+
+SCRATCH = {
+    "P": ("sbuf", [128, W], "int32"), "U": ("sbuf", [128, 16 + 2688], "int32"), "U2": ("sbuf", [128, 16 + 2432], "int32"),
+    "xi": ("sbuf", [128, 1024], "int32"), "x16": ("sbuf", [128, 1024], "float16"),
+    "x4": ("sbuf", [128, 512], "float16"), "st32": ("sbuf", [128, 48], "int32"), "stu": ("sbuf", [128, 48], "uint16"),
+    "hb": ("sbuf", [128, 16], "bfloat16"), "lam": ("sbuf", [128, 16], "float32"),
+    "cl": ("sbuf", [128, 13 * 256], "uint16"), "b16": ("sbuf", [128, 112], "uint16"), "off": ("sbuf", [128, 7 * 32], "uint16"),
+    "fx32": ("sbuf", [128, 48], "int32"), "fxu": ("sbuf", [128, 48], "uint16"), "Gf": ("sbuf", [128, 768], "float16"),
+    "c16": ("sbuf", [128, 1792], "float16"), "n16": ("sbuf", [128, 1792], "float16"), "pb": ("sbuf", [128, 256], "float16"),
+    "snd": ("sbuf", [128, 768], "int32"), "cur": ("sbuf", [128, 256], "int32"), "NM": ("sbuf", [128, 1792], "int32"),
+    "e1": ("sbuf", [128, 272], "float32"), "e2": ("sbuf", [128, 272], "float32"), "e3": ("sbuf", [128, 272], "float32"),
+    "Wm": ("sbuf", [128, 256], "float16"), "a16": ("sbuf", [128, 16], "float16"),
+    "f1": ("sbuf", [128, 272], "float32"), "f2": ("sbuf", [128, 272], "float32"), "f3": ("sbuf", [128, 272], "float32"),
+    "d0c": ("sbuf", [128, 272], "float32"), "Tc": ("sbuf", [128, 272], "float32"), "Mk": ("sbuf", [128, 256], "float32"),
+    "wl32": ("sbuf", [128, 16], "int32"), "wl": ("sbuf", [128, 16], "uint16"),
+    "ip": ("sbuf", [128, 8], "int32"), "pc": ("sbuf", [128, 4], "float32"),
+    "ones": ("sbuf", [128, 144], "bfloat16"), "Cv": ("sbuf", [128, 2048], "bfloat16"),
+    "dg": ("sbuf", [128, 8 * 128], "bfloat16"), "I32": ("sbuf", [128, 128], "float32"), "FE": ("sbuf", [128, 768], "float32"),
+    "GI": ("sbuf", [128, 16], "bfloat16"), "GI32": ("sbuf", [128, 8], "float32"), "Dm": ("sbuf", [128, 136], "bfloat16"),
+    "YM": ("sbuf", [128, 1792], "float32"), "YZ": ("sbuf", [128, 1024], "float32"), "K": ("sbuf", [128, 768], "float32"),
+    "PD0": ("psum", [128, 1024], "float32"), "PD1": ("psum", [128, 1024], "float32"),
+    "B4": ("psum", [128, 512], "float32"), "B5": ("psum", [128, 512], "float32"),
+    "B6": ("psum", [128, 512], "float32"), "B7": ("psum", [128, 512], "float32"),
+}
+for _k in range(NG):
+    SCRATCH["G%d" % _k] = ("sbuf", [128, 4096], "float16")
+for _k in range(ND):
+    SCRATCH["D%d" % _k] = ("sbuf", [128, 4096], "float32")
+for _k in range(2):
+    SCRATCH["MX%d" % _k] = ("sbuf", [128, 1024], "float16")
+POOLS = {"MX": 2, "G": NG, "D": ND, "PD": 2, "EL": 1, "DD": 1, "RD": 1, "CU": 1}
+DMAS = ["l_st", "l_su0", "l_su1", "l_th0", "l_th1", "l_xs", "l_hv", "nm", "u2", "fx3", "fx4", "out", "hF3", "hF4"] + [_c + _u for _u in USES for _c in "hoy"]
+ARR = ["a_n2", "a_c2", "a_n5", "a_c5", "a_n6", "a_c6"]
+SEMAPHORES = ["v", "s", "t", "p", "sent"] + DMAS + ARR
+
+
+def build():
+    tasks, part = [], ["c"]
+    GAM, CY, PC, VF, SF = CFG["gam"], CFG["cy"], CFG["pc"], CFG["vf"], CFG["sf"]
+    PE_SUM = CFG["pe_sum"]
+
+    def add(eng, dur, rd, wr, fn, sem=None, lat=0.0, bw=0.0, after=(), name=""):
+        tasks.append(dict(eng=eng, dur=dur, rd=list(rd), wr=list(wr), fn=fn, sem=sem, lat=lat, bw=bw, after=list(after), name=name or part[0]))
+        return len(tasks) - 1
+
+    def vec(n, rd, wr, fn, calls=1, **kw):
+        return add("v", calls * VF + max(n, 64 * calls) * CY, rd, wr, fn, **kw)
+
+    def act(n, rd, wr, fn, calls=1, **kw):
+        return add("s", calls * SF + n * CY, rd, wr, fn, **kw)
+
+    def pe(n, rd, wr, fn, **kw):
+        return add("t", 0.03 + n * PC, rd, wr, fn, **kw)
+
+    def pool(n, rd, wr, fn, **kw):
+        return add("p", 0.17 + 2 * n * CY, rd, wr, fn, **kw)
+
+    def dma(q, sem, bw, rd, wr, fn, n=1, **kw):
+        return add(q, (0.9 if q == "p" else 0.08) * n, rd, wr, fn, sem=sem, lat=1.8, bw=bw, **kw)
+
+    def segs(t, lim):
+        return [(t, "o0"), (t, "o1")] + [(t, k) for k in range((lim - F) // S)]
+
+    H = F // 2
+    dma("y", "l_st", 0.05, [], [("st32", 0)], lambda g, T, B: [g.sync.dma_start(T.st32[:], T.st[:])], name="ld")
+    dma("s", "l_su1", 0.7, [], [("U", "o1")], lambda g, T, B: [g.scalar.dma_start(T.U[:, 16 + H:16 + F], T.su[:, H:F])], name="ld")
+    dma("y", "l_su0", 0.7, [], [("U", "o0")], lambda g, T, B: [g.sync.dma_start(T.U[:, 16:16 + H], T.su[:, 0:H])], name="ld")
+    dma("s", "l_th1", 0.7, [], [("P", "o1")], lambda g, T, B: [g.scalar.dma_start(T.P[:, H:F], T.th[:, H:F])], name="ld")
+    dma("y", "l_th0", 0.7, [], [("P", "o0")], lambda g, T, B: [g.sync.dma_start(T.P[:, 0:H], T.th[:, 0:H])], name="ld")
+    dma("s", "l_hv", 0.05, [], [("hb", 0)], lambda g, T, B: [g.scalar.dma_start(T.hb[:], T.hv[:])], name="ld")
+    dma("y", "l_xs", 0.9, [], [("xi", 0)], lambda g, T, B: [g.sync.dma_start(T.xi[:], T.xs[:])], name="ld")
+
+    fl = dict(allow_small_or_imprecise_dtypes=True)
+    vec(72, [], [("ones", 0)], lambda g, T, B: [g.vector.memset(T.ones[:], 1.0)])
+    vec(1024, [], [("Cv", 0)], lambda g, T, B: [g.vector.memset(T.Cv[:], 1.0)])
+    pool(1, [], [("ip", 0)], lambda g, T, B: [g.iota(T.ip[:, 0:1], [[0, 1]], 0, 1)])
+    pool(128, [("ones", 0)], [("dg", 0)], lambda g, T, B: [g.affine_select(T.dg[:, 0:128], T.ones[:, 0:128], [[-1, 128]], A.is_equal, 0.0, 0, 1)])
+    pool(8, [("ones", 0)], [("GI", 1)], lambda g, T, B: [g.affine_select(T.GI[:, 8:16], T.ones[:, 0:8], [[-16, 8]], A.is_ge, 0.0, 0, 1)])
+    pool(8, [("GI", 1)], [("GI", 0)], lambda g, T, B: [g.affine_select(T.GI[:, 0:8], T.GI[:, 8:16], [[16, 8]], A.is_ge, 0.0, 15, -1)])
+    pool(136, [("ones", 0)], [("Dm", 0)], lambda g, T, B: [g.affine_select(T.Dm[:], T.ones[:, 0:136], [[-16, 8], [-1, 17]], A.is_equal, 0.0, 1, 1)])
+    pool(136, [("Dm", 0)], [("Dm", 0)], lambda g, T, B: [g.affine_select(T.Dm[:], T.Dm[:], [[-16, 8], [-1, 17]], A.not_equal, -1.0, 0, 1)])
+    pool(8, [("ones", 0), ("Dm", 0)], [("Dm", 0)], lambda g, T, B: [g.affine_select(T.Dm[:, 16::17], T.ones[:, 0:8], [[-16, 8]], A.is_equal, 0.0, -15, 1)])
+    pool(16, [], [("wl32", 0)], lambda g, T, B: [g.iota(T.wl32[:], [[17, 16]], 16, 0)])
+    pool(256, [], [("Mk", 0)], lambda g, T, B: [g.iota(T.Mk[:], [[0, 16], [1, 16]], 0, 0, **fl)])
+    pool(272, [], [("Tc", 0)], lambda g, T, B: [g.iota(T.Tc[:], [[0, 16], [1, 17]], -1, 0, **fl)])
+    pool(1792, [], [("U2", "o0")], lambda g, T, B: [g.iota(T.U2[:, 0:1792], [[1, 1792]], F, 0)])
+    pool(2048, [("Cv", 0)], [("Cv", 0)], lambda g, T, B: [g.affine_select(T.Cv[:], T.Cv[:], [[-1, 16], [-16, 8], [0, 16]], A.is_equal, 0.0, 0, 1)])
+    pool(2048, [("Cv", 0)], [("Cv", 0)], lambda g, T, B: [g.affine_select(T.Cv[:], T.Cv[:], [[0, 16], [-1, 128]], A.not_equal, -1.0, 0, 1)])
+    vec(1, [("ip", 0)], [("ip", 1)], lambda g, T, B: [g.vector.tensor_scalar(T.ip[:, 4:5], T.ip[:, 0:1], 15, None, A.bitwise_and)])
+    vec(1, [("ip", 1)], [("pc", 0)], lambda g, T, B: [g.vector.tensor_copy(T.pc[:, 0:1], T.ip[:, 4:5])])
+    DG = (1.0, 2.0, 4.0, 0.75, -0.25, -0.125, -0.0625, -1.0)
+    act(896, [("dg", 0)], [("dg", 1)], lambda g, T, B: [g.scalar.activation(T.dg[:, k * 128:k * 128 + 128], T.dg[:, 0:128], AF.Copy, scale=DG[k]) for k in range(1, 8)], calls=7)
+    if PE_SUM:
+        vec(128, [("dg", 0)], [("I32", 0)], lambda g, T, B: [g.vector.tensor_copy(T.I32[:], T.dg[:, 0:128])])
+    vec(8, [("GI", 0)], [("GI32", 0)], lambda g, T, B: [g.vector.tensor_scalar(T.GI32[:], T.GI[:, 0:8], 16.0, None, A.mult)])
+    vec(16, [("wl32", 0)], [("wl", 0)], lambda g, T, B: [g.vector.tensor_copy(T.wl[:], T.wl32[:])])
+    vec(256, [("Mk", 0), ("pc", 0)], [("Mk", 0)], lambda g, T, B: [g.vector.tensor_scalar(T.Mk[:], T.Mk[:], T.pc[:, 0:1], None, A.is_equal)])
+    vec(272, [("Tc", 0), ("pc", 0)], [("Tc", 0)], lambda g, T, B: [g.vector.tensor_scalar(T.Tc[:], T.Tc[:], T.pc[:, 0:1], 1.0e9, A.is_ge, A.mult)])
+    vec(272, [], [("d0c", 0)], lambda g, T, B: [g.vector.memset(T.d0c[:], -1.0)])
+    vec(16, [("d0c", 0)], [("d0c", 0)], lambda g, T, B: [g.vector.memset(T.d0c[:, 0::17], BIG)])
+    vec(272 * 3 + 64, [], [("init", 0), ("B6", 0)], lambda g, T, B: [g.vector.memset(T.B4[:, 0:272], BIG), g.vector.memset(T.B6[:, 0:272], 0.0),
+                                                           g.vector.memset(T.f1[:], 0.0), g.vector.memset(T.U[:, 0:16], 0)], calls=4)
+    vec(1792, [], [("NM", 0)], lambda g, T, B: [g.vector.memset(T.NM[:], 0)])
+    dma("y", "nm", 0.5, [("U2", "o0"), ("NM", 0)], [("NM", 0)],
+        lambda g, T, B: [g.sync.dma_start(T.NM[m::16, m * S:m * S + S], T.U2[m::16, m * S:m * S + S]) for m in range(7)], n=7)
+    act(1500, [("hb", 0)], [("lam", 0)], lambda g, T, B: [g.scalar.activation(T.lam[:], T.hb[:], AF.Ln, scale=0.0625)], name="ld")
+    vec(48, [("st32", 0)], [("stu", 0)], lambda g, T, B: [g.vector.tensor_copy(T.stu[:], T.st32[:])])
+    vec(1024, [("xi", 0)], [("x16", 0)], lambda g, T, B: [g.vector.tensor_scalar(T.x16[:], T.xi[:], -1.0, 2048.0, A.mult, A.add)], name="x")
+
+    later = {}
+
+    def CL(T, k):
+        return T.cl[:, k * S:k * S + S]
+
+    def take(tab, lim, lst, lkey, k, name):
+        vec(256 * GAM, segs(tab, lim) + [lkey], [("cl", k)],
+            lambda g, T, B: [g.vector.tensor_copy(CL(T, k), T[tab][:, 16:16 + lim].indirect(lst(T)))], name=name)
+
+    def gather(gs, k, lim):
+        for q in range(16):
+            cut = 16 - CFG["on_s"].get(gs[1], 0)
+
+            def fn(g, T, B, q=q, n=1, cut=cut):
+                out, src = B(gs)[:, q * 256:(q + n) * 256], T.P[:, 0:lim].indirect(T.cl[:, k * S + q * 16:k * S + (q + n) * 16])
+                return [g.vector.tensor_scalar(out, src, -2048.0, None, A.add) if q < cut else g.scalar.activation(out, src, AF.Identity, bias=-2048.0)]
+            i = (vec if q < cut else act)(256 * GAM, segs("P", lim) + [("cl", k)], [(gs, q)], fn, name="g" + gs[1])
+            tasks[i]["piece"] = q
+            if q and q != cut:
+                tasks[i]["follow"] = [i - 1]
+
+    def body(u, gs, xs, xk, L, skip, elect):
+        de = ("D", u)
+        lg = int(math.log2(L))
+        sc, ab = [], []
+        for j in range(4):
+            pd = ("PD", u + str(j))
+            sl = [i for i in range(16) if i not in skip][4 * j:4 * j + 4]
+            w = S * len(sl)
+            if u in CFG["by_max"]:
+                nb, mx = ("DD", u), ("MX", u + str(j))
+                if j == 0:
+                    pe(S, xk + [("dg", 1)], [(nb, 0), ("B6", 0)], lambda g, T, B: [g.tensor.matmul(T.B6[:, 0:S], T.dg[:, 896:1024], xs(T)[0], True, True)], name="mx" + u)
+                vec(w, [(gs, q) for q in range(16)] + [(nb, 0)], [(mx, 0)],
+                    lambda g, T, B, sl=sl, mx=mx: [g.vector.tensor_tensor(B(mx)[:, c * S:c * S + S], B(gs)[:, i::16], T.B6[:, 0:S], A.max) for c, i in enumerate(sl)], calls=len(sl), name="mx" + u)
+                pe(2 * w, [(gs, q) for q in range(16)] + [(mx, 0), ("dg", 1)], [(pd, 0)],
+                   lambda g, T, B, sl=sl, mx=mx, pd=pd: [g.tensor.matmul(B(pd)[:, c * S:c * S + S], T.dg[:, a:a + 128], r, a == 896, a == 128) for c, i in enumerate(sl)
+                                                         for a, r in ((896, B(gs)[:, i::16]), (128, B(mx)[:, c * S:c * S + S]))], name="d" + u)
+                continue
+
+            def fn(g, T, B, sl=sl, pd=pd):
+                o = []
+                for c, i in enumerate(sl):
+                    for n, x in enumerate(xs(T)):
+                        o.append(g.tensor.matmul(B(pd)[:, c * S:c * S + S], T.dg[:, 0:128], x, n == 0, False))
+                    o.append(g.tensor.matmul(B(pd)[:, c * S:c * S + S], T.dg[:, lg * 128:lg * 128 + 128], B(gs)[:, i::16], False, True))
+                return o
+            pe(w * (1 + min(L, 2)), [(gs, q) for q in range(16)] + xk + [("dg", 0), ("dg", 1)], [(pd, 0)], fn, name="d" + u)
+            ab.append(act(w, [(pd, 0)], [(de, j)], lambda g, T, B, j=j, pd=pd, w=w: [g.scalar.activation(B(de)[:, j * 1024:j * 1024 + w], B(pd)[:, 0:w], AF.Abs)], name="abs" + u))
+        if elect is not None:
+            for j in range(4):
+                sc.append(pe(2048, [(de, j), ("GI32", 0), ("init", 0)], [(("EL", elect), "sc%d" % j)],
+                             lambda g, T, B, j=j: [g.tensor.matmul(T.B4[:, h * 136 + i:h * 136 + 136:17], B(de)[:, i * S + h * 128:i * S + h * 128 + 128], T.GI32[:], True, True)
+                                                   for i in range(4 * j, 4 * j + 4) for h in range(2)],
+                             name="sc" + u, after=[] if LV[elect] == 0 else ab))
+        later[u] = (L, [i for i in range(16) if i not in skip])
+        return sc
+
+    def mix(u, L, sl):
+        de = ("D", u)
+        y = ("YM" if u[0] == "E" else "YZ", int(u[1]))
+        m = y[1]
+        hi = u[0] == "E" and L > 1
+        b0 = math.log(1.0 / 32 if hi else 1.0 / 16)
+        kk = list(KIDS).index(m) if hi else 0
+        part[0] = "K" + u
+
+        def Y(T):
+            c = m if u[0] == "E" else sorted({x for x in PE_SUM + CFG["by_max"] if x[0] == "R"}).index(u)
+            return T[y[0]][:, c * S:c * S + S]
+
+        def OUT(T):
+            return T[y[0].lower()][:, m * S:m * S + S]
+
+        def KK(T):
+            return T.K[:, kk * S:kk * S + S]
+        for j in range(4):
+            if u[0] == "E":
+                act(1024, [(de, j)], [(de, j)], lambda g, T, B, j=j: [g.scalar.activation(B(de)[:, j * 1024:j * 1024 + 1024], B(de)[:, j * 1024:j * 1024 + 1024], AF.Exp, bias=b0, scale=-1.0 / (512 * L))], name="exp" + u)
+            else:
+                cs = range(4 * j, min(4 * j + 4, len(sl)))
+                src, o = (("PD", u + str(j)), 4 * j) if u in CFG["by_max"] else (de, 0)
+                act(S * len(cs), [(src, j if src == de else 0), ("lam", 0)], [(de, j)],
+                    lambda g, T, B, cs=cs, src=src, o=o: [g.scalar.activation(B(de)[:, c * S:c * S + S], B(src)[:, (c - o) * S:(c - o) * S + S], AF.Exp, bias=T.lam[:, sl[c]:sl[c] + 1], scale=-1.0 / 512)
+                                                          for c in cs], calls=len(cs), name="exp" + u)
+        osem = "o" + u if len(sl) < 16 else "out"
+        bm = u in CFG["by_max"]
+        if bm:
+            n0 = F + m * S
+            vec(256, [("P", m)], [y], lambda g, T, B: [g.vector.tensor_scalar(Y(T), T.P[:, n0:n0 + S], -2048.0, None, A.add)], name="mx" + u)
+            act(256, [y], [y], lambda g, T, B: [g.scalar.activation(Y(T), Y(T), AF.Exp, scale=1.0 / 512)], name="mx" + u)
+        if u in PE_SUM:
+            rd = ("RD", u)
+            for j in range(4):
+                cs = range(4 * j, min(4 * j + 4, len(sl)))
+                i0 = pe(1024 * len(cs), [(de, j), ("I32", 0)], [(rd, j)],
+                        lambda g, T, B, cs=cs: [g.tensor.matmul(T.B7[:, 0:S], T.I32[:], B(de)[:, c * S:c * S + S], c == 0, c == len(sl) - 1) for c in cs], name="sum" + u)
+                if j:
+                    tasks[i0]["follow"] = [i0 - 1]
+            vec(256, [(rd, j) for j in range(4)] + [y] * bm, [y],
+                lambda g, T, B: [g.vector.tensor_tensor(Y(T), T.B7[:, 0:S], Y(T), A.mult) if bm else g.vector.tensor_copy(Y(T), T.B7[:, 0:S])], name="y" + u)
+        else:
+            last = u in CFG["v_add"] and u[0] == "E"
+            for w, n, rd, wr in ((2048, (len(sl) - 8) * S, (0, 1, 2, 3), (0, 1)), (1024, 1024, (0, 1), (0,)), (512, 512, (0,), (0,)), (256, 256, (0,), (0,)))[:3 if last else 4]:
+                dma("p", "h" + u, CFG["acc"] * n / 2048, [(de, j) for j in rd], [(de, j) for j in wr],
+                    lambda g, T, B, w=w, n=n: [g.dma_start(B(de)[:, 0:n], B(de)[:, w:w + n], accum_op=A.add)], name="half" + u)
+            if last:
+                vec(512, [(de, 0)], [y], lambda g, T, B: [g.vector.tensor_tensor(Y(T), B(de)[:, 0:S], B(de)[:, S:2 * S], A.add)], name="y" + u)
+            elif bm:
+                vec(512, [(de, 0), y], [y], lambda g, T, B: [g.vector.tensor_tensor(Y(T), B(de)[:, 0:S], Y(T), A.mult)], name="y" + u)
+            elif u[0] == "E":
+                dma("y", "y" + u, 0.3, [(de, 0)], [y], lambda g, T, B: [g.sync.dma_start(Y(T), B(de)[:, 0:S])], name="y" + u)
+            else:
+                dma("y", "o" + u, 0.3, [(de, 0)], [("o" + y[0], m)], lambda g, T, B: [g.sync.dma_start(OUT(T), B(de)[:, 0:S])], name="out" + u)
+                return
+        if hi:
+            ka, kb = KIDS[m]
+            vec(512, [("YM", ka), ("YM", kb)], [("K", kk)], lambda g, T, B: [g.vector.tensor_tensor(KK(T), T.YM[:, ka * S:ka * S + S], T.YM[:, kb * S:kb * S + S], A.mult)], name="K" + u)
+            act(256, [("K", kk)], [("K", kk)], lambda g, T, B: [g.scalar.activation(KK(T), KK(T), AF.Copy, scale=0.5)])
+            vec(512, [y, ("K", kk)], [y], lambda g, T, B: [g.vector.tensor_tensor(Y(T), Y(T), KK(T), A.add)], name="K" + u)
+        dma("y", osem, 0.3, [y], [("o" + y[0], m)], lambda g, T, B: [g.sync.dma_start(OUT(T), Y(T))], name="out" + u)
+
+    def late(slot, ms, f0):
+        u = "F%d" % slot
+        pd = ("PD", u)
+        w = S * len(ms)
+
+        def fn(g, T, B):
+            o = []
+            for m in ms:
+                o.append(g.tensor.matmul(B(pd)[:, m * S:m * S + S], T.dg[:, 0:128], T.n16[:, m * S:m * S + S], True, False))
+                for v in range(16):
+                    o.append(g.tensor.matmul(B(pd)[:, m * S + 16 * v:m * S + 16 * v + 16], T.dg[:, 0:128], T.Gf[:, (f0 + m) * S + v:(f0 + m + 1) * S:16], False, v == 15))
+            return o
+        pe(5 * w, [("Gf", f0 + m) for m in ms] + [("n16", m) for m in ms] + [("dg", 0)], [(pd, 0)], fn, name="d" + u)
+        act(w, [(pd, 0)], [("FE", f0)], lambda g, T, B: [g.scalar.activation(T.FE[:, f0 * S:f0 * S + w], B(pd)[:, 0:w], AF.Abs)], name="abs" + u)
+        act(w, [("FE", f0), ("lam", 0)], [("FE", f0)],
+            lambda g, T, B: [g.scalar.activation(T.FE[:, f0 * S:f0 * S + w], T.FE[:, f0 * S:f0 * S + w], AF.Exp, bias=T.lam[:, slot:slot + 1], scale=-1.0 / 512)], name="exp" + u)
+        dma("p", "h" + u, 0.8, [("FE", f0)] + [("oYZ", m) for m in ms], [("oYZ", m) for m in ms],
+            lambda g, T, B: [g.dma_start(T.yz[:, 0:w], T.FE[:, f0 * S:f0 * S + w], accum_op=A.add)], name="out" + u)
+
+    def send(sem, l, src, dst, rkey, wkey):
+        a = add("p", 0.6, [rkey], [], lambda g, T, B: [("remote", dst(T), src(T), sem, l)], sem="sent", name="send" + sem)
+        add(None, 0.0, [], [wkey], None, sem=sem, lat=3.5, after=[a])
+
+    def elect(m, k):
+        L = 1 << LV[m]
+        u = "E%d" % m
+        gs = ("G", u)
+        el = ("EL", m)
+        part[0] = "el%d" % m
+        gather(gs, k, BLIM[m])
+        vec(128, [("cl", k)], [("c16", m)], lambda g, T, B: [g.vector.tensor_scalar(T.c16[:, m * S:m * S + S], CL(T, k), -2048.0, None, A.add)])
+        if L == 4:
+            nb = ("RD", "x")
+            pe(1024, [("x16", 0), ("dg", 0)], [(nb, 0)], lambda g, T, B: [g.tensor.matmul(T.B7[:, 0:S], T.dg[:, 0:128], T.x16[:, t * S:t * S + S], t == 0, t == 3) for t in range(4)])
+            vec(256, [(nb, 0)], [("x4", 0)], lambda g, T, B: [g.vector.tensor_copy(T.x4[:, 0:S], T.B7[:, 0:S])])
+            vec(256, [(nb, 0), ("x4", 0)], [("x4", 1)], lambda g, T, B: [g.vector.tensor_tensor(T.x4[:, S:2 * S], T.B7[:, 0:S], T.x4[:, 0:S], A.subtract)])
+            sc = body(u, gs, lambda T: [T.x4[:, 0:S], T.x4[:, S:2 * S]], [("x4", 0), ("x4", 1)], L, (), m)
+        else:
+            sc = body(u, gs, lambda T: [T.x16[:, t * S:t * S + S] for t in TS[m]], [("x16", 0)], L, (), m)
+        pe(272, [("c16", m), ("Dm", 0)], [(el, "b5")],
+           lambda g, T, B: [g.tensor.matmul(T.B5[:, h * 136:h * 136 + 136], T.c16[:, m * S + h * 128:m * S + h * 128 + 128], T.Dm[:], True, True) for h in range(2)], after=sc[:1])
+        sk = [(el, "sc%d" % j) for j in range(4)]
+        vec(272, sk + [("d0c", 0)], [(el, "e1")], lambda g, T, B: [g.vector.tensor_tensor_scan(T.e1[:], T.d0c[:], T.B4[:, 0:272], 0.0, A.add, A.min)])
+        vec(272, sk + [(el, "e1")], [(el, "e2")], lambda g, T, B: [g.vector.tensor_tensor(T.e2[:], T.e1[:], T.B4[:, 0:272], A.not_equal)])
+        vec(272, [(el, "e2"), (el, "b5")], [(el, "e3")], lambda g, T, B: [g.vector.tensor_tensor_scan(T.e3[:], T.B5[:, 0:272], T.e2[:], 0.0, A.add, A.mult)])
+        vec(256 * GAM, [(el, "e3"), ("wl", 0), ("Mk", 0)], [(el, "w")], lambda g, T, B: [g.vector.tensor_tensor(T.Wm[:], T.e3[:].indirect(T.wl[:]), T.Mk[:], A.mult)])
+        pe(128, [(el, "w"), ("GI", 0)], [(el, "lp")],
+           lambda g, T, B: [g.tensor.matmul(T.B4[:, 288 + 8 * h:296 + 8 * h], T.Wm[:, h * 128:h * 128 + 128], T.GI[:, 0:8], True, True) for h in range(2)])
+        vec(16, [(el, "lp")], [("b16", m)], lambda g, T, B: [g.vector.tensor_scalar(T.b16[:, 16 * m:16 * m + 16], T.B4[:, 288:304], 2048.0, None, A.add)], name="b%d" % m)
+        vec(256 * GAM, segs("P", BLIM[m]) + [("b16", m)], [(el, "pb")],
+            lambda g, T, B: [g.vector.tensor_scalar(T.pb[:], T.P[:, 0:BLIM[m]].indirect(T.b16[:, 16 * m:16 * m + 16]), -2048.0, None, A.add)])
+        q = 4 + LV[m]
+        pe(256 * (1 + L), [(el, "pb"), ("x16", 0), ("dg", 1)], [(el, "b5")],
+           lambda g, T, B: [g.tensor.matmul(T.B5[:, 0:S], T.dg[:, 384:512], T.pb[:], True, False)]
+           + [g.tensor.matmul(T.B5[:, 0:S], T.dg[:, q * 128:q * 128 + 128], T.x16[:, t * S:t * S + S], False, t == TS[m][-1]) for t in TS[m]])
+        cst = 2048.0 - 0.5 + 1.0 / (8 * L)
+        n0 = F + m * S
+        if L == 1:
+            vec(256, [(el, "b5")], [("P", m)], lambda g, T, B: [g.vector.tensor_scalar(T.P[:, n0:n0 + S], T.B5[:, 0:S], cst, None, A.add)])
+        else:
+            kk = list(KIDS).index(m)
+            vec(256, [(el, "b5")], [("snd", kk)], lambda g, T, B: [g.vector.tensor_scalar(T.snd[:, kk * S:kk * S + S], T.B5[:, 0:S], cst, None, A.add)])
+            send("a_n%d" % m, LV[m], lambda T: T.snd[:, kk * S:kk * S + S], lambda T: T.P[:, n0:n0 + S], ("snd", kk), ("P", m))
+        vec(256, [("P", m)], [("n16", m)], lambda g, T, B: [g.vector.tensor_scalar(T.n16[:, m * S:m * S + S], T.P[:, n0:n0 + S], -1.0, 2048.0, A.mult, A.add)])
+
+    def targets(m, lst, lkey):
+        dd = ("DD", m)
+        part[0] = "tg%d" % m
+        vec(32, [lkey, ("init", 0)], [(dd, "a")], lambda g, T, B: [g.vector.tensor_scalar(T.a16[:], lst(T), -2048.0, None, A.add),
+                                                                    g.vector.tensor_scalar(T.f1[:, 0::17], lst(T), 16.0, None, A.add)], calls=2)
+        pe(1024, [(dd, "a"), ("Cv", 0)], [(dd, "b6")],
+           lambda g, T, B: [g.tensor.matmul(T.B6[:, 1 + v:272:17], T.Cv[:, v * 128:v * 128 + 128], T.a16[:], True, True) for v in range(16)])
+        vec(272, [(dd, "b6"), ("Tc", 0), ("B6", 0)], [(dd, "f2")], lambda g, T, B: [g.vector.tensor_tensor(T.f2[:], T.B6[:, 0:272], T.Tc[:], A.not_equal)])
+        vec(272, [(dd, "f2"), (dd, "a")], [(dd, "f3")], lambda g, T, B: [g.vector.tensor_tensor_scan(T.f3[:], T.f2[:], T.f1[:], 0.0, A.mult, A.add)])
+        vec(16, [(dd, "f3"), ("pc", 0)], [("off", m)], lambda g, T, B: [g.vector.tensor_scalar(T.off[:, 32 * m:32 * m + 32:2], T.f3[:, 16::17], T.pc[:, 0:1], None, A.max)])
+
+    def extend(m, tab, lst, lkey):
+        lim = ALIM[m]
+        cu = ("CU", m)
+        part[0] = "ext%d" % m
+        vec(256 * GAM, segs(tab, lim) + [lkey, ("NM", 0)], [(cu, 0)],
+            lambda g, T, B: [g.vector.tensor_tensor(T.cur[:], T[tab][:, 16:16 + lim].indirect(lst(T)), T.NM[:, m * S:m * S + S], A.max)])
+        for u in range(15, -1, -1):
+            add("v", VF + 16 * CFG["sca"] * CY, [(cu, 0), ("off", m), ("init", 0)], segs(tab, lim),
+                lambda g, T, B, u=u: [g.vector.tensor_copy(T[tab][:, 0:16 + lim].indirect(T.off[:, 32 * m + 2 * u:32 * m + 2 * u + 1]), T.cur[:, 16 * u:16 * u + 16])],
+                name="ext%d" % m)
+
+    def place(m, k):
+        vec(256, [("cl", k)], [("U", m)], lambda g, T, B: [g.vector.tensor_copy(T.U[:, 16 + F + m * S:16 + F + m * S + S], CL(T, k))])
+
+    def readout(m, gs, fix):
+        body("R%d" % m, gs, lambda T: [T.n16[:, m * S:m * S + S]], [("n16", m)], 1, fix, None)
+
+    def refetch(sem, slot, ms, f0, lim):
+        n = len(ms)
+        dma("y", sem, 0.5, [("U", m) for m in ms], [("fx32", f0)],
+            lambda g, T, B: [g.sync.dma_start(T.fx32[:, 16 * (f0 + m):16 * (f0 + m) + 16], T.U[slot::16, 16 + F + m * S:16 + F + m * S + S]) for m in ms], n=n)
+        vec(32, [("fx32", f0)], [("fxu", f0)], lambda g, T, B: [g.vector.tensor_copy(T.fxu[:, 16 * f0:16 * (f0 + n)], T.fx32[:, 16 * f0:16 * (f0 + n)])])
+        vec(256 * n * GAM, segs("P", lim) + [("fxu", f0)], [("Gf", f0 + m) for m in ms],
+            lambda g, T, B: [g.vector.tensor_scalar(T.Gf[:, f0 * S:(f0 + n) * S], T.P[:, 0:lim].indirect(T.fxu[:, 16 * f0:16 * (f0 + n)]), -2048.0, None, A.add)])
+
+    def stl(l):
+        return (lambda T: T.stu[:, 16 * l:16 * l + 16]), ("stu", 0)
+
+    def bl(m):
+        return (lambda T: T.b16[:, 16 * m:16 * m + 16]), ("b16", m)
+
+    for l in range(3):
+        take("U", F, *stl(l), l, "c%d" % l)
+    opener = {0: stl(0), 1: bl(0), 2: stl(1), 3: bl(1), 4: bl(3), 5: bl(2), 6: stl(2)}
+    elect(0, 0)
+    elect(2, 1)
+    for m in (0, 1, 2, 3, 4):
+        if m == 4:
+            elect(5, 5)
+        if m in (1, 3, 4):
+            elect(m, 3 + {1: 0, 3: 1, 4: 3}[m])
+        targets(m, *opener[m])
+        extend(m, "U", *opener[m])
+        if m == 3:
+            refetch("fx3", 3, [0], 0, 2688)
+        if m == 4:
+            dma("y", "u2", 2.2, segs("U", 2432), segs("U2", 2432), lambda g, T, B: [g.sync.dma_start(T.U2[:], T.U[:, 0:16 + 2432])])
+            refetch("fx4", 4, [0, 1], 1, 2944)
+        take("U", BLIM[m], *bl(m), 3 + m, "col%d" % m)
+        if m == 2:
+            send("a_c2", 1, lambda T: CL(T, 5), lambda T: CL(T, 10), ("cl", 5), ("cl", 10))
+            place(2, 10)
+        elif m < 4:
+            place(m, 3 + m)
+    elect(6, 2)
+    for m in (5, 6):
+        targets(m, *opener[m])
+        extend(m, "U2", *opener[m])
+        take("U2", BLIM[m], *bl(m), 3 + m, "col%d" % m)
+        send("a_c%d" % m, LV[m], lambda T, m=m: CL(T, 3 + m), lambda T, m=m: CL(T, 6 + m), ("cl", 3 + m), ("cl", 6 + m))
+    readout(0, ("G", "E1"), (3, 4))
+    readout(1, ("G", "E3"), (4,))
+    readout(3, ("G", "E4"), ())
+    for m, k in ((2, 10), (4, 7), (5, 11), (6, 12)):
+        gather(("G", "R%d" % m), k, F + (m + 1) * S)
+        readout(m, ("G", "R%d" % m), ())
+    for u in sorted(later):
+        mix(u, *later[u])
+    late(3, [0], 0)
+    late(4, [0, 1], 1)
+    return tasks
+
+
+def plan():
+    tasks = build()
+    n = len(tasks)
+    HOP = CFG["hop"]
+    lastw, readers, users = {}, {}, {}
+    for i, t in enumerate(tasks):
+        raw, oth = set(), set(t["after"])
+        for k in t["rd"]:
+            raw.add(lastw[k])
+        for k in t["wr"]:
+            if k in lastw:
+                oth.add(lastw[k])
+            oth.update(readers.get(k, []))
+        for k in t["rd"]:
+            readers.setdefault(k, []).append(i)
+        for k in t["wr"]:
+            lastw[k] = i
+            readers[k] = []
+        oth.discard(i)
+        t["raw"], t["oth"] = raw | oth, set(t.get("follow", []))
+        t["syms"] = sorted({k[0] for k in t["rd"] + t["wr"] if isinstance(k[0], tuple)}, key=str)
+        for s in t["syms"]:
+            users.setdefault(s, []).append(i)
+    succ = [[] for _ in range(n)]
+    for i, t in enumerate(tasks):
+        for d in t["raw"] | t["oth"]:
+            succ[d].append(i)
+    pr = [0.0] * n
+    for i in range(n - 1, -1, -1):
+        t = tasks[i]
+        pr[i] = t["dur"] + t["lat"] + t["bw"] + HOP + max([pr[j] for j in succ[i]] + [0.0])
+    for i, t in enumerate(tasks):
+        pr[i] = 1000.0 - i if t["name"] == "ld" else CFG["alpha"] * pr[i] + CFG["bias"].get(t["name"], 0.0)
+    end = [None] * n
+    free = {"v": 0.0, "s": 0.0, "t": 0.0, "p": 0.0, "y": 0.0, None: 0.0, "dma": 0.0}
+    tenant = {p: [None] * c for p, c in POOLS.items()}
+    slot = {}
+    order = []
+    last = {}
+    busy = {s: [len(v), 0.0] for s, v in users.items()}
+    left = [len(t["raw"] | t["oth"]) for t in tasks]
+    ready = [i for i in range(n) if left[i] == 0]
+
+    def lend(s):
+        best = None
+        for c, o in enumerate(tenant[s[0]]):
+            if o is None:
+                at = 0.0
+            elif busy[o][0] == 0:
+                at = busy[o][1] + HOP
+            else:
+                continue
+            if best is None or at < best[0]:
+                best = (at, c)
+        return best
+
+    while ready:
+        cand = []
+        for i in ready:
+            t = tasks[i]
+            if "in" not in t:
+                t["in"] = max([end[d] + HOP for d in t["raw"]] + [0.0])
+            at = max(free[t["eng"]], t["in"])
+            got, ok = [], True
+            for s in t["syms"]:
+                if s not in slot:
+                    b = lend(s)
+                    if b is None:
+                        ok = False
+                        break
+                    at = max(at, b[0])
+                    got.append((s, b[1]))
+            if ok:
+                cand.append((at, i, got))
+        if not cand:
+            raise ValueError("no buffer to lend")
+        t0, first, _ = min(cand, key=lambda c: (c[0], -pr[c[1]]))
+        eng = tasks[first]["eng"]
+        mine = sorted([c for c in cand if tasks[c[1]]["eng"] == eng], key=lambda c: -pr[c[1]])
+        now = [c for c in mine if c[0] <= t0 + CFG["slack"]]
+        pick = now[0]
+        for h in mine:
+            if pr[h[1]] < pr[pick[1]] + CFG["gap"]:
+                break
+            if h[0] + CFG["tol"] < pick[0] + tasks[pick[1]]["dur"] and h[0] <= t0 + CFG["wait"]:
+                fit = [c for c in now if c[0] + tasks[c[1]]["dur"] <= h[0] + CFG["tol"]]
+                pick = fit[0] if fit else h
+                break
+        at, i, got = pick
+        t = tasks[i]
+        for s, c in got:
+            o = tenant[s[0]][c]
+            if o is not None:
+                t["raw"] = t["raw"] | set(users[o])
+            tenant[s[0]][c] = s
+            slot[s] = c
+        if t.get("piece") and last.get(eng) == i - 1:
+            t["joined"] = True
+            t["dur"] -= CFG["vf"]
+        last[eng] = i
+        t["at"] = at
+        if eng:
+            free[eng] = at + t["dur"]
+        done = at + t["dur"]
+        if t["bw"]:
+            done = max(done + t["lat"] / 2, free["dma"]) + t["bw"]
+            free["dma"] = done
+            done -= t["lat"] / 2
+        end[i] = done + t["lat"]
+        t["end"] = end[i]
+        for s in t["syms"]:
+            busy[s][0] -= 1
+            busy[s][1] = max(busy[s][1], end[i])
+        order.append(i)
+        ready.remove(i)
+        for j in succ[i]:
+            left[j] -= 1
+            if left[j] == 0:
+                ready.append(j)
+    return tasks, order, slot, max(end)
+
+
+_PLAN = []
+
+
+def rank_program(g, core, T, topo):
+    rank = T.rank_of(core)
+    if rank is None:
+        return
+    if not _PLAN:
+        _PLAN.append(plan())
+    tasks, order, slot, _ = _PLAN[0]
+    cores = list(T.cores)
+    Q = {"v": g.vector, "s": g.scalar, "t": g.tensor, "p": g, "y": g.sync}
+
+    def B(s):
+        return T[s[0] + str(slot[s])]
+
+    def width(l):
+        return len(topo.engines(cores[(rank - l) % len(cores)], core))
+
+    needed = set()
+    for i in order:
+        t = tasks[i]
+        t["w"] = sorted(t["raw"])
+        if t["eng"]:
+            needed.update(t["w"])
+    count, sig, seen = {}, {}, {q: {} for q in Q}
+    for i in order:
+        t = tasks[i]
+        e = t["eng"]
+        if t.get("joined"):
+            continue
+        if "piece" in t:
+            n = 1
+            while i + n < len(tasks) and tasks[i + n].get("joined"):
+                n += 1
+            for sm, val in sorted(sig[d] for d in t["w"]):
+                if seen[e].get(sm, 0) < val:
+                    Q[e].wait_ge(T.sem[sm], val)
+                    seen[e][sm] = val
+            t["fn"](g, T, B, n=n)[0].then_inc(T.sem[e], 1)
+            count[e] = count.get(e, 0) + 1
+            for k in range(n):
+                sig[i + k] = (e, count[e])
+            continue
+        if e is None:
+            sig[i] = (t["sem"], width(LV[int(t["sem"][-1])]))
+            count[t["sem"]] = sig[i][1]
+            continue
+        want = {}
+        for d in t["w"]:
+            sm, val = sig[d]
+            want[sm] = max(want.get(sm, 0), val)
+        for sm in sorted(want):
+            if seen[e].get(sm, 0) < want[sm]:
+                Q[e].wait_ge(T.sem[sm], want[sm])
+                seen[e][sm] = want[sm]
+        ins = t["fn"](g, T, B)
+        if t["sem"] == "sent":
+            _, dst, src, sm, l = ins[0]
+            to = cores[(rank + l) % len(cores)]
+            rid, pid, _ = topo.addr(to)
+            g.remote_dma(dst, src, T.sem[sm], T.sem.sent, pid, rid, topo.mask(core, to))
+            count["sent"] = count.get("sent", 0) + len(topo.engines(core, to))
+        elif t["sem"]:
+            for x in ins:
+                x.then_inc(T.sem[t["sem"]], 16)
+            count[t["sem"]] = count.get(t["sem"], 0) + 16 * len(ins)
+            sig[i] = (t["sem"], count[t["sem"]])
+        elif i in needed:
+            ins[-1].then_inc(T.sem[e], 1)
+            count[e] = count.get(e, 0) + 1
+            sig[i] = (e, count[e])
+    for sm in sorted(count):
+        if max(seen[q].get(sm, 0) for q in Q) < count[sm]:
+            g.sync.wait_ge(T.sem[sm], count[sm])

@@ -10,60 +10,55 @@ BLIM = (1664, 1920, 1664, 2176, 2688, 2432, 1664)
 ALIM = (1664, 1664, 1664, 1920, 2176, 1664, 1664)
 KIDS = {2: (0, 1), 5: (3, 4), 6: (2, 5)}
 BIG = 3.0e7
-NG, ND = 4, 6
-CFG = dict(pe_sum=("R4", "R6", "E6"), gam=1.5, sca=3.5, cy=0.001, pc=0.0005, vf=0.06, sf=0.07, hop=0.12, slack=0.15, acc=3.6,
-           merge=16, alpha=1.0, v_add=(), on_s={}, by_max=(), gap=30.0, tol=0.2, wait=0.6, bias={})
 USES = ["E%d" % _k for _k in range(7)] + ["R%d" % _k for _k in range(7)]
-NAMES = sorted(["KE2", "KE5", "KE6", "c", "c0", "c1", "c2", "x"] + [_k + _u for _k in ("abs", "d", "exp", "out") for _u in USES + ["F3", "F4"]]
-               + [_k + _u for _k in ("half", "sum", "y") for _u in USES] + [_k + str(_m) for _k in ("b", "col", "el", "ext", "tg", "scE", "gE") for _m in range(7)]
-               + ["gR%d" % _m for _m in (2, 4, 5, 6)] + ["mxR%d" % _m for _m in range(2, 7)] + ["senda_%s%d" % (_k, _m) for _k in "cn" for _m in (2, 5, 6)])
-CFG.update(alpha=0, slack=0.05, pe_sum=("R4", "R6"), v_add=("E1", "E3", "E0", "E6"), gap=30, tol=0.02, wait=0.05, by_max=("R3", "R5"),
-           on_s={"E0": 6, "E2": 13, "E6": 1, "E1": 6, "R5": 7, "E5": 7, "R2": 4, "R4": 1, "E3": 1})
-URGENCY = """-180 88 -204 243 -28 165 155 101 -96 -229 -438 -25 -106 31 -242 -411 -253 14 -809 53 -33 225 -83 -123 221 41 -6 154 110 56 -295 216 205 193 177 465 136 68 -20 -4 -151 -106 -98 -598 -460 -212 -147 150 -366 -357 -299 -132 -723 108 -40 158 -69 -83 169 52 57 -71 112 -212 -220 39 -483 -150 -335 -360 146 -201 -474 -197 -88 -688 203 119 130 168 -96 286 196 -3 -31 -122 53 -485 -39 -264 -278 -242 -35 -754 323 407 -219 196 -90 400 -164 -116 -167 -156 -72 -344 -377 -53 -459 -493 -578 85 -820 -28 317 -198 288 285 59 196 -19 -118 -73 -232 -160 -127 -436 -5 76 172 -135 -100 -226 -168 -53 -170 120 -102 -15 277 135 147 -44 -24 82 -32 -193 -116 -161 -4 -71 -106 -122 -317 158 -773 120 70 32 159 87 82 51 324 -162 -1 -9 33 -198 95 -93 112 1 71 289 -260 -254 -302"""
-CFG["bias"] = dict(zip(NAMES, [int(_a) for _a in URGENCY.split()]))
+CFG = dict(gam=1.5, sca=3.5, cy=0.001, pc=0.0005, vf=0.06, sf=0.07, hop=0.12, acc=3.6,
+           slack=0.05, gap=8.0, tol=0.05, wait=0.3, alpha=1.0, shy={}, gate={}, bias={}, hold=dict(PD=40.0, EL=30.0, Q=40.0),
+           vmax=dict(R4=4, R5=4, R6=4), factor=("R4", "R5", "R6"),
+           total=dict({_u: "dma" for _u in USES}, R4="pe", R5="h1", R6="vec"),
+           pools=dict(H=5, MX=4, D=22, PD=3, Q=1), gp=False)
+CFG.update({'gp':True,'bias':{'col5':64,'yE5':116,'sE4':76,'yF4':-45,'zF4':4,'aE0':30,'zE5':-67,'sE0':13,'aR2':-1,'pl0':1,'gE5':20,'sn5':51,'sE2':59,'col4':75,'ext0':27,'ext6':7,'zF3':136,'aE2':-25,'ext5':-3,'pl3':20,'gF3':-30,'sn0':131,'el4':12,'ext1':-3,'col6':-4,'aR0':-6,'KE6':-160,'KE5':36,'zE6':-25,'x':6,'gE6':3,'c2':-92,'yR5':26,'yE2':77,'zR5':-11,'pl1':30,'aR6':15,'aR3':46,'x4':-29,'c0':84,'yF3':-27,'gE4':8,'n1':28,'el3':18,'zR6':-52,'zR4':-2,'aE1':1,'yR6':62,'gE3':10,'ext3':27,'ext2':-4,'c':22,'el1':-24,'col2':-26,'zE4':-7,'nm0':27,'yR3':-112,'aR4':131,'zR2':-6,'n5':-4,'sn3':51,'sn6':-5,'aR5':-1,'yE6':-9,'sn2':20,'yR2':35,'gF4':-5,'z0':11,'cv':61,'yE4':-14,'yE3':-1,'aE3':53,'sE3':-16,'sE6':-94,'n4':107,'yR1':-21,'sn1':-6,'gR5':104,'yR4':20,'zR0':14,'el0':-12,'sn4':-6,'col0':56,'el6':35,'gR6':-62,'nm1':-46,'pl2':17,'yR0':-43,'zE3':19,'n6':-10,'aE4':77,'n2':154,'c1':24,'col3':62,'KE2':-1,'gR2':-2,'n3':5,'gR4':-33,'el5':-36,'col1':-10,'gE0':5,'zE1':-11,'zE0':78,'yE1':23,'aE5':6,'n0':-51,'zR3':31,'yE0':-22,'zE2':-23,'aR1':-9,'gE1':55,'el2':-2,'sE1':-17,'aF4':44,'sE5':5,'aE6':70,'gE2':-3},'hold':{'PD':15,'EL':33,'Q':39,'MX':-7,'PB':28,'TG':8,'D':4,'CU':3},'gate':{'zR2':'expR0','zF3':'expE3','gF4':'expE0','zR5':'b5','gE5':'col1','zR3':'scE6','aR2':'b0','KE6':'col1','yR4':'expE0','aR5':'gR4','zF4':'col0','n6':'b5','zE6':'col2','aR4':'gE0','aE5':'expR1','yR1':'col0','sE4':'col1','gR5':'gE6','col5':'b4','sE3':'gE0','nm1':'b0','aF4':'b3','zE3':'gE5','n4':'expE0','yE4':'scE0','zR4':'b0','n2':'gE6','col6':'scE2','el4':'b3','aE4':'col2','aE6':'b2','n5':'col3'},'vmax':{'R4':1,'R5':3,'R3':4,'E1':4,'R2':4},'total':{'E0':'h3','E1':'dma','E2':'dma','E3':'dma','E4':'h3','E5':'h3','E6':'pe','R0':'dma','R1':'dma','R2':'dma','R3':'h3','R4':'h3','R5':'h1','R6':'vec'},'factor':('R2','R3'),'shy':{'gR6':3,'gE4':51,'gR5':149,'gE6':77,'gE3':64,'gE0':-79,'gR2':79,'gR4':18,'gE5':-20,'gE1':-4,'gE2':16},'pools':{'H':4,'MX':8,'D':22,'PD':3,'Q':1},'gap':15,'wait':0.3,'slack':0.05,'tol':0.2,'alpha':1.0})
 
 SCRATCH = {
-    "P": ("sbuf", [128, W], "int32"), "U": ("sbuf", [128, 16 + 2688], "int32"), "U2": ("sbuf", [128, 16 + 2432], "int32"),
-    "xi": ("sbuf", [128, 1024], "int32"), "x16": ("sbuf", [128, 1024], "float16"),
-    "x4": ("sbuf", [128, 512], "float16"), "st32": ("sbuf", [128, 48], "int32"), "stu": ("sbuf", [128, 48], "uint16"),
+    "P": ("sbuf", [128, W], "int32"), "U": ("sbuf", [128, 16 + 2688], "int32"), "Z": ("sbuf", [128, 16 + 2432], "int32"),
+    "zb": ("sbuf", [128, 512], "float32"),
+    "x16": ("sbuf", [128, 1024], "float16"), "x4": ("sbuf", [128, 512], "float16"),
+    "st32": ("sbuf", [128, 48], "int32"), "stu": ("sbuf", [128, 48], "uint16"),
     "hb": ("sbuf", [128, 16], "bfloat16"), "lam": ("sbuf", [128, 16], "float32"),
     "cl": ("sbuf", [128, 13 * 256], "uint16"), "b16": ("sbuf", [128, 112], "uint16"), "off": ("sbuf", [128, 7 * 32], "uint16"),
     "fx32": ("sbuf", [128, 48], "int32"), "fxu": ("sbuf", [128, 48], "uint16"), "Gf": ("sbuf", [128, 768], "float16"),
-    "c16": ("sbuf", [128, 1792], "float16"), "n16": ("sbuf", [128, 1792], "float16"), "pb": ("sbuf", [128, 256], "float16"),
-    "snd": ("sbuf", [128, 768], "int32"), "cur": ("sbuf", [128, 256], "int32"), "NM": ("sbuf", [128, 1792], "int32"),
+    "C0": ("sbuf", [128, 256], "float16"), "C1": ("sbuf", [128, 256], "float16"),
+    "n16": ("sbuf", [128, 1792], "float16"), "pb": ("sbuf", [128, 256], "float16"),
+    "snd": ("sbuf", [128, 768], "int32"), "cur": ("sbuf", [128, 256], "int32"), "NM": ("sbuf", [128, 1792], "float32"),
     "e1": ("sbuf", [128, 272], "float32"), "e2": ("sbuf", [128, 272], "float32"), "e3": ("sbuf", [128, 272], "float32"),
     "Wm": ("sbuf", [128, 256], "float16"), "a16": ("sbuf", [128, 16], "float16"),
-    "f1": ("sbuf", [128, 272], "float32"), "f2": ("sbuf", [128, 272], "float32"), "f3": ("sbuf", [128, 272], "float32"),
-    "d0c": ("sbuf", [128, 272], "float32"), "Tc": ("sbuf", [128, 272], "float32"), "Mk": ("sbuf", [128, 256], "float32"),
+    "f1": ("sbuf", [128, 256], "float32"), "f2": ("sbuf", [128, 256], "float32"), "f3": ("sbuf", [128, 256], "float32"),
+    "d0c": ("sbuf", [128, 272], "float32"), "Tc": ("sbuf", [128, 256], "float32"), "Mk": ("sbuf", [128, 256], "float32"),
     "wl32": ("sbuf", [128, 16], "int32"), "wl": ("sbuf", [128, 16], "uint16"),
     "ip": ("sbuf", [128, 8], "int32"), "pc": ("sbuf", [128, 4], "float32"),
-    "ones": ("sbuf", [128, 144], "bfloat16"), "Cv": ("sbuf", [128, 2048], "bfloat16"),
+    "ones": ("sbuf", [128, 144], "bfloat16"), "BD": ("sbuf", [128, 128], "bfloat16"), "Cv": ("sbuf", [128, 1920], "bfloat16"),
     "dg": ("sbuf", [128, 8 * 128], "bfloat16"), "I32": ("sbuf", [128, 128], "float32"), "FE": ("sbuf", [128, 768], "float32"),
-    "GI": ("sbuf", [128, 16], "bfloat16"), "GI32": ("sbuf", [128, 8], "float32"), "Dm": ("sbuf", [128, 136], "bfloat16"),
-    "YM": ("sbuf", [128, 1792], "float32"), "YZ": ("sbuf", [128, 1024], "float32"), "K": ("sbuf", [128, 768], "float32"),
-    "PD0": ("psum", [128, 1024], "float32"), "PD1": ("psum", [128, 1024], "float32"),
-    "B4": ("psum", [128, 512], "float32"), "B5": ("psum", [128, 512], "float32"),
-    "B6": ("psum", [128, 512], "float32"), "B7": ("psum", [128, 512], "float32"),
+    "GI": ("sbuf", [128, 32], "bfloat16"), "GI32": ("sbuf", [128, 8], "float32"), "Dm": ("sbuf", [128, 136], "bfloat16"),
+    "YM": ("sbuf", [128, 1792], "float32"), "YZ": ("sbuf", [128, 1792], "float32"),
+    "IH": ("sbuf", [128, 128], "float32"), "FA0": ("sbuf", [128, 256], "float32"), "FA1": ("sbuf", [128, 256], "float32"),
+    "B4": ("psum", [128, 512], "float32"),
 }
-for _k in range(NG):
-    SCRATCH["G%d" % _k] = ("sbuf", [128, 4096], "float16")
-for _k in range(ND):
-    SCRATCH["D%d" % _k] = ("sbuf", [128, 4096], "float32")
-for _k in range(2):
-    SCRATCH["MX%d" % _k] = ("sbuf", [128, 1024], "float16")
-POOLS = {"MX": 2, "G": NG, "D": ND, "PD": 2, "EL": 1, "DD": 1, "RD": 1, "CU": 1}
-DMAS = ["l_st", "l_su0", "l_su1", "l_th0", "l_th1", "l_xs", "l_hv", "nm", "u2", "fx3", "fx4", "out", "hF3", "hF4"] + [_c + _u for _u in USES for _c in "hoy"]
+TILES = {"H": ("sbuf", [128, 4096], "float16"), "MX": ("sbuf", [128, 1024], "float16"), "D": ("sbuf", [128, 1024], "float32"),
+         "PD": ("psum", [128, 1024], "float32"), "Q": ("psum", [128, 512], "float32")}
+SCRATCH.update({_p + str(_k): TILES[_p] for _p in TILES for _k in range(CFG["pools"][_p])})
+POOLS = {"EL": 1, "TG": 1, "CU": 1, "C": 2, "FA": 2}
+DMAS = ["nm0", "nm1", "l_st", "l_su0", "l_su1", "l_th0", "l_th1", "l_xs", "l_hv", "fx3", "fx4", "out", "hF3", "hF4", "oR0", "oR1"]
 ARR = ["a_n2", "a_c2", "a_n5", "a_c5", "a_n6", "a_c6"]
-SEMAPHORES = ["v", "s", "t", "p", "sent"] + DMAS + ARR
+SEMAPHORES = ["v", "s", "t", "p", "sent"] + DMAS + ARR + [_c + _u for _u in USES for _c in "hky"]
+I1, I2, I4, I34, IQ, IM = 0, 1, 2, 3, 4, 7
 
 
 def build():
     tasks, part = [], ["c"]
     GAM, CY, PC, VF, SF = CFG["gam"], CFG["cy"], CFG["pc"], CFG["vf"], CFG["sf"]
-    PE_SUM = CFG["pe_sum"]
+    MISC = "PD" if CFG["pools"]["Q"] < 2 else "Q"
 
-    def add(eng, dur, rd, wr, fn, sem=None, lat=0.0, bw=0.0, after=(), name=""):
-        tasks.append(dict(eng=eng, dur=dur, rd=list(rd), wr=list(wr), fn=fn, sem=sem, lat=lat, bw=bw, after=list(after), name=name or part[0]))
+    def add(eng, dur, rd, wr, fn, sem=None, lat=0.0, bw=0.0, after=(), name="", **kw):
+        tasks.append(dict(eng=eng, dur=dur, rd=list(rd), wr=list(wr), fn=fn, sem=sem, lat=lat, bw=bw, after=list(after), name=name or part[0], **kw))
         return len(tasks) - 1
 
     def vec(n, rd, wr, fn, calls=1, **kw):
@@ -75,62 +70,74 @@ def build():
     def pe(n, rd, wr, fn, **kw):
         return add("t", 0.03 + n * PC, rd, wr, fn, **kw)
 
-    def pool(n, rd, wr, fn, **kw):
-        return add("p", 0.17 + 2 * n * CY, rd, wr, fn, **kw)
+    def pool(n, rd, wr, fn, calls=1, **kw):
+        return add("p", (170 * calls + 2 * n) * CY, rd, wr, fn, **kw)
 
     def dma(q, sem, bw, rd, wr, fn, n=1, **kw):
         return add(q, (0.9 if q == "p" else 0.08) * n, rd, wr, fn, sem=sem, lat=1.8, bw=bw, **kw)
 
+    def copy(n, rd, wr, out, src, **kw):
+        if CFG["gp"]:
+            return pool(n, rd, wr, lambda g, T, B: [g.affine_select(out(T), src(T), [[0, n]], A.is_gt, 0.0, 1, 0)], **kw)
+        return vec(n, rd, wr, lambda g, T, B: [g.vector.tensor_copy(out(T), src(T))], **kw)
+
     def segs(t, lim):
         return [(t, "o0"), (t, "o1")] + [(t, k) for k in range((lim - F) // S)]
 
+    def DG(T, k):
+        return T.dg[:, k * 128:k * 128 + 128]
+
     H = F // 2
     dma("y", "l_st", 0.05, [], [("st32", 0)], lambda g, T, B: [g.sync.dma_start(T.st32[:], T.st[:])], name="ld")
+    dma("s", "l_hv", 0.05, [], [("hb", 0)], lambda g, T, B: [g.scalar.dma_start(T.hb[:], T.hv[:])], name="ld")
     dma("s", "l_su1", 0.7, [], [("U", "o1")], lambda g, T, B: [g.scalar.dma_start(T.U[:, 16 + H:16 + F], T.su[:, H:F])], name="ld")
     dma("y", "l_su0", 0.7, [], [("U", "o0")], lambda g, T, B: [g.sync.dma_start(T.U[:, 16:16 + H], T.su[:, 0:H])], name="ld")
     dma("s", "l_th1", 0.7, [], [("P", "o1")], lambda g, T, B: [g.scalar.dma_start(T.P[:, H:F], T.th[:, H:F])], name="ld")
     dma("y", "l_th0", 0.7, [], [("P", "o0")], lambda g, T, B: [g.sync.dma_start(T.P[:, 0:H], T.th[:, 0:H])], name="ld")
-    dma("s", "l_hv", 0.05, [], [("hb", 0)], lambda g, T, B: [g.scalar.dma_start(T.hb[:], T.hv[:])], name="ld")
-    dma("y", "l_xs", 0.9, [], [("xi", 0)], lambda g, T, B: [g.sync.dma_start(T.xi[:], T.xs[:])], name="ld")
+    dma("y", "l_xs", 0.9, [], segs("Z", F), lambda g, T, B: [g.sync.dma_start(T.Z[:, 0:1024], T.xs[:])], name="ld")
 
     fl = dict(allow_small_or_imprecise_dtypes=True)
-    vec(72, [], [("ones", 0)], lambda g, T, B: [g.vector.memset(T.ones[:], 1.0)])
-    vec(1024, [], [("Cv", 0)], lambda g, T, B: [g.vector.memset(T.Cv[:], 1.0)])
-    pool(1, [], [("ip", 0)], lambda g, T, B: [g.iota(T.ip[:, 0:1], [[0, 1]], 0, 1)])
-    pool(128, [("ones", 0)], [("dg", 0)], lambda g, T, B: [g.affine_select(T.dg[:, 0:128], T.ones[:, 0:128], [[-1, 128]], A.is_equal, 0.0, 0, 1)])
-    pool(8, [("ones", 0)], [("GI", 1)], lambda g, T, B: [g.affine_select(T.GI[:, 8:16], T.ones[:, 0:8], [[-16, 8]], A.is_ge, 0.0, 0, 1)])
-    pool(8, [("GI", 1)], [("GI", 0)], lambda g, T, B: [g.affine_select(T.GI[:, 0:8], T.GI[:, 8:16], [[16, 8]], A.is_ge, 0.0, 15, -1)])
-    pool(136, [("ones", 0)], [("Dm", 0)], lambda g, T, B: [g.affine_select(T.Dm[:], T.ones[:, 0:136], [[-16, 8], [-1, 17]], A.is_equal, 0.0, 1, 1)])
-    pool(136, [("Dm", 0)], [("Dm", 0)], lambda g, T, B: [g.affine_select(T.Dm[:], T.Dm[:], [[-16, 8], [-1, 17]], A.not_equal, -1.0, 0, 1)])
-    pool(8, [("ones", 0), ("Dm", 0)], [("Dm", 0)], lambda g, T, B: [g.affine_select(T.Dm[:, 16::17], T.ones[:, 0:8], [[-16, 8]], A.is_equal, 0.0, -15, 1)])
-    pool(16, [], [("wl32", 0)], lambda g, T, B: [g.iota(T.wl32[:], [[17, 16]], 16, 0)])
-    pool(256, [], [("Mk", 0)], lambda g, T, B: [g.iota(T.Mk[:], [[0, 16], [1, 16]], 0, 0, **fl)])
-    pool(272, [], [("Tc", 0)], lambda g, T, B: [g.iota(T.Tc[:], [[0, 16], [1, 17]], -1, 0, **fl)])
-    pool(1792, [], [("U2", "o0")], lambda g, T, B: [g.iota(T.U2[:, 0:1792], [[1, 1792]], F, 0)])
-    pool(2048, [("Cv", 0)], [("Cv", 0)], lambda g, T, B: [g.affine_select(T.Cv[:], T.Cv[:], [[-1, 16], [-16, 8], [0, 16]], A.is_equal, 0.0, 0, 1)])
-    pool(2048, [("Cv", 0)], [("Cv", 0)], lambda g, T, B: [g.affine_select(T.Cv[:], T.Cv[:], [[0, 16], [-1, 128]], A.not_equal, -1.0, 0, 1)])
-    vec(1, [("ip", 0)], [("ip", 1)], lambda g, T, B: [g.vector.tensor_scalar(T.ip[:, 4:5], T.ip[:, 0:1], 15, None, A.bitwise_and)])
-    vec(1, [("ip", 1)], [("pc", 0)], lambda g, T, B: [g.vector.tensor_copy(T.pc[:, 0:1], T.ip[:, 4:5])])
-    DG = (1.0, 2.0, 4.0, 0.75, -0.25, -0.125, -0.0625, -1.0)
-    act(896, [("dg", 0)], [("dg", 1)], lambda g, T, B: [g.scalar.activation(T.dg[:, k * 128:k * 128 + 128], T.dg[:, 0:128], AF.Copy, scale=DG[k]) for k in range(1, 8)], calls=7)
-    if PE_SUM:
-        vec(128, [("dg", 0)], [("I32", 0)], lambda g, T, B: [g.vector.tensor_copy(T.I32[:], T.dg[:, 0:128])])
-    vec(8, [("GI", 0)], [("GI32", 0)], lambda g, T, B: [g.vector.tensor_scalar(T.GI32[:], T.GI[:, 0:8], 16.0, None, A.mult)])
-    vec(16, [("wl32", 0)], [("wl", 0)], lambda g, T, B: [g.vector.tensor_copy(T.wl[:], T.wl32[:])])
-    vec(256, [("Mk", 0), ("pc", 0)], [("Mk", 0)], lambda g, T, B: [g.vector.tensor_scalar(T.Mk[:], T.Mk[:], T.pc[:, 0:1], None, A.is_equal)])
-    vec(272, [("Tc", 0), ("pc", 0)], [("Tc", 0)], lambda g, T, B: [g.vector.tensor_scalar(T.Tc[:], T.Tc[:], T.pc[:, 0:1], 1.0e9, A.is_ge, A.mult)])
-    vec(272, [], [("d0c", 0)], lambda g, T, B: [g.vector.memset(T.d0c[:], -1.0)])
-    vec(16, [("d0c", 0)], [("d0c", 0)], lambda g, T, B: [g.vector.memset(T.d0c[:, 0::17], BIG)])
-    vec(272 * 3 + 64, [], [("init", 0), ("B6", 0)], lambda g, T, B: [g.vector.memset(T.B4[:, 0:272], BIG), g.vector.memset(T.B6[:, 0:272], 0.0),
-                                                           g.vector.memset(T.f1[:], 0.0), g.vector.memset(T.U[:, 0:16], 0)], calls=4)
-    vec(1792, [], [("NM", 0)], lambda g, T, B: [g.vector.memset(T.NM[:], 0)])
-    dma("y", "nm", 0.5, [("U2", "o0"), ("NM", 0)], [("NM", 0)],
-        lambda g, T, B: [g.sync.dma_start(T.NM[m::16, m * S:m * S + S], T.U2[m::16, m * S:m * S + S]) for m in range(7)], n=7)
+    vec(72, [], [("ones", 0)], lambda g, T, B: [g.vector.memset(T.ones[:], 1.0)], name="ld")
+    pool(1, [], [("ip", 0)], lambda g, T, B: [g.iota(T.ip[:, 0:1], [[0, 1]], 0, 1)], name="ld")
+    pool(128, [("ones", 0)], [("dg", 0)], lambda g, T, B: [g.affine_select(DG(T, I1), T.ones[:, 0:128], [[-1, 128]], A.is_equal, 0.0, 0, 1)], name="ld")
+    pool(256, [], [("Mk", 0)], lambda g, T, B: [g.iota(T.Mk[:], [[0, 16], [1, 16]], 0, 0, **fl)], name="ld")
+    pool(128, [("ones", 0)], [("BD", 0)], lambda g, T, B: [g.affine_select(T.BD[:], T.ones[:, 0:128], [[-16, 8], [0, 16]], A.is_ge, 0.0, 0, 1)], name="ld")
+    pool(8, [("ones", 0)], [("GI", 1)], lambda g, T, B: [g.affine_select(T.GI[:, 8:16], T.ones[:, 0:8], [[-16, 8]], A.is_ge, 0.0, 0, 1)], name="ld")
+    pool(128, [("BD", 0)], [("BD", 0)], lambda g, T, B: [g.affine_select(T.BD[:], T.BD[:], [[16, 8], [0, 16]], A.is_ge, 0.0, 15, -1)], name="ld")
+    pool(8, [("GI", 1)], [("GI", 0)], lambda g, T, B: [g.affine_select(T.GI[:, 0:8], T.GI[:, 8:16], [[16, 8]], A.is_ge, 0.0, 15, -1)], name="ld")
+    pool(256, [], [("Tc", 0)], lambda g, T, B: [g.iota(T.Tc[:], [[0, 16], [1, 16]], -1, 0, **fl)], name="ld")
+    pool(136, [("ones", 0)], [("Dm", 0)], lambda g, T, B: [g.affine_select(T.Dm[:], T.ones[:, 0:136], [[-16, 8], [-1, 17]], A.is_equal, 0.0, 1, 1)], name="ld")
+    pool(16, [], [("wl32", 0)], lambda g, T, B: [g.iota(T.wl32[:], [[17, 16]], 16, 0)], name="ld")
+    pool(136, [("Dm", 0)], [("Dm", 0)], lambda g, T, B: [g.affine_select(T.Dm[:], T.Dm[:], [[-16, 8], [-1, 17]], A.not_equal, -1.0, 0, 1)], name="ld")
+    pool(8, [("ones", 0), ("Dm", 0)], [("Dm", 0)], lambda g, T, B: [g.affine_select(T.Dm[:, 16::17], T.ones[:, 0:8], [[-16, 8]], A.is_equal, 0.0, -15, 1)], name="ld")
+    vec(1, [("ip", 0)], [("ip", 1)], lambda g, T, B: [g.vector.tensor_scalar(T.ip[:, 4:5], T.ip[:, 0:1], 15, None, A.bitwise_and)], name="ld")
+    vec(272, [], [("d0c", 0)], lambda g, T, B: [g.vector.memset(T.d0c[:], -1.0)], name="ld")
+    vec(1, [("ip", 1)], [("pc", 0)], lambda g, T, B: [g.vector.tensor_copy(T.pc[:, 0:1], T.ip[:, 4:5])], name="ld")
+    vec(272 * 2 + 64, [], [("init", 0)], lambda g, T, B: [g.vector.memset(T.B4[:, 0:272], BIG), g.vector.memset(T.f1[:], 0.0), g.vector.memset(T.U[:, 0:16], 0)], calls=3, name="ld")
+    vec(256, [("Mk", 0), ("pc", 0)], [("Mk", 0)], lambda g, T, B: [g.vector.tensor_scalar(T.Mk[:], T.Mk[:], T.pc[:, 0:1], None, A.is_equal)], name="ld")
+    vec(16, [("d0c", 0)], [("d0c", 0)], lambda g, T, B: [g.vector.memset(T.d0c[:, 0::17], BIG)], name="ld")
+    vec(48, [("st32", 0)], [("stu", 0)], lambda g, T, B: [g.vector.tensor_copy(T.stu[:], T.st32[:])], name="ld")
+    SC = (1.0, 2.0, 4.0, 0.75, 0.25, 0.125, 0.0625, -1.0)
+    act(896, [("dg", 0)], [("dg", 1)], lambda g, T, B: [g.scalar.activation(DG(T, k), DG(T, I1), AF.Copy, scale=SC[k]) for k in range(1, 8)], calls=7, name="ld")
     act(1500, [("hb", 0)], [("lam", 0)], lambda g, T, B: [g.scalar.activation(T.lam[:], T.hb[:], AF.Ln, scale=0.0625)], name="ld")
-    vec(48, [("st32", 0)], [("stu", 0)], lambda g, T, B: [g.vector.tensor_copy(T.stu[:], T.st32[:])])
-    vec(1024, [("xi", 0)], [("x16", 0)], lambda g, T, B: [g.vector.tensor_scalar(T.x16[:], T.xi[:], -1.0, 2048.0, A.mult, A.add)], name="x")
-
-    later = {}
+    vec(256, [("dg", 0)], [("I32", 0)], lambda g, T, B: [g.vector.tensor_copy(T.I32[:], DG(T, I1)), g.vector.tensor_scalar(T.IH[:], DG(T, I1), 0.5, None, A.mult)], calls=2, name="ld")
+    vec(24, [("GI", 0)], [("GI32", 0)], lambda g, T, B: [g.vector.tensor_scalar(T.GI32[:], T.GI[:, 0:8], 16.0, None, A.mult),
+                                                          g.vector.tensor_scalar(T.GI[:, 16:24], T.GI[:, 0:8], 32.0, None, A.mult),
+                                                          g.vector.tensor_scalar(T.GI[:, 24:32], T.GI[:, 0:8], -16.0, None, A.mult)], calls=3, name="ld")
+    vec(16, [("wl32", 0)], [("wl", 0)], lambda g, T, B: [g.vector.tensor_copy(T.wl[:], T.wl32[:])])
+    vec(256, [("Tc", 0), ("pc", 0)], [("Tc", 0)], lambda g, T, B: [g.vector.tensor_scalar(T.Tc[:], T.Tc[:], T.pc[:, 0:1], 1.0e9, A.is_ge, A.mult)])
+    for v in range(0, 15, 5):
+        act(640, [("BD", 0), ("Mk", 0)], [("Cv", v)],
+            lambda g, T, B, v=v: [g.scalar.activation(T.Cv[:, k * 128:k * 128 + 128], T.BD[:], AF.Identity, scale=T.Mk[:, k:k + 1]) for k in range(v, v + 5)], calls=5, name="cv")
+    pool(1920, [("Cv", v) for v in (0, 5, 10)], [("Cv", 0)], lambda g, T, B: [g.affine_select(T.Cv[:], T.Cv[:], [[0, 15], [-1, 128]], A.not_equal, -1.0, 0, 1)], name="cv")
+    for sem, ms in (("nm0", [0]), ("nm1", range(1, 7))):
+        a, w = ms[0] * S, len(ms) * S
+        pool(2 * w, [], [("NM", m) for m in ms] + [("YZ", m) for m in ms],
+             lambda g, T, B, a=a, w=w: [g.iota(T.NM[:, a:a + w], [[0, w]], 0, 0, **fl), g.iota(T.YZ[:, a:a + w], [[1, w]], F + a, 0, **fl)], calls=2, name=sem)
+        dma("y", sem, 0.1, [("YZ", m) for m in ms] + [("NM", m) for m in ms], [("NM", m) for m in ms],
+            lambda g, T, B, ms=ms: [g.sync.dma_start(T.NM[m::16, m * S:m * S + S], T.YZ[m::16, m * S:m * S + S]) for m in ms], n=len(ms), name=sem)
+    vec(1024, segs("Z", F), [("x16", 0)], lambda g, T, B: [g.vector.tensor_scalar(T.x16[:], T.Z[:, 0:1024], -2048.0, None, A.add)], name="x")
+    vec(2, [("pc", 0)], [("pc", 1)], lambda g, T, B: [g.vector.tensor_scalar(T.pc[:, 1:2], T.pc[:, 0:1], 6.0, None, A.not_equal), g.vector.memset(T.pc[:, 2:3], 1.0)], calls=2)
 
     def CL(T, k):
         return T.cl[:, k * S:k * S + S]
@@ -141,115 +148,142 @@ def build():
 
     def gather(gs, k, lim):
         for q in range(16):
-            cut = 16 - CFG["on_s"].get(gs[1], 0)
+            def fn(g, T, B, e, q, n):
+                out, src = B(gs)[:, S * q:S * (q + n)], T.P[:, 0:lim].indirect(T.cl[:, k * S + q * 16:k * S + (q + n) * 16])
+                return [g.vector.tensor_scalar(out, src, -2048.0, None, A.add) if e == "v" else g.scalar.activation(out, src, AF.Identity, bias=-2048.0)]
+            vec(256 * GAM, segs("P", lim) + [("cl", k)], [(gs, q)], fn, name=gs[1], piece=q)
 
-            def fn(g, T, B, q=q, n=1, cut=cut):
-                out, src = B(gs)[:, q * 256:(q + n) * 256], T.P[:, 0:lim].indirect(T.cl[:, k * S + q * 16:k * S + (q + n) * 16])
-                return [g.vector.tensor_scalar(out, src, -2048.0, None, A.add) if q < cut else g.scalar.activation(out, src, AF.Identity, bias=-2048.0)]
-            i = (vec if q < cut else act)(256 * GAM, segs("P", lim) + [("cl", k)], [(gs, q)], fn, name="g" + gs[1])
-            tasks[i]["piece"] = q
-            if q and q != cut:
-                tasks[i]["follow"] = [i - 1]
+    sets = {}
 
     def body(u, gs, xs, xk, L, skip, elect):
-        de = ("D", u)
+        sl = [i for i in range(16) if i not in skip]
+        gk = [(gs, q) for q in range(16)]
+        el, xr = ("EL", elect), (MISC, "x" + u)
         lg = int(math.log2(L))
-        sc, ab = [], []
+        nv = CFG["vmax"].get(u, 0)
+        sets[u] = (gs, xs, xk, L, sl, nv)
+        ab = []
+        if nv:
+            pe(S, xk + gk + [("dg", 0)], [(xr, 0)], lambda g, T, B: [g.tensor.matmul(B(xr)[:, 0:S], DG(T, I1), xs(T)[0], True, True)], name="mx" + u)
         for j in range(4):
-            pd = ("PD", u + str(j))
-            sl = [i for i in range(16) if i not in skip][4 * j:4 * j + 4]
-            w = S * len(sl)
-            if u in CFG["by_max"]:
-                nb, mx = ("DD", u), ("MX", u + str(j))
-                if j == 0:
-                    pe(S, xk + [("dg", 1)], [(nb, 0), ("B6", 0)], lambda g, T, B: [g.tensor.matmul(T.B6[:, 0:S], T.dg[:, 896:1024], xs(T)[0], True, True)], name="mx" + u)
-                vec(w, [(gs, q) for q in range(16)] + [(nb, 0)], [(mx, 0)],
-                    lambda g, T, B, sl=sl, mx=mx: [g.vector.tensor_tensor(B(mx)[:, c * S:c * S + S], B(gs)[:, i::16], T.B6[:, 0:S], A.max) for c, i in enumerate(sl)], calls=len(sl), name="mx" + u)
-                pe(2 * w, [(gs, q) for q in range(16)] + [(mx, 0), ("dg", 1)], [(pd, 0)],
-                   lambda g, T, B, sl=sl, mx=mx, pd=pd: [g.tensor.matmul(B(pd)[:, c * S:c * S + S], T.dg[:, a:a + 128], r, a == 896, a == 128) for c, i in enumerate(sl)
-                                                         for a, r in ((896, B(gs)[:, i::16]), (128, B(mx)[:, c * S:c * S + S]))], name="d" + u)
+            ss = sl[4 * j:4 * j + 4]
+            w = S * len(ss)
+            if j < nv:
+                mx = ("MX", u + str(j))
+                for c0 in range(0, len(ss), 2):
+                    cs = range(c0, min(c0 + 2, len(ss)))
+                    vec(S * len(cs), gk + [(xr, 0)], [(mx, c0)],
+                        lambda g, T, B, cs=cs, ss=ss, mx=mx: [g.vector.tensor_tensor(B(mx)[:, c * S:c * S + S], B(gs)[:, ss[c]::16], B(xr)[:, 0:S], A.max) for c in cs], calls=len(cs), name="mx" + u)
+                    if elect is not None:
+                        def fn(g, T, B, cs=cs, ss=ss, mx=mx):
+                            r = []
+                            for c in cs:
+                                for h in range(2):
+                                    ops = [(B(mx)[:, c * S + h * 128:c * S + h * 128 + 128], 16), (B(gs)[:, h * 2048 + ss[c]:h * 2048 + 2048:16], 24)]
+                                    ops += [(xs(T)[0][:, h * 128:h * 128 + 128], 24)] * (nv < 4)
+                                    r += [g.tensor.matmul(T.B4[:, h * 136 + ss[c]:h * 136 + 136:17], a, T.GI[:, k:k + 8], n == 0, n == len(ops) - 1) for n, (a, k) in enumerate(ops)]
+                            return r
+                        pe(512 if nv == 4 else 768, gk + xk + [(mx, c0), ("GI32", 0), ("init", 0)], [(el, "sc%d" % (2 * j + c0 // 2))], fn, name="sc" + u)
                 continue
+            pd, de = ("PD", "a" + u + str(j)), ("D", u + str(j))
 
-            def fn(g, T, B, sl=sl, pd=pd):
+            def fn(g, T, B, ss=ss, pd=pd):
                 o = []
-                for c, i in enumerate(sl):
+                for c, i in enumerate(ss):
                     for n, x in enumerate(xs(T)):
-                        o.append(g.tensor.matmul(B(pd)[:, c * S:c * S + S], T.dg[:, 0:128], x, n == 0, False))
-                    o.append(g.tensor.matmul(B(pd)[:, c * S:c * S + S], T.dg[:, lg * 128:lg * 128 + 128], B(gs)[:, i::16], False, True))
+                        o.append(g.tensor.matmul(B(pd)[:, c * S:c * S + S], DG(T, IM), x, n == 0, False))
+                    o.append(g.tensor.matmul(B(pd)[:, c * S:c * S + S], DG(T, lg), B(gs)[:, i::16], False, True))
                 return o
-            pe(w * (1 + min(L, 2)), [(gs, q) for q in range(16)] + xk + [("dg", 0), ("dg", 1)], [(pd, 0)], fn, name="d" + u)
-            ab.append(act(w, [(pd, 0)], [(de, j)], lambda g, T, B, j=j, pd=pd, w=w: [g.scalar.activation(B(de)[:, j * 1024:j * 1024 + w], B(pd)[:, 0:w], AF.Abs)], name="abs" + u))
+            pe(w * (1 + min(L, 2)), gk + xk + [("dg", 0), ("dg", 1)], [(pd, 0)], fn, name="da" + u)
+            ab.append(act(w, [(pd, 0)], [(de, 0)], lambda g, T, B, pd=pd, de=de, w=w: [g.scalar.activation(B(de)[:, 0:w], B(pd)[:, 0:w], AF.Abs)], name="abs" + u))
         if elect is not None:
-            for j in range(4):
-                sc.append(pe(2048, [(de, j), ("GI32", 0), ("init", 0)], [(("EL", elect), "sc%d" % j)],
-                             lambda g, T, B, j=j: [g.tensor.matmul(T.B4[:, h * 136 + i:h * 136 + 136:17], B(de)[:, i * S + h * 128:i * S + h * 128 + 128], T.GI32[:], True, True)
-                                                   for i in range(4 * j, 4 * j + 4) for h in range(2)],
-                             name="sc" + u, after=[] if LV[elect] == 0 else ab))
-        later[u] = (L, [i for i in range(16) if i not in skip])
-        return sc
+            for j in range(2 * nv, 8):
+                de = ("D", u + str(j // 2))
+                pe(1024, [(de, 0), ("GI32", 0), ("init", 0)], [(el, "sc%d" % j)],
+                   lambda g, T, B, j=j, de=de: [g.tensor.matmul(T.B4[:, h * 136 + i:h * 136 + 136:17], B(de)[:, (i % 4) * S + h * 128:(i % 4) * S + h * 128 + 128], T.GI32[:], True, True)
+                                                for i in (2 * j, 2 * j + 1) for h in range(2)],
+                   name="sc" + u, after=[] if LV[elect] == 0 else ab[-2:])
 
-    def mix(u, L, sl):
-        de = ("D", u)
+    def mix(u):
+        gs, xs, xk, L, sl, nv = sets[u]
         y = ("YM" if u[0] == "E" else "YZ", int(u[1]))
         m = y[1]
         hi = u[0] == "E" and L > 1
         b0 = math.log(1.0 / 32 if hi else 1.0 / 16)
-        kk = list(KIDS).index(m) if hi else 0
-        part[0] = "K" + u
+        fac = u in CFG["factor"] and nv == 4
+        how = CFG["total"][u]
+        de = [("D", u + str(j)) for j in range(4)]
+        osem = "o" + u if len(sl) < 16 else "out"
 
         def Y(T):
-            c = m if u[0] == "E" else sorted({x for x in PE_SUM + CFG["by_max"] if x[0] == "R"}).index(u)
-            return T[y[0]][:, c * S:c * S + S]
+            return T[y[0]][:, m * S:m * S + S]
 
         def OUT(T):
             return T[y[0].lower()][:, m * S:m * S + S]
-
-        def KK(T):
-            return T.K[:, kk * S:kk * S + S]
         for j in range(4):
+            ss = sl[4 * j:4 * j + 4]
+            w = S * len(ss)
+            src = de[j]
+            if j < nv:
+                src, mx = ("PD", "e" + u + str(j)), ("MX", u + str(j))
+
+                def fn(g, T, B, ss=ss, pd=src, mx=mx):
+                    r = []
+                    for c, i in enumerate(ss):
+                        ops = [(IM, B(gs)[:, i::16]), (I2, B(mx)[:, c * S:c * S + S])] + ([] if fac else [(IM, xs(T)[0])])
+                        r += [g.tensor.matmul(B(pd)[:, c * S:c * S + S], DG(T, k), a, n == 0, n == len(ops) - 1) for n, (k, a) in enumerate(ops)]
+                    return r
+                pe(w * (2 if fac else 3), [(gs, q) for q in range(16)] + [(mx, c) for c in range(0, len(ss), 2)] + [("dg", 1)] + ([] if fac else xk), [(src, 0)], fn, name="d" + u)
             if u[0] == "E":
-                act(1024, [(de, j)], [(de, j)], lambda g, T, B, j=j: [g.scalar.activation(B(de)[:, j * 1024:j * 1024 + 1024], B(de)[:, j * 1024:j * 1024 + 1024], AF.Exp, bias=b0, scale=-1.0 / (512 * L))], name="exp" + u)
+                act(w, [(src, 0)], [(de[j], 0)], lambda g, T, B, j=j, src=src: [g.scalar.activation(B(de[j])[:], B(src)[:], AF.Exp, bias=b0, scale=-1.0 / (512 * L))], name="exp" + u)
             else:
-                cs = range(4 * j, min(4 * j + 4, len(sl)))
-                src, o = (("PD", u + str(j)), 4 * j) if u in CFG["by_max"] else (de, 0)
-                act(S * len(cs), [(src, j if src == de else 0), ("lam", 0)], [(de, j)],
-                    lambda g, T, B, cs=cs, src=src, o=o: [g.scalar.activation(B(de)[:, c * S:c * S + S], B(src)[:, (c - o) * S:(c - o) * S + S], AF.Exp, bias=T.lam[:, sl[c]:sl[c] + 1], scale=-1.0 / 512)
-                                                          for c in cs], calls=len(cs), name="exp" + u)
-        osem = "o" + u if len(sl) < 16 else "out"
-        bm = u in CFG["by_max"]
-        if bm:
-            n0 = F + m * S
-            vec(256, [("P", m)], [y], lambda g, T, B: [g.vector.tensor_scalar(Y(T), T.P[:, n0:n0 + S], -2048.0, None, A.add)], name="mx" + u)
-            act(256, [y], [y], lambda g, T, B: [g.scalar.activation(Y(T), Y(T), AF.Exp, scale=1.0 / 512)], name="mx" + u)
-        if u in PE_SUM:
-            rd = ("RD", u)
-            for j in range(4):
-                cs = range(4 * j, min(4 * j + 4, len(sl)))
-                i0 = pe(1024 * len(cs), [(de, j), ("I32", 0)], [(rd, j)],
-                        lambda g, T, B, cs=cs: [g.tensor.matmul(T.B7[:, 0:S], T.I32[:], B(de)[:, c * S:c * S + S], c == 0, c == len(sl) - 1) for c in cs], name="sum" + u)
-                if j:
+                act(w, [(src, 0), ("lam", 0)], [(de[j], 0)],
+                    lambda g, T, B, j=j, ss=ss, src=src: [g.scalar.activation(B(de[j])[:, c * S:c * S + S], B(src)[:, c * S:c * S + S], AF.Exp, bias=T.lam[:, i:i + 1], scale=-1.0 / 512)
+                                                          for c, i in enumerate(ss)], calls=len(ss), name="exp" + u)
+        fk = []
+        if fac:
+            fa = ("FA", u)
+            fk = [(fa, 0)]
+            act(256, xk + [(de[0], 0)], fk, lambda g, T, B: [g.scalar.activation(B(fa)[:], xs(T)[0], AF.Exp, scale=1.0 / 512)], name="y" + u)
+        w3 = S * (len(sl) - 12)
+        adds = (("h", 0, 1, 0, 1024), ("k", 2, 3, 0, w3), ("h", 0, 2, 0, 1024), ("h", 0, 0, 512, 512), ("h", 0, 0, 256, 256))[:{"ha": 1, "h1": 2, "h2": 3, "h3": 4, "dma": 5}.get(how, 0)]
+        for sem, a, b, o, n in adds:
+            dma("p", sem + u, CFG["acc"] * n / 2048, [(de[a], 0), (de[b], 0)], [(de[a], 0)],
+                lambda g, T, B, a=a, b=b, o=o, n=n: [g.dma_start(B(de[a])[:, 0:n], B(de[b])[:, o:o + n], accum_op=A.add)], name="half" + u)
+        rest = {"ha": ((2, 4), (3, w3 // S), (0, 4)), "h1": ((0, 4), (2, 4)), "h2": ((0, 4),), "h3": ((0, 2),)}.get(how, ((0, 4), (1, 4), (2, 4), (3, w3 // S)))
+        rest = [(j, c) for j, n in rest for c in range(n)]
+        rd = (MISC, "s" + u)
+        if how == "vec":
+            for n in range(8):
+                j, o = n // 2, n % 2 * 512
+                vec(512, [(de[j], 0)] + [(rd, 0)] * (n > 0), [(rd, 0)],
+                    lambda g, T, B, j=j, o=o, n=n: [g.vector.tensor_tensor(B(rd)[:, 0:512], B(de[j])[:, o:o + 512], B(rd)[:, 0:512], A.add) if n else g.vector.tensor_copy(B(rd)[:, 0:512], B(de[j])[:, 0:512])], name="sum" + u)
+            vec(256, [(rd, 0)], [y], lambda g, T, B: [g.vector.tensor_copy(Y(T), B(rd)[:, 0:S])], name="y" + u)
+            vec(256, [(rd, 0), y], [(rd, 0) if fac else y], lambda g, T, B: [g.vector.tensor_tensor(B(rd)[:, S:2 * S] if fac else Y(T), B(rd)[:, S:2 * S], Y(T), A.add)], name="y" + u)
+            if fac:
+                vec(256, [(rd, 0)] + fk, [y], lambda g, T, B: [g.vector.tensor_tensor(Y(T), B(rd)[:, S:2 * S], B(fa)[:], A.mult)], name="y" + u)
+        elif how != "dma":
+            for n in range(0, len(rest), 2):
+                two = rest[n:n + 2]
+                i0 = pe(1024 * len(two), sorted({(de[j], 0) for j, _ in two}) + [("I32", 0)], [(rd, n)],
+                        lambda g, T, B, two=two: [g.tensor.matmul(B(rd)[:, 0:S], T.I32[:], B(de[j])[:, c * S:c * S + S], (j, c) == rest[0], (j, c) == rest[-1]) for j, c in two], name="sum" + u)
+                if n:
                     tasks[i0]["follow"] = [i0 - 1]
-            vec(256, [(rd, j) for j in range(4)] + [y] * bm, [y],
-                lambda g, T, B: [g.vector.tensor_tensor(Y(T), T.B7[:, 0:S], Y(T), A.mult) if bm else g.vector.tensor_copy(Y(T), T.B7[:, 0:S])], name="y" + u)
+            vec(256, [(rd, n) for n in range(0, len(rest), 2)] + fk, [y],
+                lambda g, T, B: [g.vector.tensor_tensor(Y(T), B(rd)[:, 0:S], B(fa)[:], A.mult) if fac else g.vector.tensor_copy(Y(T), B(rd)[:, 0:S])], name="y" + u)
+        elif fac:
+            vec(512, [(de[0], 0)] + fk, [y], lambda g, T, B: [g.vector.tensor_tensor(Y(T), B(de[0])[:, 0:S], B(fa)[:], A.mult)], name="y" + u)
+        elif u[0] == "R":
+            dma("y", "y" + u if osem == "out" else osem, 0.3, [(de[0], 0)], [("o" + y[0], m)], lambda g, T, B: [g.sync.dma_start(OUT(T), B(de[0])[:, 0:S])], name="out" + u)
+            return
         else:
-            last = u in CFG["v_add"] and u[0] == "E"
-            for w, n, rd, wr in ((2048, (len(sl) - 8) * S, (0, 1, 2, 3), (0, 1)), (1024, 1024, (0, 1), (0,)), (512, 512, (0,), (0,)), (256, 256, (0,), (0,)))[:3 if last else 4]:
-                dma("p", "h" + u, CFG["acc"] * n / 2048, [(de, j) for j in rd], [(de, j) for j in wr],
-                    lambda g, T, B, w=w, n=n: [g.dma_start(B(de)[:, 0:n], B(de)[:, w:w + n], accum_op=A.add)], name="half" + u)
-            if last:
-                vec(512, [(de, 0)], [y], lambda g, T, B: [g.vector.tensor_tensor(Y(T), B(de)[:, 0:S], B(de)[:, S:2 * S], A.add)], name="y" + u)
-            elif bm:
-                vec(512, [(de, 0), y], [y], lambda g, T, B: [g.vector.tensor_tensor(Y(T), B(de)[:, 0:S], Y(T), A.mult)], name="y" + u)
-            elif u[0] == "E":
-                dma("y", "y" + u, 0.3, [(de, 0)], [y], lambda g, T, B: [g.sync.dma_start(Y(T), B(de)[:, 0:S])], name="y" + u)
-            else:
-                dma("y", "o" + u, 0.3, [(de, 0)], [("o" + y[0], m)], lambda g, T, B: [g.sync.dma_start(OUT(T), B(de)[:, 0:S])], name="out" + u)
-                return
+            dma("y", "y" + u, 0.3, [(de[0], 0)], [y], lambda g, T, B: [g.sync.dma_start(Y(T), B(de[0])[:, 0:S])], name="y" + u)
         if hi:
             ka, kb = KIDS[m]
-            vec(512, [("YM", ka), ("YM", kb)], [("K", kk)], lambda g, T, B: [g.vector.tensor_tensor(KK(T), T.YM[:, ka * S:ka * S + S], T.YM[:, kb * S:kb * S + S], A.mult)], name="K" + u)
-            act(256, [("K", kk)], [("K", kk)], lambda g, T, B: [g.scalar.activation(KK(T), KK(T), AF.Copy, scale=0.5)])
-            vec(512, [y, ("K", kk)], [y], lambda g, T, B: [g.vector.tensor_tensor(Y(T), Y(T), KK(T), A.add)], name="K" + u)
+            kk = ("Q", "K" + u)
+            pe(1024, [("YM", ka), ("YM", kb), y, ("I32", 0)], [(kk, 0)], lambda g, T, B: [g.tensor.matmul(B(kk)[:, 0:S], T.IH[:], T.YM[:, kb * S:kb * S + S], True, True)], name="K" + u)
+            vec(256, [(kk, 0), ("YM", ka)], [(kk, 0)], lambda g, T, B: [g.vector.tensor_tensor(B(kk)[:, 0:S], B(kk)[:, 0:S], T.YM[:, ka * S:ka * S + S], A.mult)], name="K" + u)
+            vec(256, [y, (kk, 0)], [y], lambda g, T, B: [g.vector.tensor_tensor(Y(T), B(kk)[:, 0:S], Y(T), A.add)], name="K" + u)
         dma("y", osem, 0.3, [y], [("o" + y[0], m)], lambda g, T, B: [g.sync.dma_start(OUT(T), Y(T))], name="out" + u)
 
     def late(slot, ms, f0):
@@ -260,11 +294,11 @@ def build():
         def fn(g, T, B):
             o = []
             for m in ms:
-                o.append(g.tensor.matmul(B(pd)[:, m * S:m * S + S], T.dg[:, 0:128], T.n16[:, m * S:m * S + S], True, False))
+                o.append(g.tensor.matmul(B(pd)[:, m * S:m * S + S], DG(T, IM), T.n16[:, m * S:m * S + S], True, False))
                 for v in range(16):
-                    o.append(g.tensor.matmul(B(pd)[:, m * S + 16 * v:m * S + 16 * v + 16], T.dg[:, 0:128], T.Gf[:, (f0 + m) * S + v:(f0 + m + 1) * S:16], False, v == 15))
+                    o.append(g.tensor.matmul(B(pd)[:, m * S + 16 * v:m * S + 16 * v + 16], DG(T, I1), T.Gf[:, (f0 + m) * S + v:(f0 + m + 1) * S:16], False, v == 15))
             return o
-        pe(5 * w, [("Gf", f0 + m) for m in ms] + [("n16", m) for m in ms] + [("dg", 0)], [(pd, 0)], fn, name="d" + u)
+        pe(5 * w, [("Gf", f0 + m) for m in ms] + [("n16", m) for m in ms] + [("dg", 0), ("dg", 1)], [(pd, 0)], fn, name="d" + u)
         act(w, [(pd, 0)], [("FE", f0)], lambda g, T, B: [g.scalar.activation(T.FE[:, f0 * S:f0 * S + w], B(pd)[:, 0:w], AF.Abs)], name="abs" + u)
         act(w, [("FE", f0), ("lam", 0)], [("FE", f0)],
             lambda g, T, B: [g.scalar.activation(T.FE[:, f0 * S:f0 * S + w], T.FE[:, f0 * S:f0 * S + w], AF.Exp, bias=T.lam[:, slot:slot + 1], scale=-1.0 / 512)], name="exp" + u)
@@ -272,86 +306,90 @@ def build():
             lambda g, T, B: [g.dma_start(T.yz[:, 0:w], T.FE[:, f0 * S:f0 * S + w], accum_op=A.add)], name="out" + u)
 
     def send(sem, l, src, dst, rkey, wkey):
-        a = add("p", 0.6, [rkey], [], lambda g, T, B: [("remote", dst(T), src(T), sem, l)], sem="sent", name="send" + sem)
-        add(None, 0.0, [], [wkey], None, sem=sem, lat=3.5, after=[a])
+        a = add("p", 0.6, [rkey], [], lambda g, T, B: [(dst(T), src(T), sem, l)], sem="sent", name="send" + sem)
+        add(None, 0.0, [], [wkey], None, sem=sem, lat=3.5, after=[a], name="send" + sem)
 
     def elect(m, k):
         L = 1 << LV[m]
         u = "E%d" % m
-        gs = ("G", u)
-        el = ("EL", m)
+        gs, el, cn = ("H", "g" + u), ("EL", m), ("C", m)
         part[0] = "el%d" % m
         gather(gs, k, BLIM[m])
-        vec(128, [("cl", k)], [("c16", m)], lambda g, T, B: [g.vector.tensor_scalar(T.c16[:, m * S:m * S + S], CL(T, k), -2048.0, None, A.add)])
         if L == 4:
-            nb = ("RD", "x")
-            pe(1024, [("x16", 0), ("dg", 0)], [(nb, 0)], lambda g, T, B: [g.tensor.matmul(T.B7[:, 0:S], T.dg[:, 0:128], T.x16[:, t * S:t * S + S], t == 0, t == 3) for t in range(4)])
-            vec(256, [(nb, 0)], [("x4", 0)], lambda g, T, B: [g.vector.tensor_copy(T.x4[:, 0:S], T.B7[:, 0:S])])
-            vec(256, [(nb, 0), ("x4", 0)], [("x4", 1)], lambda g, T, B: [g.vector.tensor_tensor(T.x4[:, S:2 * S], T.B7[:, 0:S], T.x4[:, 0:S], A.subtract)])
-            sc = body(u, gs, lambda T: [T.x4[:, 0:S], T.x4[:, S:2 * S]], [("x4", 0), ("x4", 1)], L, (), m)
+            nb = ("Q", "x")
+            pe(1024, [("x16", 0), ("dg", 0)], [(nb, 0)], lambda g, T, B: [g.tensor.matmul(B(nb)[:, 0:S], DG(T, I1), T.x16[:, t * S:t * S + S], t == 0, t == 3) for t in range(4)], name="x4")
+            vec(256, [(nb, 0)], [("x4", 0)], lambda g, T, B: [g.vector.tensor_copy(T.x4[:, 0:S], B(nb)[:, 0:S])], name="x4")
+            vec(256, [(nb, 0), ("x4", 0)], [("x4", 1)], lambda g, T, B: [g.vector.tensor_tensor(T.x4[:, S:2 * S], B(nb)[:, 0:S], T.x4[:, 0:S], A.subtract)], name="x4")
+            body(u, gs, lambda T: [T.x4[:, 0:S], T.x4[:, S:2 * S]], [("x4", 0), ("x4", 1)], L, (), m)
         else:
-            sc = body(u, gs, lambda T: [T.x16[:, t * S:t * S + S] for t in TS[m]], [("x16", 0)], L, (), m)
-        pe(272, [("c16", m), ("Dm", 0)], [(el, "b5")],
-           lambda g, T, B: [g.tensor.matmul(T.B5[:, h * 136:h * 136 + 136], T.c16[:, m * S + h * 128:m * S + h * 128 + 128], T.Dm[:], True, True) for h in range(2)], after=sc[:1])
-        sk = [(el, "sc%d" % j) for j in range(4)]
+            body(u, gs, lambda T: [T.x16[:, t * S:t * S + S] for t in TS[m]], [("x16", 0)], L, (), m)
+        nq, sq = ("Q", "n" + u), ("Q", "s" + u)
+        sk = [(el, "sc%d" % j) for j in range(8)]
+        vec(128, [("cl", k), sk[0]], [(cn, 0)], lambda g, T, B: [g.vector.tensor_scalar(B(cn)[:], CL(T, k), -2048.0, None, A.add)])
+        pe(272, [(cn, 0), ("Dm", 0)] + sk, [(nq, 0)],
+           lambda g, T, B: [g.tensor.matmul(B(nq)[:, h * 136:h * 136 + 136], B(cn)[:, h * 128:h * 128 + 128], T.Dm[:], True, True) for h in range(2)])
         vec(272, sk + [("d0c", 0)], [(el, "e1")], lambda g, T, B: [g.vector.tensor_tensor_scan(T.e1[:], T.d0c[:], T.B4[:, 0:272], 0.0, A.add, A.min)])
         vec(272, sk + [(el, "e1")], [(el, "e2")], lambda g, T, B: [g.vector.tensor_tensor(T.e2[:], T.e1[:], T.B4[:, 0:272], A.not_equal)])
-        vec(272, [(el, "e2"), (el, "b5")], [(el, "e3")], lambda g, T, B: [g.vector.tensor_tensor_scan(T.e3[:], T.B5[:, 0:272], T.e2[:], 0.0, A.add, A.mult)])
+        vec(272, [(el, "e2"), (nq, 0)], [(el, "e3")], lambda g, T, B: [g.vector.tensor_tensor_scan(T.e3[:], B(nq)[:, 0:272], T.e2[:], 0.0, A.add, A.mult)])
         vec(256 * GAM, [(el, "e3"), ("wl", 0), ("Mk", 0)], [(el, "w")], lambda g, T, B: [g.vector.tensor_tensor(T.Wm[:], T.e3[:].indirect(T.wl[:]), T.Mk[:], A.mult)])
         pe(128, [(el, "w"), ("GI", 0)], [(el, "lp")],
            lambda g, T, B: [g.tensor.matmul(T.B4[:, 288 + 8 * h:296 + 8 * h], T.Wm[:, h * 128:h * 128 + 128], T.GI[:, 0:8], True, True) for h in range(2)])
         vec(16, [(el, "lp")], [("b16", m)], lambda g, T, B: [g.vector.tensor_scalar(T.b16[:, 16 * m:16 * m + 16], T.B4[:, 288:304], 2048.0, None, A.add)], name="b%d" % m)
-        vec(256 * GAM, segs("P", BLIM[m]) + [("b16", m)], [(el, "pb")],
-            lambda g, T, B: [g.vector.tensor_scalar(T.pb[:], T.P[:, 0:BLIM[m]].indirect(T.b16[:, 16 * m:16 * m + 16]), -2048.0, None, A.add)])
-        q = 4 + LV[m]
-        pe(256 * (1 + L), [(el, "pb"), ("x16", 0), ("dg", 1)], [(el, "b5")],
-           lambda g, T, B: [g.tensor.matmul(T.B5[:, 0:S], T.dg[:, 384:512], T.pb[:], True, False)]
-           + [g.tensor.matmul(T.B5[:, 0:S], T.dg[:, q * 128:q * 128 + 128], T.x16[:, t * S:t * S + S], False, t == TS[m][-1]) for t in TS[m]])
+        part[0] = "sn%d" % m
+        vec(256 * GAM, segs("P", BLIM[m]) + [("b16", m)], [("pb", 0)],
+            lambda g, T, B: [g.vector.tensor_scalar(T.pb[:], T.P[:, 0:BLIM[m]].indirect(T.b16[:, 16 * m:16 * m + 16]), -2048.0, None, A.add)], lock=("PB", m))
+        pe(256 * (1 + L), [("pb", 0), ("x16", 0), ("dg", 1)], [(sq, 0)],
+           lambda g, T, B: [g.tensor.matmul(B(sq)[:, 0:S], DG(T, I34), T.pb[:], True, False)]
+           + [g.tensor.matmul(B(sq)[:, 0:S], DG(T, IQ + LV[m]), T.x16[:, t * S:t * S + S], False, t == TS[m][-1]) for t in TS[m]], lock=("PB", m))
         cst = 2048.0 - 0.5 + 1.0 / (8 * L)
         n0 = F + m * S
         if L == 1:
-            vec(256, [(el, "b5")], [("P", m)], lambda g, T, B: [g.vector.tensor_scalar(T.P[:, n0:n0 + S], T.B5[:, 0:S], cst, None, A.add)])
+            vec(256, [(sq, 0)], [("P", m)], lambda g, T, B: [g.vector.tensor_scalar(T.P[:, n0:n0 + S], B(sq)[:, 0:S], cst, None, A.add)])
         else:
             kk = list(KIDS).index(m)
-            vec(256, [(el, "b5")], [("snd", kk)], lambda g, T, B: [g.vector.tensor_scalar(T.snd[:, kk * S:kk * S + S], T.B5[:, 0:S], cst, None, A.add)])
+            vec(256, [(sq, 0)], [("snd", kk)], lambda g, T, B: [g.vector.tensor_scalar(T.snd[:, kk * S:kk * S + S], B(sq)[:, 0:S], cst, None, A.add)])
             send("a_n%d" % m, LV[m], lambda T: T.snd[:, kk * S:kk * S + S], lambda T: T.P[:, n0:n0 + S], ("snd", kk), ("P", m))
-        vec(256, [("P", m)], [("n16", m)], lambda g, T, B: [g.vector.tensor_scalar(T.n16[:, m * S:m * S + S], T.P[:, n0:n0 + S], -1.0, 2048.0, A.mult, A.add)])
+        vec(256, [("P", m)], [("n16", m)], lambda g, T, B: [g.vector.tensor_scalar(T.n16[:, m * S:m * S + S], T.P[:, n0:n0 + S], -2048.0, None, A.add)], name="n%d" % m)
 
     def targets(m, lst, lkey):
-        dd = ("DD", m)
+        dd, b6 = ("TG", m), ("Q", "t%d" % m)
         part[0] = "tg%d" % m
-        vec(32, [lkey, ("init", 0)], [(dd, "a")], lambda g, T, B: [g.vector.tensor_scalar(T.a16[:], lst(T), -2048.0, None, A.add),
-                                                                    g.vector.tensor_scalar(T.f1[:, 0::17], lst(T), 16.0, None, A.add)], calls=2)
-        pe(1024, [(dd, "a"), ("Cv", 0)], [(dd, "b6")],
-           lambda g, T, B: [g.tensor.matmul(T.B6[:, 1 + v:272:17], T.Cv[:, v * 128:v * 128 + 128], T.a16[:], True, True) for v in range(16)])
-        vec(272, [(dd, "b6"), ("Tc", 0), ("B6", 0)], [(dd, "f2")], lambda g, T, B: [g.vector.tensor_tensor(T.f2[:], T.B6[:, 0:272], T.Tc[:], A.not_equal)])
-        vec(272, [(dd, "f2"), (dd, "a")], [(dd, "f3")], lambda g, T, B: [g.vector.tensor_tensor_scan(T.f3[:], T.f2[:], T.f1[:], 0.0, A.mult, A.add)])
-        vec(16, [(dd, "f3"), ("pc", 0)], [("off", m)], lambda g, T, B: [g.vector.tensor_scalar(T.off[:, 32 * m:32 * m + 32:2], T.f3[:, 16::17], T.pc[:, 0:1], None, A.max)])
+        vec(32, [lkey, ("init", 0), ("Cv", 0)], [(dd, "a")], lambda g, T, B: [g.vector.tensor_scalar(T.a16[:], lst(T), -2048.0, None, A.add),
+                                                                               g.vector.tensor_scalar(T.f1[:, 0::16], lst(T), 16.0, None, A.add)], calls=2)
+        pe(1088, [(dd, "a"), ("dg", 0), ("dg", 1), ("Cv", 0)], [(b6, 0)],
+           lambda g, T, B: [g.tensor.matmul(B(b6)[:, 0:S:16], DG(T, k), T.a16[:], k == I1, k == IM) for k in (I1, IM)]
+           + [g.tensor.matmul(B(b6)[:, v + 1:S:16], T.Cv[:, v * 128:v * 128 + 128], T.a16[:], True, True) for v in range(15)])
+        vec(256, [(b6, 0), ("Tc", 0)], [(dd, "f2")], lambda g, T, B: [g.vector.tensor_tensor(T.f2[:], B(b6)[:, 0:S], T.Tc[:], A.not_equal)])
+        vec(256, [(dd, "f2"), (dd, "a")], [(dd, "f3")], lambda g, T, B: [g.vector.tensor_tensor_scan(T.f3[:], T.f2[:], T.f1[:], 0.0, A.mult, A.add)])
+        vec(16, [(dd, "f3"), ("pc", 0)], [("off", m)], lambda g, T, B: [g.vector.tensor_scalar(T.off[:, 32 * m:32 * m + 32:2], T.f3[:, 15::16], T.pc[:, 0:1], None, A.max)])
 
     def extend(m, tab, lst, lkey):
         lim = ALIM[m]
         cu = ("CU", m)
         part[0] = "ext%d" % m
-        vec(256 * GAM, segs(tab, lim) + [lkey, ("NM", 0)], [(cu, 0)],
-            lambda g, T, B: [g.vector.tensor_tensor(T.cur[:], T[tab][:, 16:16 + lim].indirect(lst(T)), T.NM[:, m * S:m * S + S], A.max)])
+        empty = m == 5
+        if not empty:
+            vec(256 * GAM, segs(tab, lim) + [lkey, ("NM", m), ("off", m)], [(cu, 0)],
+                lambda g, T, B: [g.vector.tensor_tensor(T.cur[:], T[tab][:, 16:16 + lim].indirect(lst(T)), T.NM[:, m * S:m * S + S], A.max)])
         for u in range(15, -1, -1):
-            add("v", VF + 16 * CFG["sca"] * CY, [(cu, 0), ("off", m), ("init", 0)], segs(tab, lim),
-                lambda g, T, B, u=u: [g.vector.tensor_copy(T[tab][:, 0:16 + lim].indirect(T.off[:, 32 * m + 2 * u:32 * m + 2 * u + 1]), T.cur[:, 16 * u:16 * u + 16])],
-                name="ext%d" % m)
+            add("v", VF + 16 * CFG["sca"] * CY, [("NM", m) if empty else (cu, 0), ("off", m), ("init", 0)], segs(tab, lim),
+                lambda g, T, B, u=u: [g.vector.tensor_copy(T[tab][:, 0:16 + lim].indirect(T.off[:, 32 * m + 2 * u:32 * m + 2 * u + 1]),
+                                                           T.NM[:, m * S + 16 * u:m * S + 16 * u + 16] if empty else T.cur[:, 16 * u:16 * u + 16])])
 
     def place(m, k):
-        vec(256, [("cl", k)], [("U", m)], lambda g, T, B: [g.vector.tensor_copy(T.U[:, 16 + F + m * S:16 + F + m * S + S], CL(T, k))])
+        copy(256, [("cl", k)], [("U", m)], lambda T: T.U[:, 16 + F + m * S:16 + F + m * S + S], lambda T: CL(T, k), name="pl%d" % m)
 
     def readout(m, gs, fix):
         body("R%d" % m, gs, lambda T: [T.n16[:, m * S:m * S + S]], [("n16", m)], 1, fix, None)
 
     def refetch(sem, slot, ms, f0, lim):
         n = len(ms)
+        nm = "gF%d" % slot
         dma("y", sem, 0.5, [("U", m) for m in ms], [("fx32", f0)],
-            lambda g, T, B: [g.sync.dma_start(T.fx32[:, 16 * (f0 + m):16 * (f0 + m) + 16], T.U[slot::16, 16 + F + m * S:16 + F + m * S + S]) for m in ms], n=n)
-        vec(32, [("fx32", f0)], [("fxu", f0)], lambda g, T, B: [g.vector.tensor_copy(T.fxu[:, 16 * f0:16 * (f0 + n)], T.fx32[:, 16 * f0:16 * (f0 + n)])])
+            lambda g, T, B: [g.sync.dma_start(T.fx32[:, 16 * (f0 + m):16 * (f0 + m) + 16], T.U[slot::16, 16 + F + m * S:16 + F + m * S + S]) for m in ms], n=n, name=nm)
+        copy(16 * n, [("fx32", f0)], [("fxu", f0)], lambda T: T.fxu[:, 16 * f0:16 * (f0 + n)], lambda T: T.fx32[:, 16 * f0:16 * (f0 + n)], name=nm)
         vec(256 * n * GAM, segs("P", lim) + [("fxu", f0)], [("Gf", f0 + m) for m in ms],
-            lambda g, T, B: [g.vector.tensor_scalar(T.Gf[:, f0 * S:(f0 + n) * S], T.P[:, 0:lim].indirect(T.fxu[:, 16 * f0:16 * (f0 + n)]), -2048.0, None, A.add)])
+            lambda g, T, B: [g.vector.tensor_scalar(T.Gf[:, f0 * S:(f0 + n) * S], T.P[:, 0:lim].indirect(T.fxu[:, 16 * f0:16 * (f0 + n)]), -2048.0, None, A.add)], name=nm)
 
     def stl(l):
         return (lambda T: T.stu[:, 16 * l:16 * l + 16]), ("stu", 0)
@@ -374,7 +412,6 @@ def build():
         if m == 3:
             refetch("fx3", 3, [0], 0, 2688)
         if m == 4:
-            dma("y", "u2", 2.2, segs("U", 2432), segs("U2", 2432), lambda g, T, B: [g.sync.dma_start(T.U2[:], T.U[:, 0:16 + 2432])])
             refetch("fx4", 4, [0, 1], 1, 2944)
         take("U", BLIM[m], *bl(m), 3 + m, "col%d" % m)
         if m == 2:
@@ -383,147 +420,171 @@ def build():
         elif m < 4:
             place(m, 3 + m)
     elect(6, 2)
+    pool(16 + 2432, [], segs("Z", 2432), lambda g, T, B: [g.iota(T.Z[:], [[0, 16 + 2432]], 0, 0)], name="z0")
     for m in (5, 6):
         targets(m, *opener[m])
-        extend(m, "U2", *opener[m])
-        take("U2", BLIM[m], *bl(m), 3 + m, "col%d" % m)
+        extend(m, "Z", *opener[m])
+    for m in (5, 6):
+        lst, lkey = bl(m)
+        zb, cu, nm = ("zb", m), ("CU", "c%d" % m), "col%d" % m
+        vec(256 * GAM, segs("Z", BLIM[m]) + [lkey, ("pc", 1)], [zb],
+            lambda g, T, B, m=m, lst=lst: [g.vector.tensor_scalar(T.zb[:, (m - 5) * S:(m - 4) * S], T.Z[:, 16:16 + BLIM[m]].indirect(lst(T)), T.pc[:, m - 4:m - 3], None, A.mult)], name=nm)
+        vec(256 * GAM, segs("U", BLIM[m]) + [lkey, zb], [(cu, 0)],
+            lambda g, T, B, m=m, lst=lst: [g.vector.tensor_tensor(T.cur[:], T.U[:, 16:16 + BLIM[m]].indirect(lst(T)), T.zb[:, (m - 5) * S:(m - 4) * S], A.max)], name=nm)
+        copy(256, [(cu, 0)], [("cl", 3 + m)], lambda T, m=m: CL(T, 3 + m), lambda T: T.cur[:], name=nm)
         send("a_c%d" % m, LV[m], lambda T, m=m: CL(T, 3 + m), lambda T, m=m: CL(T, 6 + m), ("cl", 3 + m), ("cl", 6 + m))
-    readout(0, ("G", "E1"), (3, 4))
-    readout(1, ("G", "E3"), (4,))
-    readout(3, ("G", "E4"), ())
+    readout(0, ("H", "gE1"), (3, 4))
+    readout(1, ("H", "gE3"), (4,))
+    readout(3, ("H", "gE4"), ())
     for m, k in ((2, 10), (4, 7), (5, 11), (6, 12)):
-        gather(("G", "R%d" % m), k, F + (m + 1) * S)
-        readout(m, ("G", "R%d" % m), ())
-    for u in sorted(later):
-        mix(u, *later[u])
+        gather(("H", "gR%d" % m), k, F + (m + 1) * S)
+        readout(m, ("H", "gR%d" % m), ())
+    for u in USES:
+        mix(u)
     late(3, [0], 0)
     late(4, [0, 1], 1)
+    for t in tasks:
+        if "lock" in t:
+            t["rd"] = [(t["lock"], 0) if k == ("pb", 0) else k for k in t["rd"]]
+            t["wr"] = [(t["lock"], 0) if k == ("pb", 0) else k for k in t["wr"]]
     return tasks
 
 
-def plan():
+def stage(name):
+    kind, u = name[:-2], name[-2:]
+    if u[0] in "ERF":
+        return {"g": "g", "mx": "a", "da": "a", "abs": "a", "sc": "s", "d": "z", "exp": "z", "K": "K"}.get(kind, "y") + u
+    return {"b": "el", "senda_n": "sn", "senda_c": "col", "tg": "ext"}.get(name[:-1], name[:-1]) + name[-1]
+
+
+def link():
     tasks = build()
-    n = len(tasks)
-    HOP = CFG["hop"]
     lastw, readers, users = {}, {}, {}
     for i, t in enumerate(tasks):
-        raw, oth = set(), set(t["after"])
-        for k in t["rd"]:
-            raw.add(lastw[k])
+        raw = set(t["after"]) | {lastw[k] for k in t["rd"]}
         for k in t["wr"]:
             if k in lastw:
-                oth.add(lastw[k])
-            oth.update(readers.get(k, []))
+                raw.add(lastw[k])
+            raw.update(readers.get(k, []))
         for k in t["rd"]:
             readers.setdefault(k, []).append(i)
         for k in t["wr"]:
             lastw[k] = i
             readers[k] = []
-        oth.discard(i)
-        t["raw"], t["oth"] = raw | oth, set(t.get("follow", []))
+        raw.discard(i)
+        t["dep"], t["stage"] = sorted(raw), stage(t["name"])
+        t["pre"] = sorted(raw | set(t.get("follow", [])))
         t["syms"] = sorted({k[0] for k in t["rd"] + t["wr"] if isinstance(k[0], tuple)}, key=str)
+        t["held"] = sorted({k[0][0] for k in t["rd"] if isinstance(k[0], tuple)})
+        t["succ"] = []
+        for d in t["pre"]:
+            tasks[d]["succ"].append(i)
         for s in t["syms"]:
             users.setdefault(s, []).append(i)
-    succ = [[] for _ in range(n)]
-    for i, t in enumerate(tasks):
-        for d in t["raw"] | t["oth"]:
-            succ[d].append(i)
-    pr = [0.0] * n
-    for i in range(n - 1, -1, -1):
-        t = tasks[i]
-        pr[i] = t["dur"] + t["lat"] + t["bw"] + HOP + max([pr[j] for j in succ[i]] + [0.0])
-    for i, t in enumerate(tasks):
-        pr[i] = 1000.0 - i if t["name"] == "ld" else CFG["alpha"] * pr[i] + CFG["bias"].get(t["name"], 0.0)
-    end = [None] * n
-    free = {"v": 0.0, "s": 0.0, "t": 0.0, "p": 0.0, "y": 0.0, None: 0.0, "dma": 0.0}
-    tenant = {p: [None] * c for p, c in POOLS.items()}
-    slot = {}
-    order = []
-    last = {}
+    for t in reversed(tasks):
+        t["way"] = t["dur"] + t["lat"] + t["bw"] + CFG["hop"] + max([tasks[j]["way"] for j in t["succ"]] + [0.0])
+    return tasks, users
+
+
+def plan(linked=None):
+    tasks, users = linked or link()
+    n, HOP, VF = len(tasks), CFG["hop"], CFG["vf"]
+    bias, hold, shy = CFG["bias"], CFG["hold"], CFG["shy"]
+    pr = [1000.0 - i if t["name"] == "ld" else CFG["alpha"] * t["way"] + sum(hold.get(p, 0.0) for p in t["held"]) + bias.get(t["stage"], 0.0) for i, t in enumerate(tasks)]
+    mark = {t["name"]: i for i, t in enumerate(tasks)}
+    gate = [mark.get(CFG["gate"].get(t["stage"])) for t in tasks]
+    opens = {}
+    left = [len(t["pre"]) for t in tasks]
+    for i, k in enumerate(gate):
+        if k is not None:
+            opens.setdefault(k, []).append(i)
+            left[i] += 1
+    at, end, eng, dur, inn = [None] * n, [None] * n, [t["eng"] for t in tasks], [t["dur"] for t in tasks], [None] * n
+    free = {e: 0.0 for e in ("v", "s", "t", "p", "y", None, "dma")}
+    tenant = {p: [None] * c for p, c in dict(POOLS, PB=1, **CFG["pools"]).items()}
+    slot, before, order, last, joined = {}, {}, [], {}, set()
     busy = {s: [len(v), 0.0] for s, v in users.items()}
-    left = [len(t["raw"] | t["oth"]) for t in tasks]
     ready = [i for i in range(n) if left[i] == 0]
-
-    def lend(s):
-        best = None
-        for c, o in enumerate(tenant[s[0]]):
-            if o is None:
-                at = 0.0
-            elif busy[o][0] == 0:
-                at = busy[o][1] + HOP
-            else:
-                continue
-            if best is None or at < best[0]:
-                best = (at, c)
-        return best
-
     while ready:
-        cand = []
+        cand, lend = [], {}
         for i in ready:
             t = tasks[i]
-            if "in" not in t:
-                t["in"] = max([end[d] + HOP for d in t["raw"]] + [0.0])
-            at = max(free[t["eng"]], t["in"])
-            got, ok = [], True
+            if "piece" in t:
+                front = t["piece"] == 0 or end[i - 1] is not None and eng[i - 1] == "v"
+                back = t["piece"] == 15 or end[i + 1] is not None and eng[i + 1] == "s"
+                if not (front or back):
+                    continue
+            if inn[i] is None:
+                inn[i] = max([end[d] + HOP for d in t["dep"]] + [0.0 if gate[i] is None else at[gate[i]]])
+            a, got = inn[i], []
             for s in t["syms"]:
                 if s not in slot:
-                    b = lend(s)
-                    if b is None:
-                        ok = False
+                    if s[0] not in lend:
+                        lend[s[0]] = min([(0.0 if o is None else busy[o][1] + HOP, c) for c, o in enumerate(tenant[s[0]]) if o is None or busy[o][0] == 0] + [(None,)], key=lambda x: (x[0] is None, x))
+                    b = lend[s[0]]
+                    if b[0] is None:
                         break
-                    at = max(at, b[0])
+                    a = max(a, b[0])
                     got.append((s, b[1]))
-            if ok:
-                cand.append((at, i, got))
+                elif before[s] is not None:
+                    a = max(a, busy[before[s]][1] + HOP)
+            else:
+                if "piece" in t:
+                    if front:
+                        cand.append((max(a, free["v"]), -pr[i], i, got, "v"))
+                    if back:
+                        cand.append((max(a, free["s"]), shy.get(t["name"], 0.0) - pr[i], i, got, "s"))
+                else:
+                    cand.append((max(a, free[eng[i]]), -pr[i], i, got, eng[i]))
         if not cand:
-            raise ValueError("no buffer to lend")
-        t0, first, _ = min(cand, key=lambda c: (c[0], -pr[c[1]]))
-        eng = tasks[first]["eng"]
-        mine = sorted([c for c in cand if tasks[c[1]]["eng"] == eng], key=lambda c: -pr[c[1]])
+            raise ValueError("no buffer to lend: %s %s" % ([(tasks[i]["name"], tasks[i]["syms"]) for i in ready], {p: [o for o in v if o and busy[o][0]] for p, v in tenant.items()}))
+        t0, _, _, _, e = min(cand, key=lambda c: c[:3])
+        mine = sorted([c for c in cand if c[4] == e], key=lambda c: c[1:3])
         now = [c for c in mine if c[0] <= t0 + CFG["slack"]]
         pick = now[0]
         for h in mine:
-            if pr[h[1]] < pr[pick[1]] + CFG["gap"]:
+            if h[1] > pick[1] - CFG["gap"]:
                 break
-            if h[0] + CFG["tol"] < pick[0] + tasks[pick[1]]["dur"] and h[0] <= t0 + CFG["wait"]:
-                fit = [c for c in now if c[0] + tasks[c[1]]["dur"] <= h[0] + CFG["tol"]]
+            if h[0] + CFG["tol"] < pick[0] + dur[pick[2]] and h[0] <= t0 + CFG["wait"]:
+                fit = [c for c in now if c[0] + dur[c[2]] <= h[0] + CFG["tol"]]
                 pick = fit[0] if fit else h
                 break
-        at, i, got = pick
+        a, _, i, got, _ = pick
         t = tasks[i]
         for s, c in got:
-            o = tenant[s[0]][c]
-            if o is not None:
-                t["raw"] = t["raw"] | set(users[o])
+            before[s] = tenant[s[0]][c]
             tenant[s[0]][c] = s
             slot[s] = c
-        if t.get("piece") and last.get(eng) == i - 1:
-            t["joined"] = True
-            t["dur"] -= CFG["vf"]
-        last[eng] = i
-        t["at"] = at
-        if eng:
-            free[eng] = at + t["dur"]
-        done = at + t["dur"]
+        if "piece" in t and last.get(e) == (i - 1 if e == "v" else i + 1) and tasks[last[e]]["name"] == t["name"]:
+            joined.add(i)
+            dur[i] -= VF
+        last[e], eng[i], at[i] = i, e, a
+        done = a + dur[i]
+        if e:
+            free[e] = done
         if t["bw"]:
-            done = max(done + t["lat"] / 2, free["dma"]) + t["bw"]
-            free["dma"] = done
-            done -= t["lat"] / 2
+            free["dma"] = max(done + t["lat"] / 2, free["dma"]) + t["bw"]
+            done = free["dma"] - t["lat"] / 2
         end[i] = done + t["lat"]
-        t["end"] = end[i]
         for s in t["syms"]:
             busy[s][0] -= 1
             busy[s][1] = max(busy[s][1], end[i])
         order.append(i)
         ready.remove(i)
-        for j in succ[i]:
+        for j in t["succ"] + opens.get(i, []):
             left[j] -= 1
             if left[j] == 0:
                 ready.append(j)
-    return tasks, order, slot, max(end)
-
-
-_PLAN = []
+    if len(order) < n:
+        raise ValueError("a gate closes a loop")
+    out = [dict(t, eng=eng[i], at=at[i], end=end[i], dur=dur[i], raw=set(t["dep"])) for i, t in enumerate(tasks)]
+    for i in joined:
+        out[i]["joined"] = True
+    for s, o in before.items():
+        for j in users[s] if o is not None else ():
+            if not any(s in tasks[d]["syms"] for d in tasks[j]["dep"]):
+                out[j]["raw"].update(users[o])
+    return out, order, slot, max(end)
 
 
 def rank_program(g, core, T, topo):
@@ -539,58 +600,49 @@ def rank_program(g, core, T, topo):
     def B(s):
         return T[s[0] + str(slot[s])]
 
-    def width(l):
-        return len(topo.engines(cores[(rank - l) % len(cores)], core))
-
     needed = set()
     for i in order:
-        t = tasks[i]
-        t["w"] = sorted(t["raw"])
-        if t["eng"]:
-            needed.update(t["w"])
+        if tasks[i]["eng"]:
+            needed.update(tasks[i]["raw"])
     count, sig, seen = {}, {}, {q: {} for q in Q}
     for i in order:
         t = tasks[i]
-        e = t["eng"]
+        e, sem = t["eng"], t["sem"]
         if t.get("joined"):
             continue
-        if "piece" in t:
-            n = 1
-            while i + n < len(tasks) and tasks[i + n].get("joined"):
-                n += 1
-            for sm, val in sorted(sig[d] for d in t["w"]):
-                if seen[e].get(sm, 0) < val:
-                    Q[e].wait_ge(T.sem[sm], val)
-                    seen[e][sm] = val
-            t["fn"](g, T, B, n=n)[0].then_inc(T.sem[e], 1)
-            count[e] = count.get(e, 0) + 1
-            for k in range(n):
-                sig[i + k] = (e, count[e])
-            continue
         if e is None:
-            sig[i] = (t["sem"], width(LV[int(t["sem"][-1])]))
-            count[t["sem"]] = sig[i][1]
+            count[sem] = len(topo.engines(cores[(rank - LV[int(sem[-1])]) % len(cores)], core))
+            sig[i] = (sem, count[sem])
             continue
         want = {}
-        for d in t["w"]:
+        for d in t["raw"]:
             sm, val = sig[d]
             want[sm] = max(want.get(sm, 0), val)
         for sm in sorted(want):
             if seen[e].get(sm, 0) < want[sm]:
                 Q[e].wait_ge(T.sem[sm], want[sm])
                 seen[e][sm] = want[sm]
+        if "piece" in t:
+            n, step = 1, 1 if e == "v" else -1
+            while tasks[i + n * step].get("joined") and tasks[i + n * step]["eng"] == e:
+                n += 1
+            t["fn"](g, T, B, e, min(t["piece"], t["piece"] + (n - 1) * step), n)[0].then_inc(T.sem[e], 1)
+            count[e] = count.get(e, 0) + 1
+            for k in range(n):
+                sig[i + k * step] = (e, count[e])
+            continue
         ins = t["fn"](g, T, B)
-        if t["sem"] == "sent":
-            _, dst, src, sm, l = ins[0]
+        if sem == "sent":
+            dst, src, sm, l = ins[0]
             to = cores[(rank + l) % len(cores)]
             rid, pid, _ = topo.addr(to)
             g.remote_dma(dst, src, T.sem[sm], T.sem.sent, pid, rid, topo.mask(core, to))
             count["sent"] = count.get("sent", 0) + len(topo.engines(core, to))
-        elif t["sem"]:
+        elif sem:
             for x in ins:
-                x.then_inc(T.sem[t["sem"]], 16)
-            count[t["sem"]] = count.get(t["sem"], 0) + 16 * len(ins)
-            sig[i] = (t["sem"], count[t["sem"]])
+                x.then_inc(T.sem[sem], 16)
+            count[sem] = count.get(sem, 0) + 16 * len(ins)
+            sig[i] = (sem, count[sem])
         elif i in needed:
             ins[-1].then_inc(T.sem[e], 1)
             count[e] = count.get(e, 0) + 1
@@ -598,3 +650,6 @@ def rank_program(g, core, T, topo):
     for sm in sorted(count):
         if max(seen[q].get(sm, 0) for q in Q) < count[sm]:
             g.sync.wait_ge(T.sem[sm], count[sm])
+
+
+_PLAN = []

@@ -1,4 +1,5 @@
 import math
+from concourse.bass import DstId, RemoteDMATransfer
 from concourse.mybir import AluOpType, ActivationFunctionType
 
 A = AluOpType
@@ -9,77 +10,101 @@ TS = ((0,), (1,), (0, 1), (2,), (3,), (2, 3), (0, 1, 2, 3))
 BLIM = (1664, 1920, 1664, 2176, 2688, 2432, 1664)
 ALIM = (1664, 1664, 1664, 1920, 2176, 1664, 1664)
 KIDS = {2: (0, 1), 5: (3, 4), 6: (2, 5)}
-BIG = 3.0e7
+PAIR = {1: 6, 4: 5}
+OFF = {0: 0, 2: 32, 6: 64, 1: 65, 3: 96, 5: 128, 4: 129}
+UB = 16 + 2432
+BASE = {"Z": 0, "U": UB}
+BIG = 2.0 ** 25
 USES = ["E%d" % _k for _k in range(7)] + ["R%d" % _k for _k in range(7)]
-CFG = dict(gam=1.5, sca=3.5, cy=0.001, pc=0.0005, vf=0.06, sf=0.07, hop=0.12, acc=3.6,
-           slack=0.05, gap=8.0, tol=0.05, wait=0.3, alpha=1.0, shy={}, gate={}, bias={}, hold=dict(PD=40.0, EL=30.0, Q=40.0),
-           vmax=dict(R4=4, R5=4, R6=4), factor=("R4", "R5", "R6"),
-           total=dict({_u: "dma" for _u in USES}, R4="pe", R5="h1", R6="vec"),
-           pools=dict(H=5, MX=4, D=22, PD=3, Q=1), gp=False)
-CFG.update({'gp':True,'bias':{'col5':64,'yE5':116,'sE4':76,'yF4':-45,'zF4':4,'aE0':30,'zE5':-67,'sE0':13,'aR2':-1,'pl0':1,'gE5':20,'sn5':51,'sE2':59,'col4':75,'ext0':27,'ext6':7,'zF3':136,'aE2':-25,'ext5':-3,'pl3':20,'gF3':-30,'sn0':131,'el4':12,'ext1':-3,'col6':-4,'aR0':-6,'KE6':-160,'KE5':36,'zE6':-25,'x':6,'gE6':3,'c2':-92,'yR5':26,'yE2':77,'zR5':-11,'pl1':30,'aR6':15,'aR3':46,'x4':-29,'c0':84,'yF3':-27,'gE4':8,'n1':28,'el3':18,'zR6':-52,'zR4':-2,'aE1':1,'yR6':62,'gE3':10,'ext3':27,'ext2':-4,'c':22,'el1':-24,'col2':-26,'zE4':-7,'nm0':27,'yR3':-112,'aR4':131,'zR2':-6,'n5':-4,'sn3':51,'sn6':-5,'aR5':-1,'yE6':-9,'sn2':20,'yR2':35,'gF4':-5,'z0':11,'cv':61,'yE4':-14,'yE3':-1,'aE3':53,'sE3':-16,'sE6':-94,'n4':107,'yR1':-21,'sn1':-6,'gR5':104,'yR4':20,'zR0':14,'el0':-12,'sn4':-6,'col0':56,'el6':35,'gR6':-62,'nm1':-46,'pl2':17,'yR0':-43,'zE3':19,'n6':-10,'aE4':77,'n2':154,'c1':24,'col3':62,'KE2':-1,'gR2':-2,'n3':5,'gR4':-33,'el5':-36,'col1':-10,'gE0':5,'zE1':-11,'zE0':78,'yE1':23,'aE5':6,'n0':-51,'zR3':31,'yE0':-22,'zE2':-23,'aR1':-9,'gE1':55,'el2':-2,'sE1':-17,'aF4':44,'sE5':5,'aE6':70,'gE2':-3},'hold':{'PD':15,'EL':33,'Q':39,'MX':-7,'PB':28,'TG':8,'D':4,'CU':3},'gate':{'zR2':'expR0','zF3':'expE3','gF4':'expE0','zR5':'b5','gE5':'col1','zR3':'scE6','aR2':'b0','KE6':'col1','yR4':'expE0','aR5':'gR4','zF4':'col0','n6':'b5','zE6':'col2','aR4':'gE0','aE5':'expR1','yR1':'col0','sE4':'col1','gR5':'gE6','col5':'b4','sE3':'gE0','nm1':'b0','aF4':'b3','zE3':'gE5','n4':'expE0','yE4':'scE0','zR4':'b0','n2':'gE6','col6':'scE2','el4':'b3','aE4':'col2','aE6':'b2','n5':'col3'},'vmax':{'R4':1,'R5':3,'R3':4,'E1':4,'R2':4},'total':{'E0':'h3','E1':'dma','E2':'dma','E3':'dma','E4':'h3','E5':'h3','E6':'pe','R0':'dma','R1':'dma','R2':'dma','R3':'h3','R4':'h3','R5':'h1','R6':'vec'},'factor':('R2','R3'),'shy':{'gR6':3,'gE4':51,'gR5':149,'gE6':77,'gE3':64,'gE0':-79,'gR2':79,'gR4':18,'gE5':-20,'gE1':-4,'gE2':16},'pools':{'H':4,'MX':8,'D':22,'PD':3,'Q':1},'gap':15,'wait':0.3,'slack':0.05,'tol':0.2,'alpha':1.0})
+COST = dict(gam=1.5, sca=3.5, cy=0.001, pc=0.0005, vf=0.05, sf=0.065, hop=0.22, issue=0.9, lat=1.8, bw=1.3, send=1.2, hw=0.3, pf=1.05)
+CFG = dict(slack=0.05, gap=5.0, tol=0.2, wait=0.3, alpha=0.02, shy={}, gate={}, hold={},
+           order="c x c0 fE0 gE0 aE0 sE0 el0 z0 cv nm ext0 sn0 col0 c1 fx fE1 hb gE1 aE1 sE1 el1 sn1 ext6 ext1 col1 pl0 n0 sE2 el2 fE3 ext2 col2 sn2 pl1 n1 pl2 n2 "
+                 "gE3 aE3 sE3 el3 sn3 ext3 col3 pl3 n3 fE4 xb xc lt x4 sE6 el6 sn6 sE5 el5 sn5 sE4 el4 sn4 n4 ext5 ext4 col4 col5 col6 n5 n6 "
+                 "yE0 zE0 gE2 aE2 yE2 zE2 yE1 KE2 zE1 fR0 yR0 zR0 aR0 yE3 zE3 fR1 yR1 zR1 aR1 yE6 zE6 aE6 gE6 aE4 gE4 yE5 zE5 aE5 gE5 yE4 KE5 KE6 zE4 fR3 yR3 zR3 aR3 "
+                 "gF3 gF4 yF3 yF4 aF3 aF4 zF3 zF4 fR2 yR2 zR2 aR2 gR2 fR4 yR4 zR4 aR4 gR4 fR5 yR5 zR5 aR5 gR5 fR6 yR6 zR6 aR6 gR6",
+           route=dict(E0="T", E1="T", E2="A", E3="T", E4="T", E5="A", E6="A", R0="N", R1="N", R2="N", R3="N", R4="N", R5="T", R6="T"),
+           factor=("R2", "R3"), total={_u: "dma" for _u in USES}, spread={0: "v"}, split={}, names=(), keep=(), wide=(), beta=1.0, lift={}, stick=0.0, turn={},
+           pools=dict(H=4, MX=2, X=3, D=8, Y=2))
+CFG.update({'order':'c0 aE3 cv sn0 el0 el1 z0 gE1 el2 n0 nm x aE0 c1 sE0 gE0 el4 aE1 ext0 c sE1 zE0 fE3 ext6 sn1 sE2 fE4 ext1 pl0 col2 ext2 sn2 col1 hb n1 fE0 n3 col3 fE1 ext5 gE3 pl1 sE3 ext3 x4 col0 n2 el3 pl2 aE2 xc lt sn6 fx zR0 el6 el5 zE2 yR0 sE6 sE5 zE3 col6 zE1 n5 gE2 sn4 aR0 yR1 aR3 aE4 sn5 fR1 KE2 sE4 ext4 xb aE6 aE5 yE1 gR4 KE6 zE4 gE5 fR4 gE6 yE2 col4 zF4 yR2 aF3 zR6 n6 fR3 fR0 gF4 gE4 aF4 yR4 fR5 col5 fR2 fR6 gF3 zR1 zR5 yR5 zE6 yF3 zR2 zF3 yE6 aR6 yE4 aR1 aR4 zE5 zR3 aR2 yE5 sn3 aR5 yR3 KE5 zR4 gR2 yE0 gR5 yR6 yF4 pl3 gR6 n4 yE3','hold':{'H':2,'EL':-1,'Q':1,'PB':-16,'D':-3},'gate':{},'shy':{'gR4':126,'gR5':145,'gE4':-12},'route':{'E0':'A','E1':'N','E2':'A','E3':'N','E4':'A','E5':'A','E6':'A','R0':'A','R1':'N','R2':'N','R3':'N','R4':'N','R5':'N','R6':'T'},'total':{'E0':'dma','E1':'h3','E2':'dma','E3':'dma','E4':'dma','E5':'h3','E6':'dma','R0':'dma','R1':'dma','R2':'dma','R3':'dma','R4':'h2','R5':'vec','R6':'dma'},'factor':('R1','R4','R5'),'spread':{'R44':'v'},'split':{'R6':2},'gap':10,'wait':0.15,'tol':0.3,'slack':0.05,'alpha':0.1})
+CFG.update({'order':'zE4 cv n0 sE2 sn0 gE1 c0 zE0 aE3 el0 x c aE0 nm gE0 fE1 sE0 sE1 zE3 ext0 sE5 el2 pl0 ext6 el1 z0 fE3 el4 sn1 aE1 ext1 n3 ext2 fE0 fx hb yR0 ext5 yR1 xc col3 pl2 fE4 col1 n1 c1 sE3 el3 n2 sn2 x4 lt zE1 gE3 ext3 col0 n5 el5 zE2 aE2 zR0 n6 sE4 sE6 aR3 sn6 fR5 sn4 col2 el6 yR4 fR1 col6 aR0 aF3 ext4 aE4 gE2 yR2 fR3 aF4 pl1 KE2 zR6 yE1 gR4 gF3 aE5 xb yF3 sn5 gE6 fR4 gE5 fR0 zR1 col4 yE2 fR2 aE6 yR5 gE4 yE6 KE6 zF3 zE6 aR4 yE4 zR2 aR1 yE5 zE5 aR5 aR6 yR3 zF4 aR2 gF4 zR5 zR3 pl3 zR4 n4 KE5 gR5 yR6 col5 yE0 fR6 yE3 sn3 yF4 gR6 gR2','hold':{'H':2,'PB':-28,'D':-3,'TG':-9,'MX':-2},'gate':{},'shy':{'gR4':95,'gR6':-14,'gE6':-31},'route':{'E0':'A','E1':'N','E2':'A','E3':'N','E4':'A','E5':'A','E6':'A','R0':'A','R1':'N','R2':'N','R3':'N','R4':'N','R5':'N','R6':'T'},'total':{'E0':'dma','E1':'h3','E2':'dma','E3':'h2','E4':'dma','E5':'h3','E6':'dma','R0':'dma','R1':'dma','R2':'dma','R3':'dma','R4':'vec','R5':'vec','R6':'dma'},'factor':('E1','R1','R5'),'spread':{'R44':'v','R11':'v'},'split':{'R6':2},'gap':10,'wait':0.15,'tol':0.3,'slack':0.05,'alpha':0.1})
+CFG.update({'order':'sE1 el0 n0 aE0 aE3 el1 zE0 el2 xc sE5 pl2 cv fE1 fE0 n1 el4 zE3 sE2 sn0 c0 fx pl0 x gE1 zE4 ext0 c nm gE0 aE1 sn1 ext6 col3 c1 fE4 z0 el3 fE3 ext1 ext5 sE0 yR1 sE3 ext2 col1 n3 n2 hb sn2 x4 sE4 yR0 lt col0 gE3 el5 ext3 n5 zR0 el6 aR3 yR4 zE1 fR3 aE2 xb fR5 col6 ext4 aF3 sn6 aE4 n6 sE6 fR1 zE2 sn4 aR0 col2 aR1 KE2 gE2 yR2 zR6 yE1 aE5 gR4 aF4 fR4 yR5 gE4 fR2 pl1 zR1 sn5 gE6 yE5 fR0 aE6 zR5 zE6 yE4 zF3 yR3 zR4 col4 aR6 fR6 gE5 gF3 aR2 gF4 aR4 KE6 aR5 zR3 pl3 yE2 col5 sn3 zE5 yF3 yR6 yF4 yE6 zR2 gR5 zF4 gR2 n4 KE5 gR6 yE0 yE3','lift':{},'beta':1.0,'hold':{'PB':-21,'D':-8,'MX':3,'Y':-8},'gate':{'gF4':'col5'},'shy':{'gR4':123,'gE6':-25,'gR2':60,'gE5':-24,'gE4':15,'gR5':23},'route':'ANANAAAANNNNNT','total':'fold dma fold fold fold fold fold fold fold fold fold vec vec fold','factor':('E1','R1','R3','R5'),'names':(),'keep':(),'wide':('E2',),'spread':{'R44':'v','R11':'v'},'split':{'R6':2},'gap':20,'wait':0.15,'tol':0.3,'slack':0.05,'alpha':0.1})
+CFG.update({'turn':{'H':'gE0 gE2 gE6 gE1 gE3 gE5 gE4 gR2 gR4 gR6 gR5','MX':'E0 E1 R0 E3 R1 R3 R2 E4 R6 R4 R5','X':'E0 E1 E3 R0 R1 E4 R3 R2 R4 R5 R6'},'stick':0,'order':'el2 ext1 sn0 c ld z0 fE3 nm el0 fR0 x cv x4 c1 ext6 n1 ext0 gE0 n0 c0 fE0 aE0 lt sE1 el1 n3 pl0 col0 sn2 sE3 aE1 pl1 fR1 sE0 fE1 sn1 aE2 fE4 col1 ext5 n2 col3 gE2 sE2 gE1 zE0 col2 yE0 el3 ext2 gE6 col6 sn6 sE5 zR0 gE3 ext3 pl2 zE3 aE3 fR2 aR0 ext4 pl3 sn3 zE2 gE4 n6 el5 el6 fR3 el4 yF4 sE6 zE1 col4 sn4 aE6 gR4 n4 fR4 aF3 yE2 zE5 gE5 sn5 col5 aF4 gF4 n5 fR5 aE5 aE4 sE4 zE6 KE2 gF3 aR3 aR4 aR1 yR0 zR1 yE1 fR6 yE3 zE4 zR3 yR5 yR1 yR3 zF3 gR2 aR2 yE4 gR6 yF3 zR5 KE6 zR2 zR4 yR4 zR6 aR5 aR6 KE5 yE5 gR5 yE6 yR2 yR6 zF4','lift':{},'beta':1.0,'hold':{'PD':22,'CP':-3,'PB':8,'CU':2,'EL':-7,'H':2},'gate':{'el2':'gE1'},'shy':{'gR4':129,'gE6':-37,'gE3':10,'gR5':-28,'gE4':24},'route':'ANANAAAANNNANT','total':'dma h3 dma h2 dma h2 dma dma dma dma dma vec vec pe','factor':('E1','R1','R5'),'names':('E0','E1','E2','E6'),'keep':('R4','R5','R6'),'wide':('E0','E2','E4','E6'),'spread':{},'split':{},'gap':5,'wait':0.15,'tol':0.3,'slack':0.05,'alpha':0.4})
+CFG.update({'turn':{'H':'gE0 gE2 gE6 gE1 gE3 gE5 gR2 gE4 gR4 gR6 gR5','MX':'E1 E3 R0 E0 E4 R1 R3 R2 R5 R6 R4','X':'R0 E3 E1 R1 R3 E0 R4 E4 R2 R6 R5'},'stick':10,'order':'x c n0 pl1 gE3 c0 z0 col1 k1 gE0 cv c1 fE0 aE0 sn0 ext0 fR0 sE0 x4 f0 nm ld fE1 gE2 k2 el0 ext1 col0 gE1 sE2 aE1 sn1 gE6 zE2 nn el2 sE1 fE3 fE4 sE6 aE2 lt pl0 el1 sn2 zE1 n6 gE4 ext2 aE6 aE3 n1 sE3 zE0 el6 n2 ext3 col4 col2 ext5 el3 col3 fR3 aE4 sE4 zE3 gE5 zE4 sn3 fR2 sn6 n3 ext4 aR0 fR6 gF4 fR1 sE5 el4 el5 pl2 zR1 zE6 sn4 aE5 yE1 aR1 gR2 yE2 n5 aF3 gF3 aR3 n4 yE0 col6 sn5 fR4 yE4 col5 gR4 zE5 zR0 fR5 aR2 yF3 zF3 pl3 yE6 KE5 yE3 yR0 yF4 yR5 yR2 zR3 zR5 aR5 aR6 gR5 KE2 zR4 aR4 yE5 zR2 gR6 yR1 KE6 aF4 yR3 yR4 yR6 zR6 zF4','lift':{},'beta':1.0,'hold':{'PD':24,'PB':34,'EL':15},'gate':{},'shy':{'gR4':154,'gR2':29},'route':'ANANAAAANNNANT','total':'dma h3 dma h2 dma h2 dma dma h3 dma dma vec vec dma','factor':('E1','R1','R5'),'names':('E0','E1','E2'),'keep':('R6',),'wide':('E2','E4','E6'),'spread':{},'split':{},'gap':5,'wait':0.15,'tol':0.3,'slack':0.05,'alpha':0.4})
+CFG.update({'turn':{'H':'gE0 gE6 gE2 gE1 gE3 gE5 gE4 gR2 gR4 gR6 gR5','MX':'E1 E0 R0 E3 R1 E4 R3 R2 R4 R5 R6','X':'E1 E0 E3 E4 R1 R0 R3 R2 R6 R4 R5'},'stick':0,'order':'n0 x nn ext1 col0 ld pl1 ext0 z0 c0 pl0 c1 nm sn0 cv el0 sE0 gE0 x4 sE2 aE0 c k2 fE0 col1 k1 gE2 aE2 f0 fE3 fE1 lt el1 col4 gE1 n1 sn1 ext2 sn2 sn6 el6 aE1 gE6 fR1 pl2 sE1 col2 sn3 ext3 el3 sE6 zE2 sE3 ext5 gE3 n2 fR0 zE0 n3 fE4 ext4 col3 zF4 sn4 gF4 yE0 el2 yE1 gE4 yE3 n6 sE4 el4 col5 zE1 aE6 zE6 aE3 n4 col6 fR4 el5 yF3 gE5 aR0 zE3 aE4 aR1 yE4 pl3 n5 sE5 yE2 gF3 zE5 fR3 zR0 sn5 gR2 aE5 zR1 yE6 fR2 yE5 yR5 gR6 aR3 gR4 fR5 zE4 aR2 zR3 KE2 yR2 yR0 yR1 aF3 yR3 KE6 aR5 gR5 zR2 zF3 KE5 yF4 zR4 zR6 aR6 yR4 fR6 yR6 aR4 zR5 aF4','lift':{},'beta':1.0,'hold':{'PD':33,'EL':19,'PB':6,'FA':-9,'CP':7,'TG':-1},'gate':{'n0':'expE2'},'shy':{'gR6':60,'gE4':-28,'gE3':8},'route':'ATATTAAANNNANT','total':'dma dma dma h3 dma dma dma h3 dma dma dma vec vec dma','factor':('R1','R3','R5'),'names':('E0','E1'),'keep':('R6',),'wide':('E2','E6'),'spread':{},'split':{},'gap':5,'wait':0.15,'tol':0.3,'slack':0.05,'alpha':0.4})
+CFG.update(route=dict(zip(USES, CFG["route"])), total=dict(zip(USES, CFG["total"].split())))
 
 SCRATCH = {
-    "P": ("sbuf", [128, W], "int32"), "U": ("sbuf", [128, 16 + 2688], "int32"), "Z": ("sbuf", [128, 16 + 2432], "int32"),
-    "zb": ("sbuf", [128, 512], "float32"),
-    "x16": ("sbuf", [128, 1024], "float16"), "x4": ("sbuf", [128, 512], "float16"),
+    "P": ("sbuf", [128, W], "int32"), "U": ("sbuf", [128, UB + 16 + 2688], "int32"),
+    "zb": ("sbuf", [128, 512], "float32"), "XE": ("sbuf", [128, 11 * S], "float16"), "x4": ("sbuf", [128, 512], "float16"),
     "st32": ("sbuf", [128, 48], "int32"), "stu": ("sbuf", [128, 48], "uint16"),
-    "hb": ("sbuf", [128, 16], "bfloat16"), "lam": ("sbuf", [128, 16], "float32"),
-    "cl": ("sbuf", [128, 13 * 256], "uint16"), "b16": ("sbuf", [128, 112], "uint16"), "off": ("sbuf", [128, 7 * 32], "uint16"),
+    "hb": ("sbuf", [128, 16], "bfloat16"), "lam": ("sbuf", [128, 32], "float32"), "LP": ("sbuf", [128, 32], "float16"), "LT": ("sbuf", [128, 128], "float16"),
+    "Sel": ("sbuf", [128, 512], "bfloat16"), "Bs": ("sbuf", [128, 32], "float32"),
+    "cl": ("sbuf", [128, 13 * S], "uint16"), "b16": ("sbuf", [128, 112], "uint16"), "off": ("sbuf", [128, 7 * 32], "uint16"),
     "fx32": ("sbuf", [128, 48], "int32"), "fxu": ("sbuf", [128, 48], "uint16"), "Gf": ("sbuf", [128, 768], "float16"),
-    "C0": ("sbuf", [128, 256], "float16"), "C1": ("sbuf", [128, 256], "float16"),
-    "n16": ("sbuf", [128, 1792], "float16"), "pb": ("sbuf", [128, 256], "float16"),
-    "snd": ("sbuf", [128, 768], "int32"), "cur": ("sbuf", [128, 256], "int32"), "NM": ("sbuf", [128, 1792], "float32"),
+    "C0": ("sbuf", [128, S], "float16"), "C1": ("sbuf", [128, S], "float16"), "pb": ("sbuf", [128, S], "float16"),
+    "snd": ("sbuf", [128, 768], "int32"), "cur": ("sbuf", [128, S], "int32"), "cur2": ("sbuf", [128, 16, 32], "int32"), "cur3": ("sbuf", [128, 2 * S], "int32"), "NM": ("sbuf", [128, 1792], "int32"), "NN": ("sbuf", [128, S], "int32"),
     "e1": ("sbuf", [128, 272], "float32"), "e2": ("sbuf", [128, 272], "float32"), "e3": ("sbuf", [128, 272], "float32"),
-    "Wm": ("sbuf", [128, 256], "float16"), "a16": ("sbuf", [128, 16], "float16"),
-    "f1": ("sbuf", [128, 256], "float32"), "f2": ("sbuf", [128, 256], "float32"), "f3": ("sbuf", [128, 256], "float32"),
-    "d0c": ("sbuf", [128, 272], "float32"), "Tc": ("sbuf", [128, 256], "float32"), "Mk": ("sbuf", [128, 256], "float32"),
+    "Wm": ("sbuf", [128, S], "float16"), "a16": ("sbuf", [128, 32], "float16"), "Tb": ("sbuf", [128, 2 * S], "bfloat16"),
+    "f1": ("sbuf", [128, 2 * S], "float32"), "f2": ("sbuf", [128, 3 * S], "float16"), "f3": ("sbuf", [128, 2 * S], "float32"),
+    "h1": ("sbuf", [128, 3 * S], "float16"), "h3": ("sbuf", [128, 3 * S], "float16"),
+    "d0c": ("sbuf", [128, 272], "float32"), "Mk": ("sbuf", [128, S], "float32"),
     "wl32": ("sbuf", [128, 16], "int32"), "wl": ("sbuf", [128, 16], "uint16"),
     "ip": ("sbuf", [128, 8], "int32"), "pc": ("sbuf", [128, 4], "float32"),
-    "ones": ("sbuf", [128, 144], "bfloat16"), "BD": ("sbuf", [128, 128], "bfloat16"), "Cv": ("sbuf", [128, 1920], "bfloat16"),
+    "ones": ("sbuf", [128, 144], "bfloat16"), "Cv": ("sbuf", [128, 1920], "bfloat16"),
     "dg": ("sbuf", [128, 8 * 128], "bfloat16"), "I32": ("sbuf", [128, 128], "float32"), "FE": ("sbuf", [128, 768], "float32"),
     "GI": ("sbuf", [128, 32], "bfloat16"), "GI32": ("sbuf", [128, 8], "float32"), "Dm": ("sbuf", [128, 136], "bfloat16"),
-    "YM": ("sbuf", [128, 1792], "float32"), "YZ": ("sbuf", [128, 1792], "float32"),
-    "IH": ("sbuf", [128, 128], "float32"), "FA0": ("sbuf", [128, 256], "float32"), "FA1": ("sbuf", [128, 256], "float32"),
-    "B4": ("psum", [128, 512], "float32"),
+    "YM": ("sbuf", [128, 1792], "float32"),
+    "IH": ("sbuf", [128, 128], "float32"), "FA0": ("sbuf", [128, S], "float32"), "FA1": ("sbuf", [128, S], "float32"),
+    "Bg": ("sbuf", [128, 16], "bfloat16"), "PS": ("psum", [128, 8 * 512], "float32"),
 }
-TILES = {"H": ("sbuf", [128, 4096], "float16"), "MX": ("sbuf", [128, 1024], "float16"), "D": ("sbuf", [128, 1024], "float32"),
-         "PD": ("psum", [128, 1024], "float32"), "Q": ("psum", [128, 512], "float32")}
+TILES = {"H": ("sbuf", [128, 4096 + 2 * S], "float16"), "MX": ("sbuf", [128, 4096], "float16"), "X": ("sbuf", [128, 2048], "float16"),
+         "D": ("sbuf", [128, 2048], "float32"), "Y": ("sbuf", [128, S], "float32")}
 SCRATCH.update({_p + str(_k): TILES[_p] for _p in TILES for _k in range(CFG["pools"][_p])})
-POOLS = {"EL": 1, "TG": 1, "CU": 1, "C": 2, "FA": 2}
-DMAS = ["nm0", "nm1", "l_st", "l_su0", "l_su1", "l_th0", "l_th1", "l_xs", "l_hv", "fx3", "fx4", "out", "hF3", "hF4", "oR0", "oR1"]
+LEND = {_p: [((_p, _k),) for _k in range(_n)] for _p, _n in dict(CFG["pools"], EL=1, TG=1, CU=1, CP=1, C=2, FA=2, PB=1).items()}
+LEND.update(PD=[(("PS", _k), ("PS", _k + 1)) for _k in (0, 2, 4, 6)], Q=[(("PS", _k),) for _k in (7, 6, 5, 4, 3, 2, 1, 0)])
+DMAS = ["cv", "nm0", "nm1", "l_st", "l_su0", "l_su1", "l_th0", "l_th1", "l_xs", "l_hv", "fx3", "fx4", "out", "hF3", "hF4", "oR0", "oR1"]
 ARR = ["a_n2", "a_c2", "a_n5", "a_c5", "a_n6", "a_c6"]
 SEMAPHORES = ["v", "s", "t", "p", "sent"] + DMAS + ARR + [_c + _u for _u in USES for _c in "hky"]
 I1, I2, I4, I34, IQ, IM = 0, 1, 2, 3, 4, 7
 
 
+def span(t, e, C, joined=False):
+    if t["sem"] and e:
+        return t["calls"] * (C["send"] if t["sem"] == "sent" or "fold" in t else C["issue"] if e == "p" else C["hw"])
+    if e == "t":
+        return 0.03 + t["n"] * C["pc"]
+    if e == "p":
+        return (170 * t["calls"] + 2 * t["n"]) * C["cy"] * C["pf"]
+    if e is None:
+        return 0.0
+    n = t["n"] + t["gn"] * C["gam"] + t["sn"] * C["sca"]
+    return (0 if joined else t["calls"]) * C[e + "f"] + (n if e == "s" or t["sn"] else max(n, 64 * t["calls"])) * C["cy"]
+
+
 def build():
     tasks, part = [], ["c"]
-    GAM, CY, PC, VF, SF = CFG["gam"], CFG["cy"], CFG["pc"], CFG["vf"], CFG["sf"]
-    MISC = "PD" if CFG["pools"]["Q"] < 2 else "Q"
 
-    def add(eng, dur, rd, wr, fn, sem=None, lat=0.0, bw=0.0, after=(), name="", **kw):
-        tasks.append(dict(eng=eng, dur=dur, rd=list(rd), wr=list(wr), fn=fn, sem=sem, lat=lat, bw=bw, after=list(after), name=name or part[0], **kw))
+    def add(eng, rd, wr, fn, n=0, gn=0, sn=0, calls=1, sem=None, lat=0.0, bw=0.0, after=(), name="", **kw):
+        tasks.append(dict(eng=eng, n=n, gn=gn, sn=sn, calls=calls, rd=list(rd), wr=list(wr), fn=fn, sem=sem, lat=lat, bw=bw, after=list(after), name=name or part[0], **kw))
         return len(tasks) - 1
 
-    def vec(n, rd, wr, fn, calls=1, **kw):
-        return add("v", calls * VF + max(n, 64 * calls) * CY, rd, wr, fn, **kw)
+    def vec(n, rd, wr, fn, **kw):
+        return add("v", rd, wr, fn, n=n, **kw)
 
-    def act(n, rd, wr, fn, calls=1, **kw):
-        return add("s", calls * SF + n * CY, rd, wr, fn, **kw)
+    def act(n, rd, wr, fn, **kw):
+        return add("s", rd, wr, fn, n=n, **kw)
 
     def pe(n, rd, wr, fn, **kw):
-        return add("t", 0.03 + n * PC, rd, wr, fn, **kw)
+        return add("t", rd, wr, fn, n=n, **kw)
 
-    def pool(n, rd, wr, fn, calls=1, **kw):
-        return add("p", (170 * calls + 2 * n) * CY, rd, wr, fn, **kw)
+    def pool(n, rd, wr, fn, **kw):
+        return add("p", rd, wr, fn, n=n, **kw)
 
     def dma(q, sem, bw, rd, wr, fn, n=1, **kw):
-        return add(q, (0.9 if q == "p" else 0.08) * n, rd, wr, fn, sem=sem, lat=1.8, bw=bw, **kw)
+        return add(q, rd, wr, fn, calls=n, sem=sem, lat=1.0, bw=bw, **kw)
 
     def copy(n, rd, wr, out, src, **kw):
-        if CFG["gp"]:
-            return pool(n, rd, wr, lambda g, T, B: [g.affine_select(out(T), src(T), [[0, n]], A.is_gt, 0.0, 1, 0)], **kw)
-        return vec(n, rd, wr, lambda g, T, B: [g.vector.tensor_copy(out(T), src(T))], **kw)
+        return pool(n, rd, wr, lambda g, T, B: [g.affine_select(out(T), src(T), [[0, n]], A.is_gt, 0.0, 1, 0)], **kw)
 
     def segs(t, lim):
         return [(t, "o0"), (t, "o1")] + [(t, k) for k in range((lim - F) // S)]
@@ -87,318 +112,441 @@ def build():
     def DG(T, k):
         return T.dg[:, k * 128:k * 128 + 128]
 
+    def PS(T, B, s, a, b, step=1, rows=128):
+        return T.PS[0:rows, B(s) + a:B(s) + b:step]
+
+    def XN(T, k, a=0, b=S):
+        return T.XE[:, k * S + a:k * S + b]
+
+    def SL(buf, i, a=0, b=S, kept=False):
+        return buf[:, 4096 + i * S + a:4096 + i * S + b] if kept and i < 2 else buf[:, 16 * a + i:16 * b:16]
+
+    def TB(T, tab, a, b):
+        return T.U[:, BASE[tab] + 16 + a:BASE[tab] + 16 + b]
+
     H = F // 2
     dma("y", "l_st", 0.05, [], [("st32", 0)], lambda g, T, B: [g.sync.dma_start(T.st32[:], T.st[:])], name="ld")
     dma("s", "l_hv", 0.05, [], [("hb", 0)], lambda g, T, B: [g.scalar.dma_start(T.hb[:], T.hv[:])], name="ld")
-    dma("s", "l_su1", 0.7, [], [("U", "o1")], lambda g, T, B: [g.scalar.dma_start(T.U[:, 16 + H:16 + F], T.su[:, H:F])], name="ld")
-    dma("y", "l_su0", 0.7, [], [("U", "o0")], lambda g, T, B: [g.sync.dma_start(T.U[:, 16:16 + H], T.su[:, 0:H])], name="ld")
+    dma("s", "l_su1", 0.7, [], [("U", "o1")], lambda g, T, B: [g.scalar.dma_start(TB(T, "U", H, F), T.su[:, H:F])], name="ld")
+    dma("y", "l_su0", 0.7, [], [("U", "o0")], lambda g, T, B: [g.sync.dma_start(TB(T, "U", 0, H), T.su[:, 0:H])], name="ld")
     dma("s", "l_th1", 0.7, [], [("P", "o1")], lambda g, T, B: [g.scalar.dma_start(T.P[:, H:F], T.th[:, H:F])], name="ld")
     dma("y", "l_th0", 0.7, [], [("P", "o0")], lambda g, T, B: [g.sync.dma_start(T.P[:, 0:H], T.th[:, 0:H])], name="ld")
-    dma("y", "l_xs", 0.9, [], segs("Z", F), lambda g, T, B: [g.sync.dma_start(T.Z[:, 0:1024], T.xs[:])], name="ld")
+    xk0 = [("U", k) for k in range(4)]
+    dma("y", "l_xs", 0.9, [], xk0, lambda g, T, B: [g.sync.dma_start(TB(T, "U", F, F + 1024), T.xs[:])], name="ld")
 
     fl = dict(allow_small_or_imprecise_dtypes=True)
     vec(72, [], [("ones", 0)], lambda g, T, B: [g.vector.memset(T.ones[:], 1.0)], name="ld")
     pool(1, [], [("ip", 0)], lambda g, T, B: [g.iota(T.ip[:, 0:1], [[0, 1]], 0, 1)], name="ld")
     pool(128, [("ones", 0)], [("dg", 0)], lambda g, T, B: [g.affine_select(DG(T, I1), T.ones[:, 0:128], [[-1, 128]], A.is_equal, 0.0, 0, 1)], name="ld")
     pool(256, [], [("Mk", 0)], lambda g, T, B: [g.iota(T.Mk[:], [[0, 16], [1, 16]], 0, 0, **fl)], name="ld")
-    pool(128, [("ones", 0)], [("BD", 0)], lambda g, T, B: [g.affine_select(T.BD[:], T.ones[:, 0:128], [[-16, 8], [0, 16]], A.is_ge, 0.0, 0, 1)], name="ld")
-    pool(8, [("ones", 0)], [("GI", 1)], lambda g, T, B: [g.affine_select(T.GI[:, 8:16], T.ones[:, 0:8], [[-16, 8]], A.is_ge, 0.0, 0, 1)], name="ld")
-    pool(128, [("BD", 0)], [("BD", 0)], lambda g, T, B: [g.affine_select(T.BD[:], T.BD[:], [[16, 8], [0, 16]], A.is_ge, 0.0, 15, -1)], name="ld")
-    pool(8, [("GI", 1)], [("GI", 0)], lambda g, T, B: [g.affine_select(T.GI[:, 0:8], T.GI[:, 8:16], [[16, 8]], A.is_ge, 0.0, 15, -1)], name="ld")
-    pool(256, [], [("Tc", 0)], lambda g, T, B: [g.iota(T.Tc[:], [[0, 16], [1, 16]], -1, 0, **fl)], name="ld")
-    pool(136, [("ones", 0)], [("Dm", 0)], lambda g, T, B: [g.affine_select(T.Dm[:], T.ones[:, 0:136], [[-16, 8], [-1, 17]], A.is_equal, 0.0, 1, 1)], name="ld")
-    pool(16, [], [("wl32", 0)], lambda g, T, B: [g.iota(T.wl32[:], [[17, 16]], 16, 0)], name="ld")
-    pool(136, [("Dm", 0)], [("Dm", 0)], lambda g, T, B: [g.affine_select(T.Dm[:], T.Dm[:], [[-16, 8], [-1, 17]], A.not_equal, -1.0, 0, 1)], name="ld")
-    pool(8, [("ones", 0), ("Dm", 0)], [("Dm", 0)], lambda g, T, B: [g.affine_select(T.Dm[:, 16::17], T.ones[:, 0:8], [[-16, 8]], A.is_equal, 0.0, -15, 1)], name="ld")
+    pool(8, [("ones", 0)], [("GI", 1)], lambda g, T, B: [g.affine_select(T.GI[:, 8:16], T.ones[:, 0:8], [[-16, 8]], A.is_ge, 0.0, 0, 1)], name="k1")
+    pool(8, [("GI", 1)], [("GI", 0)], lambda g, T, B: [g.affine_select(T.GI[:, 0:8], T.GI[:, 8:16], [[16, 8]], A.is_ge, 0.0, 15, -1)], name="k1")
+    pool(32, [("ones", 0)], [("Bs", 0)], lambda g, T, B: [g.affine_select(T.Bs[:], T.ones[:, 0:32], [[-4, 32]], A.is_ge, 0.0, 0, 1)], name="lt")
+    pool(32, [("Bs", 0)], [("Bs", 0)], lambda g, T, B: [g.affine_select(T.Bs[:], T.Bs[:], [[4, 32]], A.is_ge, 0.0, 3, -1)], name="lt")
+    pool(136, [("ones", 0)], [("Dm", 0)], lambda g, T, B: [g.affine_select(T.Dm[:], T.ones[:, 0:136], [[-16, 8], [-1, 17]], A.is_equal, 0.0, 1, 1)], name="k2")
+    pool(16, [], [("wl32", 0)], lambda g, T, B: [g.iota(T.wl32[:], [[17, 16]], 16, 0)], name="k2")
+    pool(136, [("Dm", 0)], [("Dm", 0)], lambda g, T, B: [g.affine_select(T.Dm[:], T.Dm[:], [[-16, 8], [-1, 17]], A.not_equal, -1.0, 0, 1)], name="k2")
+    pool(8, [("ones", 0), ("Dm", 0)], [("Dm", 0)], lambda g, T, B: [g.affine_select(T.Dm[:, 16::17], T.ones[:, 0:8], [[-16, 8]], A.is_equal, 0.0, -15, 1)], name="k2")
     vec(1, [("ip", 0)], [("ip", 1)], lambda g, T, B: [g.vector.tensor_scalar(T.ip[:, 4:5], T.ip[:, 0:1], 15, None, A.bitwise_and)], name="ld")
     vec(272, [], [("d0c", 0)], lambda g, T, B: [g.vector.memset(T.d0c[:], -1.0)], name="ld")
     vec(1, [("ip", 1)], [("pc", 0)], lambda g, T, B: [g.vector.tensor_copy(T.pc[:, 0:1], T.ip[:, 4:5])], name="ld")
-    vec(272 * 2 + 64, [], [("init", 0)], lambda g, T, B: [g.vector.memset(T.B4[:, 0:272], BIG), g.vector.memset(T.f1[:], 0.0), g.vector.memset(T.U[:, 0:16], 0)], calls=3, name="ld")
+    pool(2 * S, [], [("f1", 0)], lambda g, T, B: [g.iota(T.f1[:], [[0, 2 * S]], 0, 0, **fl)], name="f0")
+    vec(384 + 128, [], [("init", 0)], lambda g, T, B: [g.vector.memset(T.Bg[:], BIG), g.vector.memset(T.h1[:], 0.0), g.vector.memset(T.U[:, UB:UB + 16], 0)], calls=3, name="ld")
+    vec(256, [("Mk", 0), ("pc", 0)], [("Tc", 0)], lambda g, T, B: [g.vector.tensor_scalar(T.Tb[:, 0:S], T.Mk[:], T.pc[:, 0:1], 8192.0, A.is_gt, A.mult)], name="ld")
     vec(256, [("Mk", 0), ("pc", 0)], [("Mk", 0)], lambda g, T, B: [g.vector.tensor_scalar(T.Mk[:], T.Mk[:], T.pc[:, 0:1], None, A.is_equal)], name="ld")
     vec(16, [("d0c", 0)], [("d0c", 0)], lambda g, T, B: [g.vector.memset(T.d0c[:, 0::17], BIG)], name="ld")
     vec(48, [("st32", 0)], [("stu", 0)], lambda g, T, B: [g.vector.tensor_copy(T.stu[:], T.st32[:])], name="ld")
+    for k in range(CFG["pools"]["X"]):
+        vec(128, [], [(("XI", k), 0)], lambda g, T, B, k=k: [g.vector.memset(T["X%d" % k][:, 0::8], -4096.0)], name="ld")
     SC = (1.0, 2.0, 4.0, 0.75, 0.25, 0.125, 0.0625, -1.0)
     act(896, [("dg", 0)], [("dg", 1)], lambda g, T, B: [g.scalar.activation(DG(T, k), DG(T, I1), AF.Copy, scale=SC[k]) for k in range(1, 8)], calls=7, name="ld")
-    act(1500, [("hb", 0)], [("lam", 0)], lambda g, T, B: [g.scalar.activation(T.lam[:], T.hb[:], AF.Ln, scale=0.0625)], name="ld")
+    act(1500, [("hb", 0)], [("lam", 0)], lambda g, T, B: [g.scalar.activation(T.lam[:, 0:16], T.hb[:], AF.Ln, scale=0.0625)], name="ld")
     vec(256, [("dg", 0)], [("I32", 0)], lambda g, T, B: [g.vector.tensor_copy(T.I32[:], DG(T, I1)), g.vector.tensor_scalar(T.IH[:], DG(T, I1), 0.5, None, A.mult)], calls=2, name="ld")
     vec(24, [("GI", 0)], [("GI32", 0)], lambda g, T, B: [g.vector.tensor_scalar(T.GI32[:], T.GI[:, 0:8], 16.0, None, A.mult),
                                                           g.vector.tensor_scalar(T.GI[:, 16:24], T.GI[:, 0:8], 32.0, None, A.mult),
-                                                          g.vector.tensor_scalar(T.GI[:, 24:32], T.GI[:, 0:8], -16.0, None, A.mult)], calls=3, name="ld")
-    vec(16, [("wl32", 0)], [("wl", 0)], lambda g, T, B: [g.vector.tensor_copy(T.wl[:], T.wl32[:])])
-    vec(256, [("Tc", 0), ("pc", 0)], [("Tc", 0)], lambda g, T, B: [g.vector.tensor_scalar(T.Tc[:], T.Tc[:], T.pc[:, 0:1], 1.0e9, A.is_ge, A.mult)])
-    for v in range(0, 15, 5):
-        act(640, [("BD", 0), ("Mk", 0)], [("Cv", v)],
-            lambda g, T, B, v=v: [g.scalar.activation(T.Cv[:, k * 128:k * 128 + 128], T.BD[:], AF.Identity, scale=T.Mk[:, k:k + 1]) for k in range(v, v + 5)], calls=5, name="cv")
-    pool(1920, [("Cv", v) for v in (0, 5, 10)], [("Cv", 0)], lambda g, T, B: [g.affine_select(T.Cv[:], T.Cv[:], [[0, 15], [-1, 128]], A.not_equal, -1.0, 0, 1)], name="cv")
-    for sem, ms in (("nm0", [0]), ("nm1", range(1, 7))):
-        a, w = ms[0] * S, len(ms) * S
-        pool(2 * w, [], [("NM", m) for m in ms] + [("YZ", m) for m in ms],
-             lambda g, T, B, a=a, w=w: [g.iota(T.NM[:, a:a + w], [[0, w]], 0, 0, **fl), g.iota(T.YZ[:, a:a + w], [[1, w]], F + a, 0, **fl)], calls=2, name=sem)
-        dma("y", sem, 0.1, [("YZ", m) for m in ms] + [("NM", m) for m in ms], [("NM", m) for m in ms],
-            lambda g, T, B, ms=ms: [g.sync.dma_start(T.NM[m::16, m * S:m * S + S], T.YZ[m::16, m * S:m * S + S]) for m in ms], n=len(ms), name=sem)
-    vec(1024, segs("Z", F), [("x16", 0)], lambda g, T, B: [g.vector.tensor_scalar(T.x16[:], T.Z[:, 0:1024], -2048.0, None, A.add)], name="x")
+                                                          g.vector.tensor_scalar(T.GI[:, 24:32], T.GI[:, 0:8], -16.0, None, A.mult)], calls=3, name="k1")
+    vec(16, [("wl32", 0)], [("wl", 0)], lambda g, T, B: [g.vector.tensor_copy(T.wl[:], T.wl32[:])], name="k2")
+    vec(128, [("Tc", 0)], [("Tc", 0)], lambda g, T, B: [g.vector.tensor_copy(T.Tb[:, S:2 * S], T.Tb[:, 0:S])], name="ld")
+    vec(64, [("dg", 0)], [("Cv", 0)], lambda g, T, B: [g.vector.tensor_scalar(T.Cv[:, 0:128], DG(T, I1), -1.0, None, A.mult)], name="cv")
+    for n in (128, 256, 512, 896):
+        vec(n // 2, [("Cv", 0)], [("Cv", 0)], lambda g, T, B, n=n: [g.vector.tensor_copy(T.Cv[:, min(n, 1024) + (n == 896) * 128:min(n, 1024) + (n == 896) * 128 + n], T.Cv[:, 0:n])], name="cv")
+    pool(1920, [("Cv", 0)], [("Cv", 0)], lambda g, T, B: [g.affine_select(T.Cv[:], T.Cv[:], [[-1, 15], [-16, 8], [0, 16]], A.not_equal, 1.0, 0, 1)], name="cv")
+    pool(UB, [], segs("Z", 2432), lambda g, T, B: [g.iota(T.U[:, 0:UB], [[0, UB]], 0, 0)], name="z0")
+    pool(S, [], [("NN", 0)], lambda g, T, B: [g.iota(T.NN[:], [[1, S]], F, S)], name="nm")
+    vec(S, [("NN", 0)], [("NN", 0)], lambda g, T, B: [g.vector.tensor_scalar(T.NN[:], T.NN[:], 16 * S - 1, None, A.bitwise_and)], name="nm")
+    vec(S, [("NN", 0), ("Mk", 0)], [("NM", 0)], lambda g, T, B: [g.vector.tensor_scalar(T.NM[:, 0:S], T.NN[:], T.Mk[:, 0:1], None, A.mult)], name="nm")
+    nk = [("NM", m) for m in range(1, 7)]
+    dma("y", "nm0", 1.3, segs("Z", 2432), nk, lambda g, T, B: [g.sync.dma_start(T.NM[:, S:7 * S], T.U[:, 0:6 * S])], name="nn")
+    dma("y", "nm1", 0.3, [("NN", 0)] + nk, nk, lambda g, T, B: [g.sync.dma_start(T.NM[m::16, m * S:m * S + S], T.NN[m::16, :]) for m in range(1, 7)], n=6, name="nn")
+    vec(1024, xk0, [("XE", k) for k in range(4)], lambda g, T, B: [g.vector.tensor_scalar(XN(T, 0, 0, 4 * S), TB(T, "U", F, F + 1024), -2048.0, None, A.add)], name="x")
     vec(2, [("pc", 0)], [("pc", 1)], lambda g, T, B: [g.vector.tensor_scalar(T.pc[:, 1:2], T.pc[:, 0:1], 6.0, None, A.not_equal), g.vector.memset(T.pc[:, 2:3], 1.0)], calls=2)
+    if any(CFG["route"]["R%d" % m] == "T" for m in range(7)):
+        lq = ("Q", "lt")
+        vec(16, [("lam", 0)], [("LP", 0)], lambda g, T, B: [g.vector.tensor_scalar(T.LP[:, 0:16], T.lam[:, 0:16], -512.0, None, A.mult),
+                                                             g.vector.tensor_scalar(T.lam[:, 16:32], T.lam[:, 0:16], -512.0, None, A.mult)], calls=2, name="lt")
+        vec(32, [("LP", 0)], [("LP", 1)], lambda g, T, B: [g.vector.tensor_tensor(T.LP[:, 16:32], T.lam[:, 16:32], T.LP[:, 0:16], A.subtract)], name="lt")
+        pe(128, [("LP", 1), ("dg", 0)], [(lq, 0)], lambda g, T, B: [g.tensor.matmul(PS(T, B, lq, 0, 128, rows=32), T.LP[:], DG(T, I1), True, True)], name="lt")
+        vec(128, [(lq, 0)], [("LT", 0)], lambda g, T, B: [g.vector.tensor_copy(T.LT[0:32, :], PS(T, B, lq, 0, 128, rows=32))], name="lt")
+        pool(512, [], [("Sel", 0)], lambda g, T, B: [g.iota(T.Sel[0:32, :], [[0, 512]], 0, 0, **fl)], name="lt")
+        for b in (0, -16):
+            pool(512, [("Sel", 0)], [("Sel", 0)], lambda g, T, B, b=b: [g.affine_select(T.Sel[0:32, :], T.Sel[0:32, :], [[-1, 4], [0, 32], [-4, 4]], A.not_equal, 1.0, b, 1)], name="lt")
 
-    def CL(T, k):
-        return T.cl[:, k * S:k * S + S]
+    def CL(T, k, n=1):
+        return T.cl[:, k * S:(k + n) * S]
 
-    def take(tab, lim, lst, lkey, k, name):
-        vec(256 * GAM, segs(tab, lim) + [lkey], [("cl", k)],
-            lambda g, T, B: [g.vector.tensor_copy(CL(T, k), T[tab][:, 16:16 + lim].indirect(lst(T)))], name=name)
+    def take(lim, lst, lkey, k, name, n=1):
+        vec(0, segs("U", lim) + [lkey], [("cl", k + j) for j in range(n)],
+            lambda g, T, B: [g.vector.tensor_copy(CL(T, k, n), TB(T, "U", 0, lim).indirect(lst(T)))], gn=S * n, name=name)
 
     def gather(gs, k, lim):
         for q in range(16):
             def fn(g, T, B, e, q, n):
                 out, src = B(gs)[:, S * q:S * (q + n)], T.P[:, 0:lim].indirect(T.cl[:, k * S + q * 16:k * S + (q + n) * 16])
                 return [g.vector.tensor_scalar(out, src, -2048.0, None, A.add) if e == "v" else g.scalar.activation(out, src, AF.Identity, bias=-2048.0)]
-            vec(256 * GAM, segs("P", lim) + [("cl", k)], [(gs, q)], fn, name=gs[1], piece=q)
+            vec(0, segs("P", lim) + [("cl", k)], [(gs, q)], fn, gn=S, name=gs[1], piece=q)
 
     sets = {}
+    scanned = {g_: any(CFG["route"][u] != "A" for u in us) for us in (("E0",), ("E1", "R0"), ("E3", "R1"), ("E4", "R3"), ("R2",), ("R4",), ("R5",), ("R6",)) for g_ in ["g" + us[0]]}
+
+    def tile(u, j):
+        d = ("D", u + "ab"[j // 2])
+        return (d, j), lambda B, a, b: B(d)[:, j % 2 * 1024 + a:j % 2 * 1024 + b]
 
     def body(u, gs, xs, xk, L, skip, elect):
-        sl = [i for i in range(16) if i not in skip]
+        route, kept = CFG["route"][u], scanned.get(gs[1], False)
+        sl = sorted([i for i in range(16) if i not in skip], key=lambda i: i % 2 * (route != "A"))
+        parts = CFG["split"].get(u, 1) if route == "T" and gs[1] == "g" + u and u[0] == "R" else 1
+        w = S // parts
         gk = [(gs, q) for q in range(16)]
-        el, xr = ("EL", elect), (MISC, "x" + u)
-        lg = int(math.log2(L))
-        nv = CFG["vmax"].get(u, 0)
-        sets[u] = (gs, xs, xk, L, sl, nv)
-        ab = []
-        if nv:
-            pe(S, xk + gk + [("dg", 0)], [(xr, 0)], lambda g, T, B: [g.tensor.matmul(B(xr)[:, 0:S], DG(T, I1), xs(T)[0], True, True)], name="mx" + u)
+        if kept and gs[1][1:] == u:
+            for r in range(parts):
+                if u in CFG["keep"]:
+                    pool(2 * w, gk[16 * r // parts:16 * (r + 1) // parts], [(gs, ("kept", r))],
+                         lambda g, T, B, a=r * w, w=w: [g.affine_select(SL(B(gs), i, a, a + w, True), SL(B(gs), i, a, a + w), [[0, w]], A.is_gt, 0.0, 1, 0) for i in range(2)], calls=2, name="kp" + u)
+                    continue
+                vec(w, gk[16 * r // parts:16 * (r + 1) // parts], [(gs, ("kept", r))],
+                    lambda g, T, B, a=r * w, w=w: [g.vector.tensor_copy(SL(B(gs), i, a, a + w, True), SL(B(gs), i, a, a + w)) for i in range(2)], calls=2, name="mx" + u)
+        pk = gk + [(gs, ("kept", r)) for r in range(parts * kept)]
+        el = ("Q", "B" + u)
+
+        def ends(g, T, B, j):
+            return [] if j else [g.tensor.matmul(PS(T, B, el, 16, 272, 17), DG(T, I1), T.Bg[:], True, True)]
+        sets[u] = (gs, xs, xk, L, sl, kept, pk, parts)
+        if route != "A":
+            mx, xe, xr = ("MX", u), ("X", u), ("Q", "x" + u)
+            for c, n, calls in ((1, 3, 3), (4, 2, 1), (6, 2, 1)):
+                def moves(T, B, c=c):
+                    return [(B(xe)[:, k::8], xs(T)[0]) for k in (1, 5, 4)] if c == 1 else [(B(xe)[:, c // 2::4], B(xe)[:, 1::4])]
+                rd = xk if c == 1 else [(xe, 1)]
+                if CFG["spread"].get(u + str(c), "p") == "v":
+                    vec(128 * n, rd, [(xe, c)], lambda g, T, B, moves=moves: [g.vector.tensor_copy(o, i) for o, i in moves(T, B)], calls=calls, name="xf" + u)
+                else:
+                    pool(S * n, rd, [(xe, c)], lambda g, T, B, moves=moves, w=S * n // calls: [g.affine_select(o, i, [[0, w]], A.is_gt, 0.0, 1, 0) for o, i in moves(T, B)],
+                         calls=calls, name="xf" + u)
+            pe(S, pk[-1:] + xk + [("dg", 0)], [(xr, 0)], lambda g, T, B: [g.tensor.matmul(PS(T, B, xr, 0, S), DG(T, I1), xs(T)[0], True, True)], name="mx" + u)
+            for r in range(parts):
+                a = r * w
+                vec(2 * w, [(gs, ("kept", r)), (xr, 0)], [(gs, ("first", r))],
+                    lambda g, T, B, a=a: [g.vector.tensor_tensor(SL(B(gs), i, a, a + w), SL(B(gs), i, a, a + w, True), PS(T, B, xr, a, a + w), A.max) for i in range(2)], calls=2, name="mx" + u)
+                for t in range(2):
+                    vec(4 * w, gk[16 * r // parts:16 * (r + 1) // parts] + [(gs, ("first", r))] + [(xe, c) for c in (1, 4, 6)], [(mx, (t, r))],
+                        lambda g, T, B, t=t, a=a: [g.vector.tensor_tensor_scan(B(mx)[:, 16 * a + t:16 * (a + w):2], B(xe)[:, 8 * a:8 * (a + w)],
+                                                                               B(gs)[:, 16 * a + t:16 * (a + w):2], 0.0, A.min, A.max)], name="mx" + u)
+                if route == "T":
+                    vec(w, [(gs, ("kept", r))], [(gs, ("first", r))],
+                        lambda g, T, B, a=a: [g.vector.tensor_copy(SL(B(gs), i, a, a + w), SL(B(gs), i, a, a + w, True)) for i in range(2)], calls=2, name="mx" + u)
+            for q in range(4 if elect is not None else 0):
+                pe(1024, pk + [(mx, (q // 2, r)) for r in range(parts)] + [("GI32", 0), ("init", 0)], [(el, "sc%d" % (2 * q)), (el, "sc%d" % (2 * q + 1))],
+                   lambda g, T, B, q=q: ends(g, T, B, q) + [g.tensor.matmul(PS(T, B, el, h * 136 + i, h * 136 + 136, 17), SL(B(b), i, 128 * h, 128 * h + 128, b == gs), T.GI[:, c:c + 8], c == 16, c == 24)
+                                         for i in sl[4 * q:4 * q + 4] for h in range(2) for b, c in ((mx, 16), (gs, 24))], name="sc" + u)
+            return
+        lg, ab = int(math.log2(L)), []
         for j in range(4):
             ss = sl[4 * j:4 * j + 4]
             w = S * len(ss)
-            if j < nv:
-                mx = ("MX", u + str(j))
-                for c0 in range(0, len(ss), 2):
-                    cs = range(c0, min(c0 + 2, len(ss)))
-                    vec(S * len(cs), gk + [(xr, 0)], [(mx, c0)],
-                        lambda g, T, B, cs=cs, ss=ss, mx=mx: [g.vector.tensor_tensor(B(mx)[:, c * S:c * S + S], B(gs)[:, ss[c]::16], B(xr)[:, 0:S], A.max) for c in cs], calls=len(cs), name="mx" + u)
-                    if elect is not None:
-                        def fn(g, T, B, cs=cs, ss=ss, mx=mx):
-                            r = []
-                            for c in cs:
-                                for h in range(2):
-                                    ops = [(B(mx)[:, c * S + h * 128:c * S + h * 128 + 128], 16), (B(gs)[:, h * 2048 + ss[c]:h * 2048 + 2048:16], 24)]
-                                    ops += [(xs(T)[0][:, h * 128:h * 128 + 128], 24)] * (nv < 4)
-                                    r += [g.tensor.matmul(T.B4[:, h * 136 + ss[c]:h * 136 + 136:17], a, T.GI[:, k:k + 8], n == 0, n == len(ops) - 1) for n, (a, k) in enumerate(ops)]
-                            return r
-                        pe(512 if nv == 4 else 768, gk + xk + [(mx, c0), ("GI32", 0), ("init", 0)], [(el, "sc%d" % (2 * j + c0 // 2))], fn, name="sc" + u)
-                continue
-            pd, de = ("PD", "a" + u + str(j)), ("D", u + str(j))
+            pd, (dk, de) = ("PD", "a" + u + str(j)), tile(u, j)
 
             def fn(g, T, B, ss=ss, pd=pd):
                 o = []
                 for c, i in enumerate(ss):
                     for n, x in enumerate(xs(T)):
-                        o.append(g.tensor.matmul(B(pd)[:, c * S:c * S + S], DG(T, IM), x, n == 0, False))
-                    o.append(g.tensor.matmul(B(pd)[:, c * S:c * S + S], DG(T, lg), B(gs)[:, i::16], False, True))
+                        o.append(g.tensor.matmul(PS(T, B, pd, c * S, c * S + S), DG(T, IM), x, n == 0, False))
+                    o.append(g.tensor.matmul(PS(T, B, pd, c * S, c * S + S), DG(T, lg), SL(B(gs), i, kept=kept), False, True))
                 return o
-            pe(w * (1 + min(L, 2)), gk + xk + [("dg", 0), ("dg", 1)], [(pd, 0)], fn, name="da" + u)
-            ab.append(act(w, [(pd, 0)], [(de, 0)], lambda g, T, B, pd=pd, de=de, w=w: [g.scalar.activation(B(de)[:, 0:w], B(pd)[:, 0:w], AF.Abs)], name="abs" + u))
-        if elect is not None:
-            for j in range(2 * nv, 8):
-                de = ("D", u + str(j // 2))
-                pe(1024, [(de, 0), ("GI32", 0), ("init", 0)], [(el, "sc%d" % j)],
-                   lambda g, T, B, j=j, de=de: [g.tensor.matmul(T.B4[:, h * 136 + i:h * 136 + 136:17], B(de)[:, (i % 4) * S + h * 128:(i % 4) * S + h * 128 + 128], T.GI32[:], True, True)
-                                                for i in (2 * j, 2 * j + 1) for h in range(2)],
-                   name="sc" + u, after=[] if LV[elect] == 0 else ab[-2:])
+            pe(w * (1 + min(L, 2)), pk + xk + [("dg", 0), ("dg", 1)], [(pd, 0)], fn, name="da" + u)
+            ab.append(act(w, [(pd, 0)], [dk], lambda g, T, B, pd=pd, de=de, w=w: [g.scalar.activation(de(B, 0, w), PS(T, B, pd, 0, w), AF.Abs)], name="abs" + u))
+        for j in range(8 if elect is not None else 0):
+            dk, de = tile(u, j // 2)
+            pe(1024, [dk, ("GI32", 0), ("init", 0)], [(el, "sc%d" % j)],
+               lambda g, T, B, j=j, de=de: ends(g, T, B, j) + [g.tensor.matmul(PS(T, B, el, h * 136 + i, h * 136 + 136, 17), de(B, (i % 4) * S + h * 128, (i % 4) * S + h * 128 + 128), T.GI32[:], True, True)
+                                            for i in (2 * j, 2 * j + 1) for h in range(2)],
+               name="sc" + u, after=[] if LV[elect] == 0 else ab[-2:])
 
     def mix(u):
-        gs, xs, xk, L, sl, nv = sets[u]
-        y = ("YM" if u[0] == "E" else "YZ", int(u[1]))
-        m = y[1]
+        gs, xs, xk, L, sl, kept, pk, parts = sets[u]
+        m, route, mx = int(u[1]), CFG["route"][u], ("MX", u)
+        y = ("YM", m) if u[0] == "E" else (("Y", u), 0)
         hi = u[0] == "E" and L > 1
         b0 = math.log(1.0 / 32 if hi else 1.0 / 16)
-        fac = u in CFG["factor"] and nv == 4
-        how = CFG["total"][u]
-        de = [("D", u + str(j)) for j in range(4)]
+        fac = route == "T" or route == "N" and u in CFG["factor"]
+        how = "T" if route == "T" else CFG["total"][u]
+        dk, de = zip(*[tile(u, j) for j in range(4)])
         osem = "o" + u if len(sl) < 16 else "out"
+        rd = ("Q", "s" + u)
 
-        def Y(T):
-            return T[y[0]][:, m * S:m * S + S]
+        def Y(T, B):
+            return T.YM[:, m * S:m * S + S] if u[0] == "E" else B(y[0])[:]
 
         def OUT(T):
-            return T[y[0].lower()][:, m * S:m * S + S]
+            return T["ym" if u[0] == "E" else "yz"][:, m * S:m * S + S]
         for j in range(4):
             ss = sl[4 * j:4 * j + 4]
             w = S * len(ss)
-            src = de[j]
-            if j < nv:
-                src, mx = ("PD", "e" + u + str(j)), ("MX", u + str(j))
-
-                def fn(g, T, B, ss=ss, pd=src, mx=mx):
+            pd = ("PD", "e" + u + str(j))
+            if route == "T":
+                def fn(g, T, B, j=j, pd=pd):
+                    r = []
+                    for c in range(8):
+                        a, t = 1024 * j + 512 * (c // 4), c % 4
+                        ops = [(B(mx)[:, a + t:a + 512:4], DG(T, I2)), (B(gs)[:, a + t:a + 512:4], DG(T, IM))]
+                        ops += [(T.Sel[0:32, 128 * t:128 * t + 128], T.LT[0:32, :])] * (u[0] == "R")
+                        r += [g.tensor.matmul(PS(T, B, pd, 128 * c, 128 * c + 128), l, x, n == 0, n == len(ops) - 1) for n, (l, x) in enumerate(ops)]
+                    return r
+                r = j * parts // 4
+                pe(1024 * (2 if u[0] == "E" else 3), pk[4 * j:4 * j + 4] + [(gs, ("first", r)), (mx, (0, r)), (mx, (1, r)), ("dg", 1)] + [("LT", 0), ("Sel", 0)] * (u[0] == "R"), [(pd, 0)], fn, name="d" + u)
+                act(1024, [(pd, 0)], [dk[j]],
+                    lambda g, T, B, j=j, pd=pd: [g.scalar.activation(de[j](B, 0, 1024), PS(T, B, pd, 0, 1024), AF.Exp, bias=b0 if u[0] == "E" else 0.0, scale=-1.0 / 512)], name="exp" + u)
+                pe(2048, [dk[j], ("Bs", 0)], [(rd, j)],
+                   lambda g, T, B, j=j: [g.tensor.matmul(PS(T, B, rd, 64 * j + 32 * (c // 4), 64 * j + 32 * (c // 4) + 32), de[j](B, 128 * c, 128 * c + 128), T.Bs[:], c % 4 == 0, c % 4 == 3)
+                                         for c in range(8)], name="sum" + u)
+                continue
+            if route == "N":
+                def fn(g, T, B, ss=ss, pd=pd):
                     r = []
                     for c, i in enumerate(ss):
-                        ops = [(IM, B(gs)[:, i::16]), (I2, B(mx)[:, c * S:c * S + S])] + ([] if fac else [(IM, xs(T)[0])])
-                        r += [g.tensor.matmul(B(pd)[:, c * S:c * S + S], DG(T, k), a, n == 0, n == len(ops) - 1) for n, (k, a) in enumerate(ops)]
+                        ops = [(IM, SL(B(gs), i, kept=True)), (I2, SL(B(mx), i))] + ([] if fac else [(IM, xs(T)[0])])
+                        r += [g.tensor.matmul(PS(T, B, pd, c * S, c * S + S), DG(T, k), a, n == 0, n == len(ops) - 1) for n, (k, a) in enumerate(ops)]
                     return r
-                pe(w * (2 if fac else 3), [(gs, q) for q in range(16)] + [(mx, c) for c in range(0, len(ss), 2)] + [("dg", 1)] + ([] if fac else xk), [(src, 0)], fn, name="d" + u)
-            if u[0] == "E":
-                act(w, [(src, 0)], [(de[j], 0)], lambda g, T, B, j=j, src=src: [g.scalar.activation(B(de[j])[:], B(src)[:], AF.Exp, bias=b0, scale=-1.0 / (512 * L))], name="exp" + u)
+                pe(w * (2 if fac else 3), pk + sorted({(mx, (i % 2, 0)) for i in ss}) + [("dg", 1)] + ([] if fac else xk), [(pd, 0)], fn, name="d" + u)
+
+            def SRC(T, B, a, b, j=j, pd=pd):
+                return PS(T, B, pd, a, b) if route == "N" else de[j](B, a, b)
+            src = (pd, 0) if route == "N" else dk[j]
+            if u[0] == "E" and route == "A" and u in CFG["wide"]:
+                if j % 2:
+                    act(2 * w, dk[j - 1:j + 1], dk[j - 1:j + 1], lambda g, T, B, d=dk[j][0]: [g.scalar.activation(B(d)[:], B(d)[:], AF.Exp, bias=b0, scale=-1.0 / (512 * L))], name="exp" + u)
+            elif u[0] == "E":
+                act(w, [src], [dk[j]], lambda g, T, B, j=j, SRC=SRC: [g.scalar.activation(de[j](B, 0, 1024), SRC(T, B, 0, 1024), AF.Exp, bias=b0, scale=-1.0 / (512 * L))], name="exp" + u)
             else:
-                act(w, [(src, 0), ("lam", 0)], [(de[j], 0)],
-                    lambda g, T, B, j=j, ss=ss, src=src: [g.scalar.activation(B(de[j])[:, c * S:c * S + S], B(src)[:, c * S:c * S + S], AF.Exp, bias=T.lam[:, i:i + 1], scale=-1.0 / 512)
+                act(w, [src, ("lam", 0)], [dk[j]],
+                    lambda g, T, B, j=j, ss=ss, SRC=SRC: [g.scalar.activation(de[j](B, c * S, c * S + S), SRC(T, B, c * S, c * S + S), AF.Exp, bias=T.lam[:, i:i + 1], scale=-1.0 / 512)
                                                           for c, i in enumerate(ss)], calls=len(ss), name="exp" + u)
-        fk = []
+        fk, fa = [], ("FA", u)
         if fac:
-            fa = ("FA", u)
             fk = [(fa, 0)]
-            act(256, xk + [(de[0], 0)], fk, lambda g, T, B: [g.scalar.activation(B(fa)[:], xs(T)[0], AF.Exp, scale=1.0 / 512)], name="y" + u)
+            act(256, xk + [dk[0]], fk, lambda g, T, B: [g.scalar.activation(B(fa)[:], xs(T)[0], AF.Exp, scale=1.0 / 512)], name="y" + u)
+
+        def FAC(T, B):
+            return B(fa)[:]
         w3 = S * (len(sl) - 12)
-        adds = (("h", 0, 1, 0, 1024), ("k", 2, 3, 0, w3), ("h", 0, 2, 0, 1024), ("h", 0, 0, 512, 512), ("h", 0, 0, 256, 256))[:{"ha": 1, "h1": 2, "h2": 3, "h3": 4, "dma": 5}.get(how, 0)]
-        for sem, a, b, o, n in adds:
-            dma("p", sem + u, CFG["acc"] * n / 2048, [(de[a], 0), (de[b], 0)], [(de[a], 0)],
-                lambda g, T, B, a=a, b=b, o=o, n=n: [g.dma_start(B(de[a])[:, 0:n], B(de[b])[:, o:o + n], accum_op=A.add)], name="half" + u)
-        rest = {"ha": ((2, 4), (3, w3 // S), (0, 4)), "h1": ((0, 4), (2, 4)), "h2": ((0, 4),), "h3": ((0, 2),)}.get(how, ((0, 4), (1, 4), (2, 4), (3, w3 // S)))
+        da, db = dk[0][0], dk[2][0]
+        for n in (1024 + w3, 1024, 512, 256)[:{"h1": 1, "h2": 2, "h3": 3, "dma": 4}.get(how, 0)]:
+            top = n > 1024
+            dma("p", "h" + u, 3.4 * n / 2048, dk if top else dk[:2], dk[:2],
+                lambda g, T, B, n=n, top=top: [g.dma_start(B(da)[:, 0:n], B(db)[:, 0:n] if top else B(da)[:, n:2 * n], accum_op=A.add)], name="half" + u)
+        rest = {"h1": ((0, 4), (1, 4)), "h2": ((0, 4),), "h3": ((0, 2),)}.get(how, ((0, 4), (1, 4), (2, 4), (3, w3 // S)))
         rest = [(j, c) for j, n in rest for c in range(n)]
-        rd = (MISC, "s" + u)
-        if how == "vec":
-            for n in range(8):
-                j, o = n // 2, n % 2 * 512
-                vec(512, [(de[j], 0)] + [(rd, 0)] * (n > 0), [(rd, 0)],
-                    lambda g, T, B, j=j, o=o, n=n: [g.vector.tensor_tensor(B(rd)[:, 0:512], B(de[j])[:, o:o + 512], B(rd)[:, 0:512], A.add) if n else g.vector.tensor_copy(B(rd)[:, 0:512], B(de[j])[:, 0:512])], name="sum" + u)
-            vec(256, [(rd, 0)], [y], lambda g, T, B: [g.vector.tensor_copy(Y(T), B(rd)[:, 0:S])], name="y" + u)
-            vec(256, [(rd, 0), y], [(rd, 0) if fac else y], lambda g, T, B: [g.vector.tensor_tensor(B(rd)[:, S:2 * S] if fac else Y(T), B(rd)[:, S:2 * S], Y(T), A.add)], name="y" + u)
+        if how == "fold":
+            back = ("Y", "f" + u)
+            land = (back, 0) if fac else y
+            a = dma("p", "h" + u, 3.5, dk, [land], lambda g, T, B: [[de[j](B, c * S, c * S + S) for j, c in rest]], name="half" + u, fold=u,
+                    home=lambda T, B: B(back)[:] if fac else Y(T, B))
+            add(None, [land], [land], None, sem="k" + u, lat=1.5, after=[a], name="half" + u, fold=u)
             if fac:
-                vec(256, [(rd, 0)] + fk, [y], lambda g, T, B: [g.vector.tensor_tensor(Y(T), B(rd)[:, S:2 * S], B(fa)[:], A.mult)], name="y" + u)
-        elif how != "dma":
+                vec(512, [land] + fk, [y], lambda g, T, B: [g.vector.tensor_tensor(Y(T, B), B(back)[:], FAC(T, B), A.mult)], name="y" + u)
+        elif how == "vec":
             for n in range(0, len(rest), 2):
+                (j, c), w = rest[n], S * len(rest[n:n + 2])
+                vec(w, [dk[j]] + [(rd, 0)] * (n > 0), [(rd, 0)],
+                    lambda g, T, B, j=j, c=c, w=w, n=n: [g.vector.tensor_tensor(PS(T, B, rd, 0, w), de[j](B, c * S, c * S + w), PS(T, B, rd, 0, w), A.add) if n
+                                                         else g.vector.tensor_copy(PS(T, B, rd, 0, w), de[j](B, 0, w))], name="sum" + u)
+            vec(256, [(rd, 0)], [y], lambda g, T, B: [g.vector.tensor_copy(Y(T, B), PS(T, B, rd, 0, S))], name="y" + u)
+            vec(256, [(rd, 0), y], [(rd, 0) if fac else y], lambda g, T, B: [g.vector.tensor_tensor(PS(T, B, rd, S, 2 * S) if fac else Y(T, B), PS(T, B, rd, S, 2 * S), Y(T, B), A.add)], name="y" + u)
+            if fac:
+                vec(256, [(rd, 0)] + fk, [y], lambda g, T, B: [g.vector.tensor_tensor(Y(T, B), PS(T, B, rd, S, 2 * S), FAC(T, B), A.mult)], name="y" + u)
+        elif how != "dma":
+            for n in range(0, len(rest) if how != "T" else 0, 2):
                 two = rest[n:n + 2]
-                i0 = pe(1024 * len(two), sorted({(de[j], 0) for j, _ in two}) + [("I32", 0)], [(rd, n)],
-                        lambda g, T, B, two=two: [g.tensor.matmul(B(rd)[:, 0:S], T.I32[:], B(de[j])[:, c * S:c * S + S], (j, c) == rest[0], (j, c) == rest[-1]) for j, c in two], name="sum" + u)
+                i0 = pe(1024 * len(two), sorted({dk[j] for j, _ in two}) + [("I32", 0)], [(rd, n)],
+                        lambda g, T, B, two=two: [g.tensor.matmul(PS(T, B, rd, 0, S), T.I32[:], de[j](B, c * S, c * S + S), (j, c) == rest[0], (j, c) == rest[-1]) for j, c in two], name="sum" + u)
                 if n:
                     tasks[i0]["follow"] = [i0 - 1]
-            vec(256, [(rd, n) for n in range(0, len(rest), 2)] + fk, [y],
-                lambda g, T, B: [g.vector.tensor_tensor(Y(T), B(rd)[:, 0:S], B(fa)[:], A.mult) if fac else g.vector.tensor_copy(Y(T), B(rd)[:, 0:S])], name="y" + u)
+            vec(256, [(rd, n) for n in (range(4) if how == "T" else range(0, len(rest), 2))] + fk, [y],
+                lambda g, T, B: [g.vector.tensor_tensor(Y(T, B), PS(T, B, rd, 0, S), FAC(T, B), A.mult) if fac else g.vector.tensor_copy(Y(T, B), PS(T, B, rd, 0, S))], name="y" + u)
         elif fac:
-            vec(512, [(de[0], 0)] + fk, [y], lambda g, T, B: [g.vector.tensor_tensor(Y(T), B(de[0])[:, 0:S], B(fa)[:], A.mult)], name="y" + u)
+            vec(512, [dk[0]] + fk, [y], lambda g, T, B: [g.vector.tensor_tensor(Y(T, B), de[0](B, 0, S), FAC(T, B), A.mult)], name="y" + u)
         elif u[0] == "R":
-            dma("y", "y" + u if osem == "out" else osem, 0.3, [(de[0], 0)], [("o" + y[0], m)], lambda g, T, B: [g.sync.dma_start(OUT(T), B(de[0])[:, 0:S])], name="out" + u)
+            dma("y", "y" + u if osem == "out" else osem, 0.3, [dk[0]], [("oR", m)], lambda g, T, B: [g.sync.dma_start(OUT(T), de[0](B, 0, S))], name="out" + u)
             return
         else:
-            dma("y", "y" + u, 0.3, [(de[0], 0)], [y], lambda g, T, B: [g.sync.dma_start(Y(T), B(de[0])[:, 0:S])], name="y" + u)
+            dma("y", "y" + u, 0.3, [dk[0]], [y], lambda g, T, B: [g.sync.dma_start(Y(T, B), de[0](B, 0, S))], name="y" + u)
         if hi:
             ka, kb = KIDS[m]
             kk = ("Q", "K" + u)
-            pe(1024, [("YM", ka), ("YM", kb), y, ("I32", 0)], [(kk, 0)], lambda g, T, B: [g.tensor.matmul(B(kk)[:, 0:S], T.IH[:], T.YM[:, kb * S:kb * S + S], True, True)], name="K" + u)
-            vec(256, [(kk, 0), ("YM", ka)], [(kk, 0)], lambda g, T, B: [g.vector.tensor_tensor(B(kk)[:, 0:S], B(kk)[:, 0:S], T.YM[:, ka * S:ka * S + S], A.mult)], name="K" + u)
-            vec(256, [y, (kk, 0)], [y], lambda g, T, B: [g.vector.tensor_tensor(Y(T), B(kk)[:, 0:S], Y(T), A.add)], name="K" + u)
-        dma("y", osem, 0.3, [y], [("o" + y[0], m)], lambda g, T, B: [g.sync.dma_start(OUT(T), Y(T))], name="out" + u)
+            pe(1024, [("YM", ka), ("YM", kb), y, ("I32", 0)], [(kk, 0)], lambda g, T, B: [g.tensor.matmul(PS(T, B, kk, 0, S), T.IH[:], T.YM[:, kb * S:kb * S + S], True, True)], name="K" + u)
+            vec(256, [(kk, 0), ("YM", ka)], [(kk, 0)], lambda g, T, B: [g.vector.tensor_tensor(PS(T, B, kk, 0, S), PS(T, B, kk, 0, S), T.YM[:, ka * S:ka * S + S], A.mult)], name="K" + u)
+            vec(256, [y, (kk, 0)], [y], lambda g, T, B: [g.vector.tensor_tensor(Y(T, B), PS(T, B, kk, 0, S), Y(T, B), A.add)], name="K" + u)
+        dma("y", osem if u[0] == "E" or osem != "out" else "y" + u, 0.3, [y], [("o" + u[0], m)], lambda g, T, B: [g.sync.dma_start(OUT(T), Y(T, B))], name="out" + u)
 
     def late(slot, ms, f0):
         u = "F%d" % slot
-        pd = ("PD", u)
+        pd = ("Q", u)
         w = S * len(ms)
 
         def fn(g, T, B):
             o = []
             for m in ms:
-                o.append(g.tensor.matmul(B(pd)[:, m * S:m * S + S], DG(T, IM), T.n16[:, m * S:m * S + S], True, False))
+                o.append(g.tensor.matmul(PS(T, B, pd, m * S, m * S + S), DG(T, IM), XN(T, 4 + m), True, False))
                 for v in range(16):
-                    o.append(g.tensor.matmul(B(pd)[:, m * S + 16 * v:m * S + 16 * v + 16], DG(T, I1), T.Gf[:, (f0 + m) * S + v:(f0 + m + 1) * S:16], False, v == 15))
+                    o.append(g.tensor.matmul(PS(T, B, pd, m * S + 16 * v, m * S + 16 * v + 16), DG(T, I1), T.Gf[:, (f0 + m) * S + v:(f0 + m + 1) * S:16], False, v == 15))
             return o
-        pe(5 * w, [("Gf", f0 + m) for m in ms] + [("n16", m) for m in ms] + [("dg", 0), ("dg", 1)], [(pd, 0)], fn, name="d" + u)
-        act(w, [(pd, 0)], [("FE", f0)], lambda g, T, B: [g.scalar.activation(T.FE[:, f0 * S:f0 * S + w], B(pd)[:, 0:w], AF.Abs)], name="abs" + u)
+        pe(5 * w, [("Gf", f0 + m) for m in ms] + [("XE", 4 + m) for m in ms] + [("dg", 0), ("dg", 1)], [(pd, 0)], fn, name="d" + u)
+        act(w, [(pd, 0)], [("FE", f0)], lambda g, T, B: [g.scalar.activation(T.FE[:, f0 * S:f0 * S + w], PS(T, B, pd, 0, w), AF.Abs)], name="abs" + u)
         act(w, [("FE", f0), ("lam", 0)], [("FE", f0)],
             lambda g, T, B: [g.scalar.activation(T.FE[:, f0 * S:f0 * S + w], T.FE[:, f0 * S:f0 * S + w], AF.Exp, bias=T.lam[:, slot:slot + 1], scale=-1.0 / 512)], name="exp" + u)
-        dma("p", "h" + u, 0.8, [("FE", f0)] + [("oYZ", m) for m in ms], [("oYZ", m) for m in ms],
+        dma("p", "h" + u, 0.8, [("FE", f0)] + [("oR", m) for m in ms], [("oR", m) for m in ms],
             lambda g, T, B: [g.dma_start(T.yz[:, 0:w], T.FE[:, f0 * S:f0 * S + w], accum_op=A.add)], name="out" + u)
 
     def send(sem, l, src, dst, rkey, wkey):
-        a = add("p", 0.6, [rkey], [], lambda g, T, B: [(dst(T), src(T), sem, l)], sem="sent", name="send" + sem)
-        add(None, 0.0, [], [wkey], None, sem=sem, lat=3.5, after=[a], name="send" + sem)
+        a = add("p", [rkey], [], lambda g, T, B: [(dst(T), src(T), sem, l)], sem="sent", name="send" + sem)
+        add(None, [], [wkey], None, sem=sem, lat=2.0, after=[a], name="send" + sem)
 
     def elect(m, k):
         L = 1 << LV[m]
         u = "E%d" % m
-        gs, el, cn = ("H", "g" + u), ("EL", m), ("C", m)
+        gs, el, cn, pb = ("H", "g" + u), ("EL", m), ("C", m), (("PB", m), 0)
+        xk = [("XE", t) for t in TS[m]]
         part[0] = "el%d" % m
         gather(gs, k, BLIM[m])
         if L == 4:
             nb = ("Q", "x")
-            pe(1024, [("x16", 0), ("dg", 0)], [(nb, 0)], lambda g, T, B: [g.tensor.matmul(B(nb)[:, 0:S], DG(T, I1), T.x16[:, t * S:t * S + S], t == 0, t == 3) for t in range(4)], name="x4")
-            vec(256, [(nb, 0)], [("x4", 0)], lambda g, T, B: [g.vector.tensor_copy(T.x4[:, 0:S], B(nb)[:, 0:S])], name="x4")
-            vec(256, [(nb, 0), ("x4", 0)], [("x4", 1)], lambda g, T, B: [g.vector.tensor_tensor(T.x4[:, S:2 * S], B(nb)[:, 0:S], T.x4[:, 0:S], A.subtract)], name="x4")
+            pe(1024, xk + [("dg", 0)], [(nb, 0)], lambda g, T, B: [g.tensor.matmul(PS(T, B, nb, 0, S), DG(T, I1), XN(T, t), t == 0, t == 3) for t in range(4)], name="x4")
+            vec(256, [(nb, 0)], [("x4", 0)], lambda g, T, B: [g.vector.tensor_copy(T.x4[:, 0:S], PS(T, B, nb, 0, S))], name="x4")
+            vec(256, [(nb, 0), ("x4", 0)], [("x4", 1)], lambda g, T, B: [g.vector.tensor_tensor(T.x4[:, S:2 * S], PS(T, B, nb, 0, S), T.x4[:, 0:S], A.subtract)], name="x4")
             body(u, gs, lambda T: [T.x4[:, 0:S], T.x4[:, S:2 * S]], [("x4", 0), ("x4", 1)], L, (), m)
         else:
-            body(u, gs, lambda T: [T.x16[:, t * S:t * S + S] for t in TS[m]], [("x16", 0)], L, (), m)
-        nq, sq = ("Q", "n" + u), ("Q", "s" + u)
-        sk = [(el, "sc%d" % j) for j in range(8)]
-        vec(128, [("cl", k), sk[0]], [(cn, 0)], lambda g, T, B: [g.vector.tensor_scalar(B(cn)[:], CL(T, k), -2048.0, None, A.add)])
+            body(u, gs, lambda T: [XN(T, t) for t in TS[m]], xk, L, (), m)
+        nq, sq = ("Q", "n" + u), ("Q", "q" + u)
+        sb = ("Q", "B" + u)
+        sk = [(sb, "sc%d" % j) for j in range(8)]
+        off = 0.0 if BLIM[m] <= 2048 and u in CFG["names"] else 2048.0
+        if off:
+            vec(128, [("cl", k), sk[0]], [(cn, 0)], lambda g, T, B: [g.vector.tensor_scalar(B(cn)[:], CL(T, k), -off, None, A.add)])
+        else:
+            pool(S, [("cl", k)], [(cn, 0)], lambda g, T, B: [g.affine_select(B(cn)[:], CL(T, k), [[0, S]], A.is_gt, 0.0, 1, 0)], name="cn%d" % m)
         pe(272, [(cn, 0), ("Dm", 0)] + sk, [(nq, 0)],
-           lambda g, T, B: [g.tensor.matmul(B(nq)[:, h * 136:h * 136 + 136], B(cn)[:, h * 128:h * 128 + 128], T.Dm[:], True, True) for h in range(2)])
-        vec(272, sk + [("d0c", 0)], [(el, "e1")], lambda g, T, B: [g.vector.tensor_tensor_scan(T.e1[:], T.d0c[:], T.B4[:, 0:272], 0.0, A.add, A.min)])
-        vec(272, sk + [(el, "e1")], [(el, "e2")], lambda g, T, B: [g.vector.tensor_tensor(T.e2[:], T.e1[:], T.B4[:, 0:272], A.not_equal)])
-        vec(272, [(el, "e2"), (nq, 0)], [(el, "e3")], lambda g, T, B: [g.vector.tensor_tensor_scan(T.e3[:], B(nq)[:, 0:272], T.e2[:], 0.0, A.add, A.mult)])
-        vec(256 * GAM, [(el, "e3"), ("wl", 0), ("Mk", 0)], [(el, "w")], lambda g, T, B: [g.vector.tensor_tensor(T.Wm[:], T.e3[:].indirect(T.wl[:]), T.Mk[:], A.mult)])
-        pe(128, [(el, "w"), ("GI", 0)], [(el, "lp")],
-           lambda g, T, B: [g.tensor.matmul(T.B4[:, 288 + 8 * h:296 + 8 * h], T.Wm[:, h * 128:h * 128 + 128], T.GI[:, 0:8], True, True) for h in range(2)])
-        vec(16, [(el, "lp")], [("b16", m)], lambda g, T, B: [g.vector.tensor_scalar(T.b16[:, 16 * m:16 * m + 16], T.B4[:, 288:304], 2048.0, None, A.add)], name="b%d" % m)
+           lambda g, T, B: [g.tensor.matmul(PS(T, B, nq, h * 136, h * 136 + 136), B(cn)[:, h * 128:h * 128 + 128], T.Dm[:], True, True) for h in range(2)])
+        vec(272, sk + [("d0c", 0)], [(el, "e1")], lambda g, T, B: [g.vector.tensor_tensor_scan(T.e1[:], T.d0c[:], PS(T, B, sb, 0, 272), 0.0, A.add, A.min)])
+        vec(272, sk + [(el, "e1")], [(el, "e2")], lambda g, T, B: [g.vector.tensor_tensor(T.e2[:], T.e1[:], PS(T, B, sb, 0, 272), A.not_equal)])
+        vec(272, [(el, "e2"), (nq, 0)], [(el, "e3")], lambda g, T, B: [g.vector.tensor_tensor_scan(T.e3[:], PS(T, B, nq, 0, 272), T.e2[:], 0.0, A.add, A.mult)])
+        vec(0, [(el, "e3"), ("wl", 0), ("Mk", 0)], [(el, "w")], lambda g, T, B: [g.vector.tensor_tensor(T.Wm[:], T.e3[:].indirect(T.wl[:]), T.Mk[:], A.mult)], gn=S)
+        pe(128, [(el, "w"), ("GI", 0)], [(nq, "lp")],
+           lambda g, T, B: [g.tensor.matmul(PS(T, B, nq, 288 + 8 * h, 296 + 8 * h), T.Wm[:, h * 128:h * 128 + 128], T.GI[:, 0:8], True, True) for h in range(2)])
+        vec(16, [(nq, "lp")], [("b16", m)], lambda g, T, B: [g.vector.tensor_scalar(T.b16[:, 16 * m:16 * m + 16], PS(T, B, nq, 288, 304), off, None, A.add)], name="b%d" % m)
         part[0] = "sn%d" % m
-        vec(256 * GAM, segs("P", BLIM[m]) + [("b16", m)], [("pb", 0)],
-            lambda g, T, B: [g.vector.tensor_scalar(T.pb[:], T.P[:, 0:BLIM[m]].indirect(T.b16[:, 16 * m:16 * m + 16]), -2048.0, None, A.add)], lock=("PB", m))
-        pe(256 * (1 + L), [("pb", 0), ("x16", 0), ("dg", 1)], [(sq, 0)],
-           lambda g, T, B: [g.tensor.matmul(B(sq)[:, 0:S], DG(T, I34), T.pb[:], True, False)]
-           + [g.tensor.matmul(B(sq)[:, 0:S], DG(T, IQ + LV[m]), T.x16[:, t * S:t * S + S], False, t == TS[m][-1]) for t in TS[m]], lock=("PB", m))
+        vec(0, segs("P", BLIM[m]) + [("b16", m)], [pb],
+            lambda g, T, B: [g.vector.tensor_scalar(T.pb[:], T.P[:, 0:BLIM[m]].indirect(T.b16[:, 16 * m:16 * m + 16]), -2048.0, None, A.add)], gn=S)
+        pe(256 * (1 + L), [pb, ("dg", 1)] + xk, [(sq, 0)],
+           lambda g, T, B: [g.tensor.matmul(PS(T, B, sq, 0, S), DG(T, I34), T.pb[:], True, False)]
+           + [g.tensor.matmul(PS(T, B, sq, 0, S), DG(T, IQ + LV[m]), XN(T, t), False, t == TS[m][-1]) for t in TS[m]])
         cst = 2048.0 - 0.5 + 1.0 / (8 * L)
         n0 = F + m * S
         if L == 1:
-            vec(256, [(sq, 0)], [("P", m)], lambda g, T, B: [g.vector.tensor_scalar(T.P[:, n0:n0 + S], B(sq)[:, 0:S], cst, None, A.add)])
+            vec(256, [(sq, 0)], [("P", m)], lambda g, T, B: [g.vector.tensor_scalar(T.P[:, n0:n0 + S], PS(T, B, sq, 0, S), cst, None, A.add)])
         else:
             kk = list(KIDS).index(m)
-            vec(256, [(sq, 0)], [("snd", kk)], lambda g, T, B: [g.vector.tensor_scalar(T.snd[:, kk * S:kk * S + S], B(sq)[:, 0:S], cst, None, A.add)])
+            vec(256, [(sq, 0)], [("snd", kk)], lambda g, T, B: [g.vector.tensor_scalar(T.snd[:, kk * S:kk * S + S], PS(T, B, sq, 0, S), cst, None, A.add)])
             send("a_n%d" % m, LV[m], lambda T: T.snd[:, kk * S:kk * S + S], lambda T: T.P[:, n0:n0 + S], ("snd", kk), ("P", m))
-        vec(256, [("P", m)], [("n16", m)], lambda g, T, B: [g.vector.tensor_scalar(T.n16[:, m * S:m * S + S], T.P[:, n0:n0 + S], -2048.0, None, A.add)], name="n%d" % m)
+        vec(256, [("P", m)], [("XE", 4 + m)], lambda g, T, B: [g.vector.tensor_scalar(XN(T, 4 + m), T.P[:, n0:n0 + S], -2048.0, None, A.add)], name="n%d" % m)
 
-    def targets(m, lst, lkey):
-        dd, b6 = ("TG", m), ("Q", "t%d" % m)
-        part[0] = "tg%d" % m
-        vec(32, [lkey, ("init", 0), ("Cv", 0)], [(dd, "a")], lambda g, T, B: [g.vector.tensor_scalar(T.a16[:], lst(T), -2048.0, None, A.add),
-                                                                               g.vector.tensor_scalar(T.f1[:, 0::16], lst(T), 16.0, None, A.add)], calls=2)
-        pe(1088, [(dd, "a"), ("dg", 0), ("dg", 1), ("Cv", 0)], [(b6, 0)],
-           lambda g, T, B: [g.tensor.matmul(B(b6)[:, 0:S:16], DG(T, k), T.a16[:], k == I1, k == IM) for k in (I1, IM)]
-           + [g.tensor.matmul(B(b6)[:, v + 1:S:16], T.Cv[:, v * 128:v * 128 + 128], T.a16[:], True, True) for v in range(15)])
-        vec(256, [(b6, 0), ("Tc", 0)], [(dd, "f2")], lambda g, T, B: [g.vector.tensor_tensor(T.f2[:], B(b6)[:, 0:S], T.Tc[:], A.not_equal)])
-        vec(256, [(dd, "f2"), (dd, "a")], [(dd, "f3")], lambda g, T, B: [g.vector.tensor_tensor_scan(T.f3[:], T.f2[:], T.f1[:], 0.0, A.mult, A.add)])
-        vec(16, [(dd, "f3"), ("pc", 0)], [("off", m)], lambda g, T, B: [g.vector.tensor_scalar(T.off[:, 32 * m:32 * m + 32:2], T.f3[:, 15::16], T.pc[:, 0:1], None, A.max)])
+    def targets(ms, lst, lkeys):
+        n, w = len(ms), S * len(ms)
+        dd, b6 = ("TG", ms[0]), ("PD" if n > 2 else "Q", "t%d" % ms[0])
+        half = max(ALIM[m] for m in ms) + 16 <= 2048
+        f1, f3 = ("h1", "h3") if half else ("f1", "f3")
+        part[0] = "tg%d" % ms[0]
 
-    def extend(m, tab, lst, lkey):
-        lim = ALIM[m]
-        cu = ("CU", m)
+        def a16(T, a, b):
+            return T.h1[:, 16 * a:16 * b:16] if half else T.a16[:, a:b]
+        vec(16 * n, lkeys + [("init", 0), ("Cv", 0)] + [("f1", 0)] * (not half), [(dd, "a")],
+            lambda g, T, B: [g.vector.tensor_scalar(T[f1][:, 0:w:16], lst(T), 16.0, None, A.add)]
+            + [g.vector.tensor_scalar(T.a16[:, 0:16 * n], lst(T), -2048.0, None, A.add) for _ in range(not half)], calls=2 - half)
+
+        def fn(g, T, B):
+            o = []
+            for a in range(0, n, 2):
+                b = min(a + 2, n)
+                o += [g.tensor.matmul(PS(T, B, b6, a * S, b * S), DG(T, I1), T.Tb[:, 0:(b - a) * S], True, False)]
+                o += [g.tensor.matmul(PS(T, B, b6, a * S + v + 1, b * S, 16), T.Cv[:, v * 128:v * 128 + 128], a16(T, 16 * a, 16 * b), False, v == 14) for v in range(15)]
+            return o
+        pe(w + 960 * (n + 1 >> 1), [(dd, "a"), ("dg", 0), ("Cv", 0), ("Tc", 0)], [(b6, 0)], fn)
+        vec(w, [(b6, 0)], [(dd, "f2")], lambda g, T, B: [g.vector.tensor_scalar(T.f2[:, 0:w], PS(T, B, b6, 0, w), 0.0, None, A.not_equal)])
+        vec(w // (1 + half), [(dd, "f2"), (dd, "a")], [(dd, "f3")], lambda g, T, B: [g.vector.tensor_tensor_scan(T[f3][:, 0:w], T.f2[:, 0:w], T[f1][:, 0:w], 0.0, A.mult, A.add)])
+        runs = [(0, n)] if not set(ms) & set(PAIR) or n == 1 else [(k, k + 1) for k in range(n)]
+        vec(16 * n, [(dd, "f3"), ("pc", 0)], [("off", m) for m in ms],
+            lambda g, T, B: [g.vector.tensor_scalar(T.off[:, OFF[ms[a]]:OFF[ms[a]] // 2 * 2 + 32 * (b - a):2], T[f3][:, a * S + 15:b * S:16], T.pc[:, 0:1], float(UB * (ms[a] in PAIR)), A.max, A.add)
+                             for a, b in runs], calls=len(runs))
+
+    def extend(m):
+        lim, z = ALIM[m], PAIR.get(m)
+        cu = ("CU" if z is None else "CP", m)
         part[0] = "ext%d" % m
-        empty = m == 5
-        if not empty:
-            vec(256 * GAM, segs(tab, lim) + [lkey, ("NM", m), ("off", m)], [(cu, 0)],
-                lambda g, T, B: [g.vector.tensor_tensor(T.cur[:], T[tab][:, 16:16 + lim].indirect(lst(T)), T.NM[:, m * S:m * S + S], A.max)])
+
+        def current(k, tab, out, key):
+            lst, lkey = opener[k]
+            vec(0, segs(tab, ALIM[k]) + [lkey, ("NM", k), ("off", k)], [(cu, key)],
+                lambda g, T, B: [g.vector.tensor_tensor(out(T), TB(T, tab, 0, ALIM[k]).indirect(lst(T)), T.NM[:, k * S:k * S + S], A.max)], gn=S)
+        if z is None:
+            current(m, "U", lambda T: T.cur[:], 0)
+        else:
+            current(m, "U", lambda T: T.cur3[:, 0:S], 2)
+            copy(S, [(cu, 2)], [(cu, 0)], lambda T: T.cur2[:, :, 16:32], lambda T: T.cur3[:, 0:S])
+            if z == PAIR[min(PAIR)]:
+                copy(S, [("NM", z), ("off", z)], [(cu, 1)], lambda T: T.cur2[:, :, 0:16], lambda T: T.NM[:, z * S:z * S + S])
+            else:
+                current(z, "Z", lambda T: T.cur3[:, S:2 * S], 3)
+                copy(S, [(cu, 3)], [(cu, 1)], lambda T: T.cur2[:, :, 0:16], lambda T: T.cur3[:, S:2 * S])
         for u in range(15, -1, -1):
-            add("v", VF + 16 * CFG["sca"] * CY, [("NM", m) if empty else (cu, 0), ("off", m), ("init", 0)], segs(tab, lim),
-                lambda g, T, B, u=u: [g.vector.tensor_copy(T[tab][:, 0:16 + lim].indirect(T.off[:, 32 * m + 2 * u:32 * m + 2 * u + 1]),
-                                                           T.NM[:, m * S + 16 * u:m * S + 16 * u + 16] if empty else T.cur[:, 16 * u:16 * u + 16])])
+            if z is None:
+                add("v", [(cu, 0), ("off", m), ("init", 0)], segs("U", lim),
+                    lambda g, T, B, u=u: [g.vector.tensor_copy(TB(T, "U", -16, lim).indirect(T.off[:, OFF[m] + 2 * u:OFF[m] + 2 * u + 1]), T.cur[:, 16 * u:16 * u + 16])], sn=16)
+            else:
+                add("v", [(cu, 0), (cu, 1), ("off", m), ("off", z), ("init", 0)], segs("U", lim) + segs("Z", 2432),
+                    lambda g, T, B, u=u: [g.vector.tensor_copy(T.U[:, 0:UB + 16 + lim].indirect(T.off[:, OFF[z] + 2 * u:OFF[z] + 2 * u + 2]), T.cur2[:, u, :])], sn=32)
 
     def place(m, k):
-        copy(256, [("cl", k)], [("U", m)], lambda T: T.U[:, 16 + F + m * S:16 + F + m * S + S], lambda T: CL(T, k), name="pl%d" % m)
+        copy(S, [("cl", k)], [("U", m)], lambda T: TB(T, "U", F + m * S, F + m * S + S), lambda T: CL(T, k), name="pl%d" % m)
 
     def readout(m, gs, fix):
-        body("R%d" % m, gs, lambda T: [T.n16[:, m * S:m * S + S]], [("n16", m)], 1, fix, None)
+        body("R%d" % m, gs, lambda T: [XN(T, 4 + m)], [("XE", 4 + m)], 1, fix, None)
 
     def refetch(sem, slot, ms, f0, lim):
         n = len(ms)
         nm = "gF%d" % slot
         dma("y", sem, 0.5, [("U", m) for m in ms], [("fx32", f0)],
-            lambda g, T, B: [g.sync.dma_start(T.fx32[:, 16 * (f0 + m):16 * (f0 + m) + 16], T.U[slot::16, 16 + F + m * S:16 + F + m * S + S]) for m in ms], n=n, name=nm)
+            lambda g, T, B: [g.sync.dma_start(T.fx32[:, 16 * (f0 + m):16 * (f0 + m) + 16], T.U[slot::16, UB + 16 + F + m * S:UB + 16 + F + m * S + S]) for m in ms], n=n, name=nm)
         copy(16 * n, [("fx32", f0)], [("fxu", f0)], lambda T: T.fxu[:, 16 * f0:16 * (f0 + n)], lambda T: T.fx32[:, 16 * f0:16 * (f0 + n)], name=nm)
-        vec(256 * n * GAM, segs("P", lim) + [("fxu", f0)], [("Gf", f0 + m) for m in ms],
-            lambda g, T, B: [g.vector.tensor_scalar(T.Gf[:, f0 * S:(f0 + n) * S], T.P[:, 0:lim].indirect(T.fxu[:, 16 * f0:16 * (f0 + n)]), -2048.0, None, A.add)], name=nm)
+        vec(0, segs("P", lim) + [("fxu", f0)], [("Gf", f0 + m) for m in ms],
+            lambda g, T, B: [g.vector.tensor_scalar(T.Gf[:, f0 * S:(f0 + n) * S], T.P[:, 0:lim].indirect(T.fxu[:, 16 * f0:16 * (f0 + n)]), -2048.0, None, A.add)], gn=S * n, name=nm)
 
-    def stl(l):
-        return (lambda T: T.stu[:, 16 * l:16 * l + 16]), ("stu", 0)
+    def stl(l, n=1):
+        return (lambda T: T.stu[:, 16 * l:16 * (l + n)]), ("stu", 0)
 
     def bl(m):
         return (lambda T: T.b16[:, 16 * m:16 * m + 16]), ("b16", m)
 
-    for l in range(3):
-        take("U", F, *stl(l), l, "c%d" % l)
+    take(F, *stl(0), 0, "c0")
+    take(F, *stl(1, 2), 1, "c1", 2)
     opener = {0: stl(0), 1: bl(0), 2: stl(1), 3: bl(1), 4: bl(3), 5: bl(2), 6: stl(2)}
     elect(0, 0)
     elect(2, 1)
@@ -407,54 +555,54 @@ def build():
             elect(5, 5)
         if m in (1, 3, 4):
             elect(m, 3 + {1: 0, 3: 1, 4: 3}[m])
-        targets(m, *opener[m])
-        extend(m, "U", *opener[m])
+        if m == 0:
+            targets((0, 2, 6), stl(0, 3)[0], [("stu", 0)])
+        elif m == 4:
+            targets((5, 4), lambda T: T.b16[:, 32:64], [("b16", 2), ("b16", 3)])
+        elif m != 2:
+            targets((m,), opener[m][0], [opener[m][1]])
+        extend(m)
         if m == 3:
             refetch("fx3", 3, [0], 0, 2688)
         if m == 4:
             refetch("fx4", 4, [0, 1], 1, 2944)
-        take("U", BLIM[m], *bl(m), 3 + m, "col%d" % m)
+        take(BLIM[m], *bl(m), 3 + m, "col%d" % m)
         if m == 2:
             send("a_c2", 1, lambda T: CL(T, 5), lambda T: CL(T, 10), ("cl", 5), ("cl", 10))
             place(2, 10)
         elif m < 4:
             place(m, 3 + m)
     elect(6, 2)
-    pool(16 + 2432, [], segs("Z", 2432), lambda g, T, B: [g.iota(T.Z[:], [[0, 16 + 2432]], 0, 0)], name="z0")
-    for m in (5, 6):
-        targets(m, *opener[m])
-        extend(m, "Z", *opener[m])
     for m in (5, 6):
         lst, lkey = bl(m)
         zb, cu, nm = ("zb", m), ("CU", "c%d" % m), "col%d" % m
-        vec(256 * GAM, segs("Z", BLIM[m]) + [lkey, ("pc", 1)], [zb],
-            lambda g, T, B, m=m, lst=lst: [g.vector.tensor_scalar(T.zb[:, (m - 5) * S:(m - 4) * S], T.Z[:, 16:16 + BLIM[m]].indirect(lst(T)), T.pc[:, m - 4:m - 3], None, A.mult)], name=nm)
-        vec(256 * GAM, segs("U", BLIM[m]) + [lkey, zb], [(cu, 0)],
-            lambda g, T, B, m=m, lst=lst: [g.vector.tensor_tensor(T.cur[:], T.U[:, 16:16 + BLIM[m]].indirect(lst(T)), T.zb[:, (m - 5) * S:(m - 4) * S], A.max)], name=nm)
-        copy(256, [(cu, 0)], [("cl", 3 + m)], lambda T, m=m: CL(T, 3 + m), lambda T: T.cur[:], name=nm)
+        vec(0, segs("Z", BLIM[m]) + [lkey, ("pc", 1)], [zb],
+            lambda g, T, B, m=m, lst=lst: [g.vector.tensor_scalar(T.zb[:, (m - 5) * S:(m - 4) * S], TB(T, "Z", 0, BLIM[m]).indirect(lst(T)), T.pc[:, m - 4:m - 3], None, A.mult)], gn=S, name=nm)
+        vec(0, segs("U", BLIM[m]) + [lkey, zb], [(cu, 0)],
+            lambda g, T, B, m=m, lst=lst: [g.vector.tensor_tensor(T.cur[:], TB(T, "U", 0, BLIM[m]).indirect(lst(T)), T.zb[:, (m - 5) * S:(m - 4) * S], A.max)], gn=S, name=nm)
+        copy(S, [(cu, 0)], [("cl", 3 + m)], lambda T, m=m: CL(T, 3 + m), lambda T: T.cur[:], name=nm)
         send("a_c%d" % m, LV[m], lambda T, m=m: CL(T, 3 + m), lambda T, m=m: CL(T, 6 + m), ("cl", 3 + m), ("cl", 6 + m))
+    for u in USES[:7]:
+        mix(u)
     readout(0, ("H", "gE1"), (3, 4))
     readout(1, ("H", "gE3"), (4,))
     readout(3, ("H", "gE4"), ())
     for m, k in ((2, 10), (4, 7), (5, 11), (6, 12)):
         gather(("H", "gR%d" % m), k, F + (m + 1) * S)
         readout(m, ("H", "gR%d" % m), ())
-    for u in USES:
+    for u in USES[7:]:
         mix(u)
     late(3, [0], 0)
     late(4, [0, 1], 1)
-    for t in tasks:
-        if "lock" in t:
-            t["rd"] = [(t["lock"], 0) if k == ("pb", 0) else k for k in t["rd"]]
-            t["wr"] = [(t["lock"], 0) if k == ("pb", 0) else k for k in t["wr"]]
+    [t for t in tasks if t["name"] == "expE0"][0]["n"] += 1500
     return tasks
 
 
 def stage(name):
     kind, u = name[:-2], name[-2:]
     if u[0] in "ERF":
-        return {"g": "g", "mx": "a", "da": "a", "abs": "a", "sc": "s", "d": "z", "exp": "z", "K": "K"}.get(kind, "y") + u
-    return {"b": "el", "senda_n": "sn", "senda_c": "col", "tg": "ext"}.get(name[:-1], name[:-1]) + name[-1]
+        return {"g": "g", "xf": "f", "kp": "a", "mx": "a", "da": "a", "abs": "a", "sc": "s", "d": "z", "exp": "z", "K": "K"}.get(kind, "y") + u
+    return {"b": "el", "cn": "el", "senda_n": "sn", "senda_c": "col", "tg": "ext"}.get(name[:-1], name[:-1]) + name[-1]
 
 
 def link():
@@ -472,25 +620,29 @@ def link():
             lastw[k] = i
             readers[k] = []
         raw.discard(i)
-        t["dep"], t["stage"] = sorted(raw), stage(t["name"])
+        t["dep"], t["stage"], t["dur"] = sorted(raw), stage(t["name"]), span(t, t["eng"], COST)
         t["pre"] = sorted(raw | set(t.get("follow", [])))
         t["syms"] = sorted({k[0] for k in t["rd"] + t["wr"] if isinstance(k[0], tuple)}, key=str)
         t["held"] = sorted({k[0][0] for k in t["rd"] if isinstance(k[0], tuple)})
+        t["head"] = [s for s in t["syms"] if not any(s in tasks[d]["syms"] for d in t["dep"])]
         t["succ"] = []
         for d in t["pre"]:
             tasks[d]["succ"].append(i)
         for s in t["syms"]:
             users.setdefault(s, []).append(i)
     for t in reversed(tasks):
-        t["way"] = t["dur"] + t["lat"] + t["bw"] + CFG["hop"] + max([tasks[j]["way"] for j in t["succ"]] + [0.0])
+        t["way"] = t["dur"] + t["lat"] * COST["lat"] + t["bw"] * COST["bw"] + COST["hop"] + max([tasks[j]["way"] for j in t["succ"]] + [0.0])
     return tasks, users
 
 
-def plan(linked=None):
+def plan(linked=None, fast=False, urgency=None, bound=None):
     tasks, users = linked or link()
-    n, HOP, VF = len(tasks), CFG["hop"], CFG["vf"]
-    bias, hold, shy = CFG["bias"], CFG["hold"], CFG["shy"]
-    pr = [1000.0 - i if t["name"] == "ld" else CFG["alpha"] * t["way"] + sum(hold.get(p, 0.0) for p in t["held"]) + bias.get(t["stage"], 0.0) for i, t in enumerate(tasks)]
+    n, HOP = len(tasks), COST["hop"]
+    hold, shy = CFG["hold"], CFG["shy"]
+    rank = {s: k for k, s in enumerate(CFG["order"].split())}
+    pr = [1000.0 - i if t["name"] == "ld" else CFG["alpha"] * t["way"] + sum(hold.get(p, 0.0) for p in t["held"]) - CFG["beta"] * rank[t["stage"]]
+          + CFG["lift"].get(t["stage"], 0.0) + CFG["lift"].get(t["stage"][:-1], 0.0) for i, t in enumerate(tasks)]
+    pr = urgency or pr
     mark = {t["name"]: i for i, t in enumerate(tasks)}
     gate = [mark.get(CFG["gate"].get(t["stage"])) for t in tasks]
     opens = {}
@@ -501,35 +653,171 @@ def plan(linked=None):
             left[i] += 1
     at, end, eng, dur, inn = [None] * n, [None] * n, [t["eng"] for t in tasks], [t["dur"] for t in tasks], [None] * n
     free = {e: 0.0 for e in ("v", "s", "t", "p", "y", None, "dma")}
-    tenant = {p: [None] * c for p, c in dict(POOLS, PB=1, **CFG["pools"]).items()}
-    slot, before, order, last, joined = {}, {}, [], {}, set()
+    first = {("X", k): ("XI", k) for k in range(CFG["pools"]["X"])}
+    tenant, slot, before = dict(first), {s: x for x, s in first.items()}, {s: [] for s in first.values()}
+    order, last, joined = [], {}, set()
     busy = {s: [len(v), 0.0] for s, v in users.items()}
-    ready = [i for i in range(n) if left[i] == 0]
-    while ready:
-        cand, lend = [], {}
-        for i in ready:
+    piece, lent, lend = [t.get("piece") for t in tasks], [False] * n, {}
+    ready, cands = {e: [] for e in free if e != "dma"}, {}
+    turn = {p: [x for x in v.split() if (p, x) in users] for p, v in CFG["turn"].items()}
+
+    def enter(j):
+        for e in [eng[j]] if piece[j] is None else ["v"] * (piece[j] == 0) + ["s"] * (piece[j] == 15):
+            ready[e].append(j)
+            cands.pop(e, None)
+
+    def offer(e):
+        out = []
+        for i in ready[e]:
+            urge = -pr[i]
+            if piece[i] is not None:
+                urge += shy.get(tasks[i]["name"], 0.0) * (e == "s") - CFG["stick"] * (last.get(e) == i + (1 if e == "s" else -1))
+            if lent[i]:
+                out.append((inn[i], urge, i, ()))
+                continue
             t = tasks[i]
-            if "piece" in t:
-                front = t["piece"] == 0 or end[i - 1] is not None and eng[i - 1] == "v"
-                back = t["piece"] == 15 or end[i + 1] is not None and eng[i + 1] == "s"
-                if not (front or back):
-                    continue
             if inn[i] is None:
                 inn[i] = max([end[d] + HOP for d in t["dep"]] + [0.0 if gate[i] is None else at[gate[i]]])
             a, got = inn[i], []
             for s in t["syms"]:
+                if s in slot:
+                    a = max([a] + [busy[o][1] + HOP for o in before[s]])
+                    continue
+                if s[0] in turn and turn[s[0]][0] != s[1]:
+                    break
+                if s[0] not in lend:
+                    lend[s[0]] = [(max([busy[tenant[x]][1] + HOP for x in us if x in tenant] + [0.0]), c) for c, us in enumerate(LEND[s[0]])
+                                  if not any(x in tenant and busy[tenant[x]][0] for x in us)]
+                can = lend[s[0]]
+                if not can:
+                    break
+                b = min(can)
+                if s[0] == "Q":
+                    b = ([c for c in can if c[0] <= free[e]] + [b])[0]
+                a = max(a, b[0])
+                got.append((s, b[1]))
+            else:
+                if not got:
+                    lent[i], inn[i] = True, a
+                out.append((a, urge, i, got))
+        return out
+    least = [dur[i] - (piece[i] is not None) * COST["vf"] for i in range(n)]
+    rem = sum(least[i] for i in range(n) if eng[i] in ("v", "s"))
+    for i in range(n):
+        if left[i] == 0:
+            enter(i)
+    while any(ready.values()):
+        t0 = e = None
+        for q in ready:
+            if q not in cands:
+                c = offer(q)
+                cands[q] = (c, max(free[q], min(c)[0]) if c else None)
+            if cands[q][1] is not None and (t0 is None or cands[q][1] < t0):
+                t0, e = cands[q][1], q
+        if t0 is None:
+            raise ValueError("no buffer to lend")
+        mine = sorted([c[1:3] + (max(c[0], free[e]), c[3]) for c in cands.pop(e)[0] if c[0] <= t0 + CFG["wait"]])
+        now = [c for c in mine if c[2] <= t0 + CFG["slack"]]
+        pick = now[0]
+        for h in mine:
+            if h[0] > pick[0] - CFG["gap"]:
+                break
+            if h[2] + CFG["tol"] < pick[2] + dur[pick[1]]:
+                fit = [c for c in now if c[2] + dur[c[1]] <= h[2] + CFG["tol"]]
+                pick = fit[0] if fit else h
+                break
+        _, i, a, got = pick
+        t = tasks[i]
+        for s, c in got:
+            us = LEND[s[0]][c]
+            before[s] = sorted({tenant[x] for x in us if x in tenant}, key=str)
+            tenant.update({x: s for x in us})
+            slot[s] = us[0]
+            if s[0] in turn:
+                turn[s[0]].pop(0)
+        ready[e].remove(i)
+        if piece[i] is not None:
+            step, other = (1, "s") if e == "v" else (-1, "v")
+            if last.get(e) == i - step and tasks[i - step]["name"] == t["name"]:
+                joined.add(i)
+            dur[i] = span(t, e, COST, i in joined)
+            if i in ready[other]:
+                ready[other].remove(i)
+                cands.pop(other, None)
+            else:
+                ready[e].append(i + step)
+        last[e], eng[i], at[i] = i, e, a
+        done = a + dur[i]
+        if e:
+            free[e] = done
+        lat = t["lat"] * COST["lat"]
+        if t["bw"]:
+            free["dma"] = max(done + lat / 2, free["dma"]) + t["bw"] * COST["bw"]
+            done = free["dma"] - lat / 2
+        end[i] = done + lat
+        for s in t["syms"]:
+            busy[s][0] -= 1
+            busy[s][1] = max(busy[s][1], end[i])
+            if got or not busy[s][0]:
+                lend.clear()
+                cands.clear()
+        order.append(i)
+        if bound and e in ("v", "s"):
+            rem -= least[i]
+            if free["v"] + free["s"] + rem > bound:
+                raise ValueError("bound")
+        for j in t["succ"] + opens.get(i, []):
+            left[j] -= 1
+            if left[j] == 0:
+                enter(j)
+    if len(order) < n:
+        raise ValueError("a gate closes a loop")
+    raw = [t["dep"] for t in tasks]
+    for s, os_ in before.items():
+        for j in users[s] if os_ else ():
+            if s in tasks[j]["head"]:
+                raw[j] = raw[j] + [k for o in os_ for k in users[o]]
+    if fast:
+        return eng, joined, raw, order, max(end)
+    out = [dict(t, eng=eng[i], at=at[i], end=end[i], dur=dur[i], raw=set(raw[i]), joined=i in joined) for i, t in enumerate(tasks)]
+    return out, order, slot, max(end)
+    while ready:
+        cand = []
+        for i in ready:
+            q = piece[i]
+            if q is not None:
+                front = q == 0 or end[i - 1] is not None and eng[i - 1] == "v"
+                back = q == 15 or end[i + 1] is not None and eng[i + 1] == "s"
+                if not (front or back):
+                    continue
+            elif lent[i]:
+                a, e = inn[i], eng[i]
+                cand.append((a if a > free[e] else free[e], -pr[i], i, (), e))
+                continue
+            t = tasks[i]
+            if inn[i] is None:
+                inn[i] = max([end[d] + HOP for d in t["dep"]] + [0.0 if gate[i] is None else at[gate[i]]])
+            a, got = inn[i], []
+            if all(s in slot for s in t["syms"]):
+                lent[i] = True
+                a = inn[i] = max([a] + [busy[o][1] + HOP for s in t["syms"] for o in before[s]])
+            for s in () if lent[i] else t["syms"]:
                 if s not in slot:
                     if s[0] not in lend:
-                        lend[s[0]] = min([(0.0 if o is None else busy[o][1] + HOP, c) for c, o in enumerate(tenant[s[0]]) if o is None or busy[o][0] == 0] + [(None,)], key=lambda x: (x[0] is None, x))
-                    b = lend[s[0]]
-                    if b[0] is None:
+                        lend[s[0]] = [(max([busy[tenant[x]][1] + HOP for x in us if x in tenant] + [0.0]), c) for c, us in enumerate(LEND[s[0]])
+                                      if not any(x in tenant and busy[tenant[x]][0] for x in us)]
+                    can = lend[s[0]]
+                    if not can:
                         break
+                    b = min(can)
+                    if s[0] == "Q":
+                        b = ([c for c in can if c[0] <= free[eng[i]]] + [b])[0]
                     a = max(a, b[0])
                     got.append((s, b[1]))
-                elif before[s] is not None:
-                    a = max(a, busy[before[s]][1] + HOP)
+                else:
+                    a = max([a] + [busy[o][1] + HOP for o in before[s]])
             else:
-                if "piece" in t:
+                if q is not None:
                     if front:
                         cand.append((max(a, free["v"]), -pr[i], i, got, "v"))
                     if back:
@@ -537,9 +825,9 @@ def plan(linked=None):
                 else:
                     cand.append((max(a, free[eng[i]]), -pr[i], i, got, eng[i]))
         if not cand:
-            raise ValueError("no buffer to lend: %s %s" % ([(tasks[i]["name"], tasks[i]["syms"]) for i in ready], {p: [o for o in v if o and busy[o][0]] for p, v in tenant.items()}))
-        t0, _, _, _, e = min(cand, key=lambda c: c[:3])
-        mine = sorted([c for c in cand if c[4] == e], key=lambda c: c[1:3])
+            raise ValueError("no buffer to lend")
+        t0, _, _, _, e = min(cand)
+        mine = sorted([c for c in cand if c[4] == e and c[0] <= t0 + CFG["wait"]], key=lambda c: c[1:3])
         now = [c for c in mine if c[0] <= t0 + CFG["slack"]]
         pick = now[0]
         for h in mine:
@@ -552,23 +840,28 @@ def plan(linked=None):
         a, _, i, got, _ = pick
         t = tasks[i]
         for s, c in got:
-            before[s] = tenant[s[0]][c]
-            tenant[s[0]][c] = s
-            slot[s] = c
-        if "piece" in t and last.get(e) == (i - 1 if e == "v" else i + 1) and tasks[last[e]]["name"] == t["name"]:
-            joined.add(i)
-            dur[i] -= VF
+            us = LEND[s[0]][c]
+            before[s] = sorted({tenant[x] for x in us if x in tenant}, key=str)
+            tenant.update({x: s for x in us})
+            slot[s] = us[0]
+        if "piece" in t:
+            if last.get(e) == (i - 1 if e == "v" else i + 1) and tasks[last[e]]["name"] == t["name"]:
+                joined.add(i)
+            dur[i] = span(t, e, COST, i in joined)
         last[e], eng[i], at[i] = i, e, a
         done = a + dur[i]
         if e:
             free[e] = done
+        lat = t["lat"] * COST["lat"]
         if t["bw"]:
-            free["dma"] = max(done + t["lat"] / 2, free["dma"]) + t["bw"]
-            done = free["dma"] - t["lat"] / 2
-        end[i] = done + t["lat"]
+            free["dma"] = max(done + lat / 2, free["dma"]) + t["bw"] * COST["bw"]
+            done = free["dma"] - lat / 2
+        end[i] = done + lat
         for s in t["syms"]:
             busy[s][0] -= 1
             busy[s][1] = max(busy[s][1], end[i])
+            if got or not busy[s][0]:
+                lend.clear()
         order.append(i)
         ready.remove(i)
         for j in t["succ"] + opens.get(i, []):
@@ -580,25 +873,45 @@ def plan(linked=None):
     out = [dict(t, eng=eng[i], at=at[i], end=end[i], dur=dur[i], raw=set(t["dep"])) for i, t in enumerate(tasks)]
     for i in joined:
         out[i]["joined"] = True
-    for s, o in before.items():
-        for j in users[s] if o is not None else ():
+    for s, os_ in before.items():
+        for j in users[s]:
             if not any(s in tasks[d]["syms"] for d in tasks[j]["dep"]):
-                out[j]["raw"].update(users[o])
+                for o in os_:
+                    out[j]["raw"].update(users[o])
     return out, order, slot, max(end)
 
 
 def rank_program(g, core, T, topo):
     rank = T.rank_of(core)
-    if rank is None:
+    cores = list(T.cores)
+    helper = {c: [h for h in topo.cores_of(c) if h not in cores and topo.die(h) == topo.die(c)][0] for c in cores}
+    if rank is None and core not in helper.values():
         return
     if not _PLAN:
         _PLAN.append(plan())
     tasks, order, slot, _ = _PLAN[0]
-    cores = list(T.cores)
-    Q = {"v": g.vector, "s": g.scalar, "t": g.tensor, "p": g, "y": g.sync}
 
     def B(s):
-        return T[s[0] + str(slot[s])]
+        p, k = slot[s]
+        return 512 * k if p == "PS" else T[p + str(k)]
+
+    def far(u):
+        k = USES.index(u)
+        return T["D%d" % (k // 8)][:, k % 8 * S:k % 8 * S + S]
+    if rank is None:
+        home = [c for c in cores if helper[c] == core][0]
+        rid, pid, _ = topo.addr(home)
+        sent = 0
+        for i in order:
+            u = tasks[i].get("fold")
+            if u and tasks[i]["eng"]:
+                g.wait_ge(T.sem["y" + u], len(topo.engines(home, core)))
+                g.remote_dma(tasks[i]["home"](T, B), far(u), T.sem["k" + u], T.sem.sent, pid, rid, topo.mask(core, home))
+                sent += len(topo.engines(core, home))
+        if sent:
+            g.wait_ge(T.sem.sent, sent)
+        return
+    Q = {"v": g.vector, "s": g.scalar, "t": g.tensor, "p": g, "y": g.sync}
 
     needed = set()
     for i in order:
@@ -611,7 +924,7 @@ def rank_program(g, core, T, topo):
         if t.get("joined"):
             continue
         if e is None:
-            count[sem] = len(topo.engines(cores[(rank - LV[int(sem[-1])]) % len(cores)], core))
+            count[sem] = len(topo.engines(helper[core] if "fold" in t else cores[(rank - LV[int(sem[-1])]) % len(cores)], core))
             sig[i] = (sem, count[sem])
             continue
         want = {}
@@ -638,6 +951,12 @@ def rank_program(g, core, T, topo):
             rid, pid, _ = topo.addr(to)
             g.remote_dma(dst, src, T.sem[sm], T.sem.sent, pid, rid, topo.mask(core, to))
             count["sent"] = count.get("sent", 0) + len(topo.engines(core, to))
+        elif "fold" in t:
+            rid, pid, _ = topo.addr(helper[core])
+            g.remote_dma_fused([RemoteDMATransfer(dst_ids=[DstId(rid=rid, pnc=pid)], dma_engine_mask=topo.mask(core, helper[core]), remote_sem=T.sem["y" + t["fold"]],
+                                                  srcs=ins[0], dsts=[far(t["fold"])], alu_op=1)], local_sem=T.sem[sem])
+            count[sem] = len(topo.engines(core, helper[core]))
+            sig[i] = (sem, count[sem])
         elif sem:
             for x in ins:
                 x.then_inc(T.sem[sem], 16)

@@ -1,5 +1,4 @@
 import math
-from concourse.bass import DstId, RemoteDMATransfer
 from concourse.mybir import AluOpType, ActivationFunctionType
 
 A = AluOpType
@@ -11,38 +10,53 @@ BLIM = (1664, 1920, 1664, 2176, 2688, 2432, 1664)
 ALIM = (1664, 1664, 1664, 1920, 2176, 1664, 1664)
 KIDS = {2: (0, 1), 5: (3, 4), 6: (2, 5)}
 PAIR = {1: 6, 4: 5}
+HELD = {0: 0, 1: 3, 4: 6}
+NMB = {2: 0, 3: 1, 5: 2, 6: 3}
 OFF = {0: 0, 2: 32, 6: 64, 1: 65, 3: 96, 5: 128, 4: 129}
 UB = 16 + 2432
 BASE = {"Z": 0, "U": UB}
 BIG = 2.0 ** 25
 USES = ["E%d" % _k for _k in range(7)] + ["R%d" % _k for _k in range(7)]
-COST = dict(gam=1.5, sca=3.5, cy=0.001, pc=0.0005, vf=0.05, sf=0.065, hop=0.22, issue=0.9, lat=1.8, bw=1.3, send=1.2, hw=0.3, pf=1.05)
-CFG = dict(slack=0.05, gap=5.0, tol=0.2, wait=0.3, alpha=0.02, shy={}, gate={}, hold={},
-           order="c x c0 fE0 gE0 aE0 sE0 el0 z0 cv nm ext0 sn0 col0 c1 fx fE1 hb gE1 aE1 sE1 el1 sn1 ext6 ext1 col1 pl0 n0 sE2 el2 fE3 ext2 col2 sn2 pl1 n1 pl2 n2 "
-                 "gE3 aE3 sE3 el3 sn3 ext3 col3 pl3 n3 fE4 xb xc lt x4 sE6 el6 sn6 sE5 el5 sn5 sE4 el4 sn4 n4 ext5 ext4 col4 col5 col6 n5 n6 "
-                 "yE0 zE0 gE2 aE2 yE2 zE2 yE1 KE2 zE1 fR0 yR0 zR0 aR0 yE3 zE3 fR1 yR1 zR1 aR1 yE6 zE6 aE6 gE6 aE4 gE4 yE5 zE5 aE5 gE5 yE4 KE5 KE6 zE4 fR3 yR3 zR3 aR3 "
-                 "gF3 gF4 yF3 yF4 aF3 aF4 zF3 zF4 fR2 yR2 zR2 aR2 gR2 fR4 yR4 zR4 aR4 gR4 fR5 yR5 zR5 aR5 gR5 fR6 yR6 zR6 aR6 gR6",
-           route=dict(E0="T", E1="T", E2="A", E3="T", E4="T", E5="A", E6="A", R0="N", R1="N", R2="N", R3="N", R4="N", R5="T", R6="T"),
-           factor=("R2", "R3"), total={_u: "dma" for _u in USES}, spread={0: "v"}, split={}, names=(), keep=(), wide=(), beta=1.0, lift={}, stick=0.0, turn={},
-           pools=dict(H=4, MX=2, X=3, D=8, Y=2))
-CFG.update({'order':'c0 aE3 cv sn0 el0 el1 z0 gE1 el2 n0 nm x aE0 c1 sE0 gE0 el4 aE1 ext0 c sE1 zE0 fE3 ext6 sn1 sE2 fE4 ext1 pl0 col2 ext2 sn2 col1 hb n1 fE0 n3 col3 fE1 ext5 gE3 pl1 sE3 ext3 x4 col0 n2 el3 pl2 aE2 xc lt sn6 fx zR0 el6 el5 zE2 yR0 sE6 sE5 zE3 col6 zE1 n5 gE2 sn4 aR0 yR1 aR3 aE4 sn5 fR1 KE2 sE4 ext4 xb aE6 aE5 yE1 gR4 KE6 zE4 gE5 fR4 gE6 yE2 col4 zF4 yR2 aF3 zR6 n6 fR3 fR0 gF4 gE4 aF4 yR4 fR5 col5 fR2 fR6 gF3 zR1 zR5 yR5 zE6 yF3 zR2 zF3 yE6 aR6 yE4 aR1 aR4 zE5 zR3 aR2 yE5 sn3 aR5 yR3 KE5 zR4 gR2 yE0 gR5 yR6 yF4 pl3 gR6 n4 yE3','hold':{'H':2,'EL':-1,'Q':1,'PB':-16,'D':-3},'gate':{},'shy':{'gR4':126,'gR5':145,'gE4':-12},'route':{'E0':'A','E1':'N','E2':'A','E3':'N','E4':'A','E5':'A','E6':'A','R0':'A','R1':'N','R2':'N','R3':'N','R4':'N','R5':'N','R6':'T'},'total':{'E0':'dma','E1':'h3','E2':'dma','E3':'dma','E4':'dma','E5':'h3','E6':'dma','R0':'dma','R1':'dma','R2':'dma','R3':'dma','R4':'h2','R5':'vec','R6':'dma'},'factor':('R1','R4','R5'),'spread':{'R44':'v'},'split':{'R6':2},'gap':10,'wait':0.15,'tol':0.3,'slack':0.05,'alpha':0.1})
-CFG.update({'order':'zE4 cv n0 sE2 sn0 gE1 c0 zE0 aE3 el0 x c aE0 nm gE0 fE1 sE0 sE1 zE3 ext0 sE5 el2 pl0 ext6 el1 z0 fE3 el4 sn1 aE1 ext1 n3 ext2 fE0 fx hb yR0 ext5 yR1 xc col3 pl2 fE4 col1 n1 c1 sE3 el3 n2 sn2 x4 lt zE1 gE3 ext3 col0 n5 el5 zE2 aE2 zR0 n6 sE4 sE6 aR3 sn6 fR5 sn4 col2 el6 yR4 fR1 col6 aR0 aF3 ext4 aE4 gE2 yR2 fR3 aF4 pl1 KE2 zR6 yE1 gR4 gF3 aE5 xb yF3 sn5 gE6 fR4 gE5 fR0 zR1 col4 yE2 fR2 aE6 yR5 gE4 yE6 KE6 zF3 zE6 aR4 yE4 zR2 aR1 yE5 zE5 aR5 aR6 yR3 zF4 aR2 gF4 zR5 zR3 pl3 zR4 n4 KE5 gR5 yR6 col5 yE0 fR6 yE3 sn3 yF4 gR6 gR2','hold':{'H':2,'PB':-28,'D':-3,'TG':-9,'MX':-2},'gate':{},'shy':{'gR4':95,'gR6':-14,'gE6':-31},'route':{'E0':'A','E1':'N','E2':'A','E3':'N','E4':'A','E5':'A','E6':'A','R0':'A','R1':'N','R2':'N','R3':'N','R4':'N','R5':'N','R6':'T'},'total':{'E0':'dma','E1':'h3','E2':'dma','E3':'h2','E4':'dma','E5':'h3','E6':'dma','R0':'dma','R1':'dma','R2':'dma','R3':'dma','R4':'vec','R5':'vec','R6':'dma'},'factor':('E1','R1','R5'),'spread':{'R44':'v','R11':'v'},'split':{'R6':2},'gap':10,'wait':0.15,'tol':0.3,'slack':0.05,'alpha':0.1})
-CFG.update({'order':'sE1 el0 n0 aE0 aE3 el1 zE0 el2 xc sE5 pl2 cv fE1 fE0 n1 el4 zE3 sE2 sn0 c0 fx pl0 x gE1 zE4 ext0 c nm gE0 aE1 sn1 ext6 col3 c1 fE4 z0 el3 fE3 ext1 ext5 sE0 yR1 sE3 ext2 col1 n3 n2 hb sn2 x4 sE4 yR0 lt col0 gE3 el5 ext3 n5 zR0 el6 aR3 yR4 zE1 fR3 aE2 xb fR5 col6 ext4 aF3 sn6 aE4 n6 sE6 fR1 zE2 sn4 aR0 col2 aR1 KE2 gE2 yR2 zR6 yE1 aE5 gR4 aF4 fR4 yR5 gE4 fR2 pl1 zR1 sn5 gE6 yE5 fR0 aE6 zR5 zE6 yE4 zF3 yR3 zR4 col4 aR6 fR6 gE5 gF3 aR2 gF4 aR4 KE6 aR5 zR3 pl3 yE2 col5 sn3 zE5 yF3 yR6 yF4 yE6 zR2 gR5 zF4 gR2 n4 KE5 gR6 yE0 yE3','lift':{},'beta':1.0,'hold':{'PB':-21,'D':-8,'MX':3,'Y':-8},'gate':{'gF4':'col5'},'shy':{'gR4':123,'gE6':-25,'gR2':60,'gE5':-24,'gE4':15,'gR5':23},'route':'ANANAAAANNNNNT','total':'fold dma fold fold fold fold fold fold fold fold fold vec vec fold','factor':('E1','R1','R3','R5'),'names':(),'keep':(),'wide':('E2',),'spread':{'R44':'v','R11':'v'},'split':{'R6':2},'gap':20,'wait':0.15,'tol':0.3,'slack':0.05,'alpha':0.1})
-CFG.update({'turn':{'H':'gE0 gE2 gE6 gE1 gE3 gE5 gE4 gR2 gR4 gR6 gR5','MX':'E0 E1 R0 E3 R1 R3 R2 E4 R6 R4 R5','X':'E0 E1 E3 R0 R1 E4 R3 R2 R4 R5 R6'},'stick':0,'order':'el2 ext1 sn0 c ld z0 fE3 nm el0 fR0 x cv x4 c1 ext6 n1 ext0 gE0 n0 c0 fE0 aE0 lt sE1 el1 n3 pl0 col0 sn2 sE3 aE1 pl1 fR1 sE0 fE1 sn1 aE2 fE4 col1 ext5 n2 col3 gE2 sE2 gE1 zE0 col2 yE0 el3 ext2 gE6 col6 sn6 sE5 zR0 gE3 ext3 pl2 zE3 aE3 fR2 aR0 ext4 pl3 sn3 zE2 gE4 n6 el5 el6 fR3 el4 yF4 sE6 zE1 col4 sn4 aE6 gR4 n4 fR4 aF3 yE2 zE5 gE5 sn5 col5 aF4 gF4 n5 fR5 aE5 aE4 sE4 zE6 KE2 gF3 aR3 aR4 aR1 yR0 zR1 yE1 fR6 yE3 zE4 zR3 yR5 yR1 yR3 zF3 gR2 aR2 yE4 gR6 yF3 zR5 KE6 zR2 zR4 yR4 zR6 aR5 aR6 KE5 yE5 gR5 yE6 yR2 yR6 zF4','lift':{},'beta':1.0,'hold':{'PD':22,'CP':-3,'PB':8,'CU':2,'EL':-7,'H':2},'gate':{'el2':'gE1'},'shy':{'gR4':129,'gE6':-37,'gE3':10,'gR5':-28,'gE4':24},'route':'ANANAAAANNNANT','total':'dma h3 dma h2 dma h2 dma dma dma dma dma vec vec pe','factor':('E1','R1','R5'),'names':('E0','E1','E2','E6'),'keep':('R4','R5','R6'),'wide':('E0','E2','E4','E6'),'spread':{},'split':{},'gap':5,'wait':0.15,'tol':0.3,'slack':0.05,'alpha':0.4})
-CFG.update({'turn':{'H':'gE0 gE2 gE6 gE1 gE3 gE5 gR2 gE4 gR4 gR6 gR5','MX':'E1 E3 R0 E0 E4 R1 R3 R2 R5 R6 R4','X':'R0 E3 E1 R1 R3 E0 R4 E4 R2 R6 R5'},'stick':10,'order':'x c n0 pl1 gE3 c0 z0 col1 k1 gE0 cv c1 fE0 aE0 sn0 ext0 fR0 sE0 x4 f0 nm ld fE1 gE2 k2 el0 ext1 col0 gE1 sE2 aE1 sn1 gE6 zE2 nn el2 sE1 fE3 fE4 sE6 aE2 lt pl0 el1 sn2 zE1 n6 gE4 ext2 aE6 aE3 n1 sE3 zE0 el6 n2 ext3 col4 col2 ext5 el3 col3 fR3 aE4 sE4 zE3 gE5 zE4 sn3 fR2 sn6 n3 ext4 aR0 fR6 gF4 fR1 sE5 el4 el5 pl2 zR1 zE6 sn4 aE5 yE1 aR1 gR2 yE2 n5 aF3 gF3 aR3 n4 yE0 col6 sn5 fR4 yE4 col5 gR4 zE5 zR0 fR5 aR2 yF3 zF3 pl3 yE6 KE5 yE3 yR0 yF4 yR5 yR2 zR3 zR5 aR5 aR6 gR5 KE2 zR4 aR4 yE5 zR2 gR6 yR1 KE6 aF4 yR3 yR4 yR6 zR6 zF4','lift':{},'beta':1.0,'hold':{'PD':24,'PB':34,'EL':15},'gate':{},'shy':{'gR4':154,'gR2':29},'route':'ANANAAAANNNANT','total':'dma h3 dma h2 dma h2 dma dma h3 dma dma vec vec dma','factor':('E1','R1','R5'),'names':('E0','E1','E2'),'keep':('R6',),'wide':('E2','E4','E6'),'spread':{},'split':{},'gap':5,'wait':0.15,'tol':0.3,'slack':0.05,'alpha':0.4})
-CFG.update({'turn':{'H':'gE0 gE6 gE2 gE1 gE3 gE5 gE4 gR2 gR4 gR6 gR5','MX':'E1 E0 R0 E3 R1 E4 R3 R2 R4 R5 R6','X':'E1 E0 E3 E4 R1 R0 R3 R2 R6 R4 R5'},'stick':0,'order':'n0 x nn ext1 col0 ld pl1 ext0 z0 c0 pl0 c1 nm sn0 cv el0 sE0 gE0 x4 sE2 aE0 c k2 fE0 col1 k1 gE2 aE2 f0 fE3 fE1 lt el1 col4 gE1 n1 sn1 ext2 sn2 sn6 el6 aE1 gE6 fR1 pl2 sE1 col2 sn3 ext3 el3 sE6 zE2 sE3 ext5 gE3 n2 fR0 zE0 n3 fE4 ext4 col3 zF4 sn4 gF4 yE0 el2 yE1 gE4 yE3 n6 sE4 el4 col5 zE1 aE6 zE6 aE3 n4 col6 fR4 el5 yF3 gE5 aR0 zE3 aE4 aR1 yE4 pl3 n5 sE5 yE2 gF3 zE5 fR3 zR0 sn5 gR2 aE5 zR1 yE6 fR2 yE5 yR5 gR6 aR3 gR4 fR5 zE4 aR2 zR3 KE2 yR2 yR0 yR1 aF3 yR3 KE6 aR5 gR5 zR2 zF3 KE5 yF4 zR4 zR6 aR6 yR4 fR6 yR6 aR4 zR5 aF4','lift':{},'beta':1.0,'hold':{'PD':33,'EL':19,'PB':6,'FA':-9,'CP':7,'TG':-1},'gate':{'n0':'expE2'},'shy':{'gR6':60,'gE4':-28,'gE3':8},'route':'ATATTAAANNNANT','total':'dma dma dma h3 dma dma dma h3 dma dma dma vec vec dma','factor':('R1','R3','R5'),'names':('E0','E1'),'keep':('R6',),'wide':('E2','E6'),'spread':{},'split':{},'gap':5,'wait':0.15,'tol':0.3,'slack':0.05,'alpha':0.4})
-CFG.update(route=dict(zip(USES, CFG["route"])), total=dict(zip(USES, CFG["total"].split())))
+COST = dict(gam=1.45, sca=3.3, cy=0.00095, pc=0.00045, vf=0.05, sf=0.065, vp=0.04, sp=0.04, tp=0.01, hop=0.2, issue=0.85, lat=1.7, bw=1.1, send=1.2, hw=0.2, pf=1.0, once=(1.5, 4))
+POOLS = dict(H=4, MX=2, X=3, D=8, Y=2)
+NP = 16
+CFG = dict(route=dict(zip(USES, "ATATTAAANNNANT")), total=dict(dict.fromkeys(USES, "dma"), E2="h3", E5="h3", R4="vec", R5="vec"), factor=("R1", "R3", "R5"),
+           names=("E0", "E1", "E2", "E6"), keep=("R2", "R5", "R6"), back=("E1", "E3", "E4", "R6"), wide=("E2", "E6"), last="R6")
+QUEUES = dict(
+    v="""ld h0 ld cv ld*4 x nm c x ld*2 tg0 c1 c0 k1 gE0*8 gE6 k2 gE2*4 xt gE2*5 tg0 gE6 tg0 gE6 tg0 gE6
+    ext0*2 gE2 ext0 xt ext0 lt ext0 el0 ext0*2 el0 ext0 el0 ext0 lt el0 gE6 ext0 gE6 b0 ext0 gE6 tg1 ext0 gE6 ext0*2 sn0 ext0 tg1 gE6 ext0 tg1 col0 sn0
+    gE1*4 n0 gE1*4 tg1 gE1*2 ext1 el2 ext1 mxE1 ext1 el2 mxE1 el2 ext1 mxE1 ext1 el2 ext1 mxE1 ext1 b2 ext1 sn2 ext1 el1 ext1 el1 ext1 el1 ext1 sn2 ext1 el1 ext1*2 b1
+    ext1 sn1 tg3 col1 ext2 sn1 ext2 lt n1 ext2 gE3 ext2 gE3 ext2 el6 ext2 gE3 ext2 el6 ext2 gE3 ext2 el6 ext2 tg3 ext2 el6 ext2 gE3 ext2 gE3*3 ext2 tg3 b6 ext2 mxE3
+    ext2 sn6 ext2 mxE3 col2 tg3 ext3 mxE3 ext3 mxE3 el3 ext3 gE5 ext3 gE5 ext3 yE1 ext3 gE5 sn6 ext3 el3 ext3 el3 ext3 gE5 ext3 el3 ext3 ext4 gE5*2 ext3 el3 ext3 mxR1 b3
+    el5 ext3 n2 sn3 ext3 gR2 tg5 ext3 mxR1 ext3 sn3 col3 tg5 n3 tg5 gE4*2 gR2*2 mxR1 tg5 ext4 gE4*3 ext4 gE4 ext4 el4 ext4 mxE4 gR2 mxE4 n6 ext4 yE3 mxE4 ext4 gR2*2
+    ext4 mxE4 ext4 gF3 ext4 KE2 ext4 gR2 ext4 el5 ext4 KE2 ext4 el5 ext4 el5 ext4 el5 ext4 KE2 col6 b5 el4 sn5 col5 el4 col6 el4 sn5 mxR2 el4 mxR2 col5 b4
+    mxR3 sn4 mxR3 mxR2 mxR3 sn4 col4 gF4 n5 n4 gR4*5 gR5*6 gR4 gR5 gR4*6 gR6 gR5*4 gR4 yR1 gR6*6 mxR5 gR6*3 mxR5 yE4 mxR5 mxR6*3
+    sumR5 sumR4 sumR5 KE5 sumR5*2 KE5 sumR5 KE5 sumR5 sumR4 KE6 sumR5 sumR4 yR3 yR5 sumR4 yR5 KE6 sumR4*3 yR4 yR6*2""",
+    s="""l_hv l_xs1 l_su1 ld*2 l_th1 ih fx gE0*8 gE2*4 absE0*3 gE2 gE6 gE2 absE0 gE6*4 expE0*2 absE2*2 expE0 gE6*2 absE2 expE0 absE2 absE6
+    gE1*6 absE6 expE2*2 absR0 absE6 expR0 absE6 expE6 expE1 gE3*5 expE1*2 gE3*3 expE6 expE1 absR0 gE5 absR0 gE5*4 absR0 gE5*5 expE3*3 gR2*3 expE3
+    absE5*2 gE4*6 absE5 gE4*4 absE5 expR1*4 expR0*3 gR2*6 absF3 expE5*4 expE4*3 expF3 expE4 expR2 expR3*4 gR4 gR5*5 expR2*2 yR1 expR2 gR6*2 gR4*2
+    absF4 gR6*4 absR4*2 expF4 absR4 expR4 expR5*3 absR4 expR5 expR4 expR6 yR3 expR6 expR4 yR5 expR4 expR6*3 yR6""",
+    t="""xt*2 daE0*3 scE0 tg0 daE0 scE0*3 el0 scE0*4 daE2*3 el0 scE2 daE2 tg1 scE2*3 sn0 daE6*2 scE2*4 mxE1 el2 daE6 daR0 daE6 el2 scE1*4 el1 sn2 scE6*5 el1
+    lt dE1 scE6 sn1 scE6 dE1 scE6 dE1 tg3 el6 sumE1 daR0 dE1 el6 daR0 mxE3 sumE1*2 daR0 sumE1 scE3*4 sn6 dE3 el3 dE3*3 mxR1 el3
+    daE5*2 sn3 sumE3 tg5 sumE3 daE5*2 dR1 sumE3*2 dR1 mxE4 dR1*2 scE5*3 el4 scE5*3 KE2 scE5*2 dF3 scE4 el5 scE4*3 mxR2 el5 dE4 sn5 dE4*2 el4 mxR3 dE4
+    dR2 sn4 dR3*4 dR2*2 mxR5 sumE4*2 dR2 dF4 sumE4*2 mxR6 daR4*3 dR5*3 daR4 dR5 KE5 dR6*2 KE6 dR6 sumR6 dR6*2 sumR6*4""",
+    p="""ld*3 k1 nm xt z0 k2 f0 k1 xi*2 ext0 k2 xt k2 cv k2*2 cn0 xi xfE3 k2 nn xfE1 xfE3 xfE1 cn2 lt cn6 ext1 xfE4 ext1 halfE0 xfE1 xfE3 cn1 pl0 xfE4 lt
+    halfE2 lt kpE1 halfE0 senda_n2 halfE2 halfE0 xfR1 halfE6 xfE4 senda_c2 kpE3 xfR1 pl1 xfR1 halfE2 halfE6 halfE0 senda_n6 xfR2 ext4*2 halfE6 xfR2 pl3 gF3
+    xfR3 halfE6 xfR3*2 halfR1 xfR2 kpE4 halfR0 xfR6 kpR2 halfR1 col6 pl2 halfE5 senda_n5 col5 gF4 senda_c5 halfR0 halfR1 senda_c6 xfR6 halfE5 halfR0
+    halfR1 halfR3 xfR6 xfR5 halfE5 halfR2 kpR5 xfR5*2 halfR3 kpR6 halfR0 halfR2 halfR3 kpR6 halfR2 outF3 halfR3 halfR2 outF4""",
+    y="""l_xs0 l_st cv l_su0 l_th0 cv z0 ext0 nn ext1 gF3 lt outE1 yE0 ext4 yE6 gF4 outE2 outR0 outE4 outR1 outR3 outE5 outR5 outR2 outE3 outE0 outE6 outR4 outR6*2""")
 
 SCRATCH = {
     "P": ("sbuf", [128, W], "int32"), "U": ("sbuf", [128, UB + 16 + 2688], "int32"),
-    "zb": ("sbuf", [128, 512], "float32"), "XE": ("sbuf", [128, 11 * S], "float16"), "x4": ("sbuf", [128, 512], "float16"),
-    "st32": ("sbuf", [128, 48], "int32"), "stu": ("sbuf", [128, 48], "uint16"),
+    "zb": ("sbuf", [128, 512], "float32"), "XE": ("sbuf", [128, 11 * S], "float16"), "XT": ("sbuf", [128, 4 * S], "float16"), "FX": ("sbuf", [128, 4 * S], "float32"),
+    "st32": ("sbuf", [128, 48], "int32"), "stu": ("sbuf", [128, 48], "uint16"), "J": ("sbuf", [128, 64], "bfloat16"),
     "hb": ("sbuf", [128, 16], "bfloat16"), "lam": ("sbuf", [128, 32], "float32"), "LP": ("sbuf", [128, 32], "float16"), "LT": ("sbuf", [128, 128], "float16"),
     "Sel": ("sbuf", [128, 512], "bfloat16"), "Bs": ("sbuf", [128, 32], "float32"),
     "cl": ("sbuf", [128, 13 * S], "uint16"), "b16": ("sbuf", [128, 112], "uint16"), "off": ("sbuf", [128, 7 * 32], "uint16"),
     "fx32": ("sbuf", [128, 48], "int32"), "fxu": ("sbuf", [128, 48], "uint16"), "Gf": ("sbuf", [128, 768], "float16"),
     "C0": ("sbuf", [128, S], "float16"), "C1": ("sbuf", [128, S], "float16"), "pb": ("sbuf", [128, S], "float16"),
-    "snd": ("sbuf", [128, 768], "int32"), "cur": ("sbuf", [128, S], "int32"), "cur2": ("sbuf", [128, 16, 32], "int32"), "cur3": ("sbuf", [128, 2 * S], "int32"), "NM": ("sbuf", [128, 1792], "int32"), "NN": ("sbuf", [128, S], "int32"),
+    "snd": ("sbuf", [128, 768], "int32"), "cur": ("sbuf", [128, S], "int32"), "cur2": ("sbuf", [128, 16, 32], "int32"), "cur3": ("sbuf", [128, S], "int32"),
+    "NM": ("sbuf", [128, 4 * S], "int32"), "NN": ("sbuf", [128, S], "int32"),
     "e1": ("sbuf", [128, 272], "float32"), "e2": ("sbuf", [128, 272], "float32"), "e3": ("sbuf", [128, 272], "float32"),
     "Wm": ("sbuf", [128, S], "float16"), "a16": ("sbuf", [128, 32], "float16"), "Tb": ("sbuf", [128, 2 * S], "bfloat16"),
     "f1": ("sbuf", [128, 2 * S], "float32"), "f2": ("sbuf", [128, 3 * S], "float16"), "f3": ("sbuf", [128, 2 * S], "float32"),
@@ -51,7 +65,7 @@ SCRATCH = {
     "wl32": ("sbuf", [128, 16], "int32"), "wl": ("sbuf", [128, 16], "uint16"),
     "ip": ("sbuf", [128, 8], "int32"), "pc": ("sbuf", [128, 4], "float32"),
     "ones": ("sbuf", [128, 144], "bfloat16"), "Cv": ("sbuf", [128, 1920], "bfloat16"),
-    "dg": ("sbuf", [128, 8 * 128], "bfloat16"), "I32": ("sbuf", [128, 128], "float32"), "FE": ("sbuf", [128, 768], "float32"),
+    "dg": ("sbuf", [128, 8 * 128], "bfloat16"), "FE": ("sbuf", [128, 768], "float32"),
     "GI": ("sbuf", [128, 32], "bfloat16"), "GI32": ("sbuf", [128, 8], "float32"), "Dm": ("sbuf", [128, 136], "bfloat16"),
     "YM": ("sbuf", [128, 1792], "float32"),
     "IH": ("sbuf", [128, 128], "float32"), "FA0": ("sbuf", [128, S], "float32"), "FA1": ("sbuf", [128, S], "float32"),
@@ -59,26 +73,26 @@ SCRATCH = {
 }
 TILES = {"H": ("sbuf", [128, 4096 + 2 * S], "float16"), "MX": ("sbuf", [128, 4096], "float16"), "X": ("sbuf", [128, 2048], "float16"),
          "D": ("sbuf", [128, 2048], "float32"), "Y": ("sbuf", [128, S], "float32")}
-SCRATCH.update({_p + str(_k): TILES[_p] for _p in TILES for _k in range(CFG["pools"][_p])})
-LEND = {_p: [((_p, _k),) for _k in range(_n)] for _p, _n in dict(CFG["pools"], EL=1, TG=1, CU=1, CP=1, C=2, FA=2, PB=1).items()}
+SCRATCH.update({_p + str(_k): TILES[_p] for _p in TILES for _k in range(POOLS[_p])})
+LEND = {_p: [((_p, _k),) for _k in range(_n)] for _p, _n in dict(POOLS, EL=1, TG=1, CU=1, CP=1, C=2, FA=2, PB=1).items()}
 LEND.update(PD=[(("PS", _k), ("PS", _k + 1)) for _k in (0, 2, 4, 6)], Q=[(("PS", _k),) for _k in (7, 6, 5, 4, 3, 2, 1, 0)])
-DMAS = ["cv", "nm0", "nm1", "l_st", "l_su0", "l_su1", "l_th0", "l_th1", "l_xs", "l_hv", "fx3", "fx4", "out", "hF3", "hF4", "oR0", "oR1"]
+DMAS = ["cv0", "cv1", "nm0", "nm1", "z0", "sel", "l_st", "l_su0", "l_su1", "l_th0", "l_th1", "l_xs0", "l_xs1", "l_hv", "fx3", "fx4", "out", "hF3", "hF4", "oR0", "oR1", "r0", "r1", "r4"]
 ARR = ["a_n2", "a_c2", "a_n5", "a_c5", "a_n6", "a_c6"]
-SEMAPHORES = ["v", "s", "t", "p", "sent"] + DMAS + ARR + [_c + _u for _u in USES for _c in "hky"]
+SEMAPHORES = ["v", "s", "t", "p", "sent"] + DMAS + ARR + [_c + _u for _u in USES for _c in "hy"]
 I1, I2, I4, I34, IQ, IM = 0, 1, 2, 3, 4, 7
 
 
 def span(t, e, C, joined=False):
     if t["sem"] and e:
-        return t["calls"] * (C["send"] if t["sem"] == "sent" or "fold" in t else C["issue"] if e == "p" else C["hw"])
+        return t["calls"] * (C["send"] if t["sem"] == "sent" else C["issue"] if e == "p" else C["hw"])
     if e == "t":
-        return 0.03 + t["n"] * C["pc"]
+        return C["tp"] + t["n"] * C["pc"]
     if e == "p":
         return (170 * t["calls"] + 2 * t["n"]) * C["cy"] * C["pf"]
     if e is None:
         return 0.0
     n = t["n"] + t["gn"] * C["gam"] + t["sn"] * C["sca"]
-    return (0 if joined else t["calls"]) * C[e + "f"] + (n if e == "s" or t["sn"] else max(n, 64 * t["calls"])) * C["cy"]
+    return (0 if joined else t["calls"]) * C[e + ("f" if t["gn"] or t["sn"] else "p")] + (n if e == "s" or t["sn"] else max(n, 64 * t["calls"])) * C["cy"]
 
 
 def build():
@@ -101,10 +115,15 @@ def build():
         return add("p", rd, wr, fn, n=n, **kw)
 
     def dma(q, sem, bw, rd, wr, fn, n=1, **kw):
+        if sem[:2] == "l_":
+            kw["name"] = sem
         return add(q, rd, wr, fn, calls=n, sem=sem, lat=1.0, bw=bw, **kw)
 
     def copy(n, rd, wr, out, src, **kw):
         return pool(n, rd, wr, lambda g, T, B: [g.affine_select(out(T), src(T), [[0, n]], A.is_gt, 0.0, 1, 0)], **kw)
+
+    def shift(n, rd, wr, pairs, c, calls=1, name=""):
+        return vec(n, rd, wr, lambda g, T, B: [g.vector.tensor_scalar(o, i, c, None, A.add) for o, i in pairs(T, B)], calls=calls, name=name)
 
     def segs(t, lim):
         return [(t, "o0"), (t, "o1")] + [(t, k) for k in range((lim - F) // S)]
@@ -115,8 +134,8 @@ def build():
     def PS(T, B, s, a, b, step=1, rows=128):
         return T.PS[0:rows, B(s) + a:B(s) + b:step]
 
-    def XN(T, k, a=0, b=S):
-        return T.XE[:, k * S + a:k * S + b]
+    def XN(T, k):
+        return T.XE[:, k // 2 * 2 * S + k % 2:k // 2 * 2 * S + 2 * S:2] if k < 4 else T.XE[:, k * S:k * S + S]
 
     def SL(buf, i, a=0, b=S, kept=False):
         return buf[:, 4096 + i * S + a:4096 + i * S + b] if kept and i < 2 else buf[:, 16 * a + i:16 * b:16]
@@ -125,16 +144,18 @@ def build():
         return T.U[:, BASE[tab] + 16 + a:BASE[tab] + 16 + b]
 
     H = F // 2
+    xk0 = [("U", k) for k in range(4)]
     dma("y", "l_st", 0.05, [], [("st32", 0)], lambda g, T, B: [g.sync.dma_start(T.st32[:], T.st[:])], name="ld")
     dma("s", "l_hv", 0.05, [], [("hb", 0)], lambda g, T, B: [g.scalar.dma_start(T.hb[:], T.hv[:])], name="ld")
-    dma("s", "l_su1", 0.7, [], [("U", "o1")], lambda g, T, B: [g.scalar.dma_start(TB(T, "U", H, F), T.su[:, H:F])], name="ld")
+    dma("y", "l_xs0", 0.45, [], xk0[:2], lambda g, T, B: [g.sync.dma_start(TB(T, "U", F, F + 512), T.xs[:, 0:512])], name="ld")
+    dma("s", "l_xs1", 0.45, [], xk0[2:], lambda g, T, B: [g.scalar.dma_start(TB(T, "U", F + 512, F + 1024), T.xs[:, 512:1024])], name="ld")
     dma("y", "l_su0", 0.7, [], [("U", "o0")], lambda g, T, B: [g.sync.dma_start(TB(T, "U", 0, H), T.su[:, 0:H])], name="ld")
-    dma("s", "l_th1", 0.7, [], [("P", "o1")], lambda g, T, B: [g.scalar.dma_start(T.P[:, H:F], T.th[:, H:F])], name="ld")
+    dma("s", "l_su1", 0.7, [], [("U", "o1")], lambda g, T, B: [g.scalar.dma_start(TB(T, "U", H, F), T.su[:, H:F])], name="ld")
     dma("y", "l_th0", 0.7, [], [("P", "o0")], lambda g, T, B: [g.sync.dma_start(T.P[:, 0:H], T.th[:, 0:H])], name="ld")
-    xk0 = [("U", k) for k in range(4)]
-    dma("y", "l_xs", 0.9, [], xk0, lambda g, T, B: [g.sync.dma_start(TB(T, "U", F, F + 1024), T.xs[:])], name="ld")
+    dma("s", "l_th1", 0.7, [], [("P", "o1")], lambda g, T, B: [g.scalar.dma_start(T.P[:, H:F], T.th[:, H:F])], name="ld")
 
     fl = dict(allow_small_or_imprecise_dtypes=True)
+    turned = any(CFG["route"]["R%d" % m] == "T" for m in range(7))
     vec(72, [], [("ones", 0)], lambda g, T, B: [g.vector.memset(T.ones[:], 1.0)], name="ld")
     pool(1, [], [("ip", 0)], lambda g, T, B: [g.iota(T.ip[:, 0:1], [[0, 1]], 0, 1)], name="ld")
     pool(128, [("ones", 0)], [("dg", 0)], lambda g, T, B: [g.affine_select(DG(T, I1), T.ones[:, 0:128], [[-1, 128]], A.is_equal, 0.0, 0, 1)], name="ld")
@@ -143,53 +164,65 @@ def build():
     pool(8, [("GI", 1)], [("GI", 0)], lambda g, T, B: [g.affine_select(T.GI[:, 0:8], T.GI[:, 8:16], [[16, 8]], A.is_ge, 0.0, 15, -1)], name="k1")
     pool(32, [("ones", 0)], [("Bs", 0)], lambda g, T, B: [g.affine_select(T.Bs[:], T.ones[:, 0:32], [[-4, 32]], A.is_ge, 0.0, 0, 1)], name="lt")
     pool(32, [("Bs", 0)], [("Bs", 0)], lambda g, T, B: [g.affine_select(T.Bs[:], T.Bs[:], [[4, 32]], A.is_ge, 0.0, 3, -1)], name="lt")
+    pool(64, [("ones", 0)], [("J", 0)], lambda g, T, B: [g.affine_select(T.J[:], T.ones[:, 0:64], [[-2, 64]], A.is_ge, 0.0, 0, 1)], name="xt")
+    pool(64, [("J", 0)], [("J", 0)], lambda g, T, B: [g.affine_select(T.J[:], T.J[:], [[2, 64]], A.is_ge, 0.0, 1, -1)], name="xt")
     pool(136, [("ones", 0)], [("Dm", 0)], lambda g, T, B: [g.affine_select(T.Dm[:], T.ones[:, 0:136], [[-16, 8], [-1, 17]], A.is_equal, 0.0, 1, 1)], name="k2")
     pool(16, [], [("wl32", 0)], lambda g, T, B: [g.iota(T.wl32[:], [[17, 16]], 16, 0)], name="k2")
     pool(136, [("Dm", 0)], [("Dm", 0)], lambda g, T, B: [g.affine_select(T.Dm[:], T.Dm[:], [[-16, 8], [-1, 17]], A.not_equal, -1.0, 0, 1)], name="k2")
     pool(8, [("ones", 0), ("Dm", 0)], [("Dm", 0)], lambda g, T, B: [g.affine_select(T.Dm[:, 16::17], T.ones[:, 0:8], [[-16, 8]], A.is_equal, 0.0, -15, 1)], name="k2")
     vec(1, [("ip", 0)], [("ip", 1)], lambda g, T, B: [g.vector.tensor_scalar(T.ip[:, 4:5], T.ip[:, 0:1], 15, None, A.bitwise_and)], name="ld")
-    vec(272, [], [("d0c", 0)], lambda g, T, B: [g.vector.memset(T.d0c[:], -1.0)], name="ld")
+    pool(272, [], [("d0c", 0)], lambda g, T, B: [g.iota(T.d0c[:], [[0, 272]], -1, 0, **fl)], name="k2")
+    pool(272, [("d0c", 0)], [("d0c", 0)], lambda g, T, B: [g.affine_select(T.d0c[:], T.d0c[:], [[0, 16], [1, 17]], A.not_equal, BIG, 0, 0)], name="k2")
     vec(1, [("ip", 1)], [("pc", 0)], lambda g, T, B: [g.vector.tensor_copy(T.pc[:, 0:1], T.ip[:, 4:5])], name="ld")
     pool(2 * S, [], [("f1", 0)], lambda g, T, B: [g.iota(T.f1[:], [[0, 2 * S]], 0, 0, **fl)], name="f0")
-    vec(384 + 128, [], [("init", 0)], lambda g, T, B: [g.vector.memset(T.Bg[:], BIG), g.vector.memset(T.h1[:], 0.0), g.vector.memset(T.U[:, UB:UB + 16], 0)], calls=3, name="ld")
+    vec(128, [], [("init", 0)], lambda g, T, B: [g.vector.memset(T.Bg[:], BIG), g.vector.memset(T.U[:, UB:UB + 16], 0)], calls=2, name="ld")
+    vec(384, [], [("h1", 0)], lambda g, T, B: [g.vector.memset(T.h1[:], 0.0)], name="h0")
     vec(256, [("Mk", 0), ("pc", 0)], [("Tc", 0)], lambda g, T, B: [g.vector.tensor_scalar(T.Tb[:, 0:S], T.Mk[:], T.pc[:, 0:1], 8192.0, A.is_gt, A.mult)], name="ld")
     vec(256, [("Mk", 0), ("pc", 0)], [("Mk", 0)], lambda g, T, B: [g.vector.tensor_scalar(T.Mk[:], T.Mk[:], T.pc[:, 0:1], None, A.is_equal)], name="ld")
-    vec(16, [("d0c", 0)], [("d0c", 0)], lambda g, T, B: [g.vector.memset(T.d0c[:, 0::17], BIG)], name="ld")
     vec(48, [("st32", 0)], [("stu", 0)], lambda g, T, B: [g.vector.tensor_copy(T.stu[:], T.st32[:])], name="ld")
-    for k in range(CFG["pools"]["X"]):
-        vec(128, [], [(("XI", k), 0)], lambda g, T, B, k=k: [g.vector.memset(T["X%d" % k][:, 0::8], -4096.0)], name="ld")
+    for k in range(POOLS["X"]):
+        pool(S, [("f1", 0)], [(("XI", k), 0)], lambda g, T, B, k=k: [g.affine_select(T["X%d" % k][:, 0::8], T.f1[:, 0:S], [[0, S]], A.is_gt, -4096.0, 0, 0)], name="xi")
     SC = (1.0, 2.0, 4.0, 0.75, 0.25, 0.125, 0.0625, -1.0)
     act(896, [("dg", 0)], [("dg", 1)], lambda g, T, B: [g.scalar.activation(DG(T, k), DG(T, I1), AF.Copy, scale=SC[k]) for k in range(1, 8)], calls=7, name="ld")
-    act(1500, [("hb", 0)], [("lam", 0)], lambda g, T, B: [g.scalar.activation(T.lam[:, 0:16], T.hb[:], AF.Ln, scale=0.0625)], name="ld")
-    vec(256, [("dg", 0)], [("I32", 0)], lambda g, T, B: [g.vector.tensor_copy(T.I32[:], DG(T, I1)), g.vector.tensor_scalar(T.IH[:], DG(T, I1), 0.5, None, A.mult)], calls=2, name="ld")
+    act(1300, [("hb", 0)], [("lam", 0)], lambda g, T, B: [g.scalar.activation(T.lam[:, 0:16], T.hb[:], AF.Ln, scale=0.0625)], name="ld")
+    act(128, [("dg", 0)], [("IH", 0)], lambda g, T, B: [g.scalar.activation(T.IH[:], DG(T, I1), AF.Copy, scale=0.5)], name="ih")
     vec(24, [("GI", 0)], [("GI32", 0)], lambda g, T, B: [g.vector.tensor_scalar(T.GI32[:], T.GI[:, 0:8], 16.0, None, A.mult),
                                                           g.vector.tensor_scalar(T.GI[:, 16:24], T.GI[:, 0:8], 32.0, None, A.mult),
                                                           g.vector.tensor_scalar(T.GI[:, 24:32], T.GI[:, 0:8], -16.0, None, A.mult)], calls=3, name="k1")
     vec(16, [("wl32", 0)], [("wl", 0)], lambda g, T, B: [g.vector.tensor_copy(T.wl[:], T.wl32[:])], name="k2")
     vec(128, [("Tc", 0)], [("Tc", 0)], lambda g, T, B: [g.vector.tensor_copy(T.Tb[:, S:2 * S], T.Tb[:, 0:S])], name="ld")
     vec(64, [("dg", 0)], [("Cv", 0)], lambda g, T, B: [g.vector.tensor_scalar(T.Cv[:, 0:128], DG(T, I1), -1.0, None, A.mult)], name="cv")
-    for n in (128, 256, 512, 896):
-        vec(n // 2, [("Cv", 0)], [("Cv", 0)], lambda g, T, B, n=n: [g.vector.tensor_copy(T.Cv[:, min(n, 1024) + (n == 896) * 128:min(n, 1024) + (n == 896) * 128 + n], T.Cv[:, 0:n])], name="cv")
+    for n, sem in ((128, "cv0"), (512, "cv1")):
+        dma("y", sem, 0.001 * n, [("Cv", 0)], [("Cv", 0)], lambda g, T, B, n=n: [g.sync.dma_start(T.Cv[:, k * n:min(k * n + n, 1920)], T.Cv[:, 0:min(n, 1920 - k * n)]) for k in (1, 2, 3)], n=3, name="cv")
     pool(1920, [("Cv", 0)], [("Cv", 0)], lambda g, T, B: [g.affine_select(T.Cv[:], T.Cv[:], [[-1, 15], [-16, 8], [0, 16]], A.not_equal, 1.0, 0, 1)], name="cv")
-    pool(UB, [], segs("Z", 2432), lambda g, T, B: [g.iota(T.U[:, 0:UB], [[0, UB]], 0, 0)], name="z0")
+    ZQ = UB // 4
+    pool(ZQ, [], [("Z", "q")], lambda g, T, B: [g.iota(T.U[:, 0:ZQ], [[0, ZQ]], 0, 0)], name="z0")
+    dma("y", "z0", 1.6, [("Z", "q")], segs("Z", 2432), lambda g, T, B: [g.sync.dma_start(T.U[:, k * ZQ:k * ZQ + ZQ], T.U[:, 0:ZQ]) for k in (1, 2, 3)], n=3, name="z0")
     pool(S, [], [("NN", 0)], lambda g, T, B: [g.iota(T.NN[:], [[1, S]], F, S)], name="nm")
     vec(S, [("NN", 0)], [("NN", 0)], lambda g, T, B: [g.vector.tensor_scalar(T.NN[:], T.NN[:], 16 * S - 1, None, A.bitwise_and)], name="nm")
-    vec(S, [("NN", 0), ("Mk", 0)], [("NM", 0)], lambda g, T, B: [g.vector.tensor_scalar(T.NM[:, 0:S], T.NN[:], T.Mk[:, 0:1], None, A.mult)], name="nm")
-    nk = [("NM", m) for m in range(1, 7)]
-    dma("y", "nm0", 1.3, segs("Z", 2432), nk, lambda g, T, B: [g.sync.dma_start(T.NM[:, S:7 * S], T.U[:, 0:6 * S])], name="nn")
-    dma("y", "nm1", 0.3, [("NN", 0)] + nk, nk, lambda g, T, B: [g.sync.dma_start(T.NM[m::16, m * S:m * S + S], T.NN[m::16, :]) for m in range(1, 7)], n=6, name="nn")
-    vec(1024, xk0, [("XE", k) for k in range(4)], lambda g, T, B: [g.vector.tensor_scalar(XN(T, 0, 0, 4 * S), TB(T, "U", F, F + 1024), -2048.0, None, A.add)], name="x")
+    nk = [("NM", m) for m in NMB]
+    dma("p", "nm0", 0.9, [("Z", "q"), ("Z", 0)], nk, lambda g, T, B: [g.dma_start(T.NM[:], T.U[:, 0:4 * S])], name="nn")
+    dma("y", "nm1", 0.2, [("NN", 0)] + nk, nk, lambda g, T, B: [g.sync.dma_start(T.NM[m::16, k * S:k * S + S], T.NN[m::16, :]) for m, k in NMB.items()], n=4, name="nn")
+    for h in range(2):
+        shift(2 * S, xk0[2 * h:2 * h + 2], [("XE", 2 * h), ("XE", 2 * h + 1)], lambda T, B, h=h: [(XN(T, k), TB(T, "U", F + k * S, F + k * S + S)) for k in (2 * h, 2 * h + 1)], -2048.0, calls=2, name="x")
+        xq = ("Q", "xt%d" % h)
+        pe(512, [("XE", 2 * h), ("XE", 2 * h + 1), ("dg", 1)], [(xq, 0)],
+           lambda g, T, B, h=h, xq=xq: [g.tensor.matmul(PS(T, B, xq, 128 * b, 128 * b + 128), T.XE[:, 512 * h + 128 * b:512 * h + 128 * b + 128], DG(T, IM), True, True) for b in range(4)], name="xt")
+        shift(512, [(xq, 0)], [("XT", h)], lambda T, B, h=h, xq=xq: [(T.XT[:, 512 * h:512 * h + 512], PS(T, B, xq, 0, 512))], 0.0, name="xt")
+    ft = [TS[m][0] for m in (0, 1, 3, 4) if CFG["route"]["E%d" % m] == "T" or CFG["route"]["E%d" % m] == "N" and "E%d" % m in CFG["factor"]]
+    if ft:
+        a, b = min(ft) * S, max(ft) * S + S
+        act(b - a + 1500, xk0 + [("lam", 0)], [("FX", 0)], lambda g, T, B: [g.scalar.activation(T.FX[:, a:b], TB(T, "U", F + a, F + b), AF.Exp, bias=-4.0, scale=1.0 / 512)], name="fx")
     vec(2, [("pc", 0)], [("pc", 1)], lambda g, T, B: [g.vector.tensor_scalar(T.pc[:, 1:2], T.pc[:, 0:1], 6.0, None, A.not_equal), g.vector.memset(T.pc[:, 2:3], 1.0)], calls=2)
-    if any(CFG["route"]["R%d" % m] == "T" for m in range(7)):
+    if turned:
         lq = ("Q", "lt")
         vec(16, [("lam", 0)], [("LP", 0)], lambda g, T, B: [g.vector.tensor_scalar(T.LP[:, 0:16], T.lam[:, 0:16], -512.0, None, A.mult),
                                                              g.vector.tensor_scalar(T.lam[:, 16:32], T.lam[:, 0:16], -512.0, None, A.mult)], calls=2, name="lt")
         vec(32, [("LP", 0)], [("LP", 1)], lambda g, T, B: [g.vector.tensor_tensor(T.LP[:, 16:32], T.lam[:, 16:32], T.LP[:, 0:16], A.subtract)], name="lt")
         pe(128, [("LP", 1), ("dg", 0)], [(lq, 0)], lambda g, T, B: [g.tensor.matmul(PS(T, B, lq, 0, 128, rows=32), T.LP[:], DG(T, I1), True, True)], name="lt")
         vec(128, [(lq, 0)], [("LT", 0)], lambda g, T, B: [g.vector.tensor_copy(T.LT[0:32, :], PS(T, B, lq, 0, 128, rows=32))], name="lt")
-        pool(512, [], [("Sel", 0)], lambda g, T, B: [g.iota(T.Sel[0:32, :], [[0, 512]], 0, 0, **fl)], name="lt")
-        for b in (0, -16):
-            pool(512, [("Sel", 0)], [("Sel", 0)], lambda g, T, B, b=b: [g.affine_select(T.Sel[0:32, :], T.Sel[0:32, :], [[-1, 4], [0, 32], [-4, 4]], A.not_equal, 1.0, b, 1)], name="lt")
+        pool(512, [("f1", 0)], [("Sel", 0)], lambda g, T, B: [g.affine_select(T.Sel[0:32, :], T.f1[0:32, :], [[-1, 4], [0, 32], [-4, 4]], A.not_equal, 1.0, 0, 1)], name="lt")
+        dma("y", "sel", 0.1, [("Sel", 0)], [("Sel", 0)], lambda g, T, B: [g.sync.dma_start(T.Sel[16:32, :], T.Sel[0:16, :])], name="lt")
 
     def CL(T, k, n=1):
         return T.cl[:, k * S:(k + n) * S]
@@ -199,11 +232,12 @@ def build():
             lambda g, T, B: [g.vector.tensor_copy(CL(T, k, n), TB(T, "U", 0, lim).indirect(lst(T)))], gn=S * n, name=name)
 
     def gather(gs, k, lim):
-        for q in range(16):
+        w = S // NP
+        for q in range(NP):
             def fn(g, T, B, e, q, n):
-                out, src = B(gs)[:, S * q:S * (q + n)], T.P[:, 0:lim].indirect(T.cl[:, k * S + q * 16:k * S + (q + n) * 16])
+                out, src = B(gs)[:, 16 * w * q:16 * w * (q + n)], T.P[:, 0:lim].indirect(T.cl[:, k * S + q * w:k * S + (q + n) * w])
                 return [g.vector.tensor_scalar(out, src, -2048.0, None, A.add) if e == "v" else g.scalar.activation(out, src, AF.Identity, bias=-2048.0)]
-            vec(0, segs("P", lim) + [("cl", k)], [(gs, q)], fn, gn=S, name=gs[1], piece=q)
+            vec(0, segs("P", lim) + [("cl", k)], [(gs, q)], fn, gn=16 * w, name=gs[1], piece=q)
 
     sets = {}
     scanned = {g_: any(CFG["route"][u] != "A" for u in us) for us in (("E0",), ("E1", "R0"), ("E3", "R1"), ("E4", "R3"), ("R2",), ("R4",), ("R5",), ("R6",)) for g_ in ["g" + us[0]]}
@@ -212,55 +246,46 @@ def build():
         d = ("D", u + "ab"[j // 2])
         return (d, j), lambda B, a, b: B(d)[:, j % 2 * 1024 + a:j % 2 * 1024 + b]
 
+    def two(on_pool, rd, wr, gs, back, name):
+        if on_pool:
+            pool(2 * S, rd, wr, lambda g, T, B: [g.affine_select(SL(B(gs), i, kept=not back), SL(B(gs), i, kept=back), [[0, S]], A.is_gt, 0.0, 1, 0) for i in range(2)], calls=2, name="kp" + name)
+        else:
+            vec(S, rd, wr, lambda g, T, B: [g.vector.tensor_copy(SL(B(gs), i, kept=not back), SL(B(gs), i, kept=back)) for i in range(2)], calls=2, name="mx" + name)
+
     def body(u, gs, xs, xk, L, skip, elect):
         route, kept = CFG["route"][u], scanned.get(gs[1], False)
         sl = sorted([i for i in range(16) if i not in skip], key=lambda i: i % 2 * (route != "A"))
-        parts = CFG["split"].get(u, 1) if route == "T" and gs[1] == "g" + u and u[0] == "R" else 1
-        w = S // parts
-        gk = [(gs, q) for q in range(16)]
+        gk = [(gs, q) for q in range(NP)]
         if kept and gs[1][1:] == u:
-            for r in range(parts):
-                if u in CFG["keep"]:
-                    pool(2 * w, gk[16 * r // parts:16 * (r + 1) // parts], [(gs, ("kept", r))],
-                         lambda g, T, B, a=r * w, w=w: [g.affine_select(SL(B(gs), i, a, a + w, True), SL(B(gs), i, a, a + w), [[0, w]], A.is_gt, 0.0, 1, 0) for i in range(2)], calls=2, name="kp" + u)
-                    continue
-                vec(w, gk[16 * r // parts:16 * (r + 1) // parts], [(gs, ("kept", r))],
-                    lambda g, T, B, a=r * w, w=w: [g.vector.tensor_copy(SL(B(gs), i, a, a + w, True), SL(B(gs), i, a, a + w)) for i in range(2)], calls=2, name="mx" + u)
-        pk = gk + [(gs, ("kept", r)) for r in range(parts * kept)]
+            two(u in CFG["keep"], gk, [(gs, "kept")], gs, False, u)
+        pk = gk + [(gs, "kept")] * kept
         el = ("Q", "B" + u)
 
         def ends(g, T, B, j):
             return [] if j else [g.tensor.matmul(PS(T, B, el, 16, 272, 17), DG(T, I1), T.Bg[:], True, True)]
-        sets[u] = (gs, xs, xk, L, sl, kept, pk, parts)
+        sets[u] = (gs, xs, xk, L, sl, kept, pk)
         if route != "A":
             mx, xe, xr = ("MX", u), ("X", u), ("Q", "x" + u)
             for c, n, calls in ((1, 3, 3), (4, 2, 1), (6, 2, 1)):
                 def moves(T, B, c=c):
-                    return [(B(xe)[:, k::8], xs(T)[0]) for k in (1, 5, 4)] if c == 1 else [(B(xe)[:, c // 2::4], B(xe)[:, 1::4])]
-                rd = xk if c == 1 else [(xe, 1)]
-                if CFG["spread"].get(u + str(c), "p") == "v":
-                    vec(128 * n, rd, [(xe, c)], lambda g, T, B, moves=moves: [g.vector.tensor_copy(o, i) for o, i in moves(T, B)], calls=calls, name="xf" + u)
-                else:
-                    pool(S * n, rd, [(xe, c)], lambda g, T, B, moves=moves, w=S * n // calls: [g.affine_select(o, i, [[0, w]], A.is_gt, 0.0, 1, 0) for o, i in moves(T, B)],
-                         calls=calls, name="xf" + u)
-            pe(S, pk[-1:] + xk + [("dg", 0)], [(xr, 0)], lambda g, T, B: [g.tensor.matmul(PS(T, B, xr, 0, S), DG(T, I1), xs(T)[0], True, True)], name="mx" + u)
-            for r in range(parts):
-                a = r * w
-                vec(2 * w, [(gs, ("kept", r)), (xr, 0)], [(gs, ("first", r))],
-                    lambda g, T, B, a=a: [g.vector.tensor_tensor(SL(B(gs), i, a, a + w), SL(B(gs), i, a, a + w, True), PS(T, B, xr, a, a + w), A.max) for i in range(2)], calls=2, name="mx" + u)
-                for t in range(2):
-                    vec(4 * w, gk[16 * r // parts:16 * (r + 1) // parts] + [(gs, ("first", r))] + [(xe, c) for c in (1, 4, 6)], [(mx, (t, r))],
-                        lambda g, T, B, t=t, a=a: [g.vector.tensor_tensor_scan(B(mx)[:, 16 * a + t:16 * (a + w):2], B(xe)[:, 8 * a:8 * (a + w)],
-                                                                               B(gs)[:, 16 * a + t:16 * (a + w):2], 0.0, A.min, A.max)], name="mx" + u)
-                if route == "T":
-                    vec(w, [(gs, ("kept", r))], [(gs, ("first", r))],
-                        lambda g, T, B, a=a: [g.vector.tensor_copy(SL(B(gs), i, a, a + w), SL(B(gs), i, a, a + w, True)) for i in range(2)], calls=2, name="mx" + u)
+                    return [(B(xe)[:, k::8], xs(T)) for k in (1, 5, 4)] if c == 1 else [(B(xe)[:, c // 2::4], B(xe)[:, 1::4])]
+                pool(S * n, xk if c == 1 else [(xe, 1)], [(xe, c)], lambda g, T, B, moves=moves, w=S * n // calls: [g.affine_select(o, i, [[0, w]], A.is_gt, 0.0, 1, 0) for o, i in moves(T, B)],
+                     calls=calls, name="xf" + u)
+            pe(S, xk + [("dg", 0)], [(xr, 0)], lambda g, T, B: [g.tensor.matmul(PS(T, B, xr, 0, S), DG(T, I1), xs(T), True, True)], name="mx" + u)
+            vec(2 * S, [(gs, "kept"), (xr, 0)], [(gs, "first")],
+                lambda g, T, B: [g.vector.tensor_tensor(SL(B(gs), i), SL(B(gs), i, kept=True), PS(T, B, xr, 0, S), A.max) for i in range(2)], calls=2, name="mx" + u)
+            for t in range(2):
+                vec(4 * S, gk + [(gs, "first")] + [(xe, c) for c in (1, 4, 6)], [(mx, t)],
+                    lambda g, T, B, t=t: [g.vector.tensor_tensor_scan(B(mx)[:, t::2], B(xe)[:], B(gs)[:, t:16 * S:2], 0.0, A.min, A.max)], name="mx" + u)
+            if route == "T":
+                two(u in CFG["back"], [(gs, "kept")], [(gs, "first")], gs, True, u)
             for q in range(4 if elect is not None else 0):
-                pe(1024, pk + [(mx, (q // 2, r)) for r in range(parts)] + [("GI32", 0), ("init", 0)], [(el, "sc%d" % (2 * q)), (el, "sc%d" % (2 * q + 1))],
+                pe(1024, pk + [(mx, q // 2), ("GI32", 0), ("init", 0)], [(el, "sc%d" % (2 * q)), (el, "sc%d" % (2 * q + 1))],
                    lambda g, T, B, q=q: ends(g, T, B, q) + [g.tensor.matmul(PS(T, B, el, h * 136 + i, h * 136 + 136, 17), SL(B(b), i, 128 * h, 128 * h + 128, b == gs), T.GI[:, c:c + 8], c == 16, c == 24)
                                          for i in sl[4 * q:4 * q + 4] for h in range(2) for b, c in ((mx, 16), (gs, 24))], name="sc" + u)
             return
-        lg, ab = int(math.log2(L)), []
+        lg = int(math.log2(L))
+        pairs = sorted({t // 2 for t in TS[elect]}) if L > 1 else []
         for j in range(4):
             ss = sl[4 * j:4 * j + 4]
             w = S * len(ss)
@@ -269,21 +294,23 @@ def build():
             def fn(g, T, B, ss=ss, pd=pd):
                 o = []
                 for c, i in enumerate(ss):
-                    for n, x in enumerate(xs(T)):
-                        o.append(g.tensor.matmul(PS(T, B, pd, c * S, c * S + S), DG(T, IM), x, n == 0, False))
-                    o.append(g.tensor.matmul(PS(T, B, pd, c * S, c * S + S), DG(T, lg), SL(B(gs), i, kept=kept), False, True))
+                    o.append(g.tensor.matmul(PS(T, B, pd, c * S, c * S + S), DG(T, lg), SL(B(gs), i, kept=kept), True, False))
+                    if L == 1:
+                        o.append(g.tensor.matmul(PS(T, B, pd, c * S, c * S + S), DG(T, IM), xs(T), False, True))
+                    o += [g.tensor.matmul(PS(T, B, pd, c * S + 64 * b, c * S + 64 * b + 64), T.XT[:, 512 * h + 128 * b:512 * h + 128 * b + 128], T.J[:], False, h == pairs[-1] and b == 3)
+                          for h in pairs for b in range(4)]
                 return o
-            pe(w * (1 + min(L, 2)), pk + xk + [("dg", 0), ("dg", 1)], [(pd, 0)], fn, name="da" + u)
-            ab.append(act(w, [(pd, 0)], [dk], lambda g, T, B, pd=pd, de=de, w=w: [g.scalar.activation(de(B, 0, w), PS(T, B, pd, 0, w), AF.Abs)], name="abs" + u))
+            pe(w * (1 + max(L // 2, 1)), pk + xk + [("dg", 0), ("dg", 1)], [(pd, 0)], fn, name="da" + u)
+            act(w, [(pd, 0)], [dk], lambda g, T, B, pd=pd, de=de, w=w: [g.scalar.activation(de(B, 0, w), PS(T, B, pd, 0, w), AF.Abs)], name="abs" + u)
         for j in range(8 if elect is not None else 0):
             dk, de = tile(u, j // 2)
             pe(1024, [dk, ("GI32", 0), ("init", 0)], [(el, "sc%d" % j)],
                lambda g, T, B, j=j, de=de: ends(g, T, B, j) + [g.tensor.matmul(PS(T, B, el, h * 136 + i, h * 136 + 136, 17), de(B, (i % 4) * S + h * 128, (i % 4) * S + h * 128 + 128), T.GI32[:], True, True)
                                             for i in (2 * j, 2 * j + 1) for h in range(2)],
-               name="sc" + u, after=[] if LV[elect] == 0 else ab[-2:])
+               name="sc" + u)
 
     def mix(u):
-        gs, xs, xk, L, sl, kept, pk, parts = sets[u]
+        gs, xs, xk, L, sl, kept, pk = sets[u]
         m, route, mx = int(u[1]), CFG["route"][u], ("MX", u)
         y = ("YM", m) if u[0] == "E" else (("Y", u), 0)
         hi = u[0] == "E" and L > 1
@@ -292,7 +319,7 @@ def build():
         how = "T" if route == "T" else CFG["total"][u]
         dk, de = zip(*[tile(u, j) for j in range(4)])
         osem = "o" + u if len(sl) < 16 else "out"
-        rd = ("Q", "s" + u)
+        rd, r2 = ("Q", "s" + u), ("Q", "z" + u)
 
         def Y(T, B):
             return T.YM[:, m * S:m * S + S] if u[0] == "E" else B(y[0])[:]
@@ -304,30 +331,33 @@ def build():
             w = S * len(ss)
             pd = ("PD", "e" + u + str(j))
             if route == "T":
-                def fn(g, T, B, j=j, pd=pd):
-                    r = []
-                    for c in range(8):
-                        a, t = 1024 * j + 512 * (c // 4), c % 4
-                        ops = [(B(mx)[:, a + t:a + 512:4], DG(T, I2)), (B(gs)[:, a + t:a + 512:4], DG(T, IM))]
-                        ops += [(T.Sel[0:32, 128 * t:128 * t + 128], T.LT[0:32, :])] * (u[0] == "R")
-                        r += [g.tensor.matmul(PS(T, B, pd, 128 * c, 128 * c + 128), l, x, n == 0, n == len(ops) - 1) for n, (l, x) in enumerate(ops)]
-                    return r
-                r = j * parts // 4
-                pe(1024 * (2 if u[0] == "E" else 3), pk[4 * j:4 * j + 4] + [(gs, ("first", r)), (mx, (0, r)), (mx, (1, r)), ("dg", 1)] + [("LT", 0), ("Sel", 0)] * (u[0] == "R"), [(pd, 0)], fn, name="d" + u)
-                act(1024, [(pd, 0)], [dk[j]],
-                    lambda g, T, B, j=j, pd=pd: [g.scalar.activation(de[j](B, 0, 1024), PS(T, B, pd, 0, 1024), AF.Exp, bias=b0 if u[0] == "E" else 0.0, scale=-1.0 / 512)], name="exp" + u)
-                pe(2048, [dk[j], ("Bs", 0)], [(rd, j)],
-                   lambda g, T, B, j=j: [g.tensor.matmul(PS(T, B, rd, 64 * j + 32 * (c // 4), 64 * j + 32 * (c // 4) + 32), de[j](B, 128 * c, 128 * c + 128), T.Bs[:], c % 4 == 0, c % 4 == 3)
-                                         for c in range(8)], name="sum" + u)
+                end = u == CFG["last"] and j == 3
+                for k, cs in enumerate((range(4), range(4, 8)) if end else (range(8),)):
+                    pd, key, c0, w, acc = ("Q", "e" + u + "ab"[k]) if end else pd, (dk[j][0], (j, k)), cs[0], 128 * len(cs), r2 if end else rd
+
+                    def fn(g, T, B, j=j, pd=pd, cs=cs):
+                        r = []
+                        for c in cs:
+                            a, t = 1024 * j + 512 * (c // 4), c % 4
+                            ops = [(B(mx)[:, a + t:a + 512:4], DG(T, I2)), (B(gs)[:, a + t:a + 512:4], DG(T, IM))]
+                            ops += [(T.Sel[0:32, 128 * t:128 * t + 128], T.LT[0:32, :])] * (u[0] == "R")
+                            r += [g.tensor.matmul(PS(T, B, pd, 128 * (c - cs[0]), 128 * (c - cs[0] + 1)), l, x, n == 0, n == len(ops) - 1) for n, (l, x) in enumerate(ops)]
+                        return r
+                    pe(w * (2 if u[0] == "E" else 3), [(gs, "first"), (mx, 0), (mx, 1), ("dg", 1)] + [("LT", 0), ("Sel", 0)] * (u[0] == "R"), [(pd, 0)], fn, name="d" + u)
+                    act(w, [(pd, 0)], [key], lambda g, T, B, j=j, pd=pd, c0=c0, w=w:
+                        [g.scalar.activation(de[j](B, 128 * c0, 128 * c0 + w), PS(T, B, pd, 0, w), AF.Exp, bias=b0 if u[0] == "E" else 0.0, scale=-1.0 / 512)], name="exp" + u)
+                    pe(2 * w, [key, ("Bs", 0)], [(acc, (j, k))],
+                       lambda g, T, B, j=j, cs=cs, acc=acc: [g.tensor.matmul(PS(T, B, acc, 64 * j + 32 * (c // 4), 64 * j + 32 * (c // 4) + 32), de[j](B, 128 * c, 128 * c + 128), T.Bs[:], c % 4 == 0, c % 4 == 3)
+                                                             for c in cs], name="sum" + u)
                 continue
             if route == "N":
                 def fn(g, T, B, ss=ss, pd=pd):
                     r = []
                     for c, i in enumerate(ss):
-                        ops = [(IM, SL(B(gs), i, kept=True)), (I2, SL(B(mx), i))] + ([] if fac else [(IM, xs(T)[0])])
+                        ops = [(IM, SL(B(gs), i, kept=True)), (I2, SL(B(mx), i))] + ([] if fac else [(IM, xs(T))])
                         r += [g.tensor.matmul(PS(T, B, pd, c * S, c * S + S), DG(T, k), a, n == 0, n == len(ops) - 1) for n, (k, a) in enumerate(ops)]
                     return r
-                pe(w * (2 if fac else 3), pk + sorted({(mx, (i % 2, 0)) for i in ss}) + [("dg", 1)] + ([] if fac else xk), [(pd, 0)], fn, name="d" + u)
+                pe(w * (2 if fac else 3), pk + sorted({(mx, i % 2) for i in ss}) + [("dg", 1)] + ([] if fac else xk), [(pd, 0)], fn, name="d" + u)
 
             def SRC(T, B, a, b, j=j, pd=pd):
                 return PS(T, B, pd, a, b) if route == "N" else de[j](B, a, b)
@@ -338,53 +368,47 @@ def build():
             elif u[0] == "E":
                 act(w, [src], [dk[j]], lambda g, T, B, j=j, SRC=SRC: [g.scalar.activation(de[j](B, 0, 1024), SRC(T, B, 0, 1024), AF.Exp, bias=b0, scale=-1.0 / (512 * L))], name="exp" + u)
             else:
-                act(w, [src, ("lam", 0)], [dk[j]],
-                    lambda g, T, B, j=j, ss=ss, SRC=SRC: [g.scalar.activation(de[j](B, c * S, c * S + S), SRC(T, B, c * S, c * S + S), AF.Exp, bias=T.lam[:, i:i + 1], scale=-1.0 / 512)
+                begin = how == "vec" and j == 0
+                act(w, [src, ("lam", 0)], [dk[j]] + [(rd, 0)] * begin,
+                    lambda g, T, B, j=j, ss=ss, SRC=SRC, begin=begin: [g.scalar.activation(PS(T, B, rd, c * S, c * S + S) if begin and c < 2 else de[j](B, c * S, c * S + S), SRC(T, B, c * S, c * S + S), AF.Exp, bias=T.lam[:, i:i + 1], scale=-1.0 / 512)
                                                           for c, i in enumerate(ss)], calls=len(ss), name="exp" + u)
-        fk, fa = [], ("FA", u)
-        if fac:
-            fk = [(fa, 0)]
-            act(256, xk + [dk[0]], fk, lambda g, T, B: [g.scalar.activation(B(fa)[:], xs(T)[0], AF.Exp, scale=1.0 / 512)], name="y" + u)
+        fk, fa = [], ("Q" if how == "dma" else "FA", "f" + u)
 
         def FAC(T, B):
-            return B(fa)[:]
+            return T.FX[:, TS[m][0] * S:TS[m][0] * S + S] if u[0] == "E" else PS(T, B, fa, 0, S) if how == "dma" else B(fa)[:]
         w3 = S * (len(sl) - 12)
         da, db = dk[0][0], dk[2][0]
-        for n in (1024 + w3, 1024, 512, 256)[:{"h1": 1, "h2": 2, "h3": 3, "dma": 4}.get(how, 0)]:
+        for n in (1024 + w3, 1024, 512, 256)[:{"h3": 3, "dma": 4}.get(how, 0)]:
             top = n > 1024
             dma("p", "h" + u, 3.4 * n / 2048, dk if top else dk[:2], dk[:2],
                 lambda g, T, B, n=n, top=top: [g.dma_start(B(da)[:, 0:n], B(db)[:, 0:n] if top else B(da)[:, n:2 * n], accum_op=A.add)], name="half" + u)
-        rest = {"h1": ((0, 4), (1, 4)), "h2": ((0, 4),), "h3": ((0, 2),)}.get(how, ((0, 4), (1, 4), (2, 4), (3, w3 // S)))
-        rest = [(j, c) for j, n in rest for c in range(n)]
-        if how == "fold":
-            back = ("Y", "f" + u)
-            land = (back, 0) if fac else y
-            a = dma("p", "h" + u, 3.5, dk, [land], lambda g, T, B: [[de[j](B, c * S, c * S + S) for j, c in rest]], name="half" + u, fold=u,
-                    home=lambda T, B: B(back)[:] if fac else Y(T, B))
-            add(None, [land], [land], None, sem="k" + u, lat=1.5, after=[a], name="half" + u, fold=u)
-            if fac:
-                vec(512, [land] + fk, [y], lambda g, T, B: [g.vector.tensor_tensor(Y(T, B), B(back)[:], FAC(T, B), A.mult)], name="y" + u)
-        elif how == "vec":
-            for n in range(0, len(rest), 2):
-                (j, c), w = rest[n], S * len(rest[n:n + 2])
-                vec(w, [dk[j]] + [(rd, 0)] * (n > 0), [(rd, 0)],
-                    lambda g, T, B, j=j, c=c, w=w, n=n: [g.vector.tensor_tensor(PS(T, B, rd, 0, w), de[j](B, c * S, c * S + w), PS(T, B, rd, 0, w), A.add) if n
-                                                         else g.vector.tensor_copy(PS(T, B, rd, 0, w), de[j](B, 0, w))], name="sum" + u)
-            vec(256, [(rd, 0)], [y], lambda g, T, B: [g.vector.tensor_copy(Y(T, B), PS(T, B, rd, 0, S))], name="y" + u)
+        if fac and u[0] == "E":
+            fk = [("FX", 0)]
+        elif fac:
+            fk = [(fa, 0)]
+            act(256, xk, fk, lambda g, T, B: [g.scalar.activation(FAC(T, B), xs(T), AF.Exp, scale=1.0 / 512)], name="y" + u)
+        if how == "vec":
+            for j, c in [(j, c) for j in range(4) for c in (0, 2)][1:-1]:
+                vec(2 * S, [dk[j], (rd, 0)], [(rd, 0)],
+                    lambda g, T, B, j=j, c=c: [g.vector.tensor_tensor(PS(T, B, rd, 0, 2 * S), de[j](B, c * S, c * S + 2 * S), PS(T, B, rd, 0, 2 * S), A.add)], name="sum" + u)
+            vec(2 * S, [dk[3], (rd, 0)], [(rd, 0), y],
+                lambda g, T, B: [g.vector.tensor_tensor(Y(T, B), de[3](B, 2 * S, 3 * S), PS(T, B, rd, 0, S), A.add),
+                                 g.vector.tensor_tensor(PS(T, B, rd, S, 2 * S), de[3](B, 3 * S, 4 * S), PS(T, B, rd, S, 2 * S), A.add)], calls=2, name="sum" + u)
             vec(256, [(rd, 0), y], [(rd, 0) if fac else y], lambda g, T, B: [g.vector.tensor_tensor(PS(T, B, rd, S, 2 * S) if fac else Y(T, B), PS(T, B, rd, S, 2 * S), Y(T, B), A.add)], name="y" + u)
             if fac:
                 vec(256, [(rd, 0)] + fk, [y], lambda g, T, B: [g.vector.tensor_tensor(Y(T, B), PS(T, B, rd, S, 2 * S), FAC(T, B), A.mult)], name="y" + u)
-        elif how != "dma":
-            for n in range(0, len(rest) if how != "T" else 0, 2):
-                two = rest[n:n + 2]
-                i0 = pe(1024 * len(two), sorted({dk[j] for j, _ in two}) + [("I32", 0)], [(rd, n)],
-                        lambda g, T, B, two=two: [g.tensor.matmul(PS(T, B, rd, 0, S), T.I32[:], de[j](B, c * S, c * S + S), (j, c) == rest[0], (j, c) == rest[-1]) for j, c in two], name="sum" + u)
-                if n:
-                    tasks[i0]["follow"] = [i0 - 1]
-            vec(256, [(rd, n) for n in (range(4) if how == "T" else range(0, len(rest), 2))] + fk, [y],
-                lambda g, T, B: [g.vector.tensor_tensor(Y(T, B), PS(T, B, rd, 0, S), FAC(T, B), A.mult) if fac else g.vector.tensor_copy(Y(T, B), PS(T, B, rd, 0, S))], name="y" + u)
+        elif how == "h3":
+            pass
+        elif u == CFG["last"]:
+            for a, b, acc, keys in ((0, 192, rd, [(j, 0) for j in range(3)]), (192, S, r2, [(3, 0), (3, 1)])):
+                vec(b - a, [(acc, k) for k in keys] + fk, [(y[0], a)],
+                    lambda g, T, B, a=a, b=b, acc=acc: [g.vector.tensor_tensor(B(y[0])[:, a:b], PS(T, B, acc, a, b), B(fa)[:, a:b], A.mult)], name="y" + u)
+                dma("y", "y" + u, 0.3 * (b - a) / S, [(y[0], a)], [("oR", m, a)], lambda g, T, B, a=a, b=b: [g.sync.dma_start(T.yz[:, m * S + a:m * S + b], B(y[0])[:, a:b])], name="out" + u)
+            return
+        elif how == "T":
+            vec(256, [(rd, (j, 0)) for j in range(4)] + fk, [y], lambda g, T, B: [g.vector.tensor_tensor(Y(T, B), PS(T, B, rd, 0, S), FAC(T, B), A.mult)], name="y" + u)
         elif fac:
-            vec(512, [dk[0]] + fk, [y], lambda g, T, B: [g.vector.tensor_tensor(Y(T, B), de[0](B, 0, S), FAC(T, B), A.mult)], name="y" + u)
+            vec(256, [dk[0]] + fk, [y], lambda g, T, B: [g.vector.tensor_tensor(Y(T, B), de[0](B, 0, S), FAC(T, B), A.mult)], name="y" + u)
         elif u[0] == "R":
             dma("y", "y" + u if osem == "out" else osem, 0.3, [dk[0]], [("oR", m)], lambda g, T, B: [g.sync.dma_start(OUT(T), de[0](B, 0, S))], name="out" + u)
             return
@@ -393,9 +417,12 @@ def build():
         if hi:
             ka, kb = KIDS[m]
             kk = ("Q", "K" + u)
-            pe(1024, [("YM", ka), ("YM", kb), y, ("I32", 0)], [(kk, 0)], lambda g, T, B: [g.tensor.matmul(PS(T, B, kk, 0, S), T.IH[:], T.YM[:, kb * S:kb * S + S], True, True)], name="K" + u)
+            pe(1024, [("YM", kb), ("IH", 0)], [(kk, 0)], lambda g, T, B: [g.tensor.matmul(PS(T, B, kk, 0, S), T.IH[:], T.YM[:, kb * S:kb * S + S], True, True)], name="K" + u)
             vec(256, [(kk, 0), ("YM", ka)], [(kk, 0)], lambda g, T, B: [g.vector.tensor_tensor(PS(T, B, kk, 0, S), PS(T, B, kk, 0, S), T.YM[:, ka * S:ka * S + S], A.mult)], name="K" + u)
-            vec(256, [y, (kk, 0)], [y], lambda g, T, B: [g.vector.tensor_tensor(Y(T, B), PS(T, B, kk, 0, S), Y(T, B), A.add)], name="K" + u)
+            if how == "h3":
+                vec(256, [dk[0], (kk, 0)], [(kk, 0)], lambda g, T, B: [g.vector.tensor_tensor(PS(T, B, kk, 0, S), PS(T, B, kk, 0, S), de[0](B, S, 2 * S), A.add)], name="K" + u)
+            vec(256, [dk[0] if how == "h3" else y, (kk, 0)], [y],
+                lambda g, T, B: [g.vector.tensor_tensor(Y(T, B), PS(T, B, kk, 0, S), de[0](B, 0, S) if how == "h3" else Y(T, B), A.add)], name="K" + u)
         dma("y", osem if u[0] == "E" or osem != "out" else "y" + u, 0.3, [y], [("o" + u[0], m)], lambda g, T, B: [g.sync.dma_start(OUT(T), Y(T, B))], name="out" + u)
 
     def late(slot, ms, f0):
@@ -428,23 +455,16 @@ def build():
         xk = [("XE", t) for t in TS[m]]
         part[0] = "el%d" % m
         gather(gs, k, BLIM[m])
-        if L == 4:
-            nb = ("Q", "x")
-            pe(1024, xk + [("dg", 0)], [(nb, 0)], lambda g, T, B: [g.tensor.matmul(PS(T, B, nb, 0, S), DG(T, I1), XN(T, t), t == 0, t == 3) for t in range(4)], name="x4")
-            vec(256, [(nb, 0)], [("x4", 0)], lambda g, T, B: [g.vector.tensor_copy(T.x4[:, 0:S], PS(T, B, nb, 0, S))], name="x4")
-            vec(256, [(nb, 0), ("x4", 0)], [("x4", 1)], lambda g, T, B: [g.vector.tensor_tensor(T.x4[:, S:2 * S], PS(T, B, nb, 0, S), T.x4[:, 0:S], A.subtract)], name="x4")
-            body(u, gs, lambda T: [T.x4[:, 0:S], T.x4[:, S:2 * S]], [("x4", 0), ("x4", 1)], L, (), m)
-        else:
-            body(u, gs, lambda T: [XN(T, t) for t in TS[m]], xk, L, (), m)
+        body(u, gs, lambda T: XN(T, TS[m][0]), xk if L == 1 else [("XT", t // 2) for t in TS[m][::2]] + [("J", 0)], L, (), m)
         nq, sq = ("Q", "n" + u), ("Q", "q" + u)
         sb = ("Q", "B" + u)
         sk = [(sb, "sc%d" % j) for j in range(8)]
         off = 0.0 if BLIM[m] <= 2048 and u in CFG["names"] else 2048.0
         if off:
-            vec(128, [("cl", k), sk[0]], [(cn, 0)], lambda g, T, B: [g.vector.tensor_scalar(B(cn)[:], CL(T, k), -off, None, A.add)])
+            vec(128, [("cl", k)], [(cn, 0)], lambda g, T, B: [g.vector.tensor_scalar(B(cn)[:], CL(T, k), -off, None, A.add)])
         else:
             pool(S, [("cl", k)], [(cn, 0)], lambda g, T, B: [g.affine_select(B(cn)[:], CL(T, k), [[0, S]], A.is_gt, 0.0, 1, 0)], name="cn%d" % m)
-        pe(272, [(cn, 0), ("Dm", 0)] + sk, [(nq, 0)],
+        pe(272, [(cn, 0), ("Dm", 0)], [(nq, 0)],
            lambda g, T, B: [g.tensor.matmul(PS(T, B, nq, h * 136, h * 136 + 136), B(cn)[:, h * 128:h * 128 + 128], T.Dm[:], True, True) for h in range(2)])
         vec(272, sk + [("d0c", 0)], [(el, "e1")], lambda g, T, B: [g.vector.tensor_tensor_scan(T.e1[:], T.d0c[:], PS(T, B, sb, 0, 272), 0.0, A.add, A.min)])
         vec(272, sk + [(el, "e1")], [(el, "e2")], lambda g, T, B: [g.vector.tensor_tensor(T.e2[:], T.e1[:], PS(T, B, sb, 0, 272), A.not_equal)])
@@ -467,7 +487,7 @@ def build():
             kk = list(KIDS).index(m)
             vec(256, [(sq, 0)], [("snd", kk)], lambda g, T, B: [g.vector.tensor_scalar(T.snd[:, kk * S:kk * S + S], PS(T, B, sq, 0, S), cst, None, A.add)])
             send("a_n%d" % m, LV[m], lambda T: T.snd[:, kk * S:kk * S + S], lambda T: T.P[:, n0:n0 + S], ("snd", kk), ("P", m))
-        vec(256, [("P", m)], [("XE", 4 + m)], lambda g, T, B: [g.vector.tensor_scalar(XN(T, 4 + m), T.P[:, n0:n0 + S], -2048.0, None, A.add)], name="n%d" % m)
+        shift(256, [("P", m)], [("XE", 4 + m)], lambda T, B: [(XN(T, 4 + m), T.P[:, n0:n0 + S])], -2048.0, name="n%d" % m)
 
     def targets(ms, lst, lkeys):
         n, w = len(ms), S * len(ms)
@@ -478,7 +498,7 @@ def build():
 
         def a16(T, a, b):
             return T.h1[:, 16 * a:16 * b:16] if half else T.a16[:, a:b]
-        vec(16 * n, lkeys + [("init", 0), ("Cv", 0)] + [("f1", 0)] * (not half), [(dd, "a")],
+        vec(16 * n, lkeys + [(f1, 0)], [(dd, "a"), (f1, 0)],
             lambda g, T, B: [g.vector.tensor_scalar(T[f1][:, 0:w:16], lst(T), 16.0, None, A.add)]
             + [g.vector.tensor_scalar(T.a16[:, 0:16 * n], lst(T), -2048.0, None, A.add) for _ in range(not half)], calls=2 - half)
 
@@ -504,31 +524,31 @@ def build():
 
         def current(k, tab, out, key):
             lst, lkey = opener[k]
-            vec(0, segs(tab, ALIM[k]) + [lkey, ("NM", k), ("off", k)], [(cu, key)],
-                lambda g, T, B: [g.vector.tensor_tensor(out(T), TB(T, tab, 0, ALIM[k]).indirect(lst(T)), T.NM[:, k * S:k * S + S], A.max)], gn=S)
-        if z is None:
-            current(m, "U", lambda T: T.cur[:], 0)
+            vec(0, segs(tab, ALIM[k]) + [lkey, ("NM", k)], [(cu, key)],
+                lambda g, T, B: [g.vector.tensor_tensor(out(T), TB(T, tab, 0, ALIM[k]).indirect(lst(T)), T.NM[:, NMB[k] * S:NMB[k] * S + S], A.max)], gn=S)
+        if m in HELD:
+            copy(S, [("cl", HELD[m])], [(cu, 0)], lambda T: T.cur[:] if z is None else T.cur2[:, :, 16:32], lambda T: CL(T, HELD[m]))
+            dma("y", "r%d" % m, 0.1, [(cu, 0), ("NN", 0)], [(cu, 0)], lambda g, T, B: [g.sync.dma_start(T.cur[m::16, :] if z is None else T.cur2[m::16, :, 16:32], T.NN[m::16, :])])
         else:
-            current(m, "U", lambda T: T.cur3[:, 0:S], 2)
-            copy(S, [(cu, 2)], [(cu, 0)], lambda T: T.cur2[:, :, 16:32], lambda T: T.cur3[:, 0:S])
-            if z == PAIR[min(PAIR)]:
-                copy(S, [("NM", z), ("off", z)], [(cu, 1)], lambda T: T.cur2[:, :, 0:16], lambda T: T.NM[:, z * S:z * S + S])
-            else:
-                current(z, "Z", lambda T: T.cur3[:, S:2 * S], 3)
-                copy(S, [(cu, 3)], [(cu, 1)], lambda T: T.cur2[:, :, 0:16], lambda T: T.cur3[:, S:2 * S])
+            current(m, "U", lambda T: T.cur[:], 0)
+        if z == PAIR[min(PAIR)]:
+            copy(S, [("NM", z)], [(cu, 1)], lambda T: T.cur2[:, :, 0:16], lambda T: T.NM[:, NMB[z] * S:NMB[z] * S + S])
+        elif z is not None:
+            current(z, "Z", lambda T: T.cur3[:], 3)
+            copy(S, [(cu, 3)], [(cu, 1)], lambda T: T.cur2[:, :, 0:16], lambda T: T.cur3[:])
         for u in range(15, -1, -1):
             if z is None:
                 add("v", [(cu, 0), ("off", m), ("init", 0)], segs("U", lim),
                     lambda g, T, B, u=u: [g.vector.tensor_copy(TB(T, "U", -16, lim).indirect(T.off[:, OFF[m] + 2 * u:OFF[m] + 2 * u + 1]), T.cur[:, 16 * u:16 * u + 16])], sn=16)
             else:
-                add("v", [(cu, 0), (cu, 1), ("off", m), ("off", z), ("init", 0)], segs("U", lim) + segs("Z", 2432),
+                add("v", [(cu, 0), (cu, 1), ("off", m), ("off", z), ("init", 0)], segs("U", lim) + segs("Z", 2432) + [("Z", "q")],
                     lambda g, T, B, u=u: [g.vector.tensor_copy(T.U[:, 0:UB + 16 + lim].indirect(T.off[:, OFF[z] + 2 * u:OFF[z] + 2 * u + 2]), T.cur2[:, u, :])], sn=32)
 
     def place(m, k):
         copy(S, [("cl", k)], [("U", m)], lambda T: TB(T, "U", F + m * S, F + m * S + S), lambda T: CL(T, k), name="pl%d" % m)
 
     def readout(m, gs, fix):
-        body("R%d" % m, gs, lambda T: [XN(T, 4 + m)], [("XE", 4 + m)], 1, fix, None)
+        body("R%d" % m, gs, lambda T: XN(T, 4 + m), [("XE", 4 + m)], 1, fix, None)
 
     def refetch(sem, slot, ms, f0, lim):
         n = len(ms)
@@ -594,15 +614,7 @@ def build():
         mix(u)
     late(3, [0], 0)
     late(4, [0, 1], 1)
-    [t for t in tasks if t["name"] == "expE0"][0]["n"] += 1500
     return tasks
-
-
-def stage(name):
-    kind, u = name[:-2], name[-2:]
-    if u[0] in "ERF":
-        return {"g": "g", "xf": "f", "kp": "a", "mx": "a", "da": "a", "abs": "a", "sc": "s", "d": "z", "exp": "z", "K": "K"}.get(kind, "y") + u
-    return {"b": "el", "cn": "el", "senda_n": "sn", "senda_c": "col", "tg": "ext"}.get(name[:-1], name[:-1]) + name[-1]
 
 
 def link():
@@ -620,297 +632,87 @@ def link():
             lastw[k] = i
             readers[k] = []
         raw.discard(i)
-        t["dep"], t["stage"], t["dur"] = sorted(raw), stage(t["name"]), span(t, t["eng"], COST)
-        t["pre"] = sorted(raw | set(t.get("follow", [])))
+        t["dep"] = t["pre"] = sorted(raw)
         t["syms"] = sorted({k[0] for k in t["rd"] + t["wr"] if isinstance(k[0], tuple)}, key=str)
-        t["held"] = sorted({k[0][0] for k in t["rd"] if isinstance(k[0], tuple)})
         t["head"] = [s for s in t["syms"] if not any(s in tasks[d]["syms"] for d in t["dep"])]
         t["succ"] = []
         for d in t["pre"]:
             tasks[d]["succ"].append(i)
         for s in t["syms"]:
             users.setdefault(s, []).append(i)
-    for t in reversed(tasks):
-        t["way"] = t["dur"] + t["lat"] * COST["lat"] + t["bw"] * COST["bw"] + COST["hop"] + max([tasks[j]["way"] for j in t["succ"]] + [0.0])
     return tasks, users
 
 
-def plan(linked=None, fast=False, urgency=None, bound=None):
+def arrange(queues, linked=None):
     tasks, users = linked or link()
-    n, HOP = len(tasks), COST["hop"]
-    hold, shy = CFG["hold"], CFG["shy"]
-    rank = {s: k for k, s in enumerate(CFG["order"].split())}
-    pr = [1000.0 - i if t["name"] == "ld" else CFG["alpha"] * t["way"] + sum(hold.get(p, 0.0) for p in t["held"]) - CFG["beta"] * rank[t["stage"]]
-          + CFG["lift"].get(t["stage"], 0.0) + CFG["lift"].get(t["stage"][:-1], 0.0) for i, t in enumerate(tasks)]
-    pr = urgency or pr
-    mark = {t["name"]: i for i, t in enumerate(tasks)}
-    gate = [mark.get(CFG["gate"].get(t["stage"])) for t in tasks]
-    opens = {}
-    left = [len(t["pre"]) for t in tasks]
-    for i, k in enumerate(gate):
-        if k is not None:
-            opens.setdefault(k, []).append(i)
-            left[i] += 1
-    at, end, eng, dur, inn = [None] * n, [None] * n, [t["eng"] for t in tasks], [t["dur"] for t in tasks], [None] * n
-    free = {e: 0.0 for e in ("v", "s", "t", "p", "y", None, "dma")}
-    first = {("X", k): ("XI", k) for k in range(CFG["pools"]["X"])}
-    tenant, slot, before = dict(first), {s: x for x, s in first.items()}, {s: [] for s in first.values()}
-    order, last, joined = [], {}, set()
-    busy = {s: [len(v), 0.0] for s, v in users.items()}
-    piece, lent, lend = [t.get("piece") for t in tasks], [False] * n, {}
-    ready, cands = {e: [] for e in free if e != "dma"}, {}
-    turn = {p: [x for x in v.split() if (p, x) in users] for p, v in CFG["turn"].items()}
+    n, hop = len(tasks), COST["hop"]
+    named, line = {}, {}
+    for i, t in enumerate(tasks):
+        named.setdefault((t["name"], "g" if "piece" in t else t["eng"]), []).append(i)
+    for e, text in queues.items():
+        steps = [x.split("*")[0] for x in text.split() for _ in range(int((x + "*1").split("*")[1]))]
+        line[e] = [named[x, "g"].pop(-(e == "s")) if (x, "g") in named else named[x, e].pop(0) for x in steps][::-1]
+    line[None] = []
+    eng = {i: e for e in line for i in line[e]}
+    end, raw, order, slot, last = [None] * n, [None] * n, [], {}, {}
+    free, once = dict.fromkeys(list(line) + ["dma"], 0.0), dict(enumerate(COST["once"]))
+    tenant = {("X", k): ("XI", k) for k in range(POOLS["X"])}
+    before = {s: [] for s in tenant.values()}
+    left, clear = {s: len(v) for s, v in users.items()}, dict.fromkeys(users, 0.0)
+    out = [None] * n
 
-    def enter(j):
-        for e in [eng[j]] if piece[j] is None else ["v"] * (piece[j] == 0) + ["s"] * (piece[j] == 15):
-            ready[e].append(j)
-            cands.pop(e, None)
-
-    def offer(e):
-        out = []
-        for i in ready[e]:
-            urge = -pr[i]
-            if piece[i] is not None:
-                urge += shy.get(tasks[i]["name"], 0.0) * (e == "s") - CFG["stick"] * (last.get(e) == i + (1 if e == "s" else -1))
-            if lent[i]:
-                out.append((inn[i], urge, i, ()))
-                continue
-            t = tasks[i]
-            if inn[i] is None:
-                inn[i] = max([end[d] + HOP for d in t["dep"]] + [0.0 if gate[i] is None else at[gate[i]]])
-            a, got = inn[i], []
-            for s in t["syms"]:
-                if s in slot:
-                    a = max([a] + [busy[o][1] + HOP for o in before[s]])
-                    continue
-                if s[0] in turn and turn[s[0]][0] != s[1]:
-                    break
-                if s[0] not in lend:
-                    lend[s[0]] = [(max([busy[tenant[x]][1] + HOP for x in us if x in tenant] + [0.0]), c) for c, us in enumerate(LEND[s[0]])
-                                  if not any(x in tenant and busy[tenant[x]][0] for x in us)]
-                can = lend[s[0]]
+    def offer(i, e):
+        t = tasks[i]
+        if any(end[d] is None for d in t["pre"]):
+            return None
+        a, got = max([free[e]] + [end[d] + hop for d in t["dep"]]), []
+        for s in t["head"]:
+            if s not in before:
+                can = [(max([clear[tenant[x]] for x in us if x in tenant] + [0.0]), us) for us in LEND[s[0]] if not any(x in tenant and left[tenant[x]] for x in us)]
                 if not can:
-                    break
-                b = min(can)
-                if s[0] == "Q":
-                    b = ([c for c in can if c[0] <= free[e]] + [b])[0]
-                a = max(a, b[0])
-                got.append((s, b[1]))
-            else:
-                if not got:
-                    lent[i], inn[i] = True, a
-                out.append((a, urge, i, got))
-        return out
-    least = [dur[i] - (piece[i] is not None) * COST["vf"] for i in range(n)]
-    rem = sum(least[i] for i in range(n) if eng[i] in ("v", "s"))
-    for i in range(n):
-        if left[i] == 0:
-            enter(i)
-    while any(ready.values()):
-        t0 = e = None
-        for q in ready:
-            if q not in cands:
-                c = offer(q)
-                cands[q] = (c, max(free[q], min(c)[0]) if c else None)
-            if cands[q][1] is not None and (t0 is None or cands[q][1] < t0):
-                t0, e = cands[q][1], q
-        if t0 is None:
-            raise ValueError("no buffer to lend")
-        mine = sorted([c[1:3] + (max(c[0], free[e]), c[3]) for c in cands.pop(e)[0] if c[0] <= t0 + CFG["wait"]])
-        now = [c for c in mine if c[2] <= t0 + CFG["slack"]]
-        pick = now[0]
-        for h in mine:
-            if h[0] > pick[0] - CFG["gap"]:
-                break
-            if h[2] + CFG["tol"] < pick[2] + dur[pick[1]]:
-                fit = [c for c in now if c[2] + dur[c[1]] <= h[2] + CFG["tol"]]
-                pick = fit[0] if fit else h
-                break
-        _, i, a, got = pick
+                    return None
+                now = [c for c in can if c[0] + hop <= a] if s[0] == "Q" else []
+                got.append((s, (now + [min(can, key=lambda c: c[0])])[0][1]))
+            a = max([a] + [clear[o] + hop for o in (before[s] if s in before else {tenant[x] for x in got[-1][1] if x in tenant})])
+        return a, got
+    while any(line.values()):
+        offers = {e: offer(line[e][-1], e) for e in line if line[e]}
+        e = min([e for e in offers if offers[e]], key=lambda e: offers[e][0] if e else -1.0)
+        a, got = offers[e]
+        i = line[e].pop()
         t = tasks[i]
-        for s, c in got:
-            us = LEND[s[0]][c]
+        for s, us in got:
             before[s] = sorted({tenant[x] for x in us if x in tenant}, key=str)
             tenant.update({x: s for x in us})
             slot[s] = us[0]
-            if s[0] in turn:
-                turn[s[0]].pop(0)
-        ready[e].remove(i)
-        if piece[i] is not None:
-            step, other = (1, "s") if e == "v" else (-1, "v")
-            if last.get(e) == i - step and tasks[i - step]["name"] == t["name"]:
-                joined.add(i)
-            dur[i] = span(t, e, COST, i in joined)
-            if i in ready[other]:
-                ready[other].remove(i)
-                cands.pop(other, None)
-            else:
-                ready[e].append(i + step)
-        last[e], eng[i], at[i] = i, e, a
-        done = a + dur[i]
-        if e:
-            free[e] = done
-        lat = t["lat"] * COST["lat"]
+        joined = "piece" in t and last.get(e) == t["name"]
+        done = a + span(t, e, COST, joined) + (once.pop(t["sem"] == "sent", 0.0) if e == "p" and t["sem"] else 0.0)
+        last[e], free[e] = t["name"], done if e else 0.0
         if t["bw"]:
-            free["dma"] = max(done + lat / 2, free["dma"]) + t["bw"] * COST["bw"]
-            done = free["dma"] - lat / 2
-        end[i] = done + lat
+            free["dma"] = max(done + t["lat"] * COST["lat"] / 2, free["dma"]) + t["bw"] * COST["bw"]
+            done = free["dma"] - t["lat"] * COST["lat"] / 2
+        end[i] = done + t["lat"] * COST["lat"]
         for s in t["syms"]:
-            busy[s][0] -= 1
-            busy[s][1] = max(busy[s][1], end[i])
-            if got or not busy[s][0]:
-                lend.clear()
-                cands.clear()
+            left[s] -= 1
+            clear[s] = max(clear[s], end[i])
+        out[i] = dict(t, eng=e, at=a, end=end[i], joined=joined, raw=set(t["dep"]) | {k for s in t["head"] for o in before[s] for k in users[o]})
         order.append(i)
-        if bound and e in ("v", "s"):
-            rem -= least[i]
-            if free["v"] + free["s"] + rem > bound:
-                raise ValueError("bound")
-        for j in t["succ"] + opens.get(i, []):
-            left[j] -= 1
-            if left[j] == 0:
-                enter(j)
-    if len(order) < n:
-        raise ValueError("a gate closes a loop")
-    raw = [t["dep"] for t in tasks]
-    for s, os_ in before.items():
-        for j in users[s] if os_ else ():
-            if s in tasks[j]["head"]:
-                raw[j] = raw[j] + [k for o in os_ for k in users[o]]
-    if fast:
-        return eng, joined, raw, order, max(end)
-    out = [dict(t, eng=eng[i], at=at[i], end=end[i], dur=dur[i], raw=set(raw[i]), joined=i in joined) for i, t in enumerate(tasks)]
-    return out, order, slot, max(end)
-    while ready:
-        cand = []
-        for i in ready:
-            q = piece[i]
-            if q is not None:
-                front = q == 0 or end[i - 1] is not None and eng[i - 1] == "v"
-                back = q == 15 or end[i + 1] is not None and eng[i + 1] == "s"
-                if not (front or back):
-                    continue
-            elif lent[i]:
-                a, e = inn[i], eng[i]
-                cand.append((a if a > free[e] else free[e], -pr[i], i, (), e))
-                continue
-            t = tasks[i]
-            if inn[i] is None:
-                inn[i] = max([end[d] + HOP for d in t["dep"]] + [0.0 if gate[i] is None else at[gate[i]]])
-            a, got = inn[i], []
-            if all(s in slot for s in t["syms"]):
-                lent[i] = True
-                a = inn[i] = max([a] + [busy[o][1] + HOP for s in t["syms"] for o in before[s]])
-            for s in () if lent[i] else t["syms"]:
-                if s not in slot:
-                    if s[0] not in lend:
-                        lend[s[0]] = [(max([busy[tenant[x]][1] + HOP for x in us if x in tenant] + [0.0]), c) for c, us in enumerate(LEND[s[0]])
-                                      if not any(x in tenant and busy[tenant[x]][0] for x in us)]
-                    can = lend[s[0]]
-                    if not can:
-                        break
-                    b = min(can)
-                    if s[0] == "Q":
-                        b = ([c for c in can if c[0] <= free[eng[i]]] + [b])[0]
-                    a = max(a, b[0])
-                    got.append((s, b[1]))
-                else:
-                    a = max([a] + [busy[o][1] + HOP for o in before[s]])
-            else:
-                if q is not None:
-                    if front:
-                        cand.append((max(a, free["v"]), -pr[i], i, got, "v"))
-                    if back:
-                        cand.append((max(a, free["s"]), shy.get(t["name"], 0.0) - pr[i], i, got, "s"))
-                else:
-                    cand.append((max(a, free[eng[i]]), -pr[i], i, got, eng[i]))
-        if not cand:
-            raise ValueError("no buffer to lend")
-        t0, _, _, _, e = min(cand)
-        mine = sorted([c for c in cand if c[4] == e and c[0] <= t0 + CFG["wait"]], key=lambda c: c[1:3])
-        now = [c for c in mine if c[0] <= t0 + CFG["slack"]]
-        pick = now[0]
-        for h in mine:
-            if h[1] > pick[1] - CFG["gap"]:
-                break
-            if h[0] + CFG["tol"] < pick[0] + dur[pick[2]] and h[0] <= t0 + CFG["wait"]:
-                fit = [c for c in now if c[0] + dur[c[2]] <= h[0] + CFG["tol"]]
-                pick = fit[0] if fit else h
-                break
-        a, _, i, got, _ = pick
-        t = tasks[i]
-        for s, c in got:
-            us = LEND[s[0]][c]
-            before[s] = sorted({tenant[x] for x in us if x in tenant}, key=str)
-            tenant.update({x: s for x in us})
-            slot[s] = us[0]
-        if "piece" in t:
-            if last.get(e) == (i - 1 if e == "v" else i + 1) and tasks[last[e]]["name"] == t["name"]:
-                joined.add(i)
-            dur[i] = span(t, e, COST, i in joined)
-        last[e], eng[i], at[i] = i, e, a
-        done = a + dur[i]
-        if e:
-            free[e] = done
-        lat = t["lat"] * COST["lat"]
-        if t["bw"]:
-            free["dma"] = max(done + lat / 2, free["dma"]) + t["bw"] * COST["bw"]
-            done = free["dma"] - lat / 2
-        end[i] = done + lat
-        for s in t["syms"]:
-            busy[s][0] -= 1
-            busy[s][1] = max(busy[s][1], end[i])
-            if got or not busy[s][0]:
-                lend.clear()
-        order.append(i)
-        ready.remove(i)
-        for j in t["succ"] + opens.get(i, []):
-            left[j] -= 1
-            if left[j] == 0:
-                ready.append(j)
-    if len(order) < n:
-        raise ValueError("a gate closes a loop")
-    out = [dict(t, eng=eng[i], at=at[i], end=end[i], dur=dur[i], raw=set(t["dep"])) for i, t in enumerate(tasks)]
-    for i in joined:
-        out[i]["joined"] = True
-    for s, os_ in before.items():
-        for j in users[s]:
-            if not any(s in tasks[d]["syms"] for d in tasks[j]["dep"]):
-                for o in os_:
-                    out[j]["raw"].update(users[o])
+        line[None] += [j for j in t["succ"] if tasks[j]["eng"] is None]
     return out, order, slot, max(end)
 
 
 def rank_program(g, core, T, topo):
     rank = T.rank_of(core)
     cores = list(T.cores)
-    helper = {c: [h for h in topo.cores_of(c) if h not in cores and topo.die(h) == topo.die(c)][0] for c in cores}
-    if rank is None and core not in helper.values():
+    if rank is None:
         return
     if not _PLAN:
-        _PLAN.append(plan())
+        _PLAN.append(arrange(QUEUES))
     tasks, order, slot, _ = _PLAN[0]
 
     def B(s):
         p, k = slot[s]
         return 512 * k if p == "PS" else T[p + str(k)]
-
-    def far(u):
-        k = USES.index(u)
-        return T["D%d" % (k // 8)][:, k % 8 * S:k % 8 * S + S]
-    if rank is None:
-        home = [c for c in cores if helper[c] == core][0]
-        rid, pid, _ = topo.addr(home)
-        sent = 0
-        for i in order:
-            u = tasks[i].get("fold")
-            if u and tasks[i]["eng"]:
-                g.wait_ge(T.sem["y" + u], len(topo.engines(home, core)))
-                g.remote_dma(tasks[i]["home"](T, B), far(u), T.sem["k" + u], T.sem.sent, pid, rid, topo.mask(core, home))
-                sent += len(topo.engines(core, home))
-        if sent:
-            g.wait_ge(T.sem.sent, sent)
-        return
     Q = {"v": g.vector, "s": g.scalar, "t": g.tensor, "p": g, "y": g.sync}
 
     needed = set()
@@ -924,7 +726,7 @@ def rank_program(g, core, T, topo):
         if t.get("joined"):
             continue
         if e is None:
-            count[sem] = len(topo.engines(helper[core] if "fold" in t else cores[(rank - LV[int(sem[-1])]) % len(cores)], core))
+            count[sem] = len(topo.engines(cores[(rank - LV[int(sem[-1])]) % len(cores)], core))
             sig[i] = (sem, count[sem])
             continue
         want = {}
@@ -951,12 +753,6 @@ def rank_program(g, core, T, topo):
             rid, pid, _ = topo.addr(to)
             g.remote_dma(dst, src, T.sem[sm], T.sem.sent, pid, rid, topo.mask(core, to))
             count["sent"] = count.get("sent", 0) + len(topo.engines(core, to))
-        elif "fold" in t:
-            rid, pid, _ = topo.addr(helper[core])
-            g.remote_dma_fused([RemoteDMATransfer(dst_ids=[DstId(rid=rid, pnc=pid)], dma_engine_mask=topo.mask(core, helper[core]), remote_sem=T.sem["y" + t["fold"]],
-                                                  srcs=ins[0], dsts=[far(t["fold"])], alu_op=1)], local_sem=T.sem[sem])
-            count[sem] = len(topo.engines(core, helper[core]))
-            sig[i] = (sem, count[sem])
         elif sem:
             for x in ins:
                 x.then_inc(T.sem[sem], 16)

import math
from concourse.mybir import AluOpType, ActivationFunctionType

A = AluOpType
AF = ActivationFunctionType
F, S, W = 1664, 256, 3456
LV = (0, 0, 1, 0, 0, 1, 2)
TS = ((0,), (1,), (0, 1), (2,), (3,), (2, 3), (0, 1, 2, 3))
BLIM = (1664, 1920, 1664, 2176, 2688, 2432, 1664)
ALIM = (1664, 1664, 1664, 1920, 2176, 1664, 1664)
KIDS = {2: (0, 1), 5: (3, 4), 6: (2, 5)}
PAIR = {1: 6, 4: 5}
HELD = {0: 0, 1: 3, 4: 6}
NMB = {2: 0, 3: 1, 5: 2, 6: 3}
OFF = {0: 0, 2: 32, 6: 64, 1: 65, 3: 96, 5: 128, 4: 129}
UB = 16 + 2432
BASE = {"Z": 0, "U": UB}
BIG = 2.0 ** 25
USES = ["E%d" % _k for _k in range(7)] + ["R%d" % _k for _k in range(7)]
COST = dict(gam=1.45, sca=3.3, cy=0.00095, pc=0.00045, vf=0.05, sf=0.065, vp=0.04, sp=0.04, tp=0.01, hop=0.2, issue=0.85, lat=1.7, bw=1.1, send=1.2, hw=0.2, pf=1.0, once=(1.5, 4))
POOLS = dict(H=4, MX=2, X=3, D=8, Y=2)
NP = 16
CFG = dict(route=dict(zip(USES, "ATATTAAANNNANT")), total=dict(dict.fromkeys(USES, "dma"), E2="h3", E5="h3", R4="vec", R5="vec"), factor=("R1", "R3", "R5"),
           names=("E0", "E1", "E2", "E6"), keep=("R2", "R5", "R6"), back=("E1", "E3", "E4", "R6"), wide=("E2", "E6"), last="R6")
QUEUES = dict(
    v="""ld h0 ld cv ld*4 x nm c x ld*2 tg0 c1 c0 k1 gE0*8 gE6 k2 gE2*4 xt gE2*5 tg0 gE6 tg0 gE6 tg0 gE6
    ext0*2 gE2 ext0 xt ext0 lt ext0 el0 ext0*2 el0 ext0 el0 ext0 lt el0 gE6 ext0 gE6 b0 ext0 gE6 tg1 ext0 gE6 ext0*2 sn0 ext0 tg1 gE6 ext0 tg1 col0 sn0
    gE1*4 n0 gE1*4 tg1 gE1*2 ext1 el2 ext1 mxE1 ext1 el2 mxE1 el2 ext1 mxE1 ext1 el2 ext1 mxE1 ext1 b2 ext1 sn2 ext1 el1 ext1 el1 ext1 el1 ext1 sn2 ext1 el1 ext1*2 b1
    ext1 sn1 tg3 col1 ext2 sn1 ext2 lt n1 ext2 gE3 ext2 gE3 ext2 el6 ext2 gE3 ext2 el6 ext2 gE3 ext2 el6 ext2 tg3 ext2 el6 ext2 gE3 ext2 gE3*3 ext2 tg3 b6 ext2 mxE3
    ext2 sn6 ext2 mxE3 col2 tg3 ext3 mxE3 ext3 mxE3 el3 ext3 gE5 ext3 gE5 ext3 yE1 ext3 gE5 sn6 ext3 el3 ext3 el3 ext3 gE5 ext3 el3 ext3 ext4 gE5*2 ext3 el3 ext3 mxR1 b3
    el5 ext3 n2 sn3 ext3 gR2 tg5 ext3 mxR1 ext3 sn3 col3 tg5 n3 tg5 gE4*2 gR2*2 mxR1 tg5 ext4 gE4*3 ext4 gE4 ext4 el4 ext4 mxE4 gR2 mxE4 n6 ext4 yE3 mxE4 ext4 gR2*2
    ext4 mxE4 ext4 gF3 ext4 KE2 ext4 gR2 ext4 el5 ext4 KE2 ext4 el5 ext4 el5 ext4 el5 ext4 KE2 col6 b5 el4 sn5 col5 el4 col6 el4 sn5 mxR2 el4 mxR2 col5 b4
    mxR3 sn4 mxR3 mxR2 mxR3 sn4 col4 gF4 n5 n4 gR4*5 gR5*6 gR4 gR5 gR4*6 gR6 gR5*4 gR4 yR1 gR6*6 mxR5 gR6*3 mxR5 yE4 mxR5 mxR6*3
    sumR5 sumR4 sumR5 KE5 sumR5*2 KE5 sumR5 KE5 sumR5 sumR4 KE6 sumR5 sumR4 yR3 yR5 sumR4 yR5 KE6 sumR4*3 yR4 yR6*2""",
    s="""l_hv l_xs1 l_su1 ld*2 l_th1 ih fx gE0*8 gE2*4 absE0*3 gE2 gE6 gE2 absE0 gE6*4 expE0*2 absE2*2 expE0 gE6*2 absE2 expE0 absE2 absE6
    gE1*6 absE6 expE2*2 absR0 absE6 expR0 absE6 expE6 expE1 gE3*5 expE1*2 gE3*3 expE6 expE1 absR0 gE5 absR0 gE5*4 absR0 gE5*5 expE3*3 gR2*3 expE3
    absE5*2 gE4*6 absE5 gE4*4 absE5 expR1*4 expR0*3 gR2*6 absF3 expE5*4 expE4*3 expF3 expE4 expR2 expR3*4 gR4 gR5*5 expR2*2 yR1 expR2 gR6*2 gR4*2
    absF4 gR6*4 absR4*2 expF4 absR4 expR4 expR5*3 absR4 expR5 expR4 expR6 yR3 expR6 expR4 yR5 expR4 expR6*3 yR6""",
    t="""xt*2 daE0*3 scE0 tg0 daE0 scE0*3 el0 scE0*4 daE2*3 el0 scE2 daE2 tg1 scE2*3 sn0 daE6*2 scE2*4 mxE1 el2 daE6 daR0 daE6 el2 scE1*4 el1 sn2 scE6*5 el1
    lt dE1 scE6 sn1 scE6 dE1 scE6 dE1 tg3 el6 sumE1 daR0 dE1 el6 daR0 mxE3 sumE1*2 daR0 sumE1 scE3*4 sn6 dE3 el3 dE3*3 mxR1 el3
    daE5*2 sn3 sumE3 tg5 sumE3 daE5*2 dR1 sumE3*2 dR1 mxE4 dR1*2 scE5*3 el4 scE5*3 KE2 scE5*2 dF3 scE4 el5 scE4*3 mxR2 el5 dE4 sn5 dE4*2 el4 mxR3 dE4
    dR2 sn4 dR3*4 dR2*2 mxR5 sumE4*2 dR2 dF4 sumE4*2 mxR6 daR4*3 dR5*3 daR4 dR5 KE5 dR6*2 KE6 dR6 sumR6 dR6*2 sumR6*4""",
    p="""ld*3 k1 nm xt z0 k2 f0 k1 xi*2 ext0 k2 xt k2 cv k2*2 cn0 xi xfE3 k2 nn xfE1 xfE3 xfE1 cn2 lt cn6 ext1 xfE4 ext1 halfE0 xfE1 xfE3 cn1 pl0 xfE4 lt
    halfE2 lt kpE1 halfE0 senda_n2 halfE2 halfE0 xfR1 halfE6 xfE4 senda_c2 kpE3 xfR1 pl1 xfR1 halfE2 halfE6 halfE0 senda_n6 xfR2 ext4*2 halfE6 xfR2 pl3 gF3
    xfR3 halfE6 xfR3*2 halfR1 xfR2 kpE4 halfR0 xfR6 kpR2 halfR1 col6 pl2 halfE5 senda_n5 col5 gF4 senda_c5 halfR0 halfR1 senda_c6 xfR6 halfE5 halfR0
    halfR1 halfR3 xfR6 xfR5 halfE5 halfR2 kpR5 xfR5*2 halfR3 kpR6 halfR0 halfR2 halfR3 kpR6 halfR2 outF3 halfR3 halfR2 outF4""",
    y="""l_xs0 l_st cv l_su0 l_th0 cv z0 ext0 nn ext1 gF3 lt outE1 yE0 ext4 yE6 gF4 outE2 outR0 outE4 outR1 outR3 outE5 outR5 outR2 outE3 outE0 outE6 outR4 outR6*2""")

SCRATCH = {
    "P": ("sbuf", [128, W], "int32"), "U": ("sbuf", [128, UB + 16 + 2688], "int32"),
    "zb": ("sbuf", [128, 512], "float32"), "XE": ("sbuf", [128, 11 * S], "float16"), "XT": ("sbuf", [128, 4 * S], "float16"), "FX": ("sbuf", [128, 4 * S], "float32"),
    "st32": ("sbuf", [128, 48], "int32"), "stu": ("sbuf", [128, 48], "uint16"), "J": ("sbuf", [128, 64], "bfloat16"),
    "hb": ("sbuf", [128, 16], "bfloat16"), "lam": ("sbuf", [128, 32], "float32"), "LP": ("sbuf", [128, 32], "float16"), "LT": ("sbuf", [128, 128], "float16"),
    "Sel": ("sbuf", [128, 512], "bfloat16"), "Bs": ("sbuf", [128, 32], "float32"),
    "cl": ("sbuf", [128, 13 * S], "uint16"), "b16": ("sbuf", [128, 112], "uint16"), "off": ("sbuf", [128, 7 * 32], "uint16"),
    "fx32": ("sbuf", [128, 48], "int32"), "fxu": ("sbuf", [128, 48], "uint16"), "Gf": ("sbuf", [128, 768], "float16"),
    "C0": ("sbuf", [128, S], "float16"), "C1": ("sbuf", [128, S], "float16"), "pb": ("sbuf", [128, S], "float16"),
    "snd": ("sbuf", [128, 768], "int32"), "cur": ("sbuf", [128, S], "int32"), "cur2": ("sbuf", [128, 16, 32], "int32"), "cur3": ("sbuf", [128, S], "int32"),
    "NM": ("sbuf", [128, 4 * S], "int32"), "NN": ("sbuf", [128, S], "int32"),
    "e1": ("sbuf", [128, 272], "float32"), "e2": ("sbuf", [128, 272], "float32"), "e3": ("sbuf", [128, 272], "float32"),
    "Wm": ("sbuf", [128, S], "float16"), "a16": ("sbuf", [128, 32], "float16"), "Tb": ("sbuf", [128, 2 * S], "bfloat16"),
    "f1": ("sbuf", [128, 2 * S], "float32"), "f2": ("sbuf", [128, 3 * S], "float16"), "f3": ("sbuf", [128, 2 * S], "float32"),
    "h1": ("sbuf", [128, 3 * S], "float16"), "h3": ("sbuf", [128, 3 * S], "float16"),
    "d0c": ("sbuf", [128, 272], "float32"), "Mk": ("sbuf", [128, S], "float32"),
    "wl32": ("sbuf", [128, 16], "int32"), "wl": ("sbuf", [128, 16], "uint16"),
    "ip": ("sbuf", [128, 8], "int32"), "pc": ("sbuf", [128, 4], "float32"),
    "ones": ("sbuf", [128, 144], "bfloat16"), "Cv": ("sbuf", [128, 1920], "bfloat16"),
    "dg": ("sbuf", [128, 8 * 128], "bfloat16"), "FE": ("sbuf", [128, 768], "float32"),
    "GI": ("sbuf", [128, 32], "bfloat16"), "GI32": ("sbuf", [128, 8], "float32"), "Dm": ("sbuf", [128, 136], "bfloat16"),
    "YM": ("sbuf", [128, 1792], "float32"),
    "IH": ("sbuf", [128, 128], "float32"), "FA0": ("sbuf", [128, S], "float32"), "FA1": ("sbuf", [128, S], "float32"),
    "Bg": ("sbuf", [128, 16], "bfloat16"), "PS": ("psum", [128, 8 * 512], "float32"),
}
TILES = {"H": ("sbuf", [128, 4096 + 2 * S], "float16"), "MX": ("sbuf", [128, 4096], "float16"), "X": ("sbuf", [128, 2048], "float16"),
         "D": ("sbuf", [128, 2048], "float32"), "Y": ("sbuf", [128, S], "float32")}
SCRATCH.update({_p + str(_k): TILES[_p] for _p in TILES for _k in range(POOLS[_p])})
LEND = {_p: [((_p, _k),) for _k in range(_n)] for _p, _n in dict(POOLS, EL=1, TG=1, CU=1, CP=1, C=2, FA=2, PB=1).items()}
LEND.update(PD=[(("PS", _k), ("PS", _k + 1)) for _k in (0, 2, 4, 6)], Q=[(("PS", _k),) for _k in (7, 6, 5, 4, 3, 2, 1, 0)])
DMAS = ["cv0", "cv1", "nm0", "nm1", "z0", "sel", "l_st", "l_su0", "l_su1", "l_th0", "l_th1", "l_xs0", "l_xs1", "l_hv", "fx3", "fx4", "out", "hF3", "hF4", "oR0", "oR1", "r0", "r1", "r4"]
ARR = ["a_n2", "a_c2", "a_n5", "a_c5", "a_n6", "a_c6"]
SEMAPHORES = ["v", "s", "t", "p", "sent"] + DMAS + ARR + [_c + _u for _u in USES for _c in "hy"]
I1, I2, I4, I34, IQ, IM = 0, 1, 2, 3, 4, 7


def span(t, e, C, joined=False):
    if t["sem"] and e:
        return t["calls"] * (C["send"] if t["sem"] == "sent" else C["issue"] if e == "p" else C["hw"])
    if e == "t":
        return C["tp"] + t["n"] * C["pc"]
    if e == "p":
        return (170 * t["calls"] + 2 * t["n"]) * C["cy"] * C["pf"]
    if e is None:
        return 0.0
    n = t["n"] + t["gn"] * C["gam"] + t["sn"] * C["sca"]
    return (0 if joined else t["calls"]) * C[e + ("f" if t["gn"] or t["sn"] else "p")] + (n if e == "s" or t["sn"] else max(n, 64 * t["calls"])) * C["cy"]


def build():
    tasks, part = [], ["c"]

    def add(eng, rd, wr, fn, n=0, gn=0, sn=0, calls=1, sem=None, lat=0.0, bw=0.0, after=(), name="", **kw):
        tasks.append(dict(eng=eng, n=n, gn=gn, sn=sn, calls=calls, rd=list(rd), wr=list(wr), fn=fn, sem=sem, lat=lat, bw=bw, after=list(after), name=name or part[0], **kw))
        return len(tasks) - 1

    def vec(n, rd, wr, fn, **kw):
        return add("v", rd, wr, fn, n=n, **kw)

    def act(n, rd, wr, fn, **kw):
        return add("s", rd, wr, fn, n=n, **kw)

    def pe(n, rd, wr, fn, **kw):
        return add("t", rd, wr, fn, n=n, **kw)

    def pool(n, rd, wr, fn, **kw):
        return add("p", rd, wr, fn, n=n, **kw)

    def dma(q, sem, bw, rd, wr, fn, n=1, **kw):
        if sem[:2] == "l_":
            kw["name"] = sem
        return add(q, rd, wr, fn, calls=n, sem=sem, lat=1.0, bw=bw, **kw)

    def copy(n, rd, wr, out, src, **kw):
        return pool(n, rd, wr, lambda g, T, B: [g.affine_select(out(T), src(T), [[0, n]], A.is_gt, 0.0, 1, 0)], **kw)

    def shift(n, rd, wr, pairs, c, calls=1, name=""):
        return vec(n, rd, wr, lambda g, T, B: [g.vector.tensor_scalar(o, i, c, None, A.add) for o, i in pairs(T, B)], calls=calls, name=name)

    def segs(t, lim):
        return [(t, "o0"), (t, "o1")] + [(t, k) for k in range((lim - F) // S)]

    def DG(T, k):
        return T.dg[:, k * 128:k * 128 + 128]

    def PS(T, B, s, a, b, step=1, rows=128):
        return T.PS[0:rows, B(s) + a:B(s) + b:step]

    def XN(T, k):
        return T.XE[:, k // 2 * 2 * S + k % 2:k // 2 * 2 * S + 2 * S:2] if k < 4 else T.XE[:, k * S:k * S + S]

    def SL(buf, i, a=0, b=S, kept=False):
        return buf[:, 4096 + i * S + a:4096 + i * S + b] if kept and i < 2 else buf[:, 16 * a + i:16 * b:16]

    def TB(T, tab, a, b):
        return T.U[:, BASE[tab] + 16 + a:BASE[tab] + 16 + b]

    H = F // 2
    xk0 = [("U", k) for k in range(4)]
    dma("y", "l_st", 0.05, [], [("st32", 0)], lambda g, T, B: [g.sync.dma_start(T.st32[:], T.st[:])], name="ld")
    dma("s", "l_hv", 0.05, [], [("hb", 0)], lambda g, T, B: [g.scalar.dma_start(T.hb[:], T.hv[:])], name="ld")
    dma("y", "l_xs0", 0.45, [], xk0[:2], lambda g, T, B: [g.sync.dma_start(TB(T, "U", F, F + 512), T.xs[:, 0:512])], name="ld")
    dma("s", "l_xs1", 0.45, [], xk0[2:], lambda g, T, B: [g.scalar.dma_start(TB(T, "U", F + 512, F + 1024), T.xs[:, 512:1024])], name="ld")
    dma("y", "l_su0", 0.7, [], [("U", "o0")], lambda g, T, B: [g.sync.dma_start(TB(T, "U", 0, H), T.su[:, 0:H])], name="ld")
    dma("s", "l_su1", 0.7, [], [("U", "o1")], lambda g, T, B: [g.scalar.dma_start(TB(T, "U", H, F), T.su[:, H:F])], name="ld")
    dma("y", "l_th0", 0.7, [], [("P", "o0")], lambda g, T, B: [g.sync.dma_start(T.P[:, 0:H], T.th[:, 0:H])], name="ld")
    dma("s", "l_th1", 0.7, [], [("P", "o1")], lambda g, T, B: [g.scalar.dma_start(T.P[:, H:F], T.th[:, H:F])], name="ld")

    fl = dict(allow_small_or_imprecise_dtypes=True)
    turned = any(CFG["route"]["R%d" % m] == "T" for m in range(7))
    vec(72, [], [("ones", 0)], lambda g, T, B: [g.vector.memset(T.ones[:], 1.0)], name="ld")
    pool(1, [], [("ip", 0)], lambda g, T, B: [g.iota(T.ip[:, 0:1], [[0, 1]], 0, 1)], name="ld")
    pool(128, [("ones", 0)], [("dg", 0)], lambda g, T, B: [g.affine_select(DG(T, I1), T.ones[:, 0:128], [[-1, 128]], A.is_equal, 0.0, 0, 1)], name="ld")
    pool(256, [], [("Mk", 0)], lambda g, T, B: [g.iota(T.Mk[:], [[0, 16], [1, 16]], 0, 0, **fl)], name="ld")
    pool(8, [("ones", 0)], [("GI", 1)], lambda g, T, B: [g.affine_select(T.GI[:, 8:16], T.ones[:, 0:8], [[-16, 8]], A.is_ge, 0.0, 0, 1)], name="k1")
    pool(8, [("GI", 1)], [("GI", 0)], lambda g, T, B: [g.affine_select(T.GI[:, 0:8], T.GI[:, 8:16], [[16, 8]], A.is_ge, 0.0, 15, -1)], name="k1")
    pool(32, [("ones", 0)], [("Bs", 0)], lambda g, T, B: [g.affine_select(T.Bs[:], T.ones[:, 0:32], [[-4, 32]], A.is_ge, 0.0, 0, 1)], name="lt")
    pool(32, [("Bs", 0)], [("Bs", 0)], lambda g, T, B: [g.affine_select(T.Bs[:], T.Bs[:], [[4, 32]], A.is_ge, 0.0, 3, -1)], name="lt")
    pool(64, [("ones", 0)], [("J", 0)], lambda g, T, B: [g.affine_select(T.J[:], T.ones[:, 0:64], [[-2, 64]], A.is_ge, 0.0, 0, 1)], name="xt")
    pool(64, [("J", 0)], [("J", 0)], lambda g, T, B: [g.affine_select(T.J[:], T.J[:], [[2, 64]], A.is_ge, 0.0, 1, -1)], name="xt")
    pool(136, [("ones", 0)], [("Dm", 0)], lambda g, T, B: [g.affine_select(T.Dm[:], T.ones[:, 0:136], [[-16, 8], [-1, 17]], A.is_equal, 0.0, 1, 1)], name="k2")
    pool(16, [], [("wl32", 0)], lambda g, T, B: [g.iota(T.wl32[:], [[17, 16]], 16, 0)], name="k2")
    pool(136, [("Dm", 0)], [("Dm", 0)], lambda g, T, B: [g.affine_select(T.Dm[:], T.Dm[:], [[-16, 8], [-1, 17]], A.not_equal, -1.0, 0, 1)], name="k2")
    pool(8, [("ones", 0), ("Dm", 0)], [("Dm", 0)], lambda g, T, B: [g.affine_select(T.Dm[:, 16::17], T.ones[:, 0:8], [[-16, 8]], A.is_equal, 0.0, -15, 1)], name="k2")
    vec(1, [("ip", 0)], [("ip", 1)], lambda g, T, B: [g.vector.tensor_scalar(T.ip[:, 4:5], T.ip[:, 0:1], 15, None, A.bitwise_and)], name="ld")
    pool(272, [], [("d0c", 0)], lambda g, T, B: [g.iota(T.d0c[:], [[0, 272]], -1, 0, **fl)], name="k2")
    pool(272, [("d0c", 0)], [("d0c", 0)], lambda g, T, B: [g.affine_select(T.d0c[:], T.d0c[:], [[0, 16], [1, 17]], A.not_equal, BIG, 0, 0)], name="k2")
    vec(1, [("ip", 1)], [("pc", 0)], lambda g, T, B: [g.vector.tensor_copy(T.pc[:, 0:1], T.ip[:, 4:5])], name="ld")
    pool(2 * S, [], [("f1", 0)], lambda g, T, B: [g.iota(T.f1[:], [[0, 2 * S]], 0, 0, **fl)], name="f0")
    vec(128, [], [("init", 0)], lambda g, T, B: [g.vector.memset(T.Bg[:], BIG), g.vector.memset(T.U[:, UB:UB + 16], 0)], calls=2, name="ld")
    vec(384, [], [("h1", 0)], lambda g, T, B: [g.vector.memset(T.h1[:], 0.0)], name="h0")
    vec(256, [("Mk", 0), ("pc", 0)], [("Tc", 0)], lambda g, T, B: [g.vector.tensor_scalar(T.Tb[:, 0:S], T.Mk[:], T.pc[:, 0:1], 8192.0, A.is_gt, A.mult)], name="ld")
    vec(256, [("Mk", 0), ("pc", 0)], [("Mk", 0)], lambda g, T, B: [g.vector.tensor_scalar(T.Mk[:], T.Mk[:], T.pc[:, 0:1], None, A.is_equal)], name="ld")
    vec(48, [("st32", 0)], [("stu", 0)], lambda g, T, B: [g.vector.tensor_copy(T.stu[:], T.st32[:])], name="ld")
    for k in range(POOLS["X"]):
        pool(S, [("f1", 0)], [(("XI", k), 0)], lambda g, T, B, k=k: [g.affine_select(T["X%d" % k][:, 0::8], T.f1[:, 0:S], [[0, S]], A.is_gt, -4096.0, 0, 0)], name="xi")
    SC = (1.0, 2.0, 4.0, 0.75, 0.25, 0.125, 0.0625, -1.0)
    act(896, [("dg", 0)], [("dg", 1)], lambda g, T, B: [g.scalar.activation(DG(T, k), DG(T, I1), AF.Copy, scale=SC[k]) for k in range(1, 8)], calls=7, name="ld")
    act(1300, [("hb", 0)], [("lam", 0)], lambda g, T, B: [g.scalar.activation(T.lam[:, 0:16], T.hb[:], AF.Ln, scale=0.0625)], name="ld")
    act(128, [("dg", 0)], [("IH", 0)], lambda g, T, B: [g.scalar.activation(T.IH[:], DG(T, I1), AF.Copy, scale=0.5)], name="ih")
    vec(24, [("GI", 0)], [("GI32", 0)], lambda g, T, B: [g.vector.tensor_scalar(T.GI32[:], T.GI[:, 0:8], 16.0, None, A.mult),
                                                          g.vector.tensor_scalar(T.GI[:, 16:24], T.GI[:, 0:8], 32.0, None, A.mult),
                                                          g.vector.tensor_scalar(T.GI[:, 24:32], T.GI[:, 0:8], -16.0, None, A.mult)], calls=3, name="k1")
    vec(16, [("wl32", 0)], [("wl", 0)], lambda g, T, B: [g.vector.tensor_copy(T.wl[:], T.wl32[:])], name="k2")
    vec(128, [("Tc", 0)], [("Tc", 0)], lambda g, T, B: [g.vector.tensor_copy(T.Tb[:, S:2 * S], T.Tb[:, 0:S])], name="ld")
    vec(64, [("dg", 0)], [("Cv", 0)], lambda g, T, B: [g.vector.tensor_scalar(T.Cv[:, 0:128], DG(T, I1), -1.0, None, A.mult)], name="cv")
    for n, sem in ((128, "cv0"), (512, "cv1")):
        dma("y", sem, 0.001 * n, [("Cv", 0)], [("Cv", 0)], lambda g, T, B, n=n: [g.sync.dma_start(T.Cv[:, k * n:min(k * n + n, 1920)], T.Cv[:, 0:min(n, 1920 - k * n)]) for k in (1, 2, 3)], n=3, name="cv")
    pool(1920, [("Cv", 0)], [("Cv", 0)], lambda g, T, B: [g.affine_select(T.Cv[:], T.Cv[:], [[-1, 15], [-16, 8], [0, 16]], A.not_equal, 1.0, 0, 1)], name="cv")
    ZQ = UB // 4
    pool(ZQ, [], [("Z", "q")], lambda g, T, B: [g.iota(T.U[:, 0:ZQ], [[0, ZQ]], 0, 0)], name="z0")
    dma("y", "z0", 1.6, [("Z", "q")], segs("Z", 2432), lambda g, T, B: [g.sync.dma_start(T.U[:, k * ZQ:k * ZQ + ZQ], T.U[:, 0:ZQ]) for k in (1, 2, 3)], n=3, name="z0")
    pool(S, [], [("NN", 0)], lambda g, T, B: [g.iota(T.NN[:], [[1, S]], F, S)], name="nm")
    vec(S, [("NN", 0)], [("NN", 0)], lambda g, T, B: [g.vector.tensor_scalar(T.NN[:], T.NN[:], 16 * S - 1, None, A.bitwise_and)], name="nm")
    nk = [("NM", m) for m in NMB]
    dma("p", "nm0", 0.9, [("Z", "q"), ("Z", 0)], nk, lambda g, T, B: [g.dma_start(T.NM[:], T.U[:, 0:4 * S])], name="nn")
    dma("y", "nm1", 0.2, [("NN", 0)] + nk, nk, lambda g, T, B: [g.sync.dma_start(T.NM[m::16, k * S:k * S + S], T.NN[m::16, :]) for m, k in NMB.items()], n=4, name="nn")
    for h in range(2):
        shift(2 * S, xk0[2 * h:2 * h + 2], [("XE", 2 * h), ("XE", 2 * h + 1)], lambda T, B, h=h: [(XN(T, k), TB(T, "U", F + k * S, F + k * S + S)) for k in (2 * h, 2 * h + 1)], -2048.0, calls=2, name="x")
        xq = ("Q", "xt%d" % h)
        pe(512, [("XE", 2 * h), ("XE", 2 * h + 1), ("dg", 1)], [(xq, 0)],
           lambda g, T, B, h=h, xq=xq: [g.tensor.matmul(PS(T, B, xq, 128 * b, 128 * b + 128), T.XE[:, 512 * h + 128 * b:512 * h + 128 * b + 128], DG(T, IM), True, True) for b in range(4)], name="xt")
        shift(512, [(xq, 0)], [("XT", h)], lambda T, B, h=h, xq=xq: [(T.XT[:, 512 * h:512 * h + 512], PS(T, B, xq, 0, 512))], 0.0, name="xt")
    ft = [TS[m][0] for m in (0, 1, 3, 4) if CFG["route"]["E%d" % m] == "T" or CFG["route"]["E%d" % m] == "N" and "E%d" % m in CFG["factor"]]
    if ft:
        a, b = min(ft) * S, max(ft) * S + S
        act(b - a + 1500, xk0 + [("lam", 0)], [("FX", 0)], lambda g, T, B: [g.scalar.activation(T.FX[:, a:b], TB(T, "U", F + a, F + b), AF.Exp, bias=-4.0, scale=1.0 / 512)], name="fx")
    vec(2, [("pc", 0)], [("pc", 1)], lambda g, T, B: [g.vector.tensor_scalar(T.pc[:, 1:2], T.pc[:, 0:1], 6.0, None, A.not_equal), g.vector.memset(T.pc[:, 2:3], 1.0)], calls=2)
    if turned:
        lq = ("Q", "lt")
        vec(16, [("lam", 0)], [("LP", 0)], lambda g, T, B: [g.vector.tensor_scalar(T.LP[:, 0:16], T.lam[:, 0:16], -512.0, None, A.mult),
                                                             g.vector.tensor_scalar(T.lam[:, 16:32], T.lam[:, 0:16], -512.0, None, A.mult)], calls=2, name="lt")
        vec(32, [("LP", 0)], [("LP", 1)], lambda g, T, B: [g.vector.tensor_tensor(T.LP[:, 16:32], T.lam[:, 16:32], T.LP[:, 0:16], A.subtract)], name="lt")
        pe(128, [("LP", 1), ("dg", 0)], [(lq, 0)], lambda g, T, B: [g.tensor.matmul(PS(T, B, lq, 0, 128, rows=32), T.LP[:], DG(T, I1), True, True)], name="lt")
        vec(128, [(lq, 0)], [("LT", 0)], lambda g, T, B: [g.vector.tensor_copy(T.LT[0:32, :], PS(T, B, lq, 0, 128, rows=32))], name="lt")
        pool(512, [("f1", 0)], [("Sel", 0)], lambda g, T, B: [g.affine_select(T.Sel[0:32, :], T.f1[0:32, :], [[-1, 4], [0, 32], [-4, 4]], A.not_equal, 1.0, 0, 1)], name="lt")
        dma("y", "sel", 0.1, [("Sel", 0)], [("Sel", 0)], lambda g, T, B: [g.sync.dma_start(T.Sel[16:32, :], T.Sel[0:16, :])], name="lt")

    def CL(T, k, n=1):
        return T.cl[:, k * S:(k + n) * S]

    def take(lim, lst, lkey, k, name, n=1):
        vec(0, segs("U", lim) + [lkey], [("cl", k + j) for j in range(n)],
            lambda g, T, B: [g.vector.tensor_copy(CL(T, k, n), TB(T, "U", 0, lim).indirect(lst(T)))], gn=S * n, name=name)

    def gather(gs, k, lim):
        w = S // NP
        for q in range(NP):
            def fn(g, T, B, e, q, n):
                out, src = B(gs)[:, 16 * w * q:16 * w * (q + n)], T.P[:, 0:lim].indirect(T.cl[:, k * S + q * w:k * S + (q + n) * w])
                return [g.vector.tensor_scalar(out, src, -2048.0, None, A.add) if e == "v" else g.scalar.activation(out, src, AF.Identity, bias=-2048.0)]
            vec(0, segs("P", lim) + [("cl", k)], [(gs, q)], fn, gn=16 * w, name=gs[1], piece=q)

    sets = {}
    scanned = {g_: any(CFG["route"][u] != "A" for u in us) for us in (("E0",), ("E1", "R0"), ("E3", "R1"), ("E4", "R3"), ("R2",), ("R4",), ("R5",), ("R6",)) for g_ in ["g" + us[0]]}

    def tile(u, j):
        d = ("D", u + "ab"[j // 2])
        return (d, j), lambda B, a, b: B(d)[:, j % 2 * 1024 + a:j % 2 * 1024 + b]

    def two(on_pool, rd, wr, gs, back, name):
        if on_pool:
            pool(2 * S, rd, wr, lambda g, T, B: [g.affine_select(SL(B(gs), i, kept=not back), SL(B(gs), i, kept=back), [[0, S]], A.is_gt, 0.0, 1, 0) for i in range(2)], calls=2, name="kp" + name)
        else:
            vec(S, rd, wr, lambda g, T, B: [g.vector.tensor_copy(SL(B(gs), i, kept=not back), SL(B(gs), i, kept=back)) for i in range(2)], calls=2, name="mx" + name)

    def body(u, gs, xs, xk, L, skip, elect):
        route, kept = CFG["route"][u], scanned.get(gs[1], False)
        sl = sorted([i for i in range(16) if i not in skip], key=lambda i: i % 2 * (route != "A"))
        gk = [(gs, q) for q in range(NP)]
        if kept and gs[1][1:] == u:
            two(u in CFG["keep"], gk, [(gs, "kept")], gs, False, u)
        pk = gk + [(gs, "kept")] * kept
        el = ("Q", "B" + u)

        def ends(g, T, B, j):
            return [] if j else [g.tensor.matmul(PS(T, B, el, 16, 272, 17), DG(T, I1), T.Bg[:], True, True)]
        sets[u] = (gs, xs, xk, L, sl, kept, pk)
        if route != "A":
            mx, xe, xr = ("MX", u), ("X", u), ("Q", "x" + u)
            for c, n, calls in ((1, 3, 3), (4, 2, 1), (6, 2, 1)):
                def moves(T, B, c=c):
                    return [(B(xe)[:, k::8], xs(T)) for k in (1, 5, 4)] if c == 1 else [(B(xe)[:, c // 2::4], B(xe)[:, 1::4])]
                pool(S * n, xk if c == 1 else [(xe, 1)], [(xe, c)], lambda g, T, B, moves=moves, w=S * n // calls: [g.affine_select(o, i, [[0, w]], A.is_gt, 0.0, 1, 0) for o, i in moves(T, B)],
                     calls=calls, name="xf" + u)
            pe(S, xk + [("dg", 0)], [(xr, 0)], lambda g, T, B: [g.tensor.matmul(PS(T, B, xr, 0, S), DG(T, I1), xs(T), True, True)], name="mx" + u)
            vec(2 * S, [(gs, "kept"), (xr, 0)], [(gs, "first")],
                lambda g, T, B: [g.vector.tensor_tensor(SL(B(gs), i), SL(B(gs), i, kept=True), PS(T, B, xr, 0, S), A.max) for i in range(2)], calls=2, name="mx" + u)
            for t in range(2):
                vec(4 * S, gk + [(gs, "first")] + [(xe, c) for c in (1, 4, 6)], [(mx, t)],
                    lambda g, T, B, t=t: [g.vector.tensor_tensor_scan(B(mx)[:, t::2], B(xe)[:], B(gs)[:, t:16 * S:2], 0.0, A.min, A.max)], name="mx" + u)
            if route == "T":
                two(u in CFG["back"], [(gs, "kept")], [(gs, "first")], gs, True, u)
            for q in range(4 if elect is not None else 0):
                pe(1024, pk + [(mx, q // 2), ("GI32", 0), ("init", 0)], [(el, "sc%d" % (2 * q)), (el, "sc%d" % (2 * q + 1))],
                   lambda g, T, B, q=q: ends(g, T, B, q) + [g.tensor.matmul(PS(T, B, el, h * 136 + i, h * 136 + 136, 17), SL(B(b), i, 128 * h, 128 * h + 128, b == gs), T.GI[:, c:c + 8], c == 16, c == 24)
                                         for i in sl[4 * q:4 * q + 4] for h in range(2) for b, c in ((mx, 16), (gs, 24))], name="sc" + u)
            return
        lg = int(math.log2(L))
        pairs = sorted({t // 2 for t in TS[elect]}) if L > 1 else []
        for j in range(4):
            ss = sl[4 * j:4 * j + 4]
            w = S * len(ss)
            pd, (dk, de) = ("PD", "a" + u + str(j)), tile(u, j)

            def fn(g, T, B, ss=ss, pd=pd):
                o = []
                for c, i in enumerate(ss):
                    o.append(g.tensor.matmul(PS(T, B, pd, c * S, c * S + S), DG(T, lg), SL(B(gs), i, kept=kept), True, False))
                    if L == 1:
                        o.append(g.tensor.matmul(PS(T, B, pd, c * S, c * S + S), DG(T, IM), xs(T), False, True))
                    o += [g.tensor.matmul(PS(T, B, pd, c * S + 64 * b, c * S + 64 * b + 64), T.XT[:, 512 * h + 128 * b:512 * h + 128 * b + 128], T.J[:], False, h == pairs[-1] and b == 3)
                          for h in pairs for b in range(4)]
                return o
            pe(w * (1 + max(L // 2, 1)), pk + xk + [("dg", 0), ("dg", 1)], [(pd, 0)], fn, name="da" + u)
            act(w, [(pd, 0)], [dk], lambda g, T, B, pd=pd, de=de, w=w: [g.scalar.activation(de(B, 0, w), PS(T, B, pd, 0, w), AF.Abs)], name="abs" + u)
        for j in range(8 if elect is not None else 0):
            dk, de = tile(u, j // 2)
            pe(1024, [dk, ("GI32", 0), ("init", 0)], [(el, "sc%d" % j)],
               lambda g, T, B, j=j, de=de: ends(g, T, B, j) + [g.tensor.matmul(PS(T, B, el, h * 136 + i, h * 136 + 136, 17), de(B, (i % 4) * S + h * 128, (i % 4) * S + h * 128 + 128), T.GI32[:], True, True)
                                            for i in (2 * j, 2 * j + 1) for h in range(2)],
               name="sc" + u)

    def mix(u):
        gs, xs, xk, L, sl, kept, pk = sets[u]
        m, route, mx = int(u[1]), CFG["route"][u], ("MX", u)
        y = ("YM", m) if u[0] == "E" else (("Y", u), 0)
        hi = u[0] == "E" and L > 1
        b0 = math.log(1.0 / 32 if hi else 1.0 / 16)
        fac = route == "T" or route == "N" and u in CFG["factor"]
        how = "T" if route == "T" else CFG["total"][u]
        dk, de = zip(*[tile(u, j) for j in range(4)])
        osem = "o" + u if len(sl) < 16 else "out"
        rd, r2 = ("Q", "s" + u), ("Q", "z" + u)

        def Y(T, B):
            return T.YM[:, m * S:m * S + S] if u[0] == "E" else B(y[0])[:]

        def OUT(T):
            return T["ym" if u[0] == "E" else "yz"][:, m * S:m * S + S]
        for j in range(4):
            ss = sl[4 * j:4 * j + 4]
            w = S * len(ss)
            pd = ("PD", "e" + u + str(j))
            if route == "T":
                end = u == CFG["last"] and j == 3
                for k, cs in enumerate((range(4), range(4, 8)) if end else (range(8),)):
                    pd, key, c0, w, acc = ("Q", "e" + u + "ab"[k]) if end else pd, (dk[j][0], (j, k)), cs[0], 128 * len(cs), r2 if end else rd

                    def fn(g, T, B, j=j, pd=pd, cs=cs):
                        r = []
                        for c in cs:
                            a, t = 1024 * j + 512 * (c // 4), c % 4
                            ops = [(B(mx)[:, a + t:a + 512:4], DG(T, I2)), (B(gs)[:, a + t:a + 512:4], DG(T, IM))]
                            ops += [(T.Sel[0:32, 128 * t:128 * t + 128], T.LT[0:32, :])] * (u[0] == "R")
                            r += [g.tensor.matmul(PS(T, B, pd, 128 * (c - cs[0]), 128 * (c - cs[0] + 1)), l, x, n == 0, n == len(ops) - 1) for n, (l, x) in enumerate(ops)]
                        return r
                    pe(w * (2 if u[0] == "E" else 3), [(gs, "first"), (mx, 0), (mx, 1), ("dg", 1)] + [("LT", 0), ("Sel", 0)] * (u[0] == "R"), [(pd, 0)], fn, name="d" + u)
                    act(w, [(pd, 0)], [key], lambda g, T, B, j=j, pd=pd, c0=c0, w=w:
                        [g.scalar.activation(de[j](B, 128 * c0, 128 * c0 + w), PS(T, B, pd, 0, w), AF.Exp, bias=b0 if u[0] == "E" else 0.0, scale=-1.0 / 512)], name="exp" + u)
                    pe(2 * w, [key, ("Bs", 0)], [(acc, (j, k))],
                       lambda g, T, B, j=j, cs=cs, acc=acc: [g.tensor.matmul(PS(T, B, acc, 64 * j + 32 * (c // 4), 64 * j + 32 * (c // 4) + 32), de[j](B, 128 * c, 128 * c + 128), T.Bs[:], c % 4 == 0, c % 4 == 3)
                                                             for c in cs], name="sum" + u)
                continue
            if route == "N":
                def fn(g, T, B, ss=ss, pd=pd):
                    r = []
                    for c, i in enumerate(ss):
                        ops = [(IM, SL(B(gs), i, kept=True)), (I2, SL(B(mx), i))] + ([] if fac else [(IM, xs(T))])
                        r += [g.tensor.matmul(PS(T, B, pd, c * S, c * S + S), DG(T, k), a, n == 0, n == len(ops) - 1) for n, (k, a) in enumerate(ops)]
                    return r
                pe(w * (2 if fac else 3), pk + sorted({(mx, i % 2) for i in ss}) + [("dg", 1)] + ([] if fac else xk), [(pd, 0)], fn, name="d" + u)

            def SRC(T, B, a, b, j=j, pd=pd):
                return PS(T, B, pd, a, b) if route == "N" else de[j](B, a, b)
            src = (pd, 0) if route == "N" else dk[j]
            if u[0] == "E" and route == "A" and u in CFG["wide"]:
                if j % 2:
                    act(2 * w, dk[j - 1:j + 1], dk[j - 1:j + 1], lambda g, T, B, d=dk[j][0]: [g.scalar.activation(B(d)[:], B(d)[:], AF.Exp, bias=b0, scale=-1.0 / (512 * L))], name="exp" + u)
            elif u[0] == "E":
                act(w, [src], [dk[j]], lambda g, T, B, j=j, SRC=SRC: [g.scalar.activation(de[j](B, 0, 1024), SRC(T, B, 0, 1024), AF.Exp, bias=b0, scale=-1.0 / (512 * L))], name="exp" + u)
            else:
                begin = how == "vec" and j == 0
                act(w, [src, ("lam", 0)], [dk[j]] + [(rd, 0)] * begin,
                    lambda g, T, B, j=j, ss=ss, SRC=SRC, begin=begin: [g.scalar.activation(PS(T, B, rd, c * S, c * S + S) if begin and c < 2 else de[j](B, c * S, c * S + S), SRC(T, B, c * S, c * S + S), AF.Exp, bias=T.lam[:, i:i + 1], scale=-1.0 / 512)
                                                          for c, i in enumerate(ss)], calls=len(ss), name="exp" + u)
        fk, fa = [], ("Q" if how == "dma" else "FA", "f" + u)

        def FAC(T, B):
            return T.FX[:, TS[m][0] * S:TS[m][0] * S + S] if u[0] == "E" else PS(T, B, fa, 0, S) if how == "dma" else B(fa)[:]
        w3 = S * (len(sl) - 12)
        da, db = dk[0][0], dk[2][0]
        for n in (1024 + w3, 1024, 512, 256)[:{"h3": 3, "dma": 4}.get(how, 0)]:
            top = n > 1024
            dma("p", "h" + u, 3.4 * n / 2048, dk if top else dk[:2], dk[:2],
                lambda g, T, B, n=n, top=top: [g.dma_start(B(da)[:, 0:n], B(db)[:, 0:n] if top else B(da)[:, n:2 * n], accum_op=A.add)], name="half" + u)
        if fac and u[0] == "E":
            fk = [("FX", 0)]
        elif fac:
            fk = [(fa, 0)]
            act(256, xk, fk, lambda g, T, B: [g.scalar.activation(FAC(T, B), xs(T), AF.Exp, scale=1.0 / 512)], name="y" + u)
        if how == "vec":
            for j, c in [(j, c) for j in range(4) for c in (0, 2)][1:-1]:
                vec(2 * S, [dk[j], (rd, 0)], [(rd, 0)],
                    lambda g, T, B, j=j, c=c: [g.vector.tensor_tensor(PS(T, B, rd, 0, 2 * S), de[j](B, c * S, c * S + 2 * S), PS(T, B, rd, 0, 2 * S), A.add)], name="sum" + u)
            vec(2 * S, [dk[3], (rd, 0)], [(rd, 0), y],
                lambda g, T, B: [g.vector.tensor_tensor(Y(T, B), de[3](B, 2 * S, 3 * S), PS(T, B, rd, 0, S), A.add),
                                 g.vector.tensor_tensor(PS(T, B, rd, S, 2 * S), de[3](B, 3 * S, 4 * S), PS(T, B, rd, S, 2 * S), A.add)], calls=2, name="sum" + u)
            vec(256, [(rd, 0), y], [(rd, 0) if fac else y], lambda g, T, B: [g.vector.tensor_tensor(PS(T, B, rd, S, 2 * S) if fac else Y(T, B), PS(T, B, rd, S, 2 * S), Y(T, B), A.add)], name="y" + u)
            if fac:
                vec(256, [(rd, 0)] + fk, [y], lambda g, T, B: [g.vector.tensor_tensor(Y(T, B), PS(T, B, rd, S, 2 * S), FAC(T, B), A.mult)], name="y" + u)
        elif how == "h3":
            pass
        elif u == CFG["last"]:
            for a, b, acc, keys in ((0, 192, rd, [(j, 0) for j in range(3)]), (192, S, r2, [(3, 0), (3, 1)])):
                vec(b - a, [(acc, k) for k in keys] + fk, [(y[0], a)],
                    lambda g, T, B, a=a, b=b, acc=acc: [g.vector.tensor_tensor(B(y[0])[:, a:b], PS(T, B, acc, a, b), B(fa)[:, a:b], A.mult)], name="y" + u)
                dma("y", "y" + u, 0.3 * (b - a) / S, [(y[0], a)], [("oR", m, a)], lambda g, T, B, a=a, b=b: [g.sync.dma_start(T.yz[:, m * S + a:m * S + b], B(y[0])[:, a:b])], name="out" + u)
            return
        elif how == "T":
            vec(256, [(rd, (j, 0)) for j in range(4)] + fk, [y], lambda g, T, B: [g.vector.tensor_tensor(Y(T, B), PS(T, B, rd, 0, S), FAC(T, B), A.mult)], name="y" + u)
        elif fac:
            vec(256, [dk[0]] + fk, [y], lambda g, T, B: [g.vector.tensor_tensor(Y(T, B), de[0](B, 0, S), FAC(T, B), A.mult)], name="y" + u)
        elif u[0] == "R":
            dma("y", "y" + u if osem == "out" else osem, 0.3, [dk[0]], [("oR", m)], lambda g, T, B: [g.sync.dma_start(OUT(T), de[0](B, 0, S))], name="out" + u)
            return
        else:
            dma("y", "y" + u, 0.3, [dk[0]], [y], lambda g, T, B: [g.sync.dma_start(Y(T, B), de[0](B, 0, S))], name="y" + u)
        if hi:
            ka, kb = KIDS[m]
            kk = ("Q", "K" + u)
            pe(1024, [("YM", kb), ("IH", 0)], [(kk, 0)], lambda g, T, B: [g.tensor.matmul(PS(T, B, kk, 0, S), T.IH[:], T.YM[:, kb * S:kb * S + S], True, True)], name="K" + u)
            vec(256, [(kk, 0), ("YM", ka)], [(kk, 0)], lambda g, T, B: [g.vector.tensor_tensor(PS(T, B, kk, 0, S), PS(T, B, kk, 0, S), T.YM[:, ka * S:ka * S + S], A.mult)], name="K" + u)
            if how == "h3":
                vec(256, [dk[0], (kk, 0)], [(kk, 0)], lambda g, T, B: [g.vector.tensor_tensor(PS(T, B, kk, 0, S), PS(T, B, kk, 0, S), de[0](B, S, 2 * S), A.add)], name="K" + u)
            vec(256, [dk[0] if how == "h3" else y, (kk, 0)], [y],
                lambda g, T, B: [g.vector.tensor_tensor(Y(T, B), PS(T, B, kk, 0, S), de[0](B, 0, S) if how == "h3" else Y(T, B), A.add)], name="K" + u)
        dma("y", osem if u[0] == "E" or osem != "out" else "y" + u, 0.3, [y], [("o" + u[0], m)], lambda g, T, B: [g.sync.dma_start(OUT(T), Y(T, B))], name="out" + u)

    def late(slot, ms, f0):
        u = "F%d" % slot
        pd = ("Q", u)
        w = S * len(ms)

        def fn(g, T, B):
            o = []
            for m in ms:
                o.append(g.tensor.matmul(PS(T, B, pd, m * S, m * S + S), DG(T, IM), XN(T, 4 + m), True, False))
                for v in range(16):
                    o.append(g.tensor.matmul(PS(T, B, pd, m * S + 16 * v, m * S + 16 * v + 16), DG(T, I1), T.Gf[:, (f0 + m) * S + v:(f0 + m + 1) * S:16], False, v == 15))
            return o
        pe(5 * w, [("Gf", f0 + m) for m in ms] + [("XE", 4 + m) for m in ms] + [("dg", 0), ("dg", 1)], [(pd, 0)], fn, name="d" + u)
        act(w, [(pd, 0)], [("FE", f0)], lambda g, T, B: [g.scalar.activation(T.FE[:, f0 * S:f0 * S + w], PS(T, B, pd, 0, w), AF.Abs)], name="abs" + u)
        act(w, [("FE", f0), ("lam", 0)], [("FE", f0)],
            lambda g, T, B: [g.scalar.activation(T.FE[:, f0 * S:f0 * S + w], T.FE[:, f0 * S:f0 * S + w], AF.Exp, bias=T.lam[:, slot:slot + 1], scale=-1.0 / 512)], name="exp" + u)
        dma("p", "h" + u, 0.8, [("FE", f0)] + [("oR", m) for m in ms], [("oR", m) for m in ms],
            lambda g, T, B: [g.dma_start(T.yz[:, 0:w], T.FE[:, f0 * S:f0 * S + w], accum_op=A.add)], name="out" + u)

    def send(sem, l, src, dst, rkey, wkey):
        a = add("p", [rkey], [], lambda g, T, B: [(dst(T), src(T), sem, l)], sem="sent", name="send" + sem)
        add(None, [], [wkey], None, sem=sem, lat=2.0, after=[a], name="send" + sem)

    def elect(m, k):
        L = 1 << LV[m]
        u = "E%d" % m
        gs, el, cn, pb = ("H", "g" + u), ("EL", m), ("C", m), (("PB", m), 0)
        xk = [("XE", t) for t in TS[m]]
        part[0] = "el%d" % m
        gather(gs, k, BLIM[m])
        body(u, gs, lambda T: XN(T, TS[m][0]), xk if L == 1 else [("XT", t // 2) for t in TS[m][::2]] + [("J", 0)], L, (), m)
        nq, sq = ("Q", "n" + u), ("Q", "q" + u)
        sb = ("Q", "B" + u)
        sk = [(sb, "sc%d" % j) for j in range(8)]
        off = 0.0 if BLIM[m] <= 2048 and u in CFG["names"] else 2048.0
        if off:
            vec(128, [("cl", k)], [(cn, 0)], lambda g, T, B: [g.vector.tensor_scalar(B(cn)[:], CL(T, k), -off, None, A.add)])
        else:
            pool(S, [("cl", k)], [(cn, 0)], lambda g, T, B: [g.affine_select(B(cn)[:], CL(T, k), [[0, S]], A.is_gt, 0.0, 1, 0)], name="cn%d" % m)
        pe(272, [(cn, 0), ("Dm", 0)], [(nq, 0)],
           lambda g, T, B: [g.tensor.matmul(PS(T, B, nq, h * 136, h * 136 + 136), B(cn)[:, h * 128:h * 128 + 128], T.Dm[:], True, True) for h in range(2)])
        vec(272, sk + [("d0c", 0)], [(el, "e1")], lambda g, T, B: [g.vector.tensor_tensor_scan(T.e1[:], T.d0c[:], PS(T, B, sb, 0, 272), 0.0, A.add, A.min)])
        vec(272, sk + [(el, "e1")], [(el, "e2")], lambda g, T, B: [g.vector.tensor_tensor(T.e2[:], T.e1[:], PS(T, B, sb, 0, 272), A.not_equal)])
        vec(272, [(el, "e2"), (nq, 0)], [(el, "e3")], lambda g, T, B: [g.vector.tensor_tensor_scan(T.e3[:], PS(T, B, nq, 0, 272), T.e2[:], 0.0, A.add, A.mult)])
        vec(0, [(el, "e3"), ("wl", 0), ("Mk", 0)], [(el, "w")], lambda g, T, B: [g.vector.tensor_tensor(T.Wm[:], T.e3[:].indirect(T.wl[:]), T.Mk[:], A.mult)], gn=S)
        pe(128, [(el, "w"), ("GI", 0)], [(nq, "lp")],
           lambda g, T, B: [g.tensor.matmul(PS(T, B, nq, 288 + 8 * h, 296 + 8 * h), T.Wm[:, h * 128:h * 128 + 128], T.GI[:, 0:8], True, True) for h in range(2)])
        vec(16, [(nq, "lp")], [("b16", m)], lambda g, T, B: [g.vector.tensor_scalar(T.b16[:, 16 * m:16 * m + 16], PS(T, B, nq, 288, 304), off, None, A.add)], name="b%d" % m)
        part[0] = "sn%d" % m
        vec(0, segs("P", BLIM[m]) + [("b16", m)], [pb],
            lambda g, T, B: [g.vector.tensor_scalar(T.pb[:], T.P[:, 0:BLIM[m]].indirect(T.b16[:, 16 * m:16 * m + 16]), -2048.0, None, A.add)], gn=S)
        pe(256 * (1 + L), [pb, ("dg", 1)] + xk, [(sq, 0)],
           lambda g, T, B: [g.tensor.matmul(PS(T, B, sq, 0, S), DG(T, I34), T.pb[:], True, False)]
           + [g.tensor.matmul(PS(T, B, sq, 0, S), DG(T, IQ + LV[m]), XN(T, t), False, t == TS[m][-1]) for t in TS[m]])
        cst = 2048.0 - 0.5 + 1.0 / (8 * L)
        n0 = F + m * S
        if L == 1:
            vec(256, [(sq, 0)], [("P", m)], lambda g, T, B: [g.vector.tensor_scalar(T.P[:, n0:n0 + S], PS(T, B, sq, 0, S), cst, None, A.add)])
        else:
            kk = list(KIDS).index(m)
            vec(256, [(sq, 0)], [("snd", kk)], lambda g, T, B: [g.vector.tensor_scalar(T.snd[:, kk * S:kk * S + S], PS(T, B, sq, 0, S), cst, None, A.add)])
            send("a_n%d" % m, LV[m], lambda T: T.snd[:, kk * S:kk * S + S], lambda T: T.P[:, n0:n0 + S], ("snd", kk), ("P", m))
        shift(256, [("P", m)], [("XE", 4 + m)], lambda T, B: [(XN(T, 4 + m), T.P[:, n0:n0 + S])], -2048.0, name="n%d" % m)

    def targets(ms, lst, lkeys):
        n, w = len(ms), S * len(ms)
        dd, b6 = ("TG", ms[0]), ("PD" if n > 2 else "Q", "t%d" % ms[0])
        half = max(ALIM[m] for m in ms) + 16 <= 2048
        f1, f3 = ("h1", "h3") if half else ("f1", "f3")
        part[0] = "tg%d" % ms[0]

        def a16(T, a, b):
            return T.h1[:, 16 * a:16 * b:16] if half else T.a16[:, a:b]
        vec(16 * n, lkeys + [(f1, 0)], [(dd, "a"), (f1, 0)],
            lambda g, T, B: [g.vector.tensor_scalar(T[f1][:, 0:w:16], lst(T), 16.0, None, A.add)]
            + [g.vector.tensor_scalar(T.a16[:, 0:16 * n], lst(T), -2048.0, None, A.add) for _ in range(not half)], calls=2 - half)

        def fn(g, T, B):
            o = []
            for a in range(0, n, 2):
                b = min(a + 2, n)
                o += [g.tensor.matmul(PS(T, B, b6, a * S, b * S), DG(T, I1), T.Tb[:, 0:(b - a) * S], True, False)]
                o += [g.tensor.matmul(PS(T, B, b6, a * S + v + 1, b * S, 16), T.Cv[:, v * 128:v * 128 + 128], a16(T, 16 * a, 16 * b), False, v == 14) for v in range(15)]
            return o
        pe(w + 960 * (n + 1 >> 1), [(dd, "a"), ("dg", 0), ("Cv", 0), ("Tc", 0)], [(b6, 0)], fn)
        vec(w, [(b6, 0)], [(dd, "f2")], lambda g, T, B: [g.vector.tensor_scalar(T.f2[:, 0:w], PS(T, B, b6, 0, w), 0.0, None, A.not_equal)])
        vec(w // (1 + half), [(dd, "f2"), (dd, "a")], [(dd, "f3")], lambda g, T, B: [g.vector.tensor_tensor_scan(T[f3][:, 0:w], T.f2[:, 0:w], T[f1][:, 0:w], 0.0, A.mult, A.add)])
        runs = [(0, n)] if not set(ms) & set(PAIR) or n == 1 else [(k, k + 1) for k in range(n)]
        vec(16 * n, [(dd, "f3"), ("pc", 0)], [("off", m) for m in ms],
            lambda g, T, B: [g.vector.tensor_scalar(T.off[:, OFF[ms[a]]:OFF[ms[a]] // 2 * 2 + 32 * (b - a):2], T[f3][:, a * S + 15:b * S:16], T.pc[:, 0:1], float(UB * (ms[a] in PAIR)), A.max, A.add)
                             for a, b in runs], calls=len(runs))

    def extend(m):
        lim, z = ALIM[m], PAIR.get(m)
        cu = ("CU" if z is None else "CP", m)
        part[0] = "ext%d" % m

        def current(k, tab, out, key):
            lst, lkey = opener[k]
            vec(0, segs(tab, ALIM[k]) + [lkey, ("NM", k)], [(cu, key)],
                lambda g, T, B: [g.vector.tensor_tensor(out(T), TB(T, tab, 0, ALIM[k]).indirect(lst(T)), T.NM[:, NMB[k] * S:NMB[k] * S + S], A.max)], gn=S)
        if m in HELD:
            copy(S, [("cl", HELD[m])], [(cu, 0)], lambda T: T.cur[:] if z is None else T.cur2[:, :, 16:32], lambda T: CL(T, HELD[m]))
            dma("y", "r%d" % m, 0.1, [(cu, 0), ("NN", 0)], [(cu, 0)], lambda g, T, B: [g.sync.dma_start(T.cur[m::16, :] if z is None else T.cur2[m::16, :, 16:32], T.NN[m::16, :])])
        else:
            current(m, "U", lambda T: T.cur[:], 0)
        if z == PAIR[min(PAIR)]:
            copy(S, [("NM", z)], [(cu, 1)], lambda T: T.cur2[:, :, 0:16], lambda T: T.NM[:, NMB[z] * S:NMB[z] * S + S])
        elif z is not None:
            current(z, "Z", lambda T: T.cur3[:], 3)
            copy(S, [(cu, 3)], [(cu, 1)], lambda T: T.cur2[:, :, 0:16], lambda T: T.cur3[:])
        for u in range(15, -1, -1):
            if z is None:
                add("v", [(cu, 0), ("off", m), ("init", 0)], segs("U", lim),
                    lambda g, T, B, u=u: [g.vector.tensor_copy(TB(T, "U", -16, lim).indirect(T.off[:, OFF[m] + 2 * u:OFF[m] + 2 * u + 1]), T.cur[:, 16 * u:16 * u + 16])], sn=16)
            else:
                add("v", [(cu, 0), (cu, 1), ("off", m), ("off", z), ("init", 0)], segs("U", lim) + segs("Z", 2432) + [("Z", "q")],
                    lambda g, T, B, u=u: [g.vector.tensor_copy(T.U[:, 0:UB + 16 + lim].indirect(T.off[:, OFF[z] + 2 * u:OFF[z] + 2 * u + 2]), T.cur2[:, u, :])], sn=32)

    def place(m, k):
        copy(S, [("cl", k)], [("U", m)], lambda T: TB(T, "U", F + m * S, F + m * S + S), lambda T: CL(T, k), name="pl%d" % m)

    def readout(m, gs, fix):
        body("R%d" % m, gs, lambda T: XN(T, 4 + m), [("XE", 4 + m)], 1, fix, None)

    def refetch(sem, slot, ms, f0, lim):
        n = len(ms)
        nm = "gF%d" % slot
        dma("y", sem, 0.5, [("U", m) for m in ms], [("fx32", f0)],
            lambda g, T, B: [g.sync.dma_start(T.fx32[:, 16 * (f0 + m):16 * (f0 + m) + 16], T.U[slot::16, UB + 16 + F + m * S:UB + 16 + F + m * S + S]) for m in ms], n=n, name=nm)
        copy(16 * n, [("fx32", f0)], [("fxu", f0)], lambda T: T.fxu[:, 16 * f0:16 * (f0 + n)], lambda T: T.fx32[:, 16 * f0:16 * (f0 + n)], name=nm)
        vec(0, segs("P", lim) + [("fxu", f0)], [("Gf", f0 + m) for m in ms],
            lambda g, T, B: [g.vector.tensor_scalar(T.Gf[:, f0 * S:(f0 + n) * S], T.P[:, 0:lim].indirect(T.fxu[:, 16 * f0:16 * (f0 + n)]), -2048.0, None, A.add)], gn=S * n, name=nm)

    def stl(l, n=1):
        return (lambda T: T.stu[:, 16 * l:16 * (l + n)]), ("stu", 0)

    def bl(m):
        return (lambda T: T.b16[:, 16 * m:16 * m + 16]), ("b16", m)

    take(F, *stl(0), 0, "c0")
    take(F, *stl(1, 2), 1, "c1", 2)
    opener = {0: stl(0), 1: bl(0), 2: stl(1), 3: bl(1), 4: bl(3), 5: bl(2), 6: stl(2)}
    elect(0, 0)
    elect(2, 1)
    for m in (0, 1, 2, 3, 4):
        if m == 4:
            elect(5, 5)
        if m in (1, 3, 4):
            elect(m, 3 + {1: 0, 3: 1, 4: 3}[m])
        if m == 0:
            targets((0, 2, 6), stl(0, 3)[0], [("stu", 0)])
        elif m == 4:
            targets((5, 4), lambda T: T.b16[:, 32:64], [("b16", 2), ("b16", 3)])
        elif m != 2:
            targets((m,), opener[m][0], [opener[m][1]])
        extend(m)
        if m == 3:
            refetch("fx3", 3, [0], 0, 2688)
        if m == 4:
            refetch("fx4", 4, [0, 1], 1, 2944)
        take(BLIM[m], *bl(m), 3 + m, "col%d" % m)
        if m == 2:
            send("a_c2", 1, lambda T: CL(T, 5), lambda T: CL(T, 10), ("cl", 5), ("cl", 10))
            place(2, 10)
        elif m < 4:
            place(m, 3 + m)
    elect(6, 2)
    for m in (5, 6):
        lst, lkey = bl(m)
        zb, cu, nm = ("zb", m), ("CU", "c%d" % m), "col%d" % m
        vec(0, segs("Z", BLIM[m]) + [lkey, ("pc", 1)], [zb],
            lambda g, T, B, m=m, lst=lst: [g.vector.tensor_scalar(T.zb[:, (m - 5) * S:(m - 4) * S], TB(T, "Z", 0, BLIM[m]).indirect(lst(T)), T.pc[:, m - 4:m - 3], None, A.mult)], gn=S, name=nm)
        vec(0, segs("U", BLIM[m]) + [lkey, zb], [(cu, 0)],
            lambda g, T, B, m=m, lst=lst: [g.vector.tensor_tensor(T.cur[:], TB(T, "U", 0, BLIM[m]).indirect(lst(T)), T.zb[:, (m - 5) * S:(m - 4) * S], A.max)], gn=S, name=nm)
        copy(S, [(cu, 0)], [("cl", 3 + m)], lambda T, m=m: CL(T, 3 + m), lambda T: T.cur[:], name=nm)
        send("a_c%d" % m, LV[m], lambda T, m=m: CL(T, 3 + m), lambda T, m=m: CL(T, 6 + m), ("cl", 3 + m), ("cl", 6 + m))
    for u in USES[:7]:
        mix(u)
    readout(0, ("H", "gE1"), (3, 4))
    readout(1, ("H", "gE3"), (4,))
    readout(3, ("H", "gE4"), ())
    for m, k in ((2, 10), (4, 7), (5, 11), (6, 12)):
        gather(("H", "gR%d" % m), k, F + (m + 1) * S)
        readout(m, ("H", "gR%d" % m), ())
    for u in USES[7:]:
        mix(u)
    late(3, [0], 0)
    late(4, [0, 1], 1)
    return tasks


def link():
    tasks = build()
    lastw, readers, users = {}, {}, {}
    for i, t in enumerate(tasks):
        raw = set(t["after"]) | {lastw[k] for k in t["rd"]}
        for k in t["wr"]:
            if k in lastw:
                raw.add(lastw[k])
            raw.update(readers.get(k, []))
        for k in t["rd"]:
            readers.setdefault(k, []).append(i)
        for k in t["wr"]:
            lastw[k] = i
            readers[k] = []
        raw.discard(i)
        t["dep"] = t["pre"] = sorted(raw)
        t["syms"] = sorted({k[0] for k in t["rd"] + t["wr"] if isinstance(k[0], tuple)}, key=str)
        t["head"] = [s for s in t["syms"] if not any(s in tasks[d]["syms"] for d in t["dep"])]
        t["succ"] = []
        for d in t["pre"]:
            tasks[d]["succ"].append(i)
        for s in t["syms"]:
            users.setdefault(s, []).append(i)
    return tasks, users


def arrange(queues, linked=None):
    tasks, users = linked or link()
    n, hop = len(tasks), COST["hop"]
    named, line = {}, {}
    for i, t in enumerate(tasks):
        named.setdefault((t["name"], "g" if "piece" in t else t["eng"]), []).append(i)
    for e, text in queues.items():
        steps = [x.split("*")[0] for x in text.split() for _ in range(int((x + "*1").split("*")[1]))]
        line[e] = [named[x, "g"].pop(-(e == "s")) if (x, "g") in named else named[x, e].pop(0) for x in steps][::-1]
    line[None] = []
    eng = {i: e for e in line for i in line[e]}
    end, raw, order, slot, last = [None] * n, [None] * n, [], {}, {}
    free, once = dict.fromkeys(list(line) + ["dma"], 0.0), dict(enumerate(COST["once"]))
    tenant = {("X", k): ("XI", k) for k in range(POOLS["X"])}
    before = {s: [] for s in tenant.values()}
    left, clear = {s: len(v) for s, v in users.items()}, dict.fromkeys(users, 0.0)
    out = [None] * n

    def offer(i, e):
        t = tasks[i]
        if any(end[d] is None for d in t["pre"]):
            return None
        a, got = max([free[e]] + [end[d] + hop for d in t["dep"]]), []
        for s in t["head"]:
            if s not in before:
                can = [(max([clear[tenant[x]] for x in us if x in tenant] + [0.0]), us) for us in LEND[s[0]] if not any(x in tenant and left[tenant[x]] for x in us)]
                if not can:
                    return None
                now = [c for c in can if c[0] + hop <= a] if s[0] == "Q" else []
                got.append((s, (now + [min(can, key=lambda c: c[0])])[0][1]))
            a = max([a] + [clear[o] + hop for o in (before[s] if s in before else {tenant[x] for x in got[-1][1] if x in tenant})])
        return a, got
    while any(line.values()):
        offers = {e: offer(line[e][-1], e) for e in line if line[e]}
        e = min([e for e in offers if offers[e]], key=lambda e: offers[e][0] if e else -1.0)
        a, got = offers[e]
        i = line[e].pop()
        t = tasks[i]
        for s, us in got:
            before[s] = sorted({tenant[x] for x in us if x in tenant}, key=str)
            tenant.update({x: s for x in us})
            slot[s] = us[0]
        joined = "piece" in t and last.get(e) == t["name"]
        done = a + span(t, e, COST, joined) + (once.pop(t["sem"] == "sent", 0.0) if e == "p" and t["sem"] else 0.0)
        last[e], free[e] = t["name"], done if e else 0.0
        if t["bw"]:
            free["dma"] = max(done + t["lat"] * COST["lat"] / 2, free["dma"]) + t["bw"] * COST["bw"]
            done = free["dma"] - t["lat"] * COST["lat"] / 2
        end[i] = done + t["lat"] * COST["lat"]
        for s in t["syms"]:
            left[s] -= 1
            clear[s] = max(clear[s], end[i])
        out[i] = dict(t, eng=e, at=a, end=end[i], joined=joined, raw=set(t["dep"]) | {k for s in t["head"] for o in before[s] for k in users[o]})
        order.append(i)
        line[None] += [j for j in t["succ"] if tasks[j]["eng"] is None]
    return out, order, slot, max(end)


def rank_program(g, core, T, topo):
    rank = T.rank_of(core)
    cores = list(T.cores)
    if rank is None:
        return
    if not _PLAN:
        _PLAN.append(arrange(QUEUES))
    tasks, order, slot, _ = _PLAN[0]

    def B(s):
        p, k = slot[s]
        return 512 * k if p == "PS" else T[p + str(k)]
    Q = {"v": g.vector, "s": g.scalar, "t": g.tensor, "p": g, "y": g.sync}

    needed = set()
    for i in order:
        if tasks[i]["eng"]:
            needed.update(tasks[i]["raw"])
    count, sig, seen = {}, {}, {q: {} for q in Q}
    for i in order:
        t = tasks[i]
        e, sem = t["eng"], t["sem"]
        if t.get("joined"):
            continue
        if e is None:
            count[sem] = len(topo.engines(cores[(rank - LV[int(sem[-1])]) % len(cores)], core))
            sig[i] = (sem, count[sem])
            continue
        want = {}
        for d in t["raw"]:
            sm, val = sig[d]
            want[sm] = max(want.get(sm, 0), val)
        for sm in sorted(want):
            if seen[e].get(sm, 0) < want[sm]:
                Q[e].wait_ge(T.sem[sm], want[sm])
                seen[e][sm] = want[sm]
        if "piece" in t:
            n, step = 1, 1 if e == "v" else -1
            while tasks[i + n * step].get("joined") and tasks[i + n * step]["eng"] == e:
                n += 1
            t["fn"](g, T, B, e, min(t["piece"], t["piece"] + (n - 1) * step), n)[0].then_inc(T.sem[e], 1)
            count[e] = count.get(e, 0) + 1
            for k in range(n):
                sig[i + k * step] = (e, count[e])
            continue
        ins = t["fn"](g, T, B)
        if sem == "sent":
            dst, src, sm, l = ins[0]
            to = cores[(rank + l) % len(cores)]
            rid, pid, _ = topo.addr(to)
            g.remote_dma(dst, src, T.sem[sm], T.sem.sent, pid, rid, topo.mask(core, to))
            count["sent"] = count.get("sent", 0) + len(topo.engines(core, to))
        elif sem:
            for x in ins:
                x.then_inc(T.sem[sem], 16)
            count[sem] = count.get(sem, 0) + 16 * len(ins)
            sig[i] = (sem, count[sem])
        elif i in needed:
            ins[-1].then_inc(T.sem[e], 1)
            count[e] = count.get(e, 0) + 1
            sig[i] = (e, count[e])
    for sm in sorted(count):
        if max(seen[q].get(sm, 0) for q in Q) < count[sm]:
            g.sync.wait_ge(T.sem[sm], count[sm])


_PLAN = []
